import numpy as np
import ml_dtypes


def mxq(x, axis, fmt="e4m3"):
    dtype, down = {"e4m3": (ml_dtypes.float8_e4m3fn, 7), "e5m2": (ml_dtypes.float8_e5m2, 14)}[fmt]
    v = np.moveaxis(np.asarray(x, np.float32).astype(ml_dtypes.bfloat16).astype(np.float64), axis, -1)
    blocks = v.reshape(v.shape[:-1] + (-1, 32))
    amax = np.abs(blocks).max(-1, keepdims=True)
    byte = np.maximum(np.where(amax > 0, np.frexp(amax)[1] - 1 + 127, 0) - down, 1)
    scale = np.exp2(byte - 127.0)
    codes = (blocks / scale).astype(np.float32).astype(dtype).astype(np.float64)
    return np.moveaxis((codes * scale).reshape(v.shape), -1, axis)


WIDE = False


def mx_kscale(k):
    if not WIDE:
        return np.ones(k)
    levels = np.array([10, -10, 5, -5, 0])
    if k % 512:
        return np.exp2(np.random.permutation(np.resize(levels, k // 32))).repeat(32)
    a = np.empty((k // 512, 16))
    for p in range(k // 512):
        a[p, :8] = np.random.permutation(np.resize(levels, 8))
        for g in range(8):
            far = levels[np.abs(levels - a[p, g]) >= 10]
            a[p, g + 8] = far[np.random.randint(len(far))]
    return np.exp2(a.ravel()).repeat(32)


def f64(x):
    return np.asarray(x).astype(np.float64)


def striped(idx):
    return np.tile(idx.reshape(-1, 16).T, (8, 1)).astype(np.uint16)


def unstriped(offs):
    return offs[:16].T.reshape(-1).astype(np.int64)


E2M1 = np.array([0.0, 0.5, 1.0, 1.5, 2.0, 3.0, 4.0, 6.0, -0.0, -0.5, -1.0, -1.5, -2.0, -3.0, -4.0, -6.0])


def pack_weight(w, fmt):
    k, n = w.shape
    w = f64(np.asarray(w, np.float32).astype(ml_dtypes.bfloat16)).reshape(k // 32, 32, n)
    amax = np.abs(w).max(1)
    if fmt == "e4m3":
        byte = np.frexp(amax)[1] - 1 + 127 - 7
    else:
        mant, ex = np.frexp(amax / 6.0)
        byte = np.where(mant > 0.5, ex, ex - 1) + 127
    byte = np.clip(np.where(amax > 0, byte, 1), 1, 254)
    scaled = (w * np.exp2(127.0 - byte)[:, None, :]).reshape(k, n).astype(np.float32)
    by_word = np.ascontiguousarray(scaled.reshape(k // 512, 128, 4, n).transpose(0, 1, 3, 2))
    if fmt == "e4m3":
        words = by_word.astype(ml_dtypes.float8_e4m3fn).view(np.uint8)
    else:
        c = by_word.astype(ml_dtypes.float4_e2m1fn).view(np.uint8) & 0xF
        words = (c[..., 0::2] | (c[..., 1::2] << 4)).reshape(k // 512, 128, 2 * n)
    return np.ascontiguousarray(words), np.ascontiguousarray(byte.astype(np.uint8).reshape(k // 512, 16, n))


def unpack_weight(words, scales, fmt):
    g, _, n = scales.shape
    words = np.ascontiguousarray(words).reshape(g, 128, n, -1)
    if fmt == "e4m3":
        vals = words.view(ml_dtypes.float8_e4m3fn).astype(np.float64)
    else:
        nib = np.empty((g, 128, n, 4), np.uint8)
        nib[..., 0::2] = words & 0xF
        nib[..., 1::2] = words >> 4
        vals = E2M1[nib]
    vals = vals * np.repeat(np.exp2(scales.astype(np.float64) - 127.0), 8, axis=1)[..., None]
    return vals.transpose(0, 1, 3, 2).reshape(g * 512, n)


def gelu(v):
    return 0.5 * v * (1.0 + np.tanh(np.sqrt(2.0 / np.pi) * (v + 0.044715 * v**3)))


K, T, S, H, P, N = 512, 2048, 1024, 1536, 512, 768

def setup_inputs():
    n = np.random.standard_normal
    s = mx_kscale(K)[:, None]
    u = mx_kscale(H)[:, None]
    d = {}
    d["tab_words"], d["tab_scales"] = pack_weight(n((K, T)) * s, "e4m3")
    d["offs"] = striped(np.random.permutation(T)[:S])
    d["pos1"] = striped(np.random.permutation(S)[:P])
    d["pos2"] = striped(np.random.permutation(S)[:P])
    d["pos3"] = striped(np.random.permutation(S)[:P])
    d["w1"] = (0.45 * n((K, H)) / np.sqrt(K) / s).astype(np.float32)
    d["w4_words"], d["w4_scales"] = pack_weight(n((K, H)) / np.sqrt(K) / s * u.T, "e2m1")
    d["w8_words"], d["w8_scales"] = pack_weight(n((H, N)) / np.sqrt(H) / u, "e4m3")
    d["prior"] = (0.5 * n(N)).astype(np.float32)
    return d

def reference(tab_words, tab_scales, offs, pos1, pos2, pos3, w1, w4_words, w4_scales,
              w8_words, w8_scales, prior):
    v = unpack_weight(tab_words, tab_scales, "e4m3")[:, unstriped(offs)]
    w4 = unpack_weight(w4_words, w4_scales, "e2m1")
    w8 = unpack_weight(w8_words, w8_scales, "e4m3")
    phase = mxq(f64(w1), 0, "e4m3").T @ v
    colour = w4.T @ v
    ph = phase[:, unstriped(pos1)]
    sub = colour[:, unstriped(pos2)]
    bass = colour[:, unstriped(pos3)]
    z = np.cos(ph) * sub - np.sin(ph) * bass
    return (w8.T @ mxq(z, 0, "e4m3")) + f64(prior)[:, None]

@@ -1,0 +1,211 @@
+import math
+from contextlib import ExitStack
+
+import concourse.mybir as mybir
+
+K, T, S, H, B, N = 512, 2048, 1024, 1536, 512, 768
+FLOPS = 2 * K * H * S * 2 + 2 * H * N * B
+
+F32 = mybir.dt.float32
+BF16 = mybir.dt.bfloat16
+I32 = mybir.dt.int32
+U32 = mybir.dt.uint32
+U16 = mybir.dt.uint16
+U8 = mybir.dt.uint8
+FP8X4 = mybir.dt.float8_e4m3fn_x4
+FP4X4 = mybir.dt.float4_e2m1fn_x4
+ACT = mybir.ActivationFunctionType
+ALU = mybir.AluOpType
+
+P = 128
+PACK = 4
+BANK = 512
+PASSES = H // (P * PACK)
+HALVES = S // BANK
+TILES = H // P
+OUT_TILES = N // P
+
+
+def tile_list_chord_phase_voicings_kernel(tc, tab_words, tab_scales, offs, pos1, pos2, pos3, w1, w4_words,
+                                                    w4_scales, w8_words, w8_scales, prior, out):
+    nc = tc.nc
+    with ExitStack() as ctx:
+        keep = ctx.enter_context(tc.tile_pool(name="keep", bufs=1))
+        ring = ctx.enter_context(tc.tile_pool(name="ring", bufs=4))
+        pair = ctx.enter_context(tc.tile_pool(name="pair", bufs=2))
+        stage_psum = ctx.enter_context(tc.psum_pool(name="stage_psum", bufs=2))
+        score_psum = ctx.enter_context(tc.psum_pool(name="score_psum", bufs=1))
+
+        def load_scale_rows(queue, plane, rows):
+            for q in range(4):
+                queue.dma_start(out=plane[:].bitcast(I32)[32 * q : 32 * q + 4, :], in_=rows[4 * q : 4 * q + 4, :].bitcast(I32))
+
+        tab_plane = keep.tile([P, T], U8, name="tab_plane", tag="first_tab_then_w8", align_bytes=64)
+        w4_plane_raw = keep.tile([P, H], U8, name="w4_plane_raw", align_bytes=64)
+        nc.vector.memset(tab_plane[:].bitcast(I32), 0)
+        nc.vector.memset(w4_plane_raw[:].bitcast(I32), 0)
+
+        ones = keep.tile([P, 1], F32, name="ones")
+        nc.vector.memset(ones[:], 1.0)
+        half_pi = keep.tile([P, 1], F32, name="half_pi")
+        nc.vector.tensor_scalar(half_pi[:], ones[:], math.pi / 2, None, ALU.mult)
+        warm = keep.tile([P, 1], F32, name="warm")
+        nc.scalar.activation(warm[:], ones[:], ACT.Sin)
+
+        offs_sb = keep.tile([P, S // 16], U16, name="offs_sb")
+        nc.sync.dma_start(offs_sb[:], offs)
+        pos_sb = []
+        for i, pos in enumerate((pos1, pos2, pos3)):
+            one = keep.tile([P, B // 16], U16, name="pos_sb%d" % i)
+            nc.sync.dma_start(one[:], pos)
+            pos_sb.append(one)
+        load_scale_rows(nc.scalar, tab_plane, tab_scales[0])
+        w1_rows = w1.rearrange("(p j) r -> p j r", j=PACK)
+
+        def load_w1(g):
+            raw = keep.tile([P, PACK, BANK], F32, name="w1_raw")
+            nc.sync.dma_start(out=raw[:], in_=w1_rows[:, :, g * BANK : (g + 1) * BANK])
+            return raw
+
+        w1_raw = load_w1(0)
+        tab_sb = keep.tile([P, T], I32, name="tab_sb", align_bytes=64)
+        nc.sync.dma_start(out=tab_sb[:], in_=tab_words[0].rearrange("p t i -> p (t i)").bitcast(I32))
+        w4_raw = keep.tile([P, H // 2], I32, name="w4_raw", align_bytes=64)
+        nc.sync.dma_start(out=w4_raw[:], in_=w4_words[0].bitcast(I32))
+        load_scale_rows(nc.sync, w4_plane_raw, w4_scales[0])
+        prior_sb = keep.tile([P, OUT_TILES], F32, name="prior_sb")
+        with nc.allow_non_contiguous_dma(reason="one prior value for each output row"):
+            nc.gpsimd.dma_start(out=prior_sb[:], in_=prior.rearrange("(c p) -> p c", p=P))
+
+        def load_w8():
+            words = keep.tile([P, PASSES, N], I32, name="w8_sb", tag="first_w1_then_w8", align_bytes=64)
+            nc.sync.dma_start(out=words[:], in_=w8_words.rearrange("a p c i -> p a (c i)").bitcast(I32))
+            planes = keep.tile([P, N], U8, name="w8_planes", tag="first_tab_then_w8", align_bytes=64)
+            nc.vector.memset(planes[:].bitcast(I32), 0)
+            for q in range(4):
+                nc.sync.dma_start(out=planes[:].bitcast(I32)[32 * q : 32 * q + 4 * PASSES, :],
+                                  in_=w8_scales[:, 4 * q : 4 * q + 4, :].bitcast(I32))
+            return words, planes
+
+        w1_codes = {}
+        w1_plane = {}
+        w4_codes = {}
+        w4_plane = {}
+
+        def round_w1(g, raw):
+            tag = "first_w1_then_w8" if g == 0 else "w1_grouped"
+            grouped = keep.tile([P, PACK, P, PACK], BF16, name="w1_grouped", tag=tag, align_bytes=64)
+            nc.scalar.copy(grouped[:].rearrange("p t m j -> p m j t"), raw[:].rearrange("p j (m t) -> p m j t", t=PACK))
+            return grouped
+
+        def quantise_w1(g, grouped):
+            w1_codes[g] = keep.tile([P, BANK], U32, name="w1_codes%d" % g, align_bytes=64)
+            w1_plane[g] = keep.tile([P, BANK], U8, name="w1_plane%d" % g, align_bytes=64)
+            nc.vector.quantize_mx(out=w1_codes[g][:].bitcast(FP8X4), scales=w1_plane[g][:],
+                                  in_=grouped[:].rearrange("p t m j -> p (t m j)"))
+
+        def order_w4(g):
+            w4_codes[g] = keep.tile([P, BANK], U16, name="w4_codes%d" % g, align_bytes=64)
+            w4_plane[g] = keep.tile([P, BANK], U8, name="w4_plane%d" % g, align_bytes=64)
+            cols = slice(g * BANK, (g + 1) * BANK)
+            nc.vector.tensor_copy(w4_codes[g][:].rearrange("p (t m) -> p t m", t=PACK),
+                                  w4_raw[:].bitcast(U16)[:, cols].rearrange("p (m t) -> p t m", t=PACK))
+            nc.vector.tensor_copy(w4_plane[g][:].rearrange("p (t m) -> p t m", t=PACK),
+                                  w4_plane_raw[:, cols].rearrange("p (m t) -> p t m", t=PACK))
+
+        grouped0 = round_w1(0, w1_raw)
+        picked_plane = []
+        picked_codes = []
+        for h in range(HALVES):
+            one = keep.tile([P, BANK], U8, name="picked_plane%d" % h, align_bytes=64)
+            nc.vector.tensor_copy(one[:], tab_plane[:].indirect(offs_sb[:, h * 32 : (h + 1) * 32]))
+            picked_plane.append(one)
+        for h in range(HALVES):
+            one = keep.tile([P, BANK], U32, name="picked_codes%d" % h, align_bytes=64)
+            nc.vector.tensor_copy(one[:], tab_sb[:].bitcast(U32).indirect(offs_sb[:, h * 32 : (h + 1) * 32]))
+            picked_codes.append(one)
+            if h == 0:
+                quantise_w1(0, grouped0)
+        order_w4(0)
+        w8_sb, w8_planes = load_w8()
+
+        def first_stage(lhsT, lhsT_scale, rows):
+            for h in range(HALVES):
+                bank = stage_psum.tile([P, BANK], F32, name="bank")
+                nc.tensor.matmul_mx(out=bank[:], lhsT=lhsT, lhsT_scale=lhsT_scale, rhs=picked_codes[h][:].bitcast(FP8X4),
+                                    rhs_scale=picked_plane[h][:], start=True, stop=True)
+                nc.scalar.copy(rows[:, h * BANK : (h + 1) * BANK], bank[:])
+
+        picked_phase = {}
+        colour = {}
+
+        def make_rows(i):
+            g, t = divmod(i, PACK)
+            cols = slice(t * P, (t + 1) * P)
+            phase = ring.tile([P, S], F32, name="phase")
+            first_stage(w1_codes[g][:, cols].bitcast(FP8X4), w1_plane[g][:, cols], phase)
+            picked_phase[i] = ring.tile([P, B], F32, name="picked_phase")
+            nc.vector.tensor_copy(picked_phase[i][:], phase[:].indirect(pos_sb[0][:]))
+            colour[i] = ring.tile([P, S], F32, name="colour")
+            first_stage(w4_codes[g][:, cols].bitcast(FP4X4), w4_plane[g][:, cols], colour[i])
+
+        terms = {}
+
+        def turn(i):
+            g, t = divmod(i, PACK)
+            if t == 0:
+                terms[g] = (pair.tile([P, PACK, B], F32, name="cos_term"), pair.tile([P, PACK, B], F32, name="sin_term"))
+            sine = ring.tile([P, B], F32, name="sine")
+            nc.scalar.activation(sine[:], picked_phase[i][:], ACT.Sin)
+            size = ring.tile([P, B], F32, name="size")
+            nc.scalar.activation(size[:], picked_phase[i][:], ACT.Abs)
+            cosine = ring.tile([P, B], F32, name="cosine")
+            nc.scalar.activation(cosine[:], size[:], ACT.Sin, bias=half_pi[:], scale=-1.0)
+            nc.vector.tensor_tensor(terms[g][1][:, t, :], colour[i][:].indirect(pos_sb[2][:]), sine[:], ALU.mult)
+            nc.vector.tensor_tensor(terms[g][0][:, t, :], colour[i][:].indirect(pos_sb[1][:]), cosine[:], ALU.mult)
+
+        z_rounded = {}
+
+        def combine(g):
+            z_rounded[g] = pair.tile([P, B, PACK], BF16, name="z_rounded", align_bytes=64)
+            nc.vector.tensor_tensor(z_rounded[g][:].rearrange("p (c i) t -> p c t i", i=4),
+                                    terms[g][0][:].rearrange("p t (c i) -> p c t i", i=4),
+                                    terms[g][1][:].rearrange("p t (c i) -> p c t i", i=4), ALU.subtract)
+
+        scores = [score_psum.tile([P, B], F32, name="scores%d" % c) for c in range(OUT_TILES)]
+
+        def second_stage(g):
+            z_codes = pair.tile([P, B], U32, name="z_codes", align_bytes=64)
+            z_plane = pair.tile([P, B], U8, name="z_plane", align_bytes=64)
+            nc.vector.quantize_mx(out=z_codes[:].bitcast(FP8X4), scales=z_plane[:],
+                                  in_=z_rounded[g][:].rearrange("p m t -> p (m t)"))
+            for c in range(OUT_TILES):
+                cols = slice(c * P, (c + 1) * P)
+                nc.tensor.matmul_mx(out=scores[c][:], lhsT=w8_sb[:, g, cols].bitcast(FP8X4),
+                                    lhsT_scale=w8_planes[4 * g :, cols], rhs=z_codes[:].bitcast(FP8X4),
+                                    rhs_scale=z_plane[:], start=(g == 0), stop=(g == PASSES - 1))
+
+        make_rows(0)
+        for i in range(TILES):
+            g, t = divmod(i, PACK)
+            if t == 0 and g + 1 < PASSES:
+                grouped = round_w1(g + 1, load_w1(g + 1))
+            if t == 1 and g + 1 < PASSES:
+                quantise_w1(g + 1, grouped)
+                order_w4(g + 1)
+            if i + 1 < TILES:
+                make_rows(i + 1)
+            if t == 0 and g > 0:
+                second_stage(g - 1)
+            turn(i)
+            if t == PACK - 1:
+                combine(g)
+        second_stage(PASSES - 1)
+
+        for c in range(OUT_TILES):
+            result = keep.tile([P, B], F32, name="result%d" % c)
+            if c % 2 == 0:
+                nc.scalar.activation(result[:], scores[c][:], ACT.Identity, bias=prior_sb[:, c : c + 1])
+            else:
+                nc.vector.tensor_scalar(result[:], scores[c][:], prior_sb[:, c : c + 1], None, ALU.add)
+            nc.sync.dma_start(out=out[c * P : (c + 1) * P, :], in_=result[:])

@@ -20,6 +20,7 @@ ALU = mybir.AluOpType
 P = 128
 PACK = 4
 BANK = 512
+BANKS = 8
 PASSES = H // (P * PACK)
 HALVES = S // BANK
 TILES = H // P
@@ -31,10 +32,10 @@ def tile_list_chord_phase_voicings_kernel(tc, tab_words, tab_scales, offs, pos1,
     nc = tc.nc
     with ExitStack() as ctx:
         keep = ctx.enter_context(tc.tile_pool(name="keep", bufs=1))
-        ring = ctx.enter_context(tc.tile_pool(name="ring", bufs=4))
+        ring = ctx.enter_context(tc.tile_pool(name="ring", bufs=3))
+        cosines = ctx.enter_context(tc.tile_pool(name="cosines", bufs=6))
         pair = ctx.enter_context(tc.tile_pool(name="pair", bufs=2))
-        stage_psum = ctx.enter_context(tc.psum_pool(name="stage_psum", bufs=2))
-        score_psum = ctx.enter_context(tc.psum_pool(name="score_psum", bufs=1))
+        psum = ctx.enter_context(tc.psum_pool(name="psum", bufs=1))
 
         def load_scale_rows(queue, plane, rows):
             for q in range(4):
@@ -45,7 +46,7 @@ def tile_list_chord_phase_voicings_kernel(tc, tab_words, tab_scales, offs, pos1,
         nc.vector.memset(tab_plane[:].bitcast(I32), 0)
         nc.vector.memset(w4_plane_raw[:].bitcast(I32), 0)
 
-        ones = keep.tile([P, 1], F32, name="ones")
+        ones = keep.tile([P, 1], F32, name="ones", tag="w1_second")
         nc.vector.memset(ones[:], 1.0)
         half_pi = keep.tile([P, 1], F32, name="half_pi")
         nc.vector.tensor_scalar(half_pi[:], ones[:], math.pi / 2, None, ALU.mult)
@@ -62,20 +63,28 @@ def tile_list_chord_phase_voicings_kernel(tc, tab_words, tab_scales, offs, pos1,
         load_scale_rows(nc.scalar, tab_plane, tab_scales[0])
         w1_rows = w1.rearrange("(p j) r -> p j r", j=PACK)
 
+
         def load_w1(g):
-            raw = keep.tile([P, PACK, BANK], F32, name="w1_raw")
-            nc.sync.dma_start(out=raw[:], in_=w1_rows[:, :, g * BANK : (g + 1) * BANK])
+            halves = []
+            for h in range(2):
+                raw = pair.tile([P, PACK, BANK // 2], F32, name="w1_raw")
+                first = g * BANK + h * BANK // 2
+                nc.sync.dma_start(out=raw[:], in_=w1_rows[:, :, first : first + BANK // 2])
+                halves.append(raw[:])
+            return halves
+
+        def load_w4(g):
+            raw = keep.tile([P, BANK // 2], I32, name="w4_raw", align_bytes=64)
+            nc.sync.dma_start(out=raw[:], in_=w4_words[0].bitcast(I32)[:, g * BANK // 2 : (g + 1) * BANK // 2])
             return raw
 
         w1_raw = load_w1(0)
         tab_sb = keep.tile([P, T], I32, name="tab_sb", align_bytes=64)
         nc.sync.dma_start(out=tab_sb[:], in_=tab_words[0].rearrange("p t i -> p (t i)").bitcast(I32))
-        w4_raw = keep.tile([P, H // 2], I32, name="w4_raw", align_bytes=64)
-        nc.sync.dma_start(out=w4_raw[:], in_=w4_words[0].bitcast(I32))
+        w4_raw = load_w4(0)
         load_scale_rows(nc.sync, w4_plane_raw, w4_scales[0])
-        prior_sb = keep.tile([P, OUT_TILES], F32, name="prior_sb")
-        with nc.allow_non_contiguous_dma(reason="one prior value for each output row"):
-            nc.gpsimd.dma_start(out=prior_sb[:], in_=prior.rearrange("(c p) -> p c", p=P))
+        w1_second = keep.tile([P, PACK, BANK], F32, name="w1_second", tag="w1_second")
+        nc.sync.dma_start(out=w1_second[:], in_=w1_rows[:, :, BANK : 2 * BANK])
 
         def load_w8():
             words = keep.tile([P, PASSES, N], I32, name="w8_sb", tag="first_w1_then_w8", align_bytes=64)
@@ -95,7 +104,9 @@ def tile_list_chord_phase_voicings_kernel(tc, tab_words, tab_scales, offs, pos1,
         def round_w1(g, raw):
             tag = "first_w1_then_w8" if g == 0 else "w1_grouped"
             grouped = keep.tile([P, PACK, P, PACK], BF16, name="w1_grouped", tag=tag, align_bytes=64)
-            nc.scalar.copy(grouped[:].rearrange("p t m j -> p m j t"), raw[:].rearrange("p j (m t) -> p m j t", t=PACK))
+            for h in range(2):
+                nc.scalar.copy(grouped[:, :, h * P // 2 : (h + 1) * P // 2, :].rearrange("p t m j -> p m j t"),
+                               raw[h].rearrange("p j (m t) -> p m j t", t=PACK))
             return grouped
 
         def quantise_w1(g, grouped):
@@ -104,12 +115,12 @@ def tile_list_chord_phase_voicings_kernel(tc, tab_words, tab_scales, offs, pos1,
             nc.vector.quantize_mx(out=w1_codes[g][:].bitcast(FP8X4), scales=w1_plane[g][:],
                                   in_=grouped[:].rearrange("p t m j -> p (t m j)"))
 
-        def order_w4(g):
+        def order_w4(g, raw):
             w4_codes[g] = keep.tile([P, BANK], U16, name="w4_codes%d" % g, align_bytes=64)
             w4_plane[g] = keep.tile([P, BANK], U8, name="w4_plane%d" % g, align_bytes=64)
             cols = slice(g * BANK, (g + 1) * BANK)
             nc.vector.tensor_copy(w4_codes[g][:].rearrange("p (t m) -> p t m", t=PACK),
-                                  w4_raw[:].bitcast(U16)[:, cols].rearrange("p (m t) -> p t m", t=PACK))
+                                  raw[:].bitcast(U16).rearrange("p (m t) -> p t m", t=PACK))
             nc.vector.tensor_copy(w4_plane[g][:].rearrange("p (t m) -> p t m", t=PACK),
                                   w4_plane_raw[:, cols].rearrange("p (m t) -> p t m", t=PACK))
 
@@ -117,21 +128,32 @@ def tile_list_chord_phase_voicings_kernel(tc, tab_words, tab_scales, offs, pos1,
         picked_plane = []
         picked_codes = []
         for h in range(HALVES):
-            one = keep.tile([P, BANK], U8, name="picked_plane%d" % h, align_bytes=64)
-            nc.vector.tensor_copy(one[:], tab_plane[:].indirect(offs_sb[:, h * 32 : (h + 1) * 32]))
-            picked_plane.append(one)
-        for h in range(HALVES):
-            one = keep.tile([P, BANK], U32, name="picked_codes%d" % h, align_bytes=64)
-            nc.vector.tensor_copy(one[:], tab_sb[:].bitcast(U32).indirect(offs_sb[:, h * 32 : (h + 1) * 32]))
-            picked_codes.append(one)
+            codes = keep.tile([P, BANK], U32, name="picked_codes%d" % h, align_bytes=64)
+            nc.vector.tensor_copy(codes[:], tab_sb[:].bitcast(U32).indirect(offs_sb[:, h * 32 : (h + 1) * 32]))
+            picked_codes.append(codes)
+            plane = keep.tile([P, BANK], U8, name="picked_plane%d" % h, align_bytes=64)
+            nc.vector.tensor_copy(plane[:], tab_plane[:].indirect(offs_sb[:, h * 32 : (h + 1) * 32]))
+            picked_plane.append(plane)
             if h == 0:
                 quantise_w1(0, grouped0)
-        order_w4(0)
+        order_w4(0, w4_raw)
+        grouped1 = round_w1(1, [w1_second[:, :, 0 : BANK // 2], w1_second[:, :, BANK // 2 : BANK]])
+        w1_third = keep.tile([P, PACK, BANK], F32, name="w1_third", tag="w1_second")
+        nc.sync.dma_start(out=w1_third[:], in_=w1_rows[:, :, 2 * BANK : 3 * BANK])
+        w1_codes[2] = keep.tile([P, BANK], U32, name="w1_codes2", align_bytes=64)
+        w1_plane[2] = keep.tile([P, BANK], U8, name="w1_plane2", align_bytes=64)
         w8_sb, w8_planes = load_w8()
+
+        banks_taken = []
+
+        def next_bank():
+            bank = psum.tile([P, BANK], F32, name="bank%d" % (len(banks_taken) % BANKS))
+            banks_taken.append(bank)
+            return bank
 
         def first_stage(lhsT, lhsT_scale, rows):
             for h in range(HALVES):
-                bank = stage_psum.tile([P, BANK], F32, name="bank")
+                bank = next_bank()
                 nc.tensor.matmul_mx(out=bank[:], lhsT=lhsT, lhsT_scale=lhsT_scale, rhs=picked_codes[h][:].bitcast(FP8X4),
                                     rhs_scale=picked_plane[h][:], start=True, stop=True)
                 nc.scalar.copy(rows[:, h * BANK : (h + 1) * BANK], bank[:])
@@ -139,68 +161,117 @@ def tile_list_chord_phase_voicings_kernel(tc, tab_words, tab_scales, offs, pos1,
         picked_phase = {}
         colour = {}
 
-        def make_rows(i):
+        def make_phase(i):
             g, t = divmod(i, PACK)
             cols = slice(t * P, (t + 1) * P)
             phase = ring.tile([P, S], F32, name="phase")
             first_stage(w1_codes[g][:, cols].bitcast(FP8X4), w1_plane[g][:, cols], phase)
             picked_phase[i] = ring.tile([P, B], F32, name="picked_phase")
             nc.vector.tensor_copy(picked_phase[i][:], phase[:].indirect(pos_sb[0][:]))
+
+        def make_colour(i):
+            g, t = divmod(i, PACK)
+            cols = slice(t * P, (t + 1) * P)
             colour[i] = ring.tile([P, S], F32, name="colour")
             first_stage(w4_codes[g][:, cols].bitcast(FP4X4), w4_plane[g][:, cols], colour[i])
 
         terms = {}
+        cosine = {}
+        codes_on_sine = {7: 0, 10: 1}
+        last_codes = keep.tile([P, B], U32, name="last_codes", align_bytes=64)
+        z_codes = {PASSES - 1: last_codes[:]}
+        z_waiting = {0: [], 1: []}
 
         def turn(i):
             g, t = divmod(i, PACK)
             if t == 0:
                 terms[g] = (pair.tile([P, PACK, B], F32, name="cos_term"), pair.tile([P, PACK, B], F32, name="sin_term"))
-            sine = ring.tile([P, B], F32, name="sine")
+            if i in codes_on_sine:
+                sine = keep.tile([P, B], F32, name="sine", tag="sine_then_codes%d" % i, align_bytes=64)
+            else:
+                sine = ring.tile([P, B], F32, name="sine")
             nc.scalar.activation(sine[:], picked_phase[i][:], ACT.Sin)
             size = ring.tile([P, B], F32, name="size")
             nc.scalar.activation(size[:], picked_phase[i][:], ACT.Abs)
-            cosine = ring.tile([P, B], F32, name="cosine")
-            nc.scalar.activation(cosine[:], size[:], ACT.Sin, bias=half_pi[:], scale=-1.0)
+            cosine[i] = cosines.tile([P, B], F32, name="cosine", align_bytes=64)
+            nc.scalar.activation(cosine[i][:], size[:], ACT.Sin, bias=half_pi[:], scale=-1.0)
             nc.vector.tensor_tensor(terms[g][1][:, t, :], colour[i][:].indirect(pos_sb[2][:]), sine[:], ALU.mult)
-            nc.vector.tensor_tensor(terms[g][0][:, t, :], colour[i][:].indirect(pos_sb[1][:]), cosine[:], ALU.mult)
+            nc.vector.tensor_tensor(terms[g][0][:, t, :], colour[i][:].indirect(pos_sb[1][:]), cosine[i][:], ALU.mult)
 
-        z_rounded = {}
+        z_plane = [keep.tile([P, B], U8, name="z_plane%d" % g, align_bytes=64) for g in range(PASSES)]
 
-        def combine(g):
-            z_rounded[g] = pair.tile([P, B, PACK], BF16, name="z_rounded", align_bytes=64)
-            nc.vector.tensor_tensor(z_rounded[g][:].rearrange("p (c i) t -> p c t i", i=4),
-                                    terms[g][0][:].rearrange("p t (c i) -> p c t i", i=4),
-                                    terms[g][1][:].rearrange("p t (c i) -> p c t i", i=4), ALU.subtract)
+        def combine(engine, g, bars, rounded):
+            engine.tensor_tensor(rounded.rearrange("p (c i t) -> p c t i", i=4, t=PACK),
+                                 terms[g][0][:, :, bars].rearrange("p t (c i) -> p c t i", i=4),
+                                 terms[g][1][:, :, bars].rearrange("p t (c i) -> p c t i", i=4), ALU.subtract)
 
-        scores = [score_psum.tile([P, B], F32, name="scores%d" % c) for c in range(OUT_TILES)]
+        def quantise_z(g, bars, rounded):
+            nc.vector.quantize_mx(out=z_codes[g][:, bars].bitcast(FP8X4), scales=z_plane[g][:, bars], in_=rounded)
 
-        def second_stage(g):
-            z_codes = pair.tile([P, B], U32, name="z_codes", align_bytes=64)
-            z_plane = pair.tile([P, B], U8, name="z_plane", align_bytes=64)
-            nc.vector.quantize_mx(out=z_codes[:].bitcast(FP8X4), scales=z_plane[:],
-                                  in_=z_rounded[g][:].rearrange("p m t -> p (m t)"))
+        scores = []
+
+        def second_stage(g, bars, start, stop):
             for c in range(OUT_TILES):
                 cols = slice(c * P, (c + 1) * P)
-                nc.tensor.matmul_mx(out=scores[c][:], lhsT=w8_sb[:, g, cols].bitcast(FP8X4),
-                                    lhsT_scale=w8_planes[4 * g :, cols], rhs=z_codes[:].bitcast(FP8X4),
-                                    rhs_scale=z_plane[:], start=(g == 0), stop=(g == PASSES - 1))
+                nc.tensor.matmul_mx(out=scores[c][:, bars], lhsT=w8_sb[:, g, cols].bitcast(FP8X4),
+                                    lhsT_scale=w8_planes[4 * g :, cols], rhs=z_codes[g][:, bars].bitcast(FP8X4),
+                                    rhs_scale=z_plane[g][:, bars], start=start, stop=stop)
 
-        make_rows(0)
+        make_phase(0)
+        make_colour(0)
+        make_phase(1)
+        waiting = []
+        spare_rounded = keep.tile([P, P * PACK], BF16, name="spare_rounded", align_bytes=64)
         for i in range(TILES):
             g, t = divmod(i, PACK)
-            if t == 0 and g + 1 < PASSES:
-                grouped = round_w1(g + 1, load_w1(g + 1))
-            if t == 1 and g + 1 < PASSES:
-                quantise_w1(g + 1, grouped)
-                order_w4(g + 1)
-            if i + 1 < TILES:
-                make_rows(i + 1)
-            if t == 0 and g > 0:
-                second_stage(g - 1)
             turn(i)
-            if t == PACK - 1:
-                combine(g)
-        second_stage(PASSES - 1)
+            for codes, plane, rounded in waiting:
+                nc.vector.quantize_mx(out=codes.bitcast(FP8X4), scales=plane, in_=rounded)
+            waiting = []
+            if i in codes_on_sine:
+                codes = keep.tile([P, B], U32, name="z_codes", tag="sine_then_codes%d" % i, align_bytes=64)
+                z_codes[codes_on_sine[i]] = codes[:]
+                for bars, rounded in z_waiting[codes_on_sine[i]]:
+                    quantise_z(codes_on_sine[i], bars, rounded)
+            if i == 2:
+                grouped2 = keep.tile([P, PACK, P, PACK], BF16, name="w1_grouped", tag="w1_grouped", align_bytes=64)
+                nc.scalar.copy(grouped2[:].rearrange("p t m j -> p m j t"),
+                                      w1_third[:].rearrange("p j (m t) -> p m j t", t=PACK))
+                waiting.append((w1_codes[2][:], w1_plane[2][:], grouped2[:].rearrange("p t m j -> p (t m j)")))
+            done, quarter = divmod(i - (PACK - 1), PACK)
+            if 0 <= done < PASSES - 1 and i + 2 < TILES:
+                bars = slice(quarter * P, (quarter + 1) * P)
+                rounded = cosine[i][:].bitcast(BF16)[:, 0 : P * PACK]
+                combine(nc.gpsimd, done, bars, rounded)
+                z_waiting[done].append((bars, rounded))
+            if i == 8:
+                bars = slice(3 * P, B)
+                combine(nc.vector, 1, bars, spare_rounded[:])
+                z_waiting[1].append((bars, spare_rounded[:]))
+            if i == 0:
+                quantise_w1(1, grouped1)
+            if t == 0 and g + 1 < PASSES:
+                w4_raw = load_w4(g + 1)
+            if t == 1 and g + 1 < PASSES:
+                order_w4(g + 1, w4_raw)
+            if i + 2 < TILES:
+                make_phase(i + 2)
+            if i + 1 < TILES:
+                make_colour(i + 1)
+        prior_sb = keep.tile([P, OUT_TILES], F32, name="prior_sb", tag="w4_raw", align_bytes=64)
+        with nc.allow_non_contiguous_dma(reason="one prior value for each output row"):
+            nc.sync.dma_start(out=prior_sb[:], in_=prior.rearrange("(c p) -> p c", p=P))
+        scores.extend([next_bank() for c in range(OUT_TILES)])
+        for g in range(PASSES - 1):
+            second_stage(g, slice(0, B), g == 0, False)
+        last = PASSES - 1
+        last_rounded = keep.tile([P, 2, B // 2 * PACK], BF16, name="last_rounded", align_bytes=64)
+        for h in range(2):
+            combine(nc.vector, last, slice(h * B // 2, (h + 1) * B // 2), last_rounded[:, h, :])
+        for h in range(2):
+            bars = slice(h * B // 2, (h + 1) * B // 2)
+            quantise_z(last, bars, last_rounded[:, h, :])
+            second_stage(last, bars, False, h == 1)
 
         for c in range(OUT_TILES):
             result = keep.tile([P, B], F32, name="result%d" % c)

@@ -33,7 +33,7 @@ def tile_list_chord_phase_voicings_kernel(tc, tab_words, tab_scales, offs, pos1,
     with ExitStack() as ctx:
         keep = ctx.enter_context(tc.tile_pool(name="keep", bufs=1))
         ring = ctx.enter_context(tc.tile_pool(name="ring", bufs=3))
-        cosines = ctx.enter_context(tc.tile_pool(name="cosines", bufs=6))
+        sines = ctx.enter_context(tc.tile_pool(name="sines", bufs=6))
         pair = ctx.enter_context(tc.tile_pool(name="pair", bufs=2))
         psum = ctx.enter_context(tc.psum_pool(name="psum", bufs=1))
 
@@ -160,6 +160,7 @@ def tile_list_chord_phase_voicings_kernel(tc, tab_words, tab_scales, offs, pos1,
 
         picked_phase = {}
         colour = {}
+        low = {}
 
         def make_phase(i):
             g, t = divmod(i, PACK)
@@ -174,10 +175,12 @@ def tile_list_chord_phase_voicings_kernel(tc, tab_words, tab_scales, offs, pos1,
             cols = slice(t * P, (t + 1) * P)
             colour[i] = ring.tile([P, S], F32, name="colour")
             first_stage(w4_codes[g][:, cols].bitcast(FP4X4), w4_plane[g][:, cols], colour[i])
+            low[i] = ring.tile([P, B], F32, name="low")
+            nc.vector.tensor_copy(low[i][:], colour[i][:].indirect(pos_sb[2][:]))
 
         terms = {}
-        cosine = {}
-        codes_on_sine = {7: 0, 10: 1}
+        sine = {}
+        codes_on_size = {8: 0, 11: 1}
         last_codes = keep.tile([P, B], U32, name="last_codes", align_bytes=64)
         z_codes = {PASSES - 1: last_codes[:]}
         z_waiting = {0: [], 1: []}
@@ -186,17 +189,18 @@ def tile_list_chord_phase_voicings_kernel(tc, tab_words, tab_scales, offs, pos1,
             g, t = divmod(i, PACK)
             if t == 0:
                 terms[g] = (pair.tile([P, PACK, B], F32, name="cos_term"), pair.tile([P, PACK, B], F32, name="sin_term"))
-            if i in codes_on_sine:
-                sine = keep.tile([P, B], F32, name="sine", tag="sine_then_codes%d" % i, align_bytes=64)
+            sine[i] = sines.tile([P, B], F32, name="sine", align_bytes=64)
+            nc.scalar.activation(sine[i][:], picked_phase[i][:], ACT.Sin)
+            if i in codes_on_size:
+                size = keep.tile([P, B], F32, name="size", tag="size_then_codes%d" % i, align_bytes=64)
             else:
-                sine = ring.tile([P, B], F32, name="sine")
-            nc.scalar.activation(sine[:], picked_phase[i][:], ACT.Sin)
-            size = ring.tile([P, B], F32, name="size")
+                size = ring.tile([P, B], F32, name="size")
             nc.scalar.activation(size[:], picked_phase[i][:], ACT.Abs)
-            cosine[i] = cosines.tile([P, B], F32, name="cosine", align_bytes=64)
-            nc.scalar.activation(cosine[i][:], size[:], ACT.Sin, bias=half_pi[:], scale=-1.0)
-            nc.vector.tensor_tensor(terms[g][1][:, t, :], colour[i][:].indirect(pos_sb[2][:]), sine[:], ALU.mult)
-            nc.vector.tensor_tensor(terms[g][0][:, t, :], colour[i][:].indirect(pos_sb[1][:]), cosine[i][:], ALU.mult)
+            cos_term, sin_term = terms[g][0][:, t, :], terms[g][1][:, t, :]
+            nc.scalar.activation(sin_term, size[:], ACT.Sin, bias=half_pi[:], scale=-1.0)
+            nc.vector.tensor_tensor(cos_term, colour[i][:].indirect(pos_sb[1][:]), sin_term, ALU.mult)
+            engine = nc.gpsimd if i + 1 < TILES else nc.vector
+            engine.tensor_tensor(sin_term, low[i][:], sine[i][:], ALU.mult)
 
         z_plane = [keep.tile([P, B], U8, name="z_plane%d" % g, align_bytes=64) for g in range(PASSES)]
 
@@ -228,11 +232,11 @@ def tile_list_chord_phase_voicings_kernel(tc, tab_words, tab_scales, offs, pos1,
             for codes, plane, rounded in waiting:
                 nc.vector.quantize_mx(out=codes.bitcast(FP8X4), scales=plane, in_=rounded)
             waiting = []
-            if i in codes_on_sine:
-                codes = keep.tile([P, B], U32, name="z_codes", tag="sine_then_codes%d" % i, align_bytes=64)
-                z_codes[codes_on_sine[i]] = codes[:]
-                for bars, rounded in z_waiting[codes_on_sine[i]]:
-                    quantise_z(codes_on_sine[i], bars, rounded)
+            if i in codes_on_size:
+                codes = keep.tile([P, B], U32, name="z_codes", tag="size_then_codes%d" % i, align_bytes=64)
+                z_codes[codes_on_size[i]] = codes[:]
+                for bars, rounded in z_waiting[codes_on_size[i]]:
+                    quantise_z(codes_on_size[i], bars, rounded)
             if i == 2:
                 grouped2 = keep.tile([P, PACK, P, PACK], BF16, name="w1_grouped", tag="w1_grouped", align_bytes=64)
                 nc.scalar.copy(grouped2[:].rearrange("p t m j -> p m j t"),
@@ -241,7 +245,7 @@ def tile_list_chord_phase_voicings_kernel(tc, tab_words, tab_scales, offs, pos1,
             done, quarter = divmod(i - (PACK - 1), PACK)
             if 0 <= done < PASSES - 1 and i + 2 < TILES:
                 bars = slice(quarter * P, (quarter + 1) * P)
-                rounded = cosine[i][:].bitcast(BF16)[:, 0 : P * PACK]
+                rounded = sine[i][:].bitcast(BF16)[:, 0 : P * PACK]
                 combine(nc.gpsimd, done, bars, rounded)
                 z_waiting[done].append((bars, rounded))
             if i == 8:

@@ -21,6 +21,7 @@ P = 128
 PACK = 4
 BANK = 512
 BANKS = 8
+HELD = (7, 8, 10)
 PASSES = H // (P * PACK)
 HALVES = S // BANK
 TILES = H // P
@@ -137,7 +138,9 @@ def tile_list_chord_phase_voicings_kernel(tc, tab_words, tab_scales, offs, pos1,
             if h == 0:
                 quantise_w1(0, grouped0)
         order_w4(0, w4_raw)
-        grouped1 = round_w1(1, [w1_second[:, :, 0 : BANK // 2], w1_second[:, :, BANK // 2 : BANK]])
+        grouped1 = keep.tile([P, PACK, P, PACK], BF16, name="w1_grouped", tag="w1_grouped", align_bytes=64)
+        nc.vector.tensor_copy(grouped1[:].rearrange("p t m j -> p m j t"),
+                              w1_second[:].rearrange("p j (m t) -> p m j t", t=PACK))
         w1_third = keep.tile([P, PACK, BANK], F32, name="w1_third", tag="w1_second")
         nc.sync.dma_start(out=w1_third[:], in_=w1_rows[:, :, 2 * BANK : 3 * BANK])
         w1_codes[2] = keep.tile([P, BANK], U32, name="w1_codes2", align_bytes=64)
@@ -167,7 +170,10 @@ def tile_list_chord_phase_voicings_kernel(tc, tab_words, tab_scales, offs, pos1,
             cols = slice(t * P, (t + 1) * P)
             phase = ring.tile([P, S], F32, name="phase")
             first_stage(w1_codes[g][:, cols].bitcast(FP8X4), w1_plane[g][:, cols], phase)
-            picked_phase[i] = ring.tile([P, B], F32, name="picked_phase")
+            if i in HELD:
+                picked_phase[i] = keep.tile([P, B], F32, name="picked_phase", tag="held%d" % i, align_bytes=64)
+            else:
+                picked_phase[i] = ring.tile([P, B], F32, name="picked_phase")
             nc.vector.tensor_copy(picked_phase[i][:], phase[:].indirect(pos_sb[0][:]))
 
         def make_colour(i):
@@ -175,12 +181,13 @@ def tile_list_chord_phase_voicings_kernel(tc, tab_words, tab_scales, offs, pos1,
             cols = slice(t * P, (t + 1) * P)
             colour[i] = ring.tile([P, S], F32, name="colour")
             first_stage(w4_codes[g][:, cols].bitcast(FP4X4), w4_plane[g][:, cols], colour[i])
-            low[i] = ring.tile([P, B], F32, name="low")
-            nc.vector.tensor_copy(low[i][:], colour[i][:].indirect(pos_sb[2][:]))
+            if i + 1 < TILES:
+                low[i] = ring.tile([P, B], F32, name="low")
+                nc.vector.tensor_copy(low[i][:], colour[i][:].indirect(pos_sb[2][:]))
 
         terms = {}
         sine = {}
-        codes_on_size = {8: 0, 11: 1}
+        codes_on_size = {7: 0, 10: 1}
         last_codes = keep.tile([P, B], U32, name="last_codes", align_bytes=64)
         z_codes = {PASSES - 1: last_codes[:]}
         z_waiting = {0: [], 1: []}
@@ -189,18 +196,19 @@ def tile_list_chord_phase_voicings_kernel(tc, tab_words, tab_scales, offs, pos1,
             g, t = divmod(i, PACK)
             if t == 0:
                 terms[g] = (pair.tile([P, PACK, B], F32, name="cos_term"), pair.tile([P, PACK, B], F32, name="sin_term"))
+            size = ring.tile([P, B], F32, name="size")
+            nc.scalar.activation(size[:], picked_phase[i][:], ACT.Abs)
             sine[i] = sines.tile([P, B], F32, name="sine", align_bytes=64)
             nc.scalar.activation(sine[i][:], picked_phase[i][:], ACT.Sin)
-            if i in codes_on_size:
-                size = keep.tile([P, B], F32, name="size", tag="size_then_codes%d" % i, align_bytes=64)
-            else:
-                size = ring.tile([P, B], F32, name="size")
-            nc.scalar.activation(size[:], picked_phase[i][:], ACT.Abs)
             cos_term, sin_term = terms[g][0][:, t, :], terms[g][1][:, t, :]
-            nc.scalar.activation(sin_term, size[:], ACT.Sin, bias=half_pi[:], scale=-1.0)
-            nc.vector.tensor_tensor(cos_term, colour[i][:].indirect(pos_sb[1][:]), sin_term, ALU.mult)
-            engine = nc.gpsimd if i + 1 < TILES else nc.vector
-            engine.tensor_tensor(sin_term, low[i][:], sine[i][:], ALU.mult)
+            if i + 1 < TILES:
+                nc.scalar.activation(sin_term, size[:], ACT.Sin, bias=half_pi[:], scale=-1.0)
+                nc.vector.tensor_tensor(cos_term, colour[i][:].indirect(pos_sb[1][:]), sin_term, ALU.mult)
+                nc.gpsimd.tensor_tensor(sin_term, low[i][:], sine[i][:], ALU.mult)
+            else:
+                cosine = ring.tile([P, B], F32, name="size")
+                nc.scalar.activation(cosine[:], size[:], ACT.Sin, bias=half_pi[:], scale=-1.0)
+                return cosine
 
         z_plane = [keep.tile([P, B], U8, name="z_plane%d" % g, align_bytes=64) for g in range(PASSES)]
 
@@ -212,32 +220,28 @@ def tile_list_chord_phase_voicings_kernel(tc, tab_words, tab_scales, offs, pos1,
         def quantise_z(g, bars, rounded):
             nc.vector.quantize_mx(out=z_codes[g][:, bars].bitcast(FP8X4), scales=z_plane[g][:, bars], in_=rounded)
 
-        scores = []
-
-        def second_stage(g, bars, start, stop):
-            for c in range(OUT_TILES):
-                cols = slice(c * P, (c + 1) * P)
-                nc.tensor.matmul_mx(out=scores[c][:, bars], lhsT=w8_sb[:, g, cols].bitcast(FP8X4),
-                                    lhsT_scale=w8_planes[4 * g :, cols], rhs=z_codes[g][:, bars].bitcast(FP8X4),
-                                    rhs_scale=z_plane[g][:, bars], start=start, stop=stop)
+        def second_stage(score, c, g, bars):
+            cols = slice(c * P, (c + 1) * P)
+            nc.tensor.matmul_mx(out=score[:, 0 : B // 2], lhsT=w8_sb[:, g, cols].bitcast(FP8X4),
+                                lhsT_scale=w8_planes[4 * g :, cols], rhs=z_codes[g][:, bars].bitcast(FP8X4),
+                                rhs_scale=z_plane[g][:, bars], start=(g == 0), stop=(g == PASSES - 1))
 
         make_phase(0)
         make_colour(0)
         make_phase(1)
         waiting = []
-        spare_rounded = keep.tile([P, P * PACK], BF16, name="spare_rounded", align_bytes=64)
         for i in range(TILES):
             g, t = divmod(i, PACK)
-            turn(i)
+            cosine = turn(i)
             for codes, plane, rounded in waiting:
                 nc.vector.quantize_mx(out=codes.bitcast(FP8X4), scales=plane, in_=rounded)
             waiting = []
             if i in codes_on_size:
-                codes = keep.tile([P, B], U32, name="z_codes", tag="size_then_codes%d" % i, align_bytes=64)
+                codes = keep.tile([P, B], U32, name="z_codes", tag="held%d" % i, align_bytes=64)
                 z_codes[codes_on_size[i]] = codes[:]
                 for bars, rounded in z_waiting[codes_on_size[i]]:
                     quantise_z(codes_on_size[i], bars, rounded)
-            if i == 2:
+            if i == 4:
                 grouped2 = keep.tile([P, PACK, P, PACK], BF16, name="w1_grouped", tag="w1_grouped", align_bytes=64)
                 nc.scalar.copy(grouped2[:].rearrange("p t m j -> p m j t"),
                                       w1_third[:].rearrange("p j (m t) -> p m j t", t=PACK))
@@ -250,6 +254,7 @@ def tile_list_chord_phase_voicings_kernel(tc, tab_words, tab_scales, offs, pos1,
                 z_waiting[done].append((bars, rounded))
             if i == 8:
                 bars = slice(3 * P, B)
+                spare_rounded = keep.tile([P, P * PACK], BF16, name="spare_rounded", tag="held8", align_bytes=64)
                 combine(nc.vector, 1, bars, spare_rounded[:])
                 z_waiting[1].append((bars, spare_rounded[:]))
             if i == 0:
@@ -265,22 +270,43 @@ def tile_list_chord_phase_voicings_kernel(tc, tab_words, tab_scales, offs, pos1,
         prior_sb = keep.tile([P, OUT_TILES], F32, name="prior_sb", tag="w4_raw", align_bytes=64)
         with nc.allow_non_contiguous_dma(reason="one prior value for each output row"):
             nc.sync.dma_start(out=prior_sb[:], in_=prior.rearrange("(c p) -> p c", p=P))
-        scores.extend([next_bank() for c in range(OUT_TILES)])
-        for g in range(PASSES - 1):
-            second_stage(g, slice(0, B), g == 0, False)
         last = PASSES - 1
+        halves = [slice(h * B // 2, (h + 1) * B // 2) for h in range(2)]
+        lists = [slice(h * B // 32, (h + 1) * B // 32) for h in range(2)]
         last_rounded = keep.tile([P, 2, B // 2 * PACK], BF16, name="last_rounded", align_bytes=64)
-        for h in range(2):
-            combine(nc.vector, last, slice(h * B // 2, (h + 1) * B // 2), last_rounded[:, h, :])
-        for h in range(2):
-            bars = slice(h * B // 2, (h + 1) * B // 2)
-            quantise_z(last, bars, last_rounded[:, h, :])
-            second_stage(last, bars, False, h == 1)
 
-        for c in range(OUT_TILES):
-            result = keep.tile([P, B], F32, name="result%d" % c)
-            if c % 2 == 0:
-                nc.scalar.activation(result[:], scores[c][:], ACT.Identity, bias=prior_sb[:, c : c + 1])
+        def last_product(term, pos, factor, h):
+            nc.vector.tensor_tensor(term[:, PACK - 1, halves[h]], colour[TILES - 1][:].indirect(pos[:, lists[h]]),
+                                    factor[:, halves[h]], ALU.mult)
+
+        def open_scores(c, h):
+            score = next_bank()
+            for g in range(last):
+                second_stage(score, c, g, halves[h])
+            return score
+
+        def store_scores(score, c, h, engine):
+            result = keep.tile([P, B // 2], F32, name="result%d_%d" % (c, h))
+            if engine == "scalar":
+                nc.scalar.activation(result[:], score[:, 0 : B // 2], ACT.Identity, bias=prior_sb[:, c : c + 1])
             else:
-                nc.vector.tensor_scalar(result[:], scores[c][:], prior_sb[:, c : c + 1], None, ALU.add)
-            nc.sync.dma_start(out=out[c * P : (c + 1) * P, :], in_=result[:])
+                nc.vector.tensor_scalar(result[:], score[:, 0 : B // 2], prior_sb[:, c : c + 1], None, ALU.add)
+            nc.sync.dma_start(out=out[c * P : (c + 1) * P, halves[h]], in_=result[:])
+
+        first = [open_scores(c, 0) for c in range(OUT_TILES)]
+        second = [open_scores(c, 1) for c in range(BANKS - OUT_TILES)]
+        last_product(terms[last][1], pos_sb[2], sine[TILES - 1], 0)
+        last_product(terms[last][0], pos_sb[1], cosine, 0)
+        combine(nc.vector, last, halves[0], last_rounded[:, 0, :])
+        last_product(terms[last][1], pos_sb[2], sine[TILES - 1], 1)
+        quantise_z(last, halves[0], last_rounded[:, 0, :])
+        last_product(terms[last][0], pos_sb[1], cosine, 1)
+        combine(nc.vector, last, halves[1], last_rounded[:, 1, :])
+        quantise_z(last, halves[1], last_rounded[:, 1, :])
+        for c in range(OUT_TILES):
+            second_stage(first[c], c, last, halves[0])
+            store_scores(first[c], c, 0, "scalar")
+        second.extend([open_scores(c, 1) for c in range(BANKS - OUT_TILES, OUT_TILES)])
+        for c in range(OUT_TILES):
+            second_stage(second[c], c, last, halves[1])
+            store_scores(second[c], c, 1, "vector" if c % 2 == 0 else "scalar")

@@ -21,11 +21,17 @@ P = 128
 PACK = 4
 BANK = 512
 BANKS = 8
-HELD = (7, 8, 10)
-PASSES = H // (P * PACK)
-HALVES = S // BANK
+PASS = P * PACK
+PASSES = H // PASS
 TILES = H // P
+LAST_TILE = TILES - 1
+LAST_PASS = PASSES - 1
 OUT_TILES = N // P
+PER_COLUMN = 16
+
+QUANTISE_Z_AT = {8: 0, 11: 1}
+VECTOR_QUARTER_AT = 9
+ROUND_THIRD_W1_AT = 4
 
 
 def tile_list_chord_phase_voicings_kernel(tc, tab_words, tab_scales, offs, pos1, pos2, pos3, w1, w4_words,
@@ -42,56 +48,54 @@ def tile_list_chord_phase_voicings_kernel(tc, tab_words, tab_scales, offs, pos1,
             for q in range(4):
                 queue.dma_start(out=plane[:].bitcast(I32)[32 * q : 32 * q + 4, :], in_=rows[4 * q : 4 * q + 4, :].bitcast(I32))
 
-        tab_plane = keep.tile([P, T], U8, name="tab_plane", tag="first_tab_then_w8", align_bytes=64)
+        tab_plane = keep.tile([P, T], U8, name="tab_plane", align_bytes=64)
         w4_plane_raw = keep.tile([P, H], U8, name="w4_plane_raw", align_bytes=64)
         nc.vector.memset(tab_plane[:].bitcast(I32), 0)
         nc.vector.memset(w4_plane_raw[:].bitcast(I32), 0)
 
-        ones = keep.tile([P, 1], F32, name="ones", tag="w1_second")
-        nc.vector.memset(ones[:], 1.0)
+        zero = keep.tile([P, 1], F32, name="zero")
+        nc.vector.memset(zero[:], 0.0)
+        sin_zero = keep.tile([P, 1], F32, name="sin_zero")
+        nc.scalar.activation(sin_zero[:], zero[:], ACT.Sin)
         half_pi = keep.tile([P, 1], F32, name="half_pi")
-        nc.vector.tensor_scalar(half_pi[:], ones[:], math.pi / 2, None, ALU.mult)
-        warm = keep.tile([P, 1], F32, name="warm")
-        nc.scalar.activation(warm[:], ones[:], ACT.Sin)
+        nc.vector.tensor_scalar(half_pi[:], sin_zero[:], math.pi / 2, None, ALU.add)
 
-        offs_sb = keep.tile([P, S // 16], U16, name="offs_sb")
+        offs_sb = keep.tile([P, S // PER_COLUMN], U16, name="offs_sb")
         nc.sync.dma_start(offs_sb[:], offs)
-        pos_sb = []
+        bar_lists = []
         for i, pos in enumerate((pos1, pos2, pos3)):
-            one = keep.tile([P, B // 16], U16, name="pos_sb%d" % i)
-            nc.sync.dma_start(one[:], pos)
-            pos_sb.append(one)
+            bar_list = keep.tile([P, B // PER_COLUMN], U16, name="bar_list%d" % i)
+            nc.sync.dma_start(bar_list[:], pos)
+            bar_lists.append(bar_list)
+        current_of, substitute_of, low_of = bar_lists
         load_scale_rows(nc.scalar, tab_plane, tab_scales[0])
-        w1_rows = w1.rearrange("(p j) r -> p j r", j=PACK)
-
-
-        def load_w1(g):
-            halves = []
-            for h in range(2):
-                raw = pair.tile([P, PACK, BANK // 2], F32, name="w1_raw")
-                first = g * BANK + h * BANK // 2
-                nc.sync.dma_start(out=raw[:], in_=w1_rows[:, :, first : first + BANK // 2])
-                halves.append(raw[:])
-            return halves
 
         def load_w4(g):
-            raw = keep.tile([P, BANK // 2], I32, name="w4_raw", align_bytes=64)
-            nc.sync.dma_start(out=raw[:], in_=w4_words[0].bitcast(I32)[:, g * BANK // 2 : (g + 1) * BANK // 2])
+            raw = keep.tile([P, PASS // 2], I32, name="w4_raw", align_bytes=64)
+            nc.sync.dma_start(out=raw[:], in_=w4_words[0].bitcast(I32)[:, g * PASS // 2 : (g + 1) * PASS // 2])
             return raw
 
-        w1_raw = load_w1(0)
-        tab_sb = keep.tile([P, T], I32, name="tab_sb", align_bytes=64)
+        tab_sb = keep.tile([P, T], I32, name="tab_sb", tag="table_words_then_picked_plane", align_bytes=64)
         nc.sync.dma_start(out=tab_sb[:], in_=tab_words[0].rearrange("p t i -> p (t i)").bitcast(I32))
+        w1_rows = w1.rearrange("(p j) r -> p j r", j=PACK)
+        w1_first = []
+        for h in range(2):
+            raw = pair.tile([P, PACK, PASS // 2], F32, name="w1_first")
+            nc.sync.dma_start(out=raw[:], in_=w1_rows[:, :, h * PASS // 2 : (h + 1) * PASS // 2])
+            w1_first.append(raw)
         w4_raw = load_w4(0)
         load_scale_rows(nc.sync, w4_plane_raw, w4_scales[0])
-        w1_second = keep.tile([P, PACK, BANK], F32, name="w1_second", tag="w1_second")
-        nc.sync.dma_start(out=w1_second[:], in_=w1_rows[:, :, BANK : 2 * BANK])
+
+        def load_w1(g):
+            raw = keep.tile([P, PACK, PASS], F32, name="w1_raw", tag="weights_in_turn", align_bytes=64)
+            nc.sync.dma_start(out=raw[:], in_=w1_rows[:, :, g * PASS : (g + 1) * PASS])
+            return raw
 
         def load_w8():
-            words = keep.tile([P, PASSES, N], I32, name="w8_sb", tag="first_w1_then_w8", align_bytes=64)
+            words = keep.tile([P, PASSES, N], I32, name="w8_sb", tag="weights_in_turn", align_bytes=64)
             nc.sync.dma_start(out=words[:], in_=w8_words.rearrange("a p c i -> p a (c i)").bitcast(I32))
-            planes = keep.tile([P, N], U8, name="w8_planes", tag="first_tab_then_w8", align_bytes=64)
-            nc.vector.memset(planes[:].bitcast(I32), 0)
+            planes = keep.tile([P, N], U8, name="w8_planes", tag="w1_rounded", align_bytes=64)
+            nc.gpsimd.memset(planes[:].bitcast(I32), 0)
             for q in range(4):
                 nc.sync.dma_start(out=planes[:].bitcast(I32)[32 * q : 32 * q + 4 * PASSES, :],
                                   in_=w8_scales[:, 4 * q : 4 * q + 4, :].bitcast(I32))
@@ -102,50 +106,39 @@ def tile_list_chord_phase_voicings_kernel(tc, tab_words, tab_scales, offs, pos1,
         w4_codes = {}
         w4_plane = {}
 
-        def round_w1(g, raw):
-            tag = "first_w1_then_w8" if g == 0 else "w1_grouped"
-            grouped = keep.tile([P, PACK, P, PACK], BF16, name="w1_grouped", tag=tag, align_bytes=64)
-            for h in range(2):
-                nc.scalar.copy(grouped[:, :, h * P // 2 : (h + 1) * P // 2, :].rearrange("p t m j -> p m j t"),
-                               raw[h].rearrange("p j (m t) -> p m j t", t=PACK))
-            return grouped
+        def round_w1(rounded, raw):
+            nc.scalar.copy(rounded.rearrange("p t m j -> p m j t"), raw.rearrange("p j (m t) -> p m j t", t=PACK))
 
-        def quantise_w1(g, grouped):
-            w1_codes[g] = keep.tile([P, BANK], U32, name="w1_codes%d" % g, align_bytes=64)
-            w1_plane[g] = keep.tile([P, BANK], U8, name="w1_plane%d" % g, align_bytes=64)
+        def quantise_w1(g, rounded):
+            w1_codes[g] = keep.tile([P, PASS], U32, name="w1_codes%d" % g, align_bytes=64)
+            w1_plane[g] = keep.tile([P, PASS], U8, name="w1_plane%d" % g, align_bytes=64)
             nc.vector.quantize_mx(out=w1_codes[g][:].bitcast(FP8X4), scales=w1_plane[g][:],
-                                  in_=grouped[:].rearrange("p t m j -> p (t m j)"))
+                                  in_=rounded[:].rearrange("p t m j -> p (t m j)"))
 
         def order_w4(g, raw):
-            w4_codes[g] = keep.tile([P, BANK], U16, name="w4_codes%d" % g, align_bytes=64)
-            w4_plane[g] = keep.tile([P, BANK], U8, name="w4_plane%d" % g, align_bytes=64)
-            cols = slice(g * BANK, (g + 1) * BANK)
+            w4_codes[g] = keep.tile([P, PASS], U16, name="w4_codes%d" % g, align_bytes=64)
+            w4_plane[g] = keep.tile([P, PASS], U8, name="w4_plane%d" % g, align_bytes=64)
             nc.vector.tensor_copy(w4_codes[g][:].rearrange("p (t m) -> p t m", t=PACK),
                                   raw[:].bitcast(U16).rearrange("p (m t) -> p t m", t=PACK))
             nc.vector.tensor_copy(w4_plane[g][:].rearrange("p (t m) -> p t m", t=PACK),
-                                  w4_plane_raw[:, cols].rearrange("p (m t) -> p t m", t=PACK))
+                                  w4_plane_raw[:, g * PASS : (g + 1) * PASS].rearrange("p (m t) -> p t m", t=PACK))
 
-        grouped0 = round_w1(0, w1_raw)
-        picked_plane = []
+        w1_rounded = keep.tile([P, PACK, P, PACK], BF16, name="w1_rounded", tag="weights_in_turn", align_bytes=64)
+        for h in range(2):
+            round_w1(w1_rounded[:, :, h * P // 2 : (h + 1) * P // 2, :], w1_first[h][:])
+
         picked_codes = []
-        for h in range(HALVES):
+        for h in range(S // BANK):
             codes = keep.tile([P, BANK], U32, name="picked_codes%d" % h, align_bytes=64)
-            nc.vector.tensor_copy(codes[:], tab_sb[:].bitcast(U32).indirect(offs_sb[:, h * 32 : (h + 1) * 32]))
+            entries = offs_sb[:, h * BANK // PER_COLUMN : (h + 1) * BANK // PER_COLUMN]
+            nc.vector.tensor_copy(codes[:], tab_sb[:].bitcast(U32).indirect(entries))
             picked_codes.append(codes)
-            plane = keep.tile([P, BANK], U8, name="picked_plane%d" % h, align_bytes=64)
-            nc.vector.tensor_copy(plane[:], tab_plane[:].indirect(offs_sb[:, h * 32 : (h + 1) * 32]))
-            picked_plane.append(plane)
-            if h == 0:
-                quantise_w1(0, grouped0)
+        picked_plane = keep.tile([P, S], U8, name="picked_plane", tag="table_words_then_picked_plane", align_bytes=64)
+        nc.vector.tensor_copy(picked_plane[:], tab_plane[:].indirect(offs_sb[:]))
+        quantise_w1(0, w1_rounded)
         order_w4(0, w4_raw)
-        grouped1 = keep.tile([P, PACK, P, PACK], BF16, name="w1_grouped", tag="w1_grouped", align_bytes=64)
-        nc.vector.tensor_copy(grouped1[:].rearrange("p t m j -> p m j t"),
-                              w1_second[:].rearrange("p j (m t) -> p m j t", t=PACK))
-        w1_third = keep.tile([P, PACK, BANK], F32, name="w1_third", tag="w1_second")
-        nc.sync.dma_start(out=w1_third[:], in_=w1_rows[:, :, 2 * BANK : 3 * BANK])
-        w1_codes[2] = keep.tile([P, BANK], U32, name="w1_codes2", align_bytes=64)
-        w1_plane[2] = keep.tile([P, BANK], U8, name="w1_plane2", align_bytes=64)
-        w8_sb, w8_planes = load_w8()
+        w1_raw = load_w1(1)
+        w1_rounded = keep.tile([P, PACK, P, PACK], BF16, name="w1_rounded", tag="w1_rounded", align_bytes=64)
 
         banks_taken = []
 
@@ -155,13 +148,14 @@ def tile_list_chord_phase_voicings_kernel(tc, tab_words, tab_scales, offs, pos1,
             return bank
 
         def first_stage(lhsT, lhsT_scale, rows):
-            for h in range(HALVES):
+            for h in range(S // BANK):
+                chords = slice(h * BANK, (h + 1) * BANK)
                 bank = next_bank()
                 nc.tensor.matmul_mx(out=bank[:], lhsT=lhsT, lhsT_scale=lhsT_scale, rhs=picked_codes[h][:].bitcast(FP8X4),
-                                    rhs_scale=picked_plane[h][:], start=True, stop=True)
-                nc.scalar.copy(rows[:, h * BANK : (h + 1) * BANK], bank[:])
+                                    rhs_scale=picked_plane[:, chords], start=True, stop=True)
+                nc.scalar.copy(rows[:, chords], bank[:])
 
-        picked_phase = {}
+        angle = {}
         colour = {}
         low = {}
 
@@ -170,143 +164,147 @@ def tile_list_chord_phase_voicings_kernel(tc, tab_words, tab_scales, offs, pos1,
             cols = slice(t * P, (t + 1) * P)
             phase = ring.tile([P, S], F32, name="phase")
             first_stage(w1_codes[g][:, cols].bitcast(FP8X4), w1_plane[g][:, cols], phase)
-            if i in HELD:
-                picked_phase[i] = keep.tile([P, B], F32, name="picked_phase", tag="held%d" % i, align_bytes=64)
+            if i in QUANTISE_Z_AT or i == VECTOR_QUARTER_AT:
+                angle[i] = keep.tile([P, B], F32, name="angle", tag="angle_of_tile%d" % i, align_bytes=64)
             else:
-                picked_phase[i] = ring.tile([P, B], F32, name="picked_phase")
-            nc.vector.tensor_copy(picked_phase[i][:], phase[:].indirect(pos_sb[0][:]))
+                angle[i] = ring.tile([P, B], F32, name="angle")
+            nc.vector.tensor_copy(angle[i][:], phase[:].indirect(current_of[:]))
 
         def make_colour(i):
             g, t = divmod(i, PACK)
             cols = slice(t * P, (t + 1) * P)
             colour[i] = ring.tile([P, S], F32, name="colour")
             first_stage(w4_codes[g][:, cols].bitcast(FP4X4), w4_plane[g][:, cols], colour[i])
-            if i + 1 < TILES:
-                low[i] = ring.tile([P, B], F32, name="low")
-                nc.vector.tensor_copy(low[i][:], colour[i][:].indirect(pos_sb[2][:]))
+            low[i] = ring.tile([P, B], F32, name="low")
+            nc.vector.tensor_copy(low[i][:], colour[i][:].indirect(low_of[:]))
 
-        terms = {}
+        cos_terms = {}
+        sin_terms = {}
         sine = {}
-        codes_on_size = {7: 0, 10: 1}
-        last_codes = keep.tile([P, B], U32, name="last_codes", align_bytes=64)
-        z_codes = {PASSES - 1: last_codes[:]}
-        z_waiting = {0: [], 1: []}
 
-        def turn(i):
+        def sine_and_size(i):
             g, t = divmod(i, PACK)
             if t == 0:
-                terms[g] = (pair.tile([P, PACK, B], F32, name="cos_term"), pair.tile([P, PACK, B], F32, name="sin_term"))
+                cos_terms[g] = pair.tile([P, PACK, B], F32, name="cos_terms")
+                sin_terms[g] = pair.tile([P, PACK, B], F32, name="sin_terms")
             size = ring.tile([P, B], F32, name="size")
-            nc.scalar.activation(size[:], picked_phase[i][:], ACT.Abs)
+            nc.scalar.activation(size[:], angle[i][:], ACT.Abs)
             sine[i] = sines.tile([P, B], F32, name="sine", align_bytes=64)
-            nc.scalar.activation(sine[i][:], picked_phase[i][:], ACT.Sin)
-            cos_term, sin_term = terms[g][0][:, t, :], terms[g][1][:, t, :]
-            if i + 1 < TILES:
-                nc.scalar.activation(sin_term, size[:], ACT.Sin, bias=half_pi[:], scale=-1.0)
-                nc.vector.tensor_tensor(cos_term, colour[i][:].indirect(pos_sb[1][:]), sin_term, ALU.mult)
-                nc.gpsimd.tensor_tensor(sin_term, low[i][:], sine[i][:], ALU.mult)
-            else:
-                cosine = ring.tile([P, B], F32, name="size")
-                nc.scalar.activation(cosine[:], size[:], ACT.Sin, bias=half_pi[:], scale=-1.0)
-                return cosine
+            nc.scalar.activation(sine[i][:], angle[i][:], ACT.Sin)
+            return size
 
-        z_plane = [keep.tile([P, B], U8, name="z_plane%d" % g, align_bytes=64) for g in range(PASSES)]
+        def turn(i, size):
+            g, t = divmod(i, PACK)
+            place = sin_terms[g][:, t, :]
+            nc.scalar.activation(place, size[:], ACT.Sin, bias=half_pi[:], scale=-1.0)
+            nc.vector.tensor_tensor(cos_terms[g][:, t, :], colour[i][:].indirect(substitute_of[:]), place, ALU.mult)
+            nc.gpsimd.tensor_tensor(place, low[i][:], sine[i][:], ALU.mult)
 
-        def combine(engine, g, bars, rounded):
+        def subtract(engine, g, bars, rounded):
             engine.tensor_tensor(rounded.rearrange("p (c i t) -> p c t i", i=4, t=PACK),
-                                 terms[g][0][:, :, bars].rearrange("p t (c i) -> p c t i", i=4),
-                                 terms[g][1][:, :, bars].rearrange("p t (c i) -> p c t i", i=4), ALU.subtract)
+                                 cos_terms[g][:, :, bars].rearrange("p t (c i) -> p c t i", i=4),
+                                 sin_terms[g][:, :, bars].rearrange("p t (c i) -> p c t i", i=4), ALU.subtract)
+
+        z_codes = {LAST_PASS: keep.tile([P, B], U32, name="last_z_codes", align_bytes=64)}
+        z_plane = [keep.tile([P, B], U8, name="z_plane%d" % g, align_bytes=64) for g in range(PASSES)]
+        z_quarters = {g: [] for g in range(LAST_PASS)}
 
         def quantise_z(g, bars, rounded):
             nc.vector.quantize_mx(out=z_codes[g][:, bars].bitcast(FP8X4), scales=z_plane[g][:, bars], in_=rounded)
 
-        def second_stage(score, c, g, bars):
-            cols = slice(c * P, (c + 1) * P)
-            nc.tensor.matmul_mx(out=score[:, 0 : B // 2], lhsT=w8_sb[:, g, cols].bitcast(FP8X4),
-                                lhsT_scale=w8_planes[4 * g :, cols], rhs=z_codes[g][:, bars].bitcast(FP8X4),
-                                rhs_scale=z_plane[g][:, bars], start=(g == 0), stop=(g == PASSES - 1))
-
         make_phase(0)
         make_colour(0)
         make_phase(1)
-        waiting = []
         for i in range(TILES):
             g, t = divmod(i, PACK)
-            cosine = turn(i)
-            for codes, plane, rounded in waiting:
-                nc.vector.quantize_mx(out=codes.bitcast(FP8X4), scales=plane, in_=rounded)
-            waiting = []
-            if i in codes_on_size:
-                codes = keep.tile([P, B], U32, name="z_codes", tag="held%d" % i, align_bytes=64)
-                z_codes[codes_on_size[i]] = codes[:]
-                for bars, rounded in z_waiting[codes_on_size[i]]:
-                    quantise_z(codes_on_size[i], bars, rounded)
-            if i == 4:
-                grouped2 = keep.tile([P, PACK, P, PACK], BF16, name="w1_grouped", tag="w1_grouped", align_bytes=64)
-                nc.scalar.copy(grouped2[:].rearrange("p t m j -> p m j t"),
-                                      w1_third[:].rearrange("p j (m t) -> p m j t", t=PACK))
-                waiting.append((w1_codes[2][:], w1_plane[2][:], grouped2[:].rearrange("p t m j -> p (t m j)")))
+            size = sine_and_size(i)
+            if i < LAST_TILE:
+                turn(i, size)
+            else:
+                last_cosine = ring.tile([P, B], F32, name="size")
+                nc.scalar.activation(last_cosine[:], size[:], ACT.Sin, bias=half_pi[:], scale=-1.0)
+            if i == ROUND_THIRD_W1_AT + 1:
+                quantise_w1(2, w1_rounded)
+                w8_sb, w8_planes = load_w8()
+            if i in QUANTISE_Z_AT:
+                done = QUANTISE_Z_AT[i]
+                z_codes[done] = keep.tile([P, B], U32, name="z_codes", tag="angle_of_tile%d" % i, align_bytes=64)
+                for bars, rounded in z_quarters[done]:
+                    quantise_z(done, bars, rounded)
+            if i == ROUND_THIRD_W1_AT:
+                w1_rounded = keep.tile([P, PACK, P, PACK], BF16, name="w1_rounded", tag="w1_rounded", align_bytes=64)
+                round_w1(w1_rounded[:], w1_raw[:])
             done, quarter = divmod(i - (PACK - 1), PACK)
-            if 0 <= done < PASSES - 1 and i + 2 < TILES:
+            if 0 <= done < LAST_PASS and i + 2 < TILES:
                 bars = slice(quarter * P, (quarter + 1) * P)
                 rounded = sine[i][:].bitcast(BF16)[:, 0 : P * PACK]
-                combine(nc.gpsimd, done, bars, rounded)
-                z_waiting[done].append((bars, rounded))
-            if i == 8:
-                bars = slice(3 * P, B)
-                spare_rounded = keep.tile([P, P * PACK], BF16, name="spare_rounded", tag="held8", align_bytes=64)
-                combine(nc.vector, 1, bars, spare_rounded[:])
-                z_waiting[1].append((bars, spare_rounded[:]))
-            if i == 0:
-                quantise_w1(1, grouped1)
-            if t == 0 and g + 1 < PASSES:
+                subtract(nc.gpsimd, done, bars, rounded)
+                z_quarters[done].append((bars, rounded))
+            if i == VECTOR_QUARTER_AT:
+                bars = slice(B - P, B)
+                fourth = keep.tile([P, P * PACK], BF16, name="fourth", tag="angle_of_tile%d" % i, align_bytes=64)
+                subtract(nc.vector, 1, bars, fourth[:])
+                z_quarters[1].append((bars, fourth[:]))
+            if i < 2:
+                round_w1(w1_rounded[:, :, i * P // 2 : (i + 1) * P // 2, :], w1_raw[:, :, i * PASS // 2 : (i + 1) * PASS // 2])
+            if i == 1:
+                w1_raw = load_w1(2)
+            if i == 2:
+                quantise_w1(1, w1_rounded)
+            if t == 0 and g < LAST_PASS:
                 w4_raw = load_w4(g + 1)
-            if t == 1 and g + 1 < PASSES:
+            if t == 1 and g < LAST_PASS:
                 order_w4(g + 1, w4_raw)
             if i + 2 < TILES:
                 make_phase(i + 2)
             if i + 1 < TILES:
                 make_colour(i + 1)
+
         prior_sb = keep.tile([P, OUT_TILES], F32, name="prior_sb", tag="w4_raw", align_bytes=64)
         with nc.allow_non_contiguous_dma(reason="one prior value for each output row"):
             nc.sync.dma_start(out=prior_sb[:], in_=prior.rearrange("(c p) -> p c", p=P))
-        last = PASSES - 1
+
         halves = [slice(h * B // 2, (h + 1) * B // 2) for h in range(2)]
-        lists = [slice(h * B // 32, (h + 1) * B // 32) for h in range(2)]
         last_rounded = keep.tile([P, 2, B // 2 * PACK], BF16, name="last_rounded", align_bytes=64)
 
-        def last_product(term, pos, factor, h):
-            nc.vector.tensor_tensor(term[:, PACK - 1, halves[h]], colour[TILES - 1][:].indirect(pos[:, lists[h]]),
-                                    factor[:, halves[h]], ALU.mult)
+        def score_pass(score, c, g, bars):
+            cols = slice(c * P, (c + 1) * P)
+            nc.tensor.matmul_mx(out=score[:, 0 : B // 2], lhsT=w8_sb[:, g, cols].bitcast(FP8X4),
+                                lhsT_scale=w8_planes[4 * g :, cols], rhs=z_codes[g][:, bars].bitcast(FP8X4),
+                                rhs_scale=z_plane[g][:, bars], start=(g == 0), stop=(g == LAST_PASS))
 
         def open_scores(c, h):
             score = next_bank()
-            for g in range(last):
-                second_stage(score, c, g, halves[h])
+            for g in range(LAST_PASS):
+                score_pass(score, c, g, halves[h])
             return score
 
-        def store_scores(score, c, h, engine):
+        def last_cos_term(h):
+            entries = substitute_of[:, halves[h].start // PER_COLUMN : halves[h].stop // PER_COLUMN]
+            nc.vector.tensor_tensor(cos_terms[LAST_PASS][:, PACK - 1, halves[h]], colour[LAST_TILE][:].indirect(entries),
+                                    last_cosine[:, halves[h]], ALU.mult)
+
+        def store_scores(score, c, h, on_scalar):
             result = keep.tile([P, B // 2], F32, name="result%d_%d" % (c, h))
-            if engine == "scalar":
+            if on_scalar:
                 nc.scalar.activation(result[:], score[:, 0 : B // 2], ACT.Identity, bias=prior_sb[:, c : c + 1])
             else:
                 nc.vector.tensor_scalar(result[:], score[:, 0 : B // 2], prior_sb[:, c : c + 1], None, ALU.add)
             nc.sync.dma_start(out=out[c * P : (c + 1) * P, halves[h]], in_=result[:])
 
-        first = [open_scores(c, 0) for c in range(OUT_TILES)]
-        second = [open_scores(c, 1) for c in range(BANKS - OUT_TILES)]
-        last_product(terms[last][1], pos_sb[2], sine[TILES - 1], 0)
-        last_product(terms[last][0], pos_sb[1], cosine, 0)
-        combine(nc.vector, last, halves[0], last_rounded[:, 0, :])
-        last_product(terms[last][1], pos_sb[2], sine[TILES - 1], 1)
-        quantise_z(last, halves[0], last_rounded[:, 0, :])
-        last_product(terms[last][0], pos_sb[1], cosine, 1)
-        combine(nc.vector, last, halves[1], last_rounded[:, 1, :])
-        quantise_z(last, halves[1], last_rounded[:, 1, :])
+        first_scores = [open_scores(c, 0) for c in range(OUT_TILES)]
+        second_scores = [open_scores(c, 1) for c in range(BANKS - OUT_TILES)]
+        nc.vector.tensor_tensor(sin_terms[LAST_PASS][:, PACK - 1, :], low[LAST_TILE][:], sine[LAST_TILE][:], ALU.mult)
+        last_cos_term(0)
+        subtract(nc.vector, LAST_PASS, halves[0], last_rounded[:, 0, :])
+        last_cos_term(1)
+        quantise_z(LAST_PASS, halves[0], last_rounded[:, 0, :])
+        subtract(nc.vector, LAST_PASS, halves[1], last_rounded[:, 1, :])
+        quantise_z(LAST_PASS, halves[1], last_rounded[:, 1, :])
         for c in range(OUT_TILES):
-            second_stage(first[c], c, last, halves[0])
-            store_scores(first[c], c, 0, "scalar")
-        second.extend([open_scores(c, 1) for c in range(BANKS - OUT_TILES, OUT_TILES)])
+            score_pass(first_scores[c], c, LAST_PASS, halves[0])
+            store_scores(first_scores[c], c, 0, True)
+        second_scores.extend([open_scores(c, 1) for c in range(BANKS - OUT_TILES, OUT_TILES)])
         for c in range(OUT_TILES):
-            second_stage(second[c], c, last, halves[1])
-            store_scores(second[c], c, 1, "vector" if c % 2 == 0 else "scalar")
+            score_pass(second_scores[c], c, LAST_PASS, halves[1])
+            store_scores(second_scores[c], c, 1, c % 2 == 1)

@@ -28,10 +28,7 @@ LAST_TILE = TILES - 1
 LAST_PASS = PASSES - 1
 OUT_TILES = N // P
 PER_COLUMN = 16
-
-QUANTISE_Z_AT = {8: 0, 11: 1}
-VECTOR_QUARTER_AT = 9
-ROUND_THIRD_W1_AT = 4
+HALF = B // 2
 
 
 def tile_list_chord_phase_voicings_kernel(tc, tab_words, tab_scales, offs, pos1, pos2, pos3, w1, w4_words,
@@ -40,21 +37,23 @@ def tile_list_chord_phase_voicings_kernel(tc, tab_words, tab_scales, offs, pos1,
     with ExitStack() as ctx:
         keep = ctx.enter_context(tc.tile_pool(name="keep", bufs=1))
         ring = ctx.enter_context(tc.tile_pool(name="ring", bufs=3))
-        sines = ctx.enter_context(tc.tile_pool(name="sines", bufs=6))
+        deep = ctx.enter_context(tc.tile_pool(name="deep", bufs=4))
         pair = ctx.enter_context(tc.tile_pool(name="pair", bufs=2))
+        spot = ctx.enter_context(tc.tile_pool(name="spot", bufs=1))
         psum = ctx.enter_context(tc.psum_pool(name="psum", bufs=1))
 
         def load_scale_rows(queue, plane, rows):
             for q in range(4):
                 queue.dma_start(out=plane[:].bitcast(I32)[32 * q : 32 * q + 4, :], in_=rows[4 * q : 4 * q + 4, :].bitcast(I32))
 
-        tab_plane = keep.tile([P, T], U8, name="tab_plane", align_bytes=64)
+        tab_plane = keep.tile([P, T], U8, name="tab_plane", tag="first_tenant_tab_plane", align_bytes=64)
         w4_plane_raw = keep.tile([P, H], U8, name="w4_plane_raw", align_bytes=64)
-        nc.vector.memset(tab_plane[:].bitcast(I32), 0)
-        nc.vector.memset(w4_plane_raw[:].bitcast(I32), 0)
-
         zero = keep.tile([P, 1], F32, name="zero")
-        nc.vector.memset(zero[:], 0.0)
+        nc.gpsimd.memset(tab_plane[:].bitcast(I32), 0)
+        nc.gpsimd.memset(zero[:], 0.0)
+        nc.gpsimd.memset(w4_plane_raw[:].bitcast(I32), 0)
+        load_scale_rows(nc.scalar, tab_plane, tab_scales[0])
+
         sin_zero = keep.tile([P, 1], F32, name="sin_zero")
         nc.scalar.activation(sin_zero[:], zero[:], ACT.Sin)
         half_pi = keep.tile([P, 1], F32, name="half_pi")
@@ -63,82 +62,72 @@ def tile_list_chord_phase_voicings_kernel(tc, tab_words, tab_scales, offs, pos1,
         offs_sb = keep.tile([P, S // PER_COLUMN], U16, name="offs_sb")
         nc.sync.dma_start(offs_sb[:], offs)
         bar_lists = []
-        for i, pos in enumerate((pos1, pos2, pos3)):
+        for i, pos in enumerate((pos1, pos3, pos2)):
             bar_list = keep.tile([P, B // PER_COLUMN], U16, name="bar_list%d" % i)
             nc.sync.dma_start(bar_list[:], pos)
             bar_lists.append(bar_list)
-        current_of, substitute_of, low_of = bar_lists
-        load_scale_rows(nc.scalar, tab_plane, tab_scales[0])
-
-        def load_w4(g):
-            raw = keep.tile([P, PASS // 2], I32, name="w4_raw", align_bytes=64)
-            nc.sync.dma_start(out=raw[:], in_=w4_words[0].bitcast(I32)[:, g * PASS // 2 : (g + 1) * PASS // 2])
-            return raw
-
-        tab_sb = keep.tile([P, T], I32, name="tab_sb", tag="table_words_then_picked_plane", align_bytes=64)
-        nc.sync.dma_start(out=tab_sb[:], in_=tab_words[0].rearrange("p t i -> p (t i)").bitcast(I32))
+        current_of, low_of, substitute_of = bar_lists
         w1_rows = w1.rearrange("(p j) r -> p j r", j=PACK)
-        w1_first = []
-        for h in range(2):
-            raw = pair.tile([P, PACK, PASS // 2], F32, name="w1_first")
-            nc.sync.dma_start(out=raw[:], in_=w1_rows[:, :, h * PASS // 2 : (h + 1) * PASS // 2])
-            w1_first.append(raw)
-        w4_raw = load_w4(0)
-        load_scale_rows(nc.sync, w4_plane_raw, w4_scales[0])
 
-        def load_w1(g):
-            raw = keep.tile([P, PACK, PASS], F32, name="w1_raw", tag="weights_in_turn", align_bytes=64)
-            nc.sync.dma_start(out=raw[:], in_=w1_rows[:, :, g * PASS : (g + 1) * PASS])
+        def load_w1(g, h, tag):
+            raw = keep.tile([P, PACK, PASS // 2], F32, name="w1_raw", tag=tag, align_bytes=64)
+            first = g * PASS + h * PASS // 2
+            nc.sync.dma_start(out=raw[:], in_=w1_rows[:, :, first : first + PASS // 2])
             return raw
 
-        def load_w8():
-            words = keep.tile([P, PASSES, N], I32, name="w8_sb", tag="weights_in_turn", align_bytes=64)
-            nc.sync.dma_start(out=words[:], in_=w8_words.rearrange("a p c i -> p a (c i)").bitcast(I32))
-            planes = keep.tile([P, N], U8, name="w8_planes", tag="w1_rounded", align_bytes=64)
-            nc.gpsimd.memset(planes[:].bitcast(I32), 0)
-            for q in range(4):
-                nc.sync.dma_start(out=planes[:].bitcast(I32)[32 * q : 32 * q + 4 * PASSES, :],
-                                  in_=w8_scales[:, 4 * q : 4 * q + 4, :].bitcast(I32))
-            return words, planes
+        def load_w4(first, last):
+            raw = keep.tile([P, (last - first) * PASS // 2], I32, name="w4_raw", tag="first_tenant_w1_a", align_bytes=64)
+            nc.sync.dma_start(out=raw[:], in_=w4_words[0].bitcast(I32)[:, first * PASS // 2 : last * PASS // 2])
+            return raw
+
+        w1_halves = [load_w1(0, 0, "first_tenant_w1_a"), load_w1(0, 1, "first_tenant_w1_b")]
+        tab_sb = spot.tile([P, T], I32, name="tab_sb", align_bytes=64, offset=0)
+        nc.sync.dma_start(out=tab_sb[:], in_=tab_words[0].rearrange("p t i -> p (t i)").bitcast(I32))
+        load_scale_rows(nc.sync, w4_plane_raw, w4_scales[0])
 
         w1_codes = {}
         w1_plane = {}
+        w1_rounded = {}
+        for g in range(PASSES):
+            w1_codes[g] = keep.tile([P, PASS], U32, name="w1_codes%d" % g, align_bytes=64)
+            w1_plane[g] = keep.tile([P, PASS], U8, name="w1_plane%d" % g, align_bytes=64)
+
+        def round_w1(g, h, raw, copy):
+            rounded = w1_rounded[g][:, :, h * P // 2 : (h + 1) * P // 2, :].rearrange("p t m j -> p m j t")
+            copy(rounded, raw[:].rearrange("p j (m t) -> p m j t", t=PACK))
+
+        def quantise_w1(g):
+            nc.vector.quantize_mx(out=w1_codes[g][:].bitcast(FP8X4), scales=w1_plane[g][:],
+                                  in_=w1_rounded[g][:].rearrange("p t m j -> p (t m j)"))
+
         w4_codes = {}
         w4_plane = {}
 
-        def round_w1(rounded, raw):
-            nc.scalar.copy(rounded.rearrange("p t m j -> p m j t"), raw.rearrange("p j (m t) -> p m j t", t=PACK))
-
-        def quantise_w1(g, rounded):
-            w1_codes[g] = keep.tile([P, PASS], U32, name="w1_codes%d" % g, align_bytes=64)
-            w1_plane[g] = keep.tile([P, PASS], U8, name="w1_plane%d" % g, align_bytes=64)
-            nc.vector.quantize_mx(out=w1_codes[g][:].bitcast(FP8X4), scales=w1_plane[g][:],
-                                  in_=rounded[:].rearrange("p t m j -> p (t m j)"))
-
-        def order_w4(g, raw):
-            w4_codes[g] = keep.tile([P, PASS], U16, name="w4_codes%d" % g, align_bytes=64)
-            w4_plane[g] = keep.tile([P, PASS], U8, name="w4_plane%d" % g, align_bytes=64)
+        def order_w4(g, words):
+            w4_codes[g] = spot.tile([P, PASS], U16, name="w4_codes%d" % g, align_bytes=64, offset=2048 * g)
+            w4_plane[g] = spot.tile([P, PASS], U8, name="w4_plane%d" % g, align_bytes=64, offset=2048 * g + 1024)
             nc.vector.tensor_copy(w4_codes[g][:].rearrange("p (t m) -> p t m", t=PACK),
-                                  raw[:].bitcast(U16).rearrange("p (m t) -> p t m", t=PACK))
+                                  words.bitcast(U16).rearrange("p (m t) -> p t m", t=PACK))
             nc.vector.tensor_copy(w4_plane[g][:].rearrange("p (t m) -> p t m", t=PACK),
                                   w4_plane_raw[:, g * PASS : (g + 1) * PASS].rearrange("p (m t) -> p t m", t=PACK))
 
-        w1_rounded = keep.tile([P, PACK, P, PACK], BF16, name="w1_rounded", tag="weights_in_turn", align_bytes=64)
+        w1_rounded[0] = keep.tile([P, PACK, P, PACK], BF16, name="w1_rounded", tag="w1_rounded", align_bytes=64)
         for h in range(2):
-            round_w1(w1_rounded[:, :, h * P // 2 : (h + 1) * P // 2, :], w1_first[h][:])
+            round_w1(0, h, w1_halves[h], nc.scalar.copy)
+        w4_first = load_w4(0, 1)
 
+        picked_plane = keep.tile([P, S], U8, name="picked_plane", align_bytes=64)
+        nc.vector.tensor_copy(picked_plane[:], tab_plane[:].indirect(offs_sb[:]))
+        quantise_w1(0)
+        w1_halves = [load_w1(1, 0, "first_tenant_tab_plane"), load_w1(1, 1, "first_tenant_w1_b")]
         picked_codes = []
         for h in range(S // BANK):
             codes = keep.tile([P, BANK], U32, name="picked_codes%d" % h, align_bytes=64)
             entries = offs_sb[:, h * BANK // PER_COLUMN : (h + 1) * BANK // PER_COLUMN]
             nc.vector.tensor_copy(codes[:], tab_sb[:].bitcast(U32).indirect(entries))
             picked_codes.append(codes)
-        picked_plane = keep.tile([P, S], U8, name="picked_plane", tag="table_words_then_picked_plane", align_bytes=64)
-        nc.vector.tensor_copy(picked_plane[:], tab_plane[:].indirect(offs_sb[:]))
-        quantise_w1(0, w1_rounded)
-        order_w4(0, w4_raw)
-        w1_raw = load_w1(1)
-        w1_rounded = keep.tile([P, PACK, P, PACK], BF16, name="w1_rounded", tag="w1_rounded", align_bytes=64)
+        order_w4(0, w4_first[:])
+        w4_rest = load_w4(1, PASSES)
 
         banks_taken = []
 
@@ -157,154 +146,161 @@ def tile_list_chord_phase_voicings_kernel(tc, tab_words, tab_scales, offs, pos1,
 
         angle = {}
         colour = {}
-        low = {}
 
         def make_phase(i):
             g, t = divmod(i, PACK)
             cols = slice(t * P, (t + 1) * P)
             phase = ring.tile([P, S], F32, name="phase")
             first_stage(w1_codes[g][:, cols].bitcast(FP8X4), w1_plane[g][:, cols], phase)
-            if i in QUANTISE_Z_AT or i == VECTOR_QUARTER_AT:
-                angle[i] = keep.tile([P, B], F32, name="angle", tag="angle_of_tile%d" % i, align_bytes=64)
-            else:
-                angle[i] = ring.tile([P, B], F32, name="angle")
+            angle[i] = deep.tile([P, B], F32, name="angle")
             nc.vector.tensor_copy(angle[i][:], phase[:].indirect(current_of[:]))
 
         def make_colour(i):
+            colour[i] = deep.tile([P, S], F32, name="colour")
             g, t = divmod(i, PACK)
             cols = slice(t * P, (t + 1) * P)
-            colour[i] = ring.tile([P, S], F32, name="colour")
             first_stage(w4_codes[g][:, cols].bitcast(FP4X4), w4_plane[g][:, cols], colour[i])
-            low[i] = ring.tile([P, B], F32, name="low")
-            nc.vector.tensor_copy(low[i][:], colour[i][:].indirect(low_of[:]))
 
         cos_terms = {}
         sin_terms = {}
         sine = {}
+        cosine = {}
+        halves = [slice(h * HALF, (h + 1) * HALF) for h in range(2)]
+        reused = (4, 5, 6, 7, 8, 9, 10)
 
-        def sine_and_size(i):
+        def sines(i):
+            if i == 9:
+                sine[i] = keep.tile([P, B], F32, name="sine_kept", tag="sine_of9", align_bytes=64)
+            else:
+                sine[i] = deep.tile([P, B], F32, name="sine")
+            if i in reused:
+                cosine[i] = keep.tile([P, B], F32, name="cosine_kept", tag="cosine_of%d" % i, align_bytes=64)
+            else:
+                cosine[i] = ring.tile([P, B], F32, name="cosine")
+            size = pair.tile([P, B], F32, name="size")
+            nc.scalar.activation(sine[i][:], angle[i][:], ACT.Sin)
+            nc.scalar.activation(size[:], angle[i][:], ACT.Abs)
+            nc.scalar.activation(cosine[i][:], size[:], ACT.Sin, bias=half_pi[:], scale=-1.0)
+
+        def products(i, bars):
+            g, t = divmod(i, PACK)
+            entries = slice(bars.start // PER_COLUMN, bars.stop // PER_COLUMN)
+            nc.vector.tensor_tensor(sin_terms[g][:, t, bars], colour[i][:].indirect(low_of[:, entries]),
+                                    sine[i][:, bars], ALU.mult)
+            nc.vector.tensor_tensor(cos_terms[g][:, t, bars], colour[i][:].indirect(substitute_of[:, entries]),
+                                    cosine[i][:, bars], ALU.mult)
+
+        def subtract(engine, g, bars, rounded):
+            engine.tensor_tensor(rounded.rearrange("p (c i t) -> p c t i", i=4, t=PACK),
+                                    cos_terms[g][:, :, bars].rearrange("p t (c i) -> p c t i", i=4),
+                                    sin_terms[g][:, :, bars].rearrange("p t (c i) -> p c t i", i=4), ALU.subtract)
+
+        z_codes = {}
+        z_plane = {}
+
+        def quantise_z(g, h, rounded, tag):
+            z_codes[g, h] = keep.tile([P, HALF], U32, name="z_codes", tag=tag, align_bytes=64)
+            z_plane[g, h] = keep.tile([P, HALF], U8, name="z_plane%d_%d" % (g, h), align_bytes=64)
+            nc.vector.quantize_mx(out=z_codes[g, h][:].bitcast(FP8X4), scales=z_plane[g, h][:], in_=rounded)
+
+        rounded_z = {}
+
+        def new_rounded(g, h, tag):
+            rounded_z[g, h] = keep.tile([P, HALF * PACK], BF16, name="rounded_z", tag=tag, align_bytes=64)
+            return rounded_z[g, h][:]
+
+        make_phase(0)
+        make_phase(1)
+        for i in range(TILES):
             g, t = divmod(i, PACK)
             if t == 0:
                 cos_terms[g] = pair.tile([P, PACK, B], F32, name="cos_terms")
                 sin_terms[g] = pair.tile([P, PACK, B], F32, name="sin_terms")
-            size = ring.tile([P, B], F32, name="size")
-            nc.scalar.activation(size[:], angle[i][:], ACT.Abs)
-            sine[i] = sines.tile([P, B], F32, name="sine", align_bytes=64)
-            nc.scalar.activation(sine[i][:], angle[i][:], ACT.Sin)
-            return size
-
-        def turn(i, size):
-            g, t = divmod(i, PACK)
-            place = sin_terms[g][:, t, :]
-            nc.scalar.activation(place, size[:], ACT.Sin, bias=half_pi[:], scale=-1.0)
-            nc.vector.tensor_tensor(cos_terms[g][:, t, :], colour[i][:].indirect(substitute_of[:]), place, ALU.mult)
-            nc.gpsimd.tensor_tensor(place, low[i][:], sine[i][:], ALU.mult)
-
-        def subtract(engine, g, bars, rounded):
-            engine.tensor_tensor(rounded.rearrange("p (c i t) -> p c t i", i=4, t=PACK),
-                                 cos_terms[g][:, :, bars].rearrange("p t (c i) -> p c t i", i=4),
-                                 sin_terms[g][:, :, bars].rearrange("p t (c i) -> p c t i", i=4), ALU.subtract)
-
-        z_codes = {LAST_PASS: keep.tile([P, B], U32, name="last_z_codes", align_bytes=64)}
-        z_plane = [keep.tile([P, B], U8, name="z_plane%d" % g, align_bytes=64) for g in range(PASSES)]
-        z_quarters = {g: [] for g in range(LAST_PASS)}
-
-        def quantise_z(g, bars, rounded):
-            nc.vector.quantize_mx(out=z_codes[g][:, bars].bitcast(FP8X4), scales=z_plane[g][:, bars], in_=rounded)
-
-        make_phase(0)
-        make_colour(0)
-        make_phase(1)
-        for i in range(TILES):
-            g, t = divmod(i, PACK)
-            size = sine_and_size(i)
+            make_colour(i)
+            sines(i)
             if i < LAST_TILE:
-                turn(i, size)
-            else:
-                last_cosine = ring.tile([P, B], F32, name="size")
-                nc.scalar.activation(last_cosine[:], size[:], ACT.Sin, bias=half_pi[:], scale=-1.0)
-            if i == ROUND_THIRD_W1_AT + 1:
-                quantise_w1(2, w1_rounded)
-                w8_sb, w8_planes = load_w8()
-            if i in QUANTISE_Z_AT:
-                done = QUANTISE_Z_AT[i]
-                z_codes[done] = keep.tile([P, B], U32, name="z_codes", tag="angle_of_tile%d" % i, align_bytes=64)
-                for bars, rounded in z_quarters[done]:
-                    quantise_z(done, bars, rounded)
-            if i == ROUND_THIRD_W1_AT:
-                w1_rounded = keep.tile([P, PACK, P, PACK], BF16, name="w1_rounded", tag="w1_rounded", align_bytes=64)
-                round_w1(w1_rounded[:], w1_raw[:])
-            done, quarter = divmod(i - (PACK - 1), PACK)
-            if 0 <= done < LAST_PASS and i + 2 < TILES:
-                bars = slice(quarter * P, (quarter + 1) * P)
-                rounded = sine[i][:].bitcast(BF16)[:, 0 : P * PACK]
-                subtract(nc.gpsimd, done, bars, rounded)
-                z_quarters[done].append((bars, rounded))
-            if i == VECTOR_QUARTER_AT:
-                bars = slice(B - P, B)
-                fourth = keep.tile([P, P * PACK], BF16, name="fourth", tag="angle_of_tile%d" % i, align_bytes=64)
-                subtract(nc.vector, 1, bars, fourth[:])
-                z_quarters[1].append((bars, fourth[:]))
-            if i < 2:
-                round_w1(w1_rounded[:, :, i * P // 2 : (i + 1) * P // 2, :], w1_raw[:, :, i * PASS // 2 : (i + 1) * PASS // 2])
-            if i == 1:
-                w1_raw = load_w1(2)
-            if i == 2:
-                quantise_w1(1, w1_rounded)
-            if t == 0 and g < LAST_PASS:
-                w4_raw = load_w4(g + 1)
-            if t == 1 and g < LAST_PASS:
-                order_w4(g + 1, w4_raw)
-            if i + 2 < TILES:
+                products(i, slice(0, B))
+            if i in (0, 3):
+                later = 1 + i // 3
+                w1_rounded[later] = keep.tile([P, PACK, P, PACK], BF16, name="w1_rounded", tag="w1_rounded", align_bytes=64)
+                for h in range(2):
+                    round_w1(later, h, w1_halves[h], nc.vector.tensor_copy if later == 1 else nc.scalar.copy)
+                quantise_w1(later)
+            if i == 0:
+                w1_halves = [load_w1(2, 0, "first_tenant_tab_plane"), load_w1(2, 1, "first_tenant_w1_b")]
+            if i in (1, 2):
+                order_w4(i, w4_rest[:, (i - 1) * PASS // 2 : i * PASS // 2])
+            if i == 3:
+                w8_sb = keep.tile([P, PASSES, N], I32, name="w8_sb", tag="w1_rounded", align_bytes=64)
+                nc.sync.dma_start(out=w8_sb[:], in_=w8_words.rearrange("a p c i -> p a (c i)").bitcast(I32))
+                w8_planes = keep.tile([P, N], U8, name="w8_planes", tag="first_tenant_w1_a", align_bytes=64)
+                nc.vector.memset(w8_planes[:].bitcast(I32), 0)
+                for q in range(4):
+                    nc.sync.dma_start(out=w8_planes[:].bitcast(I32)[32 * q : 32 * q + 4 * PASSES, :],
+                                      in_=w8_scales[:, 4 * q : 4 * q + 4, :].bitcast(I32))
+                prior_sb = keep.tile([P, OUT_TILES], F32, name="prior_sb", tag="first_tenant_w1_b", align_bytes=64)
+                with nc.allow_non_contiguous_dma(reason="one prior value for each output row"):
+                    nc.sync.dma_start(out=prior_sb[:], in_=prior.rearrange("(c p) -> p c", p=P))
+            if i == 4:
+                subtract(nc.gpsimd, 0, halves[0], new_rounded(0, 0, "cosine_of4"))
+            if i == 5:
+                quantise_z(0, 0, rounded_z[0, 0][:], "cosine_of5")
+            if i == 6:
+                subtract(nc.gpsimd, 0, halves[1], new_rounded(0, 1, "cosine_of6"))
+            if i == 7:
+                quantise_z(0, 1, rounded_z[0, 1][:], "cosine_of7")
+            if i == 8:
+                subtract(nc.gpsimd, 1, halves[0], new_rounded(1, 0, "cosine_of8"))
+            if i == 9:
+                subtract(nc.vector, 1, halves[1], new_rounded(1, 1, "cosine_of9"))
+                quantise_z(1, 0, rounded_z[1, 0][:], "sine_of9")
+            if i == 10:
+                quantise_z(1, 1, rounded_z[1, 1][:], "cosine_of10")
+            if i % 2 == 0 and i + 2 < TILES:
                 make_phase(i + 2)
-            if i + 1 < TILES:
-                make_colour(i + 1)
+                make_phase(i + 3)
 
-        prior_sb = keep.tile([P, OUT_TILES], F32, name="prior_sb", tag="w4_raw", align_bytes=64)
-        with nc.allow_non_contiguous_dma(reason="one prior value for each output row"):
-            nc.sync.dma_start(out=prior_sb[:], in_=prior.rearrange("(c p) -> p c", p=P))
+        last_rounded = keep.tile([P, 2, HALF * PACK], BF16, name="last_rounded", align_bytes=64)
 
-        halves = [slice(h * B // 2, (h + 1) * B // 2) for h in range(2)]
-        last_rounded = keep.tile([P, 2, B // 2 * PACK], BF16, name="last_rounded", align_bytes=64)
-
-        def score_pass(score, c, g, bars):
+        def score_pass(score, c, g, h):
             cols = slice(c * P, (c + 1) * P)
-            nc.tensor.matmul_mx(out=score[:, 0 : B // 2], lhsT=w8_sb[:, g, cols].bitcast(FP8X4),
-                                lhsT_scale=w8_planes[4 * g :, cols], rhs=z_codes[g][:, bars].bitcast(FP8X4),
-                                rhs_scale=z_plane[g][:, bars], start=(g == 0), stop=(g == LAST_PASS))
-
-        def open_scores(c, h):
-            score = next_bank()
-            for g in range(LAST_PASS):
-                score_pass(score, c, g, halves[h])
-            return score
-
-        def last_cos_term(h):
-            entries = substitute_of[:, halves[h].start // PER_COLUMN : halves[h].stop // PER_COLUMN]
-            nc.vector.tensor_tensor(cos_terms[LAST_PASS][:, PACK - 1, halves[h]], colour[LAST_TILE][:].indirect(entries),
-                                    last_cosine[:, halves[h]], ALU.mult)
+            nc.tensor.matmul_mx(out=score, lhsT=w8_sb[:, g, cols].bitcast(FP8X4),
+                                lhsT_scale=w8_planes[4 * g :, cols], rhs=z_codes[g, h][:].bitcast(FP8X4),
+                                rhs_scale=z_plane[g, h][:], start=(g == 0), stop=(g == LAST_PASS))
 
         def store_scores(score, c, h, on_scalar):
-            result = keep.tile([P, B // 2], F32, name="result%d_%d" % (c, h))
+            result = keep.tile([P, HALF], F32, name="result%d_%d" % (c, h))
             if on_scalar:
-                nc.scalar.activation(result[:], score[:, 0 : B // 2], ACT.Identity, bias=prior_sb[:, c : c + 1])
+                nc.scalar.activation(result[:], score, ACT.Identity, bias=prior_sb[:, c : c + 1])
             else:
-                nc.vector.tensor_scalar(result[:], score[:, 0 : B // 2], prior_sb[:, c : c + 1], None, ALU.add)
+                nc.vector.tensor_scalar(result[:], score, prior_sb[:, c : c + 1], None, ALU.add)
             nc.sync.dma_start(out=out[c * P : (c + 1) * P, halves[h]], in_=result[:])
 
-        first_scores = [open_scores(c, 0) for c in range(OUT_TILES)]
-        second_scores = [open_scores(c, 1) for c in range(BANKS - OUT_TILES)]
-        nc.vector.tensor_tensor(sin_terms[LAST_PASS][:, PACK - 1, :], low[LAST_TILE][:], sine[LAST_TILE][:], ALU.mult)
-        last_cos_term(0)
-        subtract(nc.vector, LAST_PASS, halves[0], last_rounded[:, 0, :])
-        last_cos_term(1)
-        quantise_z(LAST_PASS, halves[0], last_rounded[:, 0, :])
-        subtract(nc.vector, LAST_PASS, halves[1], last_rounded[:, 1, :])
-        quantise_z(LAST_PASS, halves[1], last_rounded[:, 1, :])
+        shared = [next_bank() for b in range(2)]
+        own = [next_bank() for c in range(OUT_TILES)]
+        for c in range(2):
+            for g in range(LAST_PASS):
+                score_pass(shared[c][:, halves[0]], c, g, 0)
         for c in range(OUT_TILES):
-            score_pass(first_scores[c], c, LAST_PASS, halves[0])
-            store_scores(first_scores[c], c, 0, True)
-        second_scores.extend([open_scores(c, 1) for c in range(BANKS - OUT_TILES, OUT_TILES)])
+            for g in range(LAST_PASS):
+                score_pass(own[c][:, halves[0]], c, g, 1)
+        for h in range(2):
+            products(LAST_TILE, halves[h])
+            subtract(nc.vector, LAST_PASS, halves[h], last_rounded[:, h, :])
+            quantise_z(LAST_PASS, h, last_rounded[:, h, :], "last_z_codes%d" % h)
+        for c in range(2):
+            score_pass(shared[c][:, halves[0]], c, LAST_PASS, 0)
+        for c in range(2, 4):
+            for g in range(PASSES):
+                score_pass(shared[c - 2][:, halves[1]], c, g, 0)
+        for b in range(2):
+            store_scores(shared[b][:, halves[0]], b, 0, True)
+            store_scores(shared[b][:, halves[1]], b + 2, 0, True)
+        for c in range(4, OUT_TILES):
+            again = next_bank()
+            for g in range(PASSES):
+                score_pass(again[:, halves[0]], c, g, 0)
+            store_scores(again[:, halves[0]], c, 0, True)
         for c in range(OUT_TILES):
-            score_pass(second_scores[c], c, LAST_PASS, halves[1])
-            store_scores(second_scores[c], c, 1, c % 2 == 1)
+            score_pass(own[c][:, halves[0]], c, LAST_PASS, 1)
+            store_scores(own[c][:, halves[0]], c, 1, c % 2 == 0)

@@ -29,6 +29,8 @@ LAST_PASS = PASSES - 1
 OUT_TILES = N // P
 PER_COLUMN = 16
 HALF = B // 2
+ROUND_Z_AT = {5: (0, 0, False), 7: (0, 1, False)}
+HELD = {6: (0, 0), 8: (0, 1)}
 
 
 def tile_list_chord_phase_voicings_kernel(tc, tab_words, tab_scales, offs, pos1, pos2, pos3, w1, w4_words,
@@ -47,26 +49,24 @@ def tile_list_chord_phase_voicings_kernel(tc, tab_words, tab_scales, offs, pos1,
                 queue.dma_start(out=plane[:].bitcast(I32)[32 * q : 32 * q + 4, :], in_=rows[4 * q : 4 * q + 4, :].bitcast(I32))
 
         tab_plane = keep.tile([P, T], U8, name="tab_plane", tag="first_tenant_tab_plane", align_bytes=64)
+        for q in range(4):
+            nc.sync.dma_start(out=tab_plane[:].bitcast(I32)[32 * q : 32 * q + 32, :],
+                              in_=tab_scales[0][4 * q : 4 * q + 4, :].bitcast(I32).partition_broadcast(8))
         w4_plane_raw = keep.tile([P, H], U8, name="w4_plane_raw", align_bytes=64)
         zero = keep.tile([P, 1], F32, name="zero")
-        nc.gpsimd.memset(tab_plane[:].bitcast(I32), 0)
         nc.gpsimd.memset(zero[:], 0.0)
         nc.gpsimd.memset(w4_plane_raw[:].bitcast(I32), 0)
-        load_scale_rows(nc.scalar, tab_plane, tab_scales[0])
 
         sin_zero = keep.tile([P, 1], F32, name="sin_zero")
         nc.scalar.activation(sin_zero[:], zero[:], ACT.Sin)
         half_pi = keep.tile([P, 1], F32, name="half_pi")
-        nc.vector.tensor_scalar(half_pi[:], sin_zero[:], math.pi / 2, None, ALU.add)
+        nc.gpsimd.tensor_scalar(half_pi[:], sin_zero[:], math.pi / 2, None, ALU.add)
 
-        offs_sb = keep.tile([P, S // PER_COLUMN], U16, name="offs_sb")
-        nc.sync.dma_start(offs_sb[:], offs)
-        bar_lists = []
-        for i, pos in enumerate((pos1, pos3, pos2)):
-            bar_list = keep.tile([P, B // PER_COLUMN], U16, name="bar_list%d" % i)
-            nc.sync.dma_start(bar_list[:], pos)
-            bar_lists.append(bar_list)
-        current_of, low_of, substitute_of = bar_lists
+        def load_list(name, entries, count):
+            tile = keep.tile([P, count // PER_COLUMN], U16, name=name)
+            nc.sync.dma_start(tile[:], entries)
+            return tile
+
         w1_rows = w1.rearrange("(p j) r -> p j r", j=PACK)
 
         def load_w1(g, h, tag):
@@ -76,14 +76,17 @@ def tile_list_chord_phase_voicings_kernel(tc, tab_words, tab_scales, offs, pos1,
             return raw
 
         def load_w4(first, last):
-            raw = keep.tile([P, (last - first) * PASS // 2], I32, name="w4_raw", tag="first_tenant_w1_a", align_bytes=64)
+            raw = keep.tile([P, (last - first) * PASS // 2], I32, name="w4_raw", tag="w4_raw", align_bytes=64)
             nc.sync.dma_start(out=raw[:], in_=w4_words[0].bitcast(I32)[:, first * PASS // 2 : last * PASS // 2])
             return raw
 
-        w1_halves = [load_w1(0, 0, "first_tenant_w1_a"), load_w1(0, 1, "first_tenant_w1_b")]
+        offs_sb = load_list("offs_sb", offs, S)
         tab_sb = spot.tile([P, T], I32, name="tab_sb", align_bytes=64, offset=0)
         nc.sync.dma_start(out=tab_sb[:], in_=tab_words[0].rearrange("p t i -> p (t i)").bitcast(I32))
+        w1_halves = [load_w1(0, 0, "first_tenant_w1_a"), load_w1(0, 1, "first_tenant_w1_b")]
         load_scale_rows(nc.sync, w4_plane_raw, w4_scales[0])
+        w4_first = load_w4(0, 1)
+        current_of = load_list("current_of", pos1, B)
 
         w1_codes = {}
         w1_plane = {}
@@ -96,9 +99,10 @@ def tile_list_chord_phase_voicings_kernel(tc, tab_words, tab_scales, offs, pos1,
             rounded = w1_rounded[g][:, :, h * P // 2 : (h + 1) * P // 2, :].rearrange("p t m j -> p m j t")
             copy(rounded, raw[:].rearrange("p j (m t) -> p m j t", t=PACK))
 
-        def quantise_w1(g):
-            nc.vector.quantize_mx(out=w1_codes[g][:].bitcast(FP8X4), scales=w1_plane[g][:],
-                                  in_=w1_rounded[g][:].rearrange("p t m j -> p (t m j)"))
+        def quantise_w1(g, first, last):
+            nc.vector.quantize_mx(out=w1_codes[g][:, first * P : last * P].bitcast(FP8X4),
+                                  scales=w1_plane[g][:, first * P : last * P],
+                                  in_=w1_rounded[g][:, first:last].rearrange("p t m j -> p (t m j)"))
 
         w4_codes = {}
         w4_plane = {}
@@ -114,19 +118,22 @@ def tile_list_chord_phase_voicings_kernel(tc, tab_words, tab_scales, offs, pos1,
         w1_rounded[0] = keep.tile([P, PACK, P, PACK], BF16, name="w1_rounded", tag="w1_rounded", align_bytes=64)
         for h in range(2):
             round_w1(0, h, w1_halves[h], nc.scalar.copy)
-        w4_first = load_w4(0, 1)
 
         picked_plane = keep.tile([P, S], U8, name="picked_plane", align_bytes=64)
         nc.vector.tensor_copy(picked_plane[:], tab_plane[:].indirect(offs_sb[:]))
-        quantise_w1(0)
-        w1_halves = [load_w1(1, 0, "first_tenant_tab_plane"), load_w1(1, 1, "first_tenant_w1_b")]
+        w1_halves = [load_w1(1, 0, "first_tenant_tab_plane"), load_w1(1, 1, "first_tenant_w1_a")]
+        low_of = load_list("low_of", pos3, B)
+        substitute_of = load_list("substitute_of", pos2, B)
         picked_codes = []
         for h in range(S // BANK):
             codes = keep.tile([P, BANK], U32, name="picked_codes%d" % h, align_bytes=64)
             entries = offs_sb[:, h * BANK // PER_COLUMN : (h + 1) * BANK // PER_COLUMN]
             nc.vector.tensor_copy(codes[:], tab_sb[:].bitcast(U32).indirect(entries))
             picked_codes.append(codes)
+        quantise_w1(0, 0, 1)
         order_w4(0, w4_first[:])
+        quantise_w1(0, 1, 2)
+        quantise_w1(0, 2, 4)
         w4_rest = load_w4(1, PASSES)
 
         banks_taken = []
@@ -161,61 +168,64 @@ def tile_list_chord_phase_voicings_kernel(tc, tab_words, tab_scales, offs, pos1,
             cols = slice(t * P, (t + 1) * P)
             first_stage(w4_codes[g][:, cols].bitcast(FP4X4), w4_plane[g][:, cols], colour[i])
 
-        cos_terms = {}
+        turned = keep.tile([P, TILES, B], F32, name="turned")
+        cos_terms = {i: turned[:, i, :] for i in range(TILES)}
+        spare = keep.tile([P, B], F32, name="spare")
+        cos_terms[7] = spare[:]
         sin_terms = {}
         sine = {}
         cosine = {}
         halves = [slice(h * HALF, (h + 1) * HALF) for h in range(2)]
-        reused = (4, 5, 6, 7, 8, 9, 10)
 
         def sines(i):
-            if i == 9:
-                sine[i] = keep.tile([P, B], F32, name="sine_kept", tag="sine_of9", align_bytes=64)
+            if i in HELD or i in ROUND_Z_AT:
+                sine[i] = keep.tile([P, B], F32, name="sine_kept", tag="sine_of%d" % i, align_bytes=64)
             else:
-                sine[i] = deep.tile([P, B], F32, name="sine")
-            if i in reused:
-                cosine[i] = keep.tile([P, B], F32, name="cosine_kept", tag="cosine_of%d" % i, align_bytes=64)
+                sine[i] = ring.tile([P, B], F32, name="sine")
+            if i == 8:
+                cosine[i] = turned[:, 7, :]
             else:
-                cosine[i] = ring.tile([P, B], F32, name="cosine")
+                lone = ring.tile([P, B], F32, name="cosine")
+                cosine[i] = lone[:]
             size = pair.tile([P, B], F32, name="size")
             nc.scalar.activation(sine[i][:], angle[i][:], ACT.Sin)
             nc.scalar.activation(size[:], angle[i][:], ACT.Abs)
-            nc.scalar.activation(cosine[i][:], size[:], ACT.Sin, bias=half_pi[:], scale=-1.0)
+            nc.scalar.activation(cosine[i], size[:], ACT.Sin, bias=half_pi[:], scale=-1.0)
 
         def products(i, bars):
-            g, t = divmod(i, PACK)
             entries = slice(bars.start // PER_COLUMN, bars.stop // PER_COLUMN)
-            nc.vector.tensor_tensor(sin_terms[g][:, t, bars], colour[i][:].indirect(low_of[:, entries]),
+            nc.vector.tensor_tensor(sin_terms[i][:, bars], colour[i][:].indirect(low_of[:, entries]),
                                     sine[i][:, bars], ALU.mult)
-            nc.vector.tensor_tensor(cos_terms[g][:, t, bars], colour[i][:].indirect(substitute_of[:, entries]),
+            nc.vector.tensor_tensor(cos_terms[i][:, bars], colour[i][:].indirect(substitute_of[:, entries]),
                                     cosine[i][:, bars], ALU.mult)
 
-        def subtract(engine, g, bars, rounded):
-            engine.tensor_tensor(rounded.rearrange("p (c i t) -> p c t i", i=4, t=PACK),
-                                    cos_terms[g][:, :, bars].rearrange("p t (c i) -> p c t i", i=4),
-                                    sin_terms[g][:, :, bars].rearrange("p t (c i) -> p c t i", i=4), ALU.subtract)
+        rounded_z = {}
+
+        def round_z(g, h, copy, tag):
+            rounded_z[g, h] = keep.tile([P, HALF * PACK], BF16, name="rounded_z", tag=tag, align_bytes=64)
+            copy(rounded_z[g, h][:].rearrange("p (c i t) -> p c t i", i=4, t=PACK),
+                 turned[:, g * PACK : (g + 1) * PACK, halves[h]].rearrange("p t (c i) -> p c t i", i=4))
 
         z_codes = {}
         z_plane = {}
 
-        def quantise_z(g, h, rounded, tag):
+        def quantise_z(g, h, tag):
             z_codes[g, h] = keep.tile([P, HALF], U32, name="z_codes", tag=tag, align_bytes=64)
             z_plane[g, h] = keep.tile([P, HALF], U8, name="z_plane%d_%d" % (g, h), align_bytes=64)
-            nc.vector.quantize_mx(out=z_codes[g, h][:].bitcast(FP8X4), scales=z_plane[g, h][:], in_=rounded)
-
-        rounded_z = {}
-
-        def new_rounded(g, h, tag):
-            rounded_z[g, h] = keep.tile([P, HALF * PACK], BF16, name="rounded_z", tag=tag, align_bytes=64)
-            return rounded_z[g, h][:]
+            nc.vector.quantize_mx(out=z_codes[g, h][:].bitcast(FP8X4), scales=z_plane[g, h][:], in_=rounded_z[g, h][:])
 
         make_phase(0)
         make_phase(1)
         for i in range(TILES):
             g, t = divmod(i, PACK)
-            if t == 0:
-                cos_terms[g] = pair.tile([P, PACK, B], F32, name="cos_terms")
-                sin_terms[g] = pair.tile([P, PACK, B], F32, name="sin_terms")
+            if g == LAST_PASS:
+                if t == 0:
+                    last_terms = keep.tile([P, PACK, B], F32, name="last_terms")
+                sin_terms[i] = last_terms[:, t, :]
+            elif i % 2 == 1 or i == 0:
+                both = pair.tile([P, 2 * B], F32, name="sin_terms")
+                sin_terms[i] = both[:, 0:B]
+                sin_terms[i + 1] = both[:, B : 2 * B]
             make_colour(i)
             sines(i)
             if i < LAST_TILE:
@@ -225,7 +235,7 @@ def tile_list_chord_phase_voicings_kernel(tc, tab_words, tab_scales, offs, pos1,
                 w1_rounded[later] = keep.tile([P, PACK, P, PACK], BF16, name="w1_rounded", tag="w1_rounded", align_bytes=64)
                 for h in range(2):
                     round_w1(later, h, w1_halves[h], nc.vector.tensor_copy if later == 1 else nc.scalar.copy)
-                quantise_w1(later)
+                quantise_w1(later, 0, PACK)
             if i == 0:
                 w1_halves = [load_w1(2, 0, "first_tenant_tab_plane"), load_w1(2, 1, "first_tenant_w1_b")]
             if i in (1, 2):
@@ -233,7 +243,7 @@ def tile_list_chord_phase_voicings_kernel(tc, tab_words, tab_scales, offs, pos1,
             if i == 3:
                 w8_sb = keep.tile([P, PASSES, N], I32, name="w8_sb", tag="w1_rounded", align_bytes=64)
                 nc.sync.dma_start(out=w8_sb[:], in_=w8_words.rearrange("a p c i -> p a (c i)").bitcast(I32))
-                w8_planes = keep.tile([P, N], U8, name="w8_planes", tag="first_tenant_w1_a", align_bytes=64)
+                w8_planes = keep.tile([P, N], U8, name="w8_planes", tag="w4_raw", align_bytes=64)
                 nc.vector.memset(w8_planes[:].bitcast(I32), 0)
                 for q in range(4):
                     nc.sync.dma_start(out=w8_planes[:].bitcast(I32)[32 * q : 32 * q + 4 * PASSES, :],
@@ -241,26 +251,26 @@ def tile_list_chord_phase_voicings_kernel(tc, tab_words, tab_scales, offs, pos1,
                 prior_sb = keep.tile([P, OUT_TILES], F32, name="prior_sb", tag="first_tenant_w1_b", align_bytes=64)
                 with nc.allow_non_contiguous_dma(reason="one prior value for each output row"):
                     nc.sync.dma_start(out=prior_sb[:], in_=prior.rearrange("(c p) -> p c", p=P))
-            if i == 4:
-                subtract(nc.gpsimd, 0, halves[0], new_rounded(0, 0, "cosine_of4"))
-            if i == 5:
-                quantise_z(0, 0, rounded_z[0, 0][:], "cosine_of5")
-            if i == 6:
-                subtract(nc.gpsimd, 0, halves[1], new_rounded(0, 1, "cosine_of6"))
-            if i == 7:
-                quantise_z(0, 1, rounded_z[0, 1][:], "cosine_of7")
-            if i == 8:
-                subtract(nc.gpsimd, 1, halves[0], new_rounded(1, 0, "cosine_of8"))
-            if i == 9:
-                subtract(nc.vector, 1, halves[1], new_rounded(1, 1, "cosine_of9"))
-                quantise_z(1, 0, rounded_z[1, 0][:], "sine_of9")
-            if i == 10:
-                quantise_z(1, 1, rounded_z[1, 1][:], "cosine_of10")
+            if i == 0:
+                nc.gpsimd.tensor_tensor(turned[:, 0, :], turned[:, 0, :], sin_terms[0], ALU.subtract)
+            elif i in (2, 4, 6):
+                place = turned[:, i - 1 : i + 1, :].rearrange("p t b -> p (t b)")
+                nc.gpsimd.tensor_tensor(place, place, both[:], ALU.subtract)
+            elif i == 8:
+                nc.gpsimd.tensor_tensor(turned[:, 7, :], cos_terms[7], sin_terms[7], ALU.subtract)
+            if i in ROUND_Z_AT:
+                done, h, on_scalar = ROUND_Z_AT[i]
+                round_z(done, h, nc.scalar.copy if on_scalar else nc.vector.tensor_copy, "sine_of%d" % i)
+            if i in HELD:
+                done, h = HELD[i]
+                quantise_z(done, h, "sine_of%d" % i)
             if i % 2 == 0 and i + 2 < TILES:
                 make_phase(i + 2)
                 make_phase(i + 3)
 
-        last_rounded = keep.tile([P, 2, HALF * PACK], BF16, name="last_rounded", align_bytes=64)
+        for h in range(2):
+            round_z(1, h, nc.scalar.copy, "rounded_middle%d" % h)
+            quantise_z(1, h, "z_codes_middle%d" % h)
 
         def score_pass(score, c, g, h):
             cols = slice(c * P, (c + 1) * P)
@@ -286,8 +296,11 @@ def tile_list_chord_phase_voicings_kernel(tc, tab_words, tab_scales, offs, pos1,
                 score_pass(own[c][:, halves[0]], c, g, 1)
         for h in range(2):
             products(LAST_TILE, halves[h])
-            subtract(nc.vector, LAST_PASS, halves[h], last_rounded[:, h, :])
-            quantise_z(LAST_PASS, h, last_rounded[:, h, :], "last_z_codes%d" % h)
+            rounded_z[LAST_PASS, h] = keep.tile([P, HALF * PACK], BF16, name="rounded_last%d" % h, align_bytes=64)
+            nc.vector.tensor_tensor(rounded_z[LAST_PASS, h][:].rearrange("p (c i t) -> p c t i", i=4, t=PACK),
+                                    turned[:, LAST_PASS * PACK :, halves[h]].rearrange("p t (c i) -> p c t i", i=4),
+                                    last_terms[:, :, halves[h]].rearrange("p t (c i) -> p c t i", i=4), ALU.subtract)
+            quantise_z(LAST_PASS, h, "last_z_codes%d" % h)
         for c in range(2):
             score_pass(shared[c][:, halves[0]], c, LAST_PASS, 0)
         for c in range(2, 4):

@@ -29,8 +29,9 @@ LAST_PASS = PASSES - 1
 OUT_TILES = N // P
 PER_COLUMN = 16
 HALF = B // 2
+VECTOR_SHARE = 192
 ROUND_Z_AT = {5: (0, 0, False), 7: (0, 1, False)}
-HELD = {6: (0, 0), 8: (0, 1)}
+HELD = {6: (0, 0), 10: (0, 1)}
 
 
 def tile_list_chord_phase_voicings_kernel(tc, tab_words, tab_scales, offs, pos1, pos2, pos3, w1, w4_words,
@@ -107,13 +108,17 @@ def tile_list_chord_phase_voicings_kernel(tc, tab_words, tab_scales, offs, pos1,
         w4_codes = {}
         w4_plane = {}
 
-        def order_w4(g, words):
-            w4_codes[g] = spot.tile([P, PASS], U16, name="w4_codes%d" % g, align_bytes=64, offset=2048 * g)
-            w4_plane[g] = spot.tile([P, PASS], U8, name="w4_plane%d" % g, align_bytes=64, offset=2048 * g + 1024)
-            nc.vector.tensor_copy(w4_codes[g][:].rearrange("p (t m) -> p t m", t=PACK),
-                                  words.bitcast(U16).rearrange("p (m t) -> p t m", t=PACK))
-            nc.vector.tensor_copy(w4_plane[g][:].rearrange("p (t m) -> p t m", t=PACK),
-                                  w4_plane_raw[:, g * PASS : (g + 1) * PASS].rearrange("p (m t) -> p t m", t=PACK))
+        def order_w4(first, last, raw, offset):
+            width = (last - first) * PASS
+            codes = spot.tile([P, width], U16, name="w4_codes%d" % first, align_bytes=64, offset=offset)
+            plane = spot.tile([P, width], U8, name="w4_plane%d" % first, align_bytes=64, offset=offset + 2 * width)
+            nc.vector.tensor_copy(codes[:].rearrange("p (g t m) -> p g t m", t=PACK, m=P),
+                                  raw[:].bitcast(U16).rearrange("p (g m t) -> p g t m", t=PACK, m=P))
+            nc.vector.tensor_copy(plane[:].rearrange("p (g t m) -> p g t m", t=PACK, m=P),
+                                  w4_plane_raw[:, first * PASS : last * PASS].rearrange("p (g m t) -> p g t m", t=PACK, m=P))
+            for g in range(first, last):
+                w4_codes[g] = codes[:, (g - first) * PASS : (g - first + 1) * PASS]
+                w4_plane[g] = plane[:, (g - first) * PASS : (g - first + 1) * PASS]
 
         w1_rounded[0] = keep.tile([P, PACK, P, PACK], BF16, name="w1_rounded", tag="w1_rounded", align_bytes=64)
         for h in range(2):
@@ -130,11 +135,14 @@ def tile_list_chord_phase_voicings_kernel(tc, tab_words, tab_scales, offs, pos1,
             entries = offs_sb[:, h * BANK // PER_COLUMN : (h + 1) * BANK // PER_COLUMN]
             nc.vector.tensor_copy(codes[:], tab_sb[:].bitcast(U32).indirect(entries))
             picked_codes.append(codes)
-        quantise_w1(0, 0, 1)
-        order_w4(0, w4_first[:])
-        quantise_w1(0, 1, 2)
+        quantise_w1(0, 0, 2)
+        order_w4(0, 1, w4_first, 0)
         quantise_w1(0, 2, 4)
         w4_rest = load_w4(1, PASSES)
+        w1_rounded[1] = keep.tile([P, PACK, P, PACK], BF16, name="w1_rounded", tag="w1_rounded", align_bytes=64)
+        for h in range(2):
+            nc.gpsimd.tensor_copy(w1_rounded[1][:, :, h * P // 2 : (h + 1) * P // 2, :],
+                                  w1_halves[h][:].rearrange("p j (m t) -> p t m j", t=PACK))
 
         banks_taken = []
 
@@ -180,6 +188,8 @@ def tile_list_chord_phase_voicings_kernel(tc, tab_words, tab_scales, offs, pos1,
         def sines(i):
             if i in HELD or i in ROUND_Z_AT:
                 sine[i] = keep.tile([P, B], F32, name="sine_kept", tag="sine_of%d" % i, align_bytes=64)
+            elif i == 0:
+                sine[i] = spot.tile([P, B], F32, name="sine_first", align_bytes=64, offset=3072)
             else:
                 sine[i] = ring.tile([P, B], F32, name="sine")
             if i == 8:
@@ -230,16 +240,20 @@ def tile_list_chord_phase_voicings_kernel(tc, tab_words, tab_scales, offs, pos1,
             sines(i)
             if i < LAST_TILE:
                 products(i, slice(0, B))
-            if i in (0, 3):
-                later = 1 + i // 3
-                w1_rounded[later] = keep.tile([P, PACK, P, PACK], BF16, name="w1_rounded", tag="w1_rounded", align_bytes=64)
+            if i in (2, 4, 6):
+                place = turned[:, i - 1, 0:VECTOR_SHARE]
+                nc.vector.tensor_tensor(place, place, both[:, 0:VECTOR_SHARE], ALU.subtract)
+            if i == 0:
+                quantise_w1(1, 0, PACK)
+            if i == 3:
+                w1_rounded[2] = keep.tile([P, PACK, P, PACK], BF16, name="w1_rounded", tag="w1_rounded", align_bytes=64)
                 for h in range(2):
-                    round_w1(later, h, w1_halves[h], nc.vector.tensor_copy if later == 1 else nc.scalar.copy)
-                quantise_w1(later, 0, PACK)
+                    round_w1(2, h, w1_halves[h], nc.scalar.copy)
+                quantise_w1(2, 0, PACK)
             if i == 0:
                 w1_halves = [load_w1(2, 0, "first_tenant_tab_plane"), load_w1(2, 1, "first_tenant_w1_b")]
-            if i in (1, 2):
-                order_w4(i, w4_rest[:, (i - 1) * PASS // 2 : i * PASS // 2])
+            if i == 0:
+                order_w4(1, PASSES, w4_rest, 2048)
             if i == 3:
                 w8_sb = keep.tile([P, PASSES, N], I32, name="w8_sb", tag="w1_rounded", align_bytes=64)
                 nc.sync.dma_start(out=w8_sb[:], in_=w8_words.rearrange("a p c i -> p a (c i)").bitcast(I32))
@@ -254,8 +268,8 @@ def tile_list_chord_phase_voicings_kernel(tc, tab_words, tab_scales, offs, pos1,
             if i == 0:
                 nc.gpsimd.tensor_tensor(turned[:, 0, :], turned[:, 0, :], sin_terms[0], ALU.subtract)
             elif i in (2, 4, 6):
-                place = turned[:, i - 1 : i + 1, :].rearrange("p t b -> p (t b)")
-                nc.gpsimd.tensor_tensor(place, place, both[:], ALU.subtract)
+                place = turned[:, i - 1 : i + 1, :].rearrange("p t b -> p (t b)")[:, VECTOR_SHARE:]
+                nc.gpsimd.tensor_tensor(place, place, both[:, VECTOR_SHARE:], ALU.subtract)
             elif i == 8:
                 nc.gpsimd.tensor_tensor(turned[:, 7, :], cos_terms[7], sin_terms[7], ALU.subtract)
             if i in ROUND_Z_AT:
@@ -268,7 +282,7 @@ def tile_list_chord_phase_voicings_kernel(tc, tab_words, tab_scales, offs, pos1,
                 make_phase(i + 2)
                 make_phase(i + 3)
 
-        for h in range(2):
+        for h in (1, 0):
             round_z(1, h, nc.scalar.copy, "rounded_middle%d" % h)
             quantise_z(1, h, "z_codes_middle%d" % h)
 
@@ -288,12 +302,12 @@ def tile_list_chord_phase_voicings_kernel(tc, tab_words, tab_scales, offs, pos1,
 
         shared = [next_bank() for b in range(2)]
         own = [next_bank() for c in range(OUT_TILES)]
+        for g in range(LAST_PASS):
+            for c in range(OUT_TILES):
+                score_pass(own[c][:, halves[0]], c, g, 1)
         for c in range(2):
             for g in range(LAST_PASS):
                 score_pass(shared[c][:, halves[0]], c, g, 0)
-        for c in range(OUT_TILES):
-            for g in range(LAST_PASS):
-                score_pass(own[c][:, halves[0]], c, g, 1)
         for h in range(2):
             products(LAST_TILE, halves[h])
             rounded_z[LAST_PASS, h] = keep.tile([P, HALF * PACK], BF16, name="rounded_last%d" % h, align_bytes=64)

@@ -30,8 +30,6 @@ OUT_TILES = N // P
 PER_COLUMN = 16
 HALF = B // 2
 VECTOR_SHARE = 192
-ROUND_Z_AT = {5: (0, 0, False), 7: (0, 1, False)}
-HELD = {6: (0, 0), 10: (0, 1)}
 
 
 def tile_list_chord_phase_voicings_kernel(tc, tab_words, tab_scales, offs, pos1, pos2, pos3, w1, w4_words,
@@ -167,7 +165,10 @@ def tile_list_chord_phase_voicings_kernel(tc, tab_words, tab_scales, offs, pos1,
             cols = slice(t * P, (t + 1) * P)
             phase = ring.tile([P, S], F32, name="phase")
             first_stage(w1_codes[g][:, cols].bitcast(FP8X4), w1_plane[g][:, cols], phase)
-            angle[i] = deep.tile([P, B], F32, name="angle")
+            if i == 6:
+                angle[i] = keep.tile([P, B], F32, name="angle_kept", tag="angle_of6", align_bytes=64)
+            else:
+                angle[i] = deep.tile([P, B], F32, name="angle")
             nc.vector.tensor_copy(angle[i][:], phase[:].indirect(current_of[:]))
 
         def make_colour(i):
@@ -176,31 +177,33 @@ def tile_list_chord_phase_voicings_kernel(tc, tab_words, tab_scales, offs, pos1,
             cols = slice(t * P, (t + 1) * P)
             first_stage(w4_codes[g][:, cols].bitcast(FP4X4), w4_plane[g][:, cols], colour[i])
 
-        turned = keep.tile([P, TILES, B], F32, name="turned")
-        cos_terms = {i: turned[:, i, :] for i in range(TILES)}
-        spare = keep.tile([P, B], F32, name="spare")
-        cos_terms[7] = spare[:]
+        turned = keep.tile([P, LAST_PASS * PACK, B], F32, name="turned")
+        cos_terms = {}
         sin_terms = {}
         sine = {}
         cosine = {}
         halves = [slice(h * HALF, (h + 1) * HALF) for h in range(2)]
 
         def sines(i):
-            if i in HELD or i in ROUND_Z_AT:
-                sine[i] = keep.tile([P, B], F32, name="sine_kept", tag="sine_of%d" % i, align_bytes=64)
-            elif i == 0:
-                sine[i] = spot.tile([P, B], F32, name="sine_first", align_bytes=64, offset=3072)
-            else:
-                sine[i] = ring.tile([P, B], F32, name="sine")
+            sine[i] = ring.tile([P, B], F32, name="sine")
             if i == 8:
                 cosine[i] = turned[:, 7, :]
             else:
                 lone = ring.tile([P, B], F32, name="cosine")
                 cosine[i] = lone[:]
-            size = pair.tile([P, B], F32, name="size")
+            if i in (2, 4, 6):
+                size = turned[:, i - 1, :]
+            else:
+                if i == 0:
+                    own_size = spot.tile([P, B], F32, name="size_first", align_bytes=64, offset=3072)
+                elif i in (5, 7, 10):
+                    own_size = keep.tile([P, B], F32, name="size_kept", tag="size_of%d" % i, align_bytes=64)
+                else:
+                    own_size = pair.tile([P, B], F32, name="size")
+                size = own_size[:]
             nc.scalar.activation(sine[i][:], angle[i][:], ACT.Sin)
-            nc.scalar.activation(size[:], angle[i][:], ACT.Abs)
-            nc.scalar.activation(cosine[i], size[:], ACT.Sin, bias=half_pi[:], scale=-1.0)
+            nc.scalar.activation(size, angle[i][:], ACT.Abs)
+            nc.scalar.activation(cosine[i], size, ACT.Sin, bias=half_pi[:], scale=-1.0)
 
         def products(i, bars):
             entries = slice(bars.start // PER_COLUMN, bars.stop // PER_COLUMN)
@@ -231,18 +234,31 @@ def tile_list_chord_phase_voicings_kernel(tc, tab_words, tab_scales, offs, pos1,
             if g == LAST_PASS:
                 if t == 0:
                     last_terms = keep.tile([P, PACK, B], F32, name="last_terms")
+                    last_cos = keep.tile([P, PACK, B], F32, name="last_cos")
                 sin_terms[i] = last_terms[:, t, :]
+                cos_terms[i] = last_cos[:, t, :]
             elif i % 2 == 1 or i == 0:
                 both = pair.tile([P, 2 * B], F32, name="sin_terms")
                 sin_terms[i] = both[:, 0:B]
                 sin_terms[i + 1] = both[:, B : 2 * B]
+                both_cos = pair.tile([P, 2 * B], F32, name="cos_terms")
+                cos_terms[i] = both_cos[:, 0:B]
+                cos_terms[i + 1] = both_cos[:, B : 2 * B]
             make_colour(i)
             sines(i)
+            if i == 0:
+                order_w4(1, PASSES, w4_rest, 2048)
+            if i in (2, 4, 6):
+                nc.vector.tensor_tensor(turned[:, i - 1, 0:VECTOR_SHARE], both_cos[:, 0:VECTOR_SHARE],
+                                        both[:, 0:VECTOR_SHARE], ALU.subtract)
+            if i in (5, 7):
+                round_z(0, (i - 5) // 2, nc.vector.tensor_copy, "size_of%d" % i)
+            if i == 6:
+                quantise_z(0, 0, "angle_of6")
+            if i == 10:
+                quantise_z(0, 1, "size_of10")
             if i < LAST_TILE:
                 products(i, slice(0, B))
-            if i in (2, 4, 6):
-                place = turned[:, i - 1, 0:VECTOR_SHARE]
-                nc.vector.tensor_tensor(place, place, both[:, 0:VECTOR_SHARE], ALU.subtract)
             if i == 0:
                 quantise_w1(1, 0, PACK)
             if i == 3:
@@ -252,8 +268,6 @@ def tile_list_chord_phase_voicings_kernel(tc, tab_words, tab_scales, offs, pos1,
                 quantise_w1(2, 0, PACK)
             if i == 0:
                 w1_halves = [load_w1(2, 0, "first_tenant_tab_plane"), load_w1(2, 1, "first_tenant_w1_b")]
-            if i == 0:
-                order_w4(1, PASSES, w4_rest, 2048)
             if i == 3:
                 w8_sb = keep.tile([P, PASSES, N], I32, name="w8_sb", tag="w1_rounded", align_bytes=64)
                 nc.sync.dma_start(out=w8_sb[:], in_=w8_words.rearrange("a p c i -> p a (c i)").bitcast(I32))
@@ -266,31 +280,26 @@ def tile_list_chord_phase_voicings_kernel(tc, tab_words, tab_scales, offs, pos1,
                 with nc.allow_non_contiguous_dma(reason="one prior value for each output row"):
                     nc.sync.dma_start(out=prior_sb[:], in_=prior.rearrange("(c p) -> p c", p=P))
             if i == 0:
-                nc.gpsimd.tensor_tensor(turned[:, 0, :], turned[:, 0, :], sin_terms[0], ALU.subtract)
+                nc.gpsimd.tensor_tensor(turned[:, 0, :], cos_terms[0], sin_terms[0], ALU.subtract)
             elif i in (2, 4, 6):
                 place = turned[:, i - 1 : i + 1, :].rearrange("p t b -> p (t b)")[:, VECTOR_SHARE:]
-                nc.gpsimd.tensor_tensor(place, place, both[:, VECTOR_SHARE:], ALU.subtract)
+                nc.gpsimd.tensor_tensor(place, both_cos[:, VECTOR_SHARE:], both[:, VECTOR_SHARE:], ALU.subtract)
             elif i == 8:
                 nc.gpsimd.tensor_tensor(turned[:, 7, :], cos_terms[7], sin_terms[7], ALU.subtract)
-            if i in ROUND_Z_AT:
-                done, h, on_scalar = ROUND_Z_AT[i]
-                round_z(done, h, nc.scalar.copy if on_scalar else nc.vector.tensor_copy, "sine_of%d" % i)
-            if i in HELD:
-                done, h = HELD[i]
-                quantise_z(done, h, "sine_of%d" % i)
             if i % 2 == 0 and i + 2 < TILES:
                 make_phase(i + 2)
                 make_phase(i + 3)
 
-        for h in (1, 0):
+        for h in range(2):
             round_z(1, h, nc.scalar.copy, "rounded_middle%d" % h)
             quantise_z(1, h, "z_codes_middle%d" % h)
 
-        def score_pass(score, c, g, h):
+        def score_pass(bank, members, c, g, h):
             cols = slice(c * P, (c + 1) * P)
-            nc.tensor.matmul_mx(out=score, lhsT=w8_sb[:, g, cols].bitcast(FP8X4),
+            nc.tensor.matmul_mx(out=bank[:, halves[members.index(c)]], lhsT=w8_sb[:, g, cols].bitcast(FP8X4),
                                 lhsT_scale=w8_planes[4 * g :, cols], rhs=z_codes[g, h][:].bitcast(FP8X4),
-                                rhs_scale=z_plane[g, h][:], start=(g == 0), stop=(g == LAST_PASS))
+                                rhs_scale=z_plane[g, h][:], start=(g == 0 and c == members[0]),
+                                stop=(g == LAST_PASS and c == members[-1]))
 
         def store_scores(score, c, h, on_scalar):
             result = keep.tile([P, HALF], F32, name="result%d_%d" % (c, h))
@@ -300,34 +309,23 @@ def tile_list_chord_phase_voicings_kernel(tc, tab_words, tab_scales, offs, pos1,
                 nc.vector.tensor_scalar(result[:], score, prior_sb[:, c : c + 1], None, ALU.add)
             nc.sync.dma_start(out=out[c * P : (c + 1) * P, halves[h]], in_=result[:])
 
-        shared = [next_bank() for b in range(2)]
-        own = [next_bank() for c in range(OUT_TILES)]
+        groups = {0: [(0, 1), (2, 3), (4, 5)], 1: [(0, 1), (2,), (3,), (4,), (5,)]}
+        score_banks = {h: [next_bank() for members in groups[h]] for h in range(2)}
         for g in range(LAST_PASS):
-            for c in range(OUT_TILES):
-                score_pass(own[c][:, halves[0]], c, g, 1)
-        for c in range(2):
-            for g in range(LAST_PASS):
-                score_pass(shared[c][:, halves[0]], c, g, 0)
+            for h in range(2):
+                for bank, members in zip(score_banks[h], groups[h]):
+                    for c in members:
+                        score_pass(bank, members, c, g, h)
         for h in range(2):
             products(LAST_TILE, halves[h])
             rounded_z[LAST_PASS, h] = keep.tile([P, HALF * PACK], BF16, name="rounded_last%d" % h, align_bytes=64)
             nc.vector.tensor_tensor(rounded_z[LAST_PASS, h][:].rearrange("p (c i t) -> p c t i", i=4, t=PACK),
-                                    turned[:, LAST_PASS * PACK :, halves[h]].rearrange("p t (c i) -> p c t i", i=4),
+                                    last_cos[:, :, halves[h]].rearrange("p t (c i) -> p c t i", i=4),
                                     last_terms[:, :, halves[h]].rearrange("p t (c i) -> p c t i", i=4), ALU.subtract)
             quantise_z(LAST_PASS, h, "last_z_codes%d" % h)
-        for c in range(2):
-            score_pass(shared[c][:, halves[0]], c, LAST_PASS, 0)
-        for c in range(2, 4):
-            for g in range(PASSES):
-                score_pass(shared[c - 2][:, halves[1]], c, g, 0)
-        for b in range(2):
-            store_scores(shared[b][:, halves[0]], b, 0, True)
-            store_scores(shared[b][:, halves[1]], b + 2, 0, True)
-        for c in range(4, OUT_TILES):
-            again = next_bank()
-            for g in range(PASSES):
-                score_pass(again[:, halves[0]], c, g, 0)
-            store_scores(again[:, halves[0]], c, 0, True)
-        for c in range(OUT_TILES):
-            score_pass(own[c][:, halves[0]], c, LAST_PASS, 1)
-            store_scores(own[c][:, halves[0]], c, 1, c % 2 == 0)
+        for h in range(2):
+            for bank, members in zip(score_banks[h], groups[h]):
+                for c in members:
+                    score_pass(bank, members, c, LAST_PASS, h)
+                for c in members:
+                    store_scores(bank[:, halves[members.index(c)]], c, h, h == 0 or len(members) == 2)

@@ -29,7 +29,6 @@ LAST_PASS = PASSES - 1
 OUT_TILES = N // P
 PER_COLUMN = 16
 HALF = B // 2
-VECTOR_SHARE = 192
 
 
 def tile_list_chord_phase_voicings_kernel(tc, tab_words, tab_scales, offs, pos1, pos2, pos3, w1, w4_words,
@@ -39,7 +38,6 @@ def tile_list_chord_phase_voicings_kernel(tc, tab_words, tab_scales, offs, pos1,
         keep = ctx.enter_context(tc.tile_pool(name="keep", bufs=1))
         ring = ctx.enter_context(tc.tile_pool(name="ring", bufs=3))
         deep = ctx.enter_context(tc.tile_pool(name="deep", bufs=4))
-        pair = ctx.enter_context(tc.tile_pool(name="pair", bufs=2))
         spot = ctx.enter_context(tc.tile_pool(name="spot", bufs=1))
         psum = ctx.enter_context(tc.psum_pool(name="psum", bufs=1))
 
@@ -69,30 +67,37 @@ def tile_list_chord_phase_voicings_kernel(tc, tab_words, tab_scales, offs, pos1,
         w1_rows = w1.rearrange("(p j) r -> p j r", j=PACK)
 
         def load_w1(g, h, tag):
-            raw = keep.tile([P, PACK, PASS // 2], F32, name="w1_raw", tag=tag, align_bytes=64)
+            if tag is None:
+                raw = spot.tile([P, PACK, PASS // 2], F32, name="w1_raw%d" % g, align_bytes=64, offset=8192)
+            else:
+                raw = keep.tile([P, PACK, PASS // 2], F32, name="w1_raw", tag=tag, align_bytes=64)
             first = g * PASS + h * PASS // 2
             nc.sync.dma_start(out=raw[:], in_=w1_rows[:, :, first : first + PASS // 2])
             return raw
 
         def load_w4(first, last):
-            raw = keep.tile([P, (last - first) * PASS // 2], I32, name="w4_raw", tag="w4_raw", align_bytes=64)
+            raw = keep.tile([P, (last - first) * PASS // 2], I32, name="w4_raw", tag="w4_raw%d" % first, align_bytes=64)
             nc.sync.dma_start(out=raw[:], in_=w4_words[0].bitcast(I32)[:, first * PASS // 2 : last * PASS // 2])
             return raw
 
         offs_sb = load_list("offs_sb", offs, S)
         tab_sb = spot.tile([P, T], I32, name="tab_sb", align_bytes=64, offset=0)
         nc.sync.dma_start(out=tab_sb[:], in_=tab_words[0].rearrange("p t i -> p (t i)").bitcast(I32))
-        w1_halves = [load_w1(0, 0, "first_tenant_w1_a"), load_w1(0, 1, "first_tenant_w1_b")]
-        load_scale_rows(nc.sync, w4_plane_raw, w4_scales[0])
         w4_first = load_w4(0, 1)
+        load_scale_rows(nc.sync, w4_plane_raw, w4_scales[0])
+        w1_halves = [load_w1(0, 0, None), load_w1(0, 1, "first_tenant_w1_b")]
+        w4_rest = load_w4(1, PASSES)
         current_of = load_list("current_of", pos1, B)
 
         w1_codes = {}
         w1_plane = {}
         w1_rounded = {}
-        for g in range(PASSES):
-            w1_codes[g] = keep.tile([P, PASS], U32, name="w1_codes%d" % g, align_bytes=64)
+
+        def make_w1_codes(g, tag):
+            w1_codes[g] = keep.tile([P, PASS], U32, name="w1_codes", tag=tag, align_bytes=64)
             w1_plane[g] = keep.tile([P, PASS], U8, name="w1_plane%d" % g, align_bytes=64)
+
+        make_w1_codes(0, "w1_codes_first")
 
         def round_w1(g, h, raw, copy):
             rounded = w1_rounded[g][:, :, h * P // 2 : (h + 1) * P // 2, :].rearrange("p t m j -> p m j t")
@@ -106,37 +111,41 @@ def tile_list_chord_phase_voicings_kernel(tc, tab_words, tab_scales, offs, pos1,
         w4_codes = {}
         w4_plane = {}
 
-        def order_w4(first, last, raw, offset):
-            width = (last - first) * PASS
-            codes = spot.tile([P, width], U16, name="w4_codes%d" % first, align_bytes=64, offset=offset)
-            plane = spot.tile([P, width], U8, name="w4_plane%d" % first, align_bytes=64, offset=offset + 2 * width)
-            nc.vector.tensor_copy(codes[:].rearrange("p (g t m) -> p g t m", t=PACK, m=P),
-                                  raw[:].bitcast(U16).rearrange("p (g m t) -> p g t m", t=PACK, m=P))
-            nc.vector.tensor_copy(plane[:].rearrange("p (g t m) -> p g t m", t=PACK, m=P),
-                                  w4_plane_raw[:, first * PASS : last * PASS].rearrange("p (g m t) -> p g t m", t=PACK, m=P))
+        def order_w4_codes(first, last, raw, copy, tag):
+            codes = keep.tile([P, (last - first) * PASS], U16, name="w4_codes", tag=tag, align_bytes=64)
+            copy(codes[:].rearrange("p (g t m) -> p g t m", t=PACK, m=P),
+                 raw[:].bitcast(U16).rearrange("p (g m t) -> p g t m", t=PACK, m=P))
             for g in range(first, last):
                 w4_codes[g] = codes[:, (g - first) * PASS : (g - first + 1) * PASS]
+
+        def order_w4_plane(first, last, tag):
+            plane = keep.tile([P, (last - first) * PASS], U8, name="w4_plane", tag=tag, align_bytes=64)
+            nc.gpsimd.tensor_copy(plane[:].rearrange("p (g t m) -> p g t m", t=PACK, m=P),
+                                  w4_plane_raw[:, first * PASS : last * PASS].rearrange("p (g m t) -> p g t m", t=PACK, m=P))
+            for g in range(first, last):
                 w4_plane[g] = plane[:, (g - first) * PASS : (g - first + 1) * PASS]
 
+        order_w4_codes(0, 1, w4_first, nc.gpsimd.tensor_copy, "w4_codes_first")
+        order_w4_plane(0, 1, "w4_plane_first")
         w1_rounded[0] = keep.tile([P, PACK, P, PACK], BF16, name="w1_rounded", tag="w1_rounded", align_bytes=64)
-        for h in range(2):
-            round_w1(0, h, w1_halves[h], nc.scalar.copy)
+        round_w1(0, 0, w1_halves[0], nc.scalar.copy)
 
         picked_plane = keep.tile([P, S], U8, name="picked_plane", align_bytes=64)
         nc.vector.tensor_copy(picked_plane[:], tab_plane[:].indirect(offs_sb[:]))
-        w1_halves = [load_w1(1, 0, "first_tenant_tab_plane"), load_w1(1, 1, "first_tenant_w1_a")]
-        low_of = load_list("low_of", pos3, B)
-        substitute_of = load_list("substitute_of", pos2, B)
         picked_codes = []
         for h in range(S // BANK):
             codes = keep.tile([P, BANK], U32, name="picked_codes%d" % h, align_bytes=64)
             entries = offs_sb[:, h * BANK // PER_COLUMN : (h + 1) * BANK // PER_COLUMN]
             nc.vector.tensor_copy(codes[:], tab_sb[:].bitcast(U32).indirect(entries))
             picked_codes.append(codes)
-        quantise_w1(0, 0, 2)
-        order_w4(0, 1, w4_first, 0)
+        round_w1(0, 1, w1_halves[1], nc.vector.tensor_copy)
+        w1_halves = [load_w1(1, 0, "first_tenant_tab_plane"), load_w1(1, 1, None)]
+        low_of = load_list("low_of", pos3, B)
+        substitute_of = load_list("substitute_of", pos2, B)
+        quantise_w1(0, 0, 1)
+        quantise_w1(0, 1, 2)
+        order_w4_codes(1, PASSES, w4_rest, nc.vector.tensor_copy, "w4_codes_rest")
         quantise_w1(0, 2, 4)
-        w4_rest = load_w4(1, PASSES)
         w1_rounded[1] = keep.tile([P, PACK, P, PACK], BF16, name="w1_rounded", tag="w1_rounded", align_bytes=64)
         for h in range(2):
             nc.gpsimd.tensor_copy(w1_rounded[1][:, :, h * P // 2 : (h + 1) * P // 2, :],
@@ -149,35 +158,40 @@ def tile_list_chord_phase_voicings_kernel(tc, tab_words, tab_scales, offs, pos1,
             banks_taken.append(bank)
             return bank
 
-        def first_stage(lhsT, lhsT_scale, rows):
+        def first_stage(lhsT, lhsT_scale, rows, copies):
             for h in range(S // BANK):
                 chords = slice(h * BANK, (h + 1) * BANK)
                 bank = next_bank()
                 nc.tensor.matmul_mx(out=bank[:], lhsT=lhsT, lhsT_scale=lhsT_scale, rhs=picked_codes[h][:].bitcast(FP8X4),
                                     rhs_scale=picked_plane[:, chords], start=True, stop=True)
-                nc.scalar.copy(rows[:, chords], bank[:])
+                copies[h](rows[:, chords], bank[:])
 
         angle = {}
+        last_angles = keep.tile([P, 2, B], F32, name="last_angles")
         colour = {}
 
         def make_phase(i):
             g, t = divmod(i, PACK)
             cols = slice(t * P, (t + 1) * P)
             phase = ring.tile([P, S], F32, name="phase")
-            first_stage(w1_codes[g][:, cols].bitcast(FP8X4), w1_plane[g][:, cols], phase)
-            if i == 6:
-                angle[i] = keep.tile([P, B], F32, name="angle_kept", tag="angle_of6", align_bytes=64)
+            first_stage(w1_codes[g][:, cols].bitcast(FP8X4), w1_plane[g][:, cols], phase,
+                        [nc.scalar.copy, nc.vector.tensor_copy if i == 0 else nc.scalar.copy])
+            if i >= 10:
+                angle[i] = last_angles[:, i - 10, :]
+            elif i == 8:
+                kept = keep.tile([P, B], F32, name="angle_kept", tag="angle_of8", align_bytes=64)
+                angle[i] = kept[:]
             else:
-                angle[i] = deep.tile([P, B], F32, name="angle")
-            nc.vector.tensor_copy(angle[i][:], phase[:].indirect(current_of[:]))
+                lone = deep.tile([P, B], F32, name="angle")
+                angle[i] = lone[:]
+            nc.vector.tensor_copy(angle[i], phase[:].indirect(current_of[:]))
 
         def make_colour(i):
             colour[i] = deep.tile([P, S], F32, name="colour")
             g, t = divmod(i, PACK)
             cols = slice(t * P, (t + 1) * P)
-            first_stage(w4_codes[g][:, cols].bitcast(FP4X4), w4_plane[g][:, cols], colour[i])
+            first_stage(w4_codes[g][:, cols].bitcast(FP4X4), w4_plane[g][:, cols], colour[i], [nc.scalar.copy, nc.scalar.copy])
 
-        turned = keep.tile([P, LAST_PASS * PACK, B], F32, name="turned")
         cos_terms = {}
         sin_terms = {}
         sine = {}
@@ -186,113 +200,110 @@ def tile_list_chord_phase_voicings_kernel(tc, tab_words, tab_scales, offs, pos1,
 
         def sines(i):
             sine[i] = ring.tile([P, B], F32, name="sine")
-            if i == 8:
-                cosine[i] = turned[:, 7, :]
-            else:
-                lone = ring.tile([P, B], F32, name="cosine")
-                cosine[i] = lone[:]
-            if i in (2, 4, 6):
-                size = turned[:, i - 1, :]
-            else:
-                if i == 0:
-                    own_size = spot.tile([P, B], F32, name="size_first", align_bytes=64, offset=3072)
-                elif i in (5, 7, 10):
-                    own_size = keep.tile([P, B], F32, name="size_kept", tag="size_of%d" % i, align_bytes=64)
-                else:
-                    own_size = pair.tile([P, B], F32, name="size")
-                size = own_size[:]
-            nc.scalar.activation(sine[i][:], angle[i][:], ACT.Sin)
-            nc.scalar.activation(size, angle[i][:], ACT.Abs)
-            nc.scalar.activation(cosine[i], size, ACT.Sin, bias=half_pi[:], scale=-1.0)
+            cosine[i] = keep.tile([P, B], F32, name="cosine", tag="cosine_of%d" % i, align_bytes=64)
+            size = keep.tile([P, B], F32, name="size", tag="size_of%d" % i, align_bytes=64)
+            nc.scalar.activation(sine[i][:], angle[i], ACT.Sin)
+            nc.scalar.activation(size[:], angle[i], ACT.Abs)
+            nc.scalar.activation(cosine[i][:], size[:], ACT.Sin, bias=half_pi[:], scale=-1.0)
 
-        def products(i, bars):
+        def last_sines(h):
+            both_sines = keep.tile([P, 2, HALF], F32, name="last_sines%d" % h)
+            both_cosines = keep.tile([P, 2, HALF], F32, name="last_cosines%d" % h)
+            size = keep.tile([P, 2, HALF], F32, name="size", tag="last_size%d" % h, align_bytes=64)
+            nc.scalar.activation(both_sines[:], last_angles[:, :, halves[h]], ACT.Sin)
+            nc.scalar.activation(size[:], last_angles[:, :, halves[h]], ACT.Abs)
+            nc.scalar.activation(both_cosines[:], size[:], ACT.Sin, bias=half_pi[:], scale=-1.0)
+            return both_sines, both_cosines
+
+        def sin_product(i, bars, factor):
+            g, t = divmod(i, PACK)
             entries = slice(bars.start // PER_COLUMN, bars.stop // PER_COLUMN)
-            nc.vector.tensor_tensor(sin_terms[i][:, bars], colour[i][:].indirect(low_of[:, entries]),
-                                    sine[i][:, bars], ALU.mult)
-            nc.vector.tensor_tensor(cos_terms[i][:, bars], colour[i][:].indirect(substitute_of[:, entries]),
-                                    cosine[i][:, bars], ALU.mult)
+            nc.vector.tensor_tensor(sin_terms[g][:, t, bars], colour[i][:].indirect(low_of[:, entries]),
+                                    factor, ALU.mult)
 
-        rounded_z = {}
+        def cos_product(i, bars, factor):
+            g, t = divmod(i, PACK)
+            entries = slice(bars.start // PER_COLUMN, bars.stop // PER_COLUMN)
+            nc.vector.tensor_tensor(cos_terms[g][:, t, bars], colour[i][:].indirect(substitute_of[:, entries]),
+                                    factor, ALU.mult)
 
-        def round_z(g, h, copy, tag):
-            rounded_z[g, h] = keep.tile([P, HALF * PACK], BF16, name="rounded_z", tag=tag, align_bytes=64)
-            copy(rounded_z[g, h][:].rearrange("p (c i t) -> p c t i", i=4, t=PACK),
-                 turned[:, g * PACK : (g + 1) * PACK, halves[h]].rearrange("p t (c i) -> p c t i", i=4))
+        def turn(engine, g, bars, tag):
+            rounded = keep.tile([P, (bars.stop - bars.start) * PACK], BF16, name="rounded_z", tag=tag, align_bytes=64)
+            engine.tensor_tensor(rounded[:].rearrange("p (c i t) -> p c t i", i=4, t=PACK),
+                                 cos_terms[g][:, :, bars].rearrange("p t (c i) -> p c t i", i=4),
+                                 sin_terms[g][:, :, bars].rearrange("p t (c i) -> p c t i", i=4), ALU.subtract)
+            return rounded
 
         z_codes = {}
         z_plane = {}
 
-        def quantise_z(g, h, tag):
+        def quantise_z(g, h, tag, pieces):
             z_codes[g, h] = keep.tile([P, HALF], U32, name="z_codes", tag=tag, align_bytes=64)
             z_plane[g, h] = keep.tile([P, HALF], U8, name="z_plane%d_%d" % (g, h), align_bytes=64)
-            nc.vector.quantize_mx(out=z_codes[g, h][:].bitcast(FP8X4), scales=z_plane[g, h][:], in_=rounded_z[g, h][:])
+            width = HALF // len(pieces)
+            for n, rounded in enumerate(pieces):
+                cols = slice(n * width, (n + 1) * width)
+                nc.vector.quantize_mx(out=z_codes[g, h][:, cols].bitcast(FP8X4), scales=z_plane[g, h][:, cols], in_=rounded[:])
 
+        def gpsimd_round_w1(g, tag, raws):
+            w1_rounded[g] = keep.tile([P, PACK, P, PACK], BF16, name="w1_rounded", tag=tag, align_bytes=64)
+            for h in range(2):
+                nc.gpsimd.tensor_copy(w1_rounded[g][:, :, h * P // 2 : (h + 1) * P // 2, :],
+                                      raws[h][:].rearrange("p j (m t) -> p t m j", t=PACK))
+
+        phases_after = {0: (2, 3), 2: (4,), 3: (5, 6), 5: (7, 8), 7: (9, 10), 8: (11,)}
+        quarters = [slice(HALF, HALF + P), slice(HALF + P, B)]
+        rounded_z = {}
+        make_colour(0)
         make_phase(0)
         make_phase(1)
-        for i in range(TILES):
+        for i in range(TILES - 2):
             g, t = divmod(i, PACK)
-            if g == LAST_PASS:
-                if t == 0:
-                    last_terms = keep.tile([P, PACK, B], F32, name="last_terms")
-                    last_cos = keep.tile([P, PACK, B], F32, name="last_cos")
-                sin_terms[i] = last_terms[:, t, :]
-                cos_terms[i] = last_cos[:, t, :]
-            elif i % 2 == 1 or i == 0:
-                both = pair.tile([P, 2 * B], F32, name="sin_terms")
-                sin_terms[i] = both[:, 0:B]
-                sin_terms[i + 1] = both[:, B : 2 * B]
-                both_cos = pair.tile([P, 2 * B], F32, name="cos_terms")
-                cos_terms[i] = both_cos[:, 0:B]
-                cos_terms[i + 1] = both_cos[:, B : 2 * B]
-            make_colour(i)
+            if t == 0:
+                sin_terms[g] = keep.tile([P, PACK, B], F32, name="sin_terms", tag="sin_terms%d" % (g % 2))
+                cos_terms[g] = keep.tile([P, PACK, B], F32, name="cos_terms", tag="cos_terms%d" % (g % 2))
+            if i > 0:
+                make_colour(i)
             sines(i)
-            if i == 0:
-                order_w4(1, PASSES, w4_rest, 2048)
-            if i in (2, 4, 6):
-                nc.vector.tensor_tensor(turned[:, i - 1, 0:VECTOR_SHARE], both_cos[:, 0:VECTOR_SHARE],
-                                        both[:, 0:VECTOR_SHARE], ALU.subtract)
-            if i in (5, 7):
-                round_z(0, (i - 5) // 2, nc.vector.tensor_copy, "size_of%d" % i)
+            sin_product(i, slice(0, B), sine[i][:])
+            if i in (0, 1):
+                make_w1_codes(i + 1, "size_of%d" % i)
+                quantise_w1(i + 1, 0, PACK)
             if i == 6:
-                quantise_z(0, 0, "angle_of6")
-            if i == 10:
-                quantise_z(0, 1, "size_of10")
-            if i < LAST_TILE:
-                products(i, slice(0, B))
-            if i == 0:
-                quantise_w1(1, 0, PACK)
-            if i == 3:
-                w1_rounded[2] = keep.tile([P, PACK, P, PACK], BF16, name="w1_rounded", tag="w1_rounded", align_bytes=64)
-                for h in range(2):
-                    round_w1(2, h, w1_halves[h], nc.scalar.copy)
-                quantise_w1(2, 0, PACK)
+                quantise_z(0, 1, "size_of6", [rounded_z[0, 1]])
+            if i == 8:
+                vector_quarter = turn(nc.vector, 1, quarters[1], "angle_of8")
+                quantise_z(1, 0, "size_of8", [rounded_z[1, 0]])
+            cos_product(i, slice(0, B), cosine[i][:])
             if i == 0:
                 w1_halves = [load_w1(2, 0, "first_tenant_tab_plane"), load_w1(2, 1, "first_tenant_w1_b")]
-            if i == 3:
-                w8_sb = keep.tile([P, PASSES, N], I32, name="w8_sb", tag="w1_rounded", align_bytes=64)
+                gpsimd_round_w1(2, "cosine_of0", w1_halves)
+            if i == 1:
+                w8_sb = keep.tile([P, PASSES, N], I32, name="w8_sb", tag="cosine_of0", align_bytes=64)
                 nc.sync.dma_start(out=w8_sb[:], in_=w8_words.rearrange("a p c i -> p a (c i)").bitcast(I32))
-                w8_planes = keep.tile([P, N], U8, name="w8_planes", tag="w4_raw", align_bytes=64)
-                nc.vector.memset(w8_planes[:].bitcast(I32), 0)
+                w8_planes = keep.tile([P, N], U8, name="w8_planes", tag="w4_raw1", align_bytes=64)
+                nc.gpsimd.memset(w8_planes[:].bitcast(I32), 0)
                 for q in range(4):
                     nc.sync.dma_start(out=w8_planes[:].bitcast(I32)[32 * q : 32 * q + 4 * PASSES, :],
                                       in_=w8_scales[:, 4 * q : 4 * q + 4, :].bitcast(I32))
                 prior_sb = keep.tile([P, OUT_TILES], F32, name="prior_sb", tag="first_tenant_w1_b", align_bytes=64)
                 with nc.allow_non_contiguous_dma(reason="one prior value for each output row"):
                     nc.sync.dma_start(out=prior_sb[:], in_=prior.rearrange("(c p) -> p c", p=P))
-            if i == 0:
-                nc.gpsimd.tensor_tensor(turned[:, 0, :], cos_terms[0], sin_terms[0], ALU.subtract)
-            elif i in (2, 4, 6):
-                place = turned[:, i - 1 : i + 1, :].rearrange("p t b -> p (t b)")[:, VECTOR_SHARE:]
-                nc.gpsimd.tensor_tensor(place, both_cos[:, VECTOR_SHARE:], both[:, VECTOR_SHARE:], ALU.subtract)
-            elif i == 8:
-                nc.gpsimd.tensor_tensor(turned[:, 7, :], cos_terms[7], sin_terms[7], ALU.subtract)
-            if i % 2 == 0 and i + 2 < TILES:
-                make_phase(i + 2)
-                make_phase(i + 3)
+            if i == 2:
+                order_w4_plane(1, PASSES, "cosine_of2")
+            if i == 3:
+                rounded_z[0, 0] = turn(nc.gpsimd, 0, halves[0], "rounded_first")
+            if i == 5:
+                rounded_z[0, 1] = turn(nc.gpsimd, 0, halves[1], "cosine_of5")
+            if i == 7:
+                rounded_z[1, 0] = turn(nc.gpsimd, 1, halves[0], "rounded_middle")
+            if i == 8:
+                gpsimd_quarter = turn(nc.gpsimd, 1, quarters[0], "cosine_of8")
+            for later in phases_after.get(i, ()):
+                make_phase(later)
 
-        for h in range(2):
-            round_z(1, h, nc.scalar.copy, "rounded_middle%d" % h)
-            quantise_z(1, h, "z_codes_middle%d" % h)
+        make_colour(TILES - 2)
+        make_colour(TILES - 1)
 
         def score_pass(bank, members, c, g, h):
             cols = slice(c * P, (c + 1) * P)
@@ -311,21 +322,33 @@ def tile_list_chord_phase_voicings_kernel(tc, tab_words, tab_scales, offs, pos1,
 
         groups = {0: [(0, 1), (2, 3), (4, 5)], 1: [(0, 1), (2,), (3,), (4,), (5,)]}
         score_banks = {h: [next_bank() for members in groups[h]] for h in range(2)}
-        for g in range(LAST_PASS):
-            for h in range(2):
-                for bank, members in zip(score_banks[h], groups[h]):
-                    for c in members:
-                        score_pass(bank, members, c, g, h)
-        for h in range(2):
-            products(LAST_TILE, halves[h])
-            rounded_z[LAST_PASS, h] = keep.tile([P, HALF * PACK], BF16, name="rounded_last%d" % h, align_bytes=64)
-            nc.vector.tensor_tensor(rounded_z[LAST_PASS, h][:].rearrange("p (c i t) -> p c t i", i=4, t=PACK),
-                                    last_cos[:, :, halves[h]].rearrange("p t (c i) -> p c t i", i=4),
-                                    last_terms[:, :, halves[h]].rearrange("p t (c i) -> p c t i", i=4), ALU.subtract)
-            quantise_z(LAST_PASS, h, "last_z_codes%d" % h)
-        for h in range(2):
+
+        def score_passes(g, h):
+            for bank, members in zip(score_banks[h], groups[h]):
+                for c in members:
+                    score_pass(bank, members, c, g, h)
+
+        def close_scores(h):
             for bank, members in zip(score_banks[h], groups[h]):
                 for c in members:
                     score_pass(bank, members, c, LAST_PASS, h)
                 for c in members:
                     store_scores(bank[:, halves[members.index(c)]], c, h, h == 0 or len(members) == 2)
+
+        score_passes(0, 1)
+        for h in range(2):
+            both_sines, both_cosines = last_sines(h)
+            for n in range(2):
+                sin_product(TILES - 2 + n, halves[h], both_sines[:, n, :])
+            if h == 0:
+                quantise_z(0, 0, "last_size0", [rounded_z[0, 0]])
+                score_passes(0, 0)
+                score_passes(1, 0)
+            else:
+                quantise_z(1, 1, "last_size1", [gpsimd_quarter, vector_quarter])
+                score_passes(1, 1)
+            for n in range(2):
+                cos_product(TILES - 2 + n, halves[h], both_cosines[:, n, :])
+            rounded = turn(nc.vector, LAST_PASS, halves[h], "rounded_last%d" % h)
+            quantise_z(LAST_PASS, h, "last_z_codes%d" % h, [rounded])
+            close_scores(h)

@@ -41,18 +41,16 @@ def tile_list_chord_phase_voicings_kernel(tc, tab_words, tab_scales, offs, pos1,
         spot = ctx.enter_context(tc.tile_pool(name="spot", bufs=1))
         psum = ctx.enter_context(tc.psum_pool(name="psum", bufs=1))
 
-        def load_scale_rows(queue, plane, rows):
-            for q in range(4):
-                queue.dma_start(out=plane[:].bitcast(I32)[32 * q : 32 * q + 4, :], in_=rows[4 * q : 4 * q + 4, :].bitcast(I32))
-
         tab_plane = keep.tile([P, T], U8, name="tab_plane", tag="first_tenant_tab_plane", align_bytes=64)
         for q in range(4):
             nc.sync.dma_start(out=tab_plane[:].bitcast(I32)[32 * q : 32 * q + 32, :],
                               in_=tab_scales[0][4 * q : 4 * q + 4, :].bitcast(I32).partition_broadcast(8))
-        w4_plane_raw = keep.tile([P, H], U8, name="w4_plane_raw", align_bytes=64)
+        w4_plane_raw = keep.tile([P, PASS], U8, name="w4_plane_raw", align_bytes=64)
+        w4_planes_later = keep.tile([P, LAST_PASS * PASS], U8, name="w4_planes_later", align_bytes=64)
         zero = keep.tile([P, 1], F32, name="zero")
         nc.gpsimd.memset(zero[:], 0.0)
         nc.gpsimd.memset(w4_plane_raw[:].bitcast(I32), 0)
+        nc.gpsimd.memset(w4_planes_later[:].bitcast(I32), 0)
 
         sin_zero = keep.tile([P, 1], F32, name="sin_zero")
         nc.scalar.activation(sin_zero[:], zero[:], ACT.Sin)
@@ -75,18 +73,15 @@ def tile_list_chord_phase_voicings_kernel(tc, tab_words, tab_scales, offs, pos1,
             nc.sync.dma_start(out=raw[:], in_=w1_rows[:, :, first : first + PASS // 2])
             return raw
 
-        def load_w4(first, last):
-            raw = keep.tile([P, (last - first) * PASS // 2], I32, name="w4_raw", tag="w4_raw%d" % first, align_bytes=64)
-            nc.sync.dma_start(out=raw[:], in_=w4_words[0].bitcast(I32)[:, first * PASS // 2 : last * PASS // 2])
-            return raw
-
         offs_sb = load_list("offs_sb", offs, S)
         tab_sb = spot.tile([P, T], I32, name="tab_sb", align_bytes=64, offset=0)
         nc.sync.dma_start(out=tab_sb[:], in_=tab_words[0].rearrange("p t i -> p (t i)").bitcast(I32))
-        w4_first = load_w4(0, 1)
-        load_scale_rows(nc.sync, w4_plane_raw, w4_scales[0])
         w1_halves = [load_w1(0, 0, None), load_w1(0, 1, "first_tenant_w1_b")]
-        w4_rest = load_w4(1, PASSES)
+        for q in range(4):
+            nc.sync.dma_start(out=w4_plane_raw[:].bitcast(I32)[32 * q : 32 * q + 4 * PASSES, :],
+                              in_=w4_scales[0][4 * q : 4 * q + 4, :].bitcast(I32).rearrange("j (g c) -> g j c", g=PASSES))
+        w4_raw = spot.tile([P, H // 2], I32, name="w4_raw", align_bytes=64, offset=12288)
+        nc.sync.dma_start(out=w4_raw[:], in_=w4_words[0].bitcast(I32))
         current_of = load_list("current_of", pos1, B)
 
         w1_codes = {}
@@ -99,9 +94,9 @@ def tile_list_chord_phase_voicings_kernel(tc, tab_words, tab_scales, offs, pos1,
 
         make_w1_codes(0, "w1_codes_first")
 
-        def round_w1(g, h, raw, copy):
-            rounded = w1_rounded[g][:, :, h * P // 2 : (h + 1) * P // 2, :].rearrange("p t m j -> p m j t")
-            copy(rounded, raw[:].rearrange("p j (m t) -> p m j t", t=PACK))
+        def round_w1(g, h, raw, copy, first=0, last=P // 2):
+            rounded = w1_rounded[g][:, :, h * P // 2 + first : h * P // 2 + last, :].rearrange("p t m j -> p m j t")
+            copy(rounded, raw[:, :, first * PACK : last * PACK].rearrange("p j (m t) -> p m j t", t=PACK))
 
         def quantise_w1(g, first, last):
             nc.vector.quantize_mx(out=w1_codes[g][:, first * P : last * P].bitcast(FP8X4),
@@ -111,23 +106,7 @@ def tile_list_chord_phase_voicings_kernel(tc, tab_words, tab_scales, offs, pos1,
         w4_codes = {}
         w4_plane = {}
 
-        def order_w4_codes(first, last, raw, copy, tag):
-            codes = keep.tile([P, (last - first) * PASS], U16, name="w4_codes", tag=tag, align_bytes=64)
-            copy(codes[:].rearrange("p (g t m) -> p g t m", t=PACK, m=P),
-                 raw[:].bitcast(U16).rearrange("p (g m t) -> p g t m", t=PACK, m=P))
-            for g in range(first, last):
-                w4_codes[g] = codes[:, (g - first) * PASS : (g - first + 1) * PASS]
-
-        def order_w4_plane(first, last, tag):
-            plane = keep.tile([P, (last - first) * PASS], U8, name="w4_plane", tag=tag, align_bytes=64)
-            nc.gpsimd.tensor_copy(plane[:].rearrange("p (g t m) -> p g t m", t=PACK, m=P),
-                                  w4_plane_raw[:, first * PASS : last * PASS].rearrange("p (g m t) -> p g t m", t=PACK, m=P))
-            for g in range(first, last):
-                w4_plane[g] = plane[:, (g - first) * PASS : (g - first + 1) * PASS]
-
-        order_w4_codes(0, 1, w4_first, nc.gpsimd.tensor_copy, "w4_codes_first")
-        order_w4_plane(0, 1, "w4_plane_first")
-        w1_rounded[0] = keep.tile([P, PACK, P, PACK], BF16, name="w1_rounded", tag="w1_rounded", align_bytes=64)
+        w1_rounded[0] = spot.tile([P, PACK, P, PACK], BF16, name="w1_rounded0", align_bytes=64, offset=15360)
         round_w1(0, 0, w1_halves[0], nc.scalar.copy)
 
         picked_plane = keep.tile([P, S], U8, name="picked_plane", align_bytes=64)
@@ -138,15 +117,27 @@ def tile_list_chord_phase_voicings_kernel(tc, tab_words, tab_scales, offs, pos1,
             entries = offs_sb[:, h * BANK // PER_COLUMN : (h + 1) * BANK // PER_COLUMN]
             nc.vector.tensor_copy(codes[:], tab_sb[:].bitcast(U32).indirect(entries))
             picked_codes.append(codes)
-        round_w1(0, 1, w1_halves[1], nc.vector.tensor_copy)
+        round_w1(0, 1, w1_halves[1], nc.scalar.copy, 0, P // 4)
+        round_w1(0, 1, w1_halves[1], nc.vector.tensor_copy, P // 4, P // 2)
         w1_halves = [load_w1(1, 0, "first_tenant_tab_plane"), load_w1(1, 1, None)]
         low_of = load_list("low_of", pos3, B)
         substitute_of = load_list("substitute_of", pos2, B)
         quantise_w1(0, 0, 1)
         quantise_w1(0, 1, 2)
-        order_w4_codes(1, PASSES, w4_rest, nc.vector.tensor_copy, "w4_codes_rest")
+        w4_plane_first = keep.tile([P, PASS], U8, name="w4_plane_first", align_bytes=64)
+        nc.vector.tensor_copy(w4_plane_first[:].rearrange("p (t m) -> p t m", t=PACK),
+                              w4_plane_raw[:].rearrange("p (m t) -> p t m", t=PACK))
+        w4_plane[0] = w4_plane_first[:]
+        for g in range(1, PASSES):
+            w4_plane[g] = w4_planes_later[:, (g - 1) * PASS : g * PASS]
+            nc.sync.dma_start(out=w4_plane[g].bitcast(I32)[0 : P - 4 * g, :], in_=w4_plane_first[:].bitcast(I32)[4 * g : P, :])
+        w4_ordered = keep.tile([P, H], U16, name="w4_ordered", align_bytes=64)
+        nc.vector.tensor_copy(w4_ordered[:].rearrange("p (g t m) -> p g t m", t=PACK, m=P),
+                              w4_raw[:].bitcast(U16).rearrange("p (g m t) -> p g t m", t=PACK, m=P))
+        for g in range(PASSES):
+            w4_codes[g] = w4_ordered[:, g * PASS : (g + 1) * PASS]
         quantise_w1(0, 2, 4)
-        w1_rounded[1] = keep.tile([P, PACK, P, PACK], BF16, name="w1_rounded", tag="w1_rounded", align_bytes=64)
+        w1_rounded[1] = spot.tile([P, PACK, P, PACK], BF16, name="w1_rounded1", align_bytes=64, offset=14336)
         for h in range(2):
             nc.gpsimd.tensor_copy(w1_rounded[1][:, :, h * P // 2 : (h + 1) * P // 2, :],
                                   w1_halves[h][:].rearrange("p j (m t) -> p t m j", t=PACK))
@@ -175,7 +166,7 @@ def tile_list_chord_phase_voicings_kernel(tc, tab_words, tab_scales, offs, pos1,
             cols = slice(t * P, (t + 1) * P)
             phase = ring.tile([P, S], F32, name="phase")
             first_stage(w1_codes[g][:, cols].bitcast(FP8X4), w1_plane[g][:, cols], phase,
-                        [nc.scalar.copy, nc.vector.tensor_copy if i == 0 else nc.scalar.copy])
+                        [nc.scalar.copy, nc.scalar.copy])
             if i >= 10:
                 angle[i] = last_angles[:, i - 10, :]
             elif i == 8:
@@ -247,14 +238,11 @@ def tile_list_chord_phase_voicings_kernel(tc, tab_words, tab_scales, offs, pos1,
 
         def gpsimd_round_w1(g, tag, raws):
             w1_rounded[g] = keep.tile([P, PACK, P, PACK], BF16, name="w1_rounded", tag=tag, align_bytes=64)
-            for h in range(2):
-                nc.gpsimd.tensor_copy(w1_rounded[g][:, :, h * P // 2 : (h + 1) * P // 2, :],
-                                      raws[h][:].rearrange("p j (m t) -> p t m j", t=PACK))
+            nc.gpsimd.tensor_copy(w1_rounded[g][:, :, 0 : P // 2, :], raws[0][:].rearrange("p j (m t) -> p t m j", t=PACK))
 
         phases_after = {0: (2, 3), 2: (4,), 3: (5, 6), 5: (7, 8), 7: (9, 10), 8: (11,)}
         quarters = [slice(HALF, HALF + P), slice(HALF + P, B)]
         rounded_z = {}
-        make_colour(0)
         make_phase(0)
         make_phase(1)
         for i in range(TILES - 2):
@@ -262,8 +250,9 @@ def tile_list_chord_phase_voicings_kernel(tc, tab_words, tab_scales, offs, pos1,
             if t == 0:
                 sin_terms[g] = keep.tile([P, PACK, B], F32, name="sin_terms", tag="sin_terms%d" % (g % 2))
                 cos_terms[g] = keep.tile([P, PACK, B], F32, name="cos_terms", tag="cos_terms%d" % (g % 2))
-            if i > 0:
-                make_colour(i)
+            make_colour(i)
+            if i == 1:
+                round_w1(2, 1, w1_halves[1], nc.scalar.copy)
             sines(i)
             sin_product(i, slice(0, B), sine[i][:])
             if i in (0, 1):
@@ -281,7 +270,7 @@ def tile_list_chord_phase_voicings_kernel(tc, tab_words, tab_scales, offs, pos1,
             if i == 1:
                 w8_sb = keep.tile([P, PASSES, N], I32, name="w8_sb", tag="cosine_of0", align_bytes=64)
                 nc.sync.dma_start(out=w8_sb[:], in_=w8_words.rearrange("a p c i -> p a (c i)").bitcast(I32))
-                w8_planes = keep.tile([P, N], U8, name="w8_planes", tag="w4_raw1", align_bytes=64)
+                w8_planes = spot.tile([P, N], U8, name="w8_planes", align_bytes=64, offset=14336)
                 nc.gpsimd.memset(w8_planes[:].bitcast(I32), 0)
                 for q in range(4):
                     nc.sync.dma_start(out=w8_planes[:].bitcast(I32)[32 * q : 32 * q + 4 * PASSES, :],
@@ -289,8 +278,6 @@ def tile_list_chord_phase_voicings_kernel(tc, tab_words, tab_scales, offs, pos1,
                 prior_sb = keep.tile([P, OUT_TILES], F32, name="prior_sb", tag="first_tenant_w1_b", align_bytes=64)
                 with nc.allow_non_contiguous_dma(reason="one prior value for each output row"):
                     nc.sync.dma_start(out=prior_sb[:], in_=prior.rearrange("(c p) -> p c", p=P))
-            if i == 2:
-                order_w4_plane(1, PASSES, "cosine_of2")
             if i == 3:
                 rounded_z[0, 0] = turn(nc.gpsimd, 0, halves[0], "rounded_first")
             if i == 5:

@@ -197,12 +197,13 @@ def tile_list_chord_phase_voicings_kernel(tc, tab_words, tab_scales, offs, pos1,
             nc.scalar.activation(size[:], angle[i], ACT.Abs)
             nc.scalar.activation(cosine[i][:], size[:], ACT.Sin, bias=half_pi[:], scale=-1.0)
 
-        def last_sines(h):
-            both_sines = keep.tile([P, 2, HALF], F32, name="last_sines%d" % h)
-            both_cosines = keep.tile([P, 2, HALF], F32, name="last_cosines%d" % h)
-            size = keep.tile([P, 2, HALF], F32, name="size", tag="last_size%d" % h, align_bytes=64)
-            nc.scalar.activation(both_sines[:], last_angles[:, :, halves[h]], ACT.Sin)
-            nc.scalar.activation(size[:], last_angles[:, :, halves[h]], ACT.Abs)
+        def last_sines(h, bars):
+            width = bars.stop - bars.start
+            both_sines = keep.tile([P, 2, width], F32, name="last_sines%d" % h)
+            both_cosines = keep.tile([P, 2, width], F32, name="last_cosines%d" % h)
+            size = keep.tile([P, 2, width], F32, name="size", tag="last_size%d" % h, align_bytes=64)
+            nc.scalar.activation(both_sines[:], last_angles[:, :, bars], ACT.Sin)
+            nc.scalar.activation(size[:], last_angles[:, :, bars], ACT.Abs)
             nc.scalar.activation(both_cosines[:], size[:], ACT.Sin, bias=half_pi[:], scale=-1.0)
             return both_sines, both_cosines
 
@@ -225,20 +226,35 @@ def tile_list_chord_phase_voicings_kernel(tc, tab_words, tab_scales, offs, pos1,
                                  sin_terms[g][:, :, bars].rearrange("p t (c i) -> p c t i", i=4), ALU.subtract)
             return rounded
 
+        pieces = [slice(0, HALF), slice(HALF, HALF + P), slice(HALF + P, B)]
         z_codes = {}
         z_plane = {}
 
-        def quantise_z(g, h, tag, pieces):
-            z_codes[g, h] = keep.tile([P, HALF], U32, name="z_codes", tag=tag, align_bytes=64)
-            z_plane[g, h] = keep.tile([P, HALF], U8, name="z_plane%d_%d" % (g, h), align_bytes=64)
-            width = HALF // len(pieces)
-            for n, rounded in enumerate(pieces):
-                cols = slice(n * width, (n + 1) * width)
-                nc.vector.quantize_mx(out=z_codes[g, h][:, cols].bitcast(FP8X4), scales=z_plane[g, h][:, cols], in_=rounded[:])
+        def quantise_z(g, first, tag, rounded_pieces):
+            width = sum(rounded.shape[1] for rounded in rounded_pieces) // PACK
+            codes = keep.tile([P, width], U32, name="z_codes", tag=tag, align_bytes=64)
+            plane = keep.tile([P, width], U8, name="z_plane%d_%d" % (g, first), align_bytes=64)
+            done = 0
+            for rounded in rounded_pieces:
+                cols = slice(done, done + rounded.shape[1] // PACK)
+                nc.vector.quantize_mx(out=codes[:, cols].bitcast(FP8X4), scales=plane[:, cols], in_=rounded[:])
+                done = cols.stop
+            done = 0
+            for n in range(first, len(pieces)):
+                cols = slice(done, done + pieces[n].stop - pieces[n].start)
+                if cols.stop <= width:
+                    z_codes[g, n] = codes[:, cols]
+                    z_plane[g, n] = plane[:, cols]
+                done = cols.stop
 
-        def gpsimd_round_w1(g, tag, raws):
-            w1_rounded[g] = keep.tile([P, PACK, P, PACK], BF16, name="w1_rounded", tag=tag, align_bytes=64)
-            nc.gpsimd.tensor_copy(w1_rounded[g][:, :, 0 : P // 2, :], raws[0][:].rearrange("p j (m t) -> p t m j", t=PACK))
+        def round_w1_last(first, last, tag):
+            rounded = keep.tile([P, last - first, P, PACK], BF16, name="w1_rounded", tag=tag, align_bytes=64)
+            nc.gpsimd.tensor_copy(rounded[:], w1_last[:].rearrange("p j (m t) -> p t m j", t=PACK)[:, first:last])
+            return rounded
+
+        def quantise_w1_last(first, last, rounded):
+            nc.vector.quantize_mx(out=w1_codes[2][:, first * P : last * P].bitcast(FP8X4),
+                                  scales=w1_plane[2][:, first * P : last * P], in_=rounded.rearrange("p t m j -> p (t m j)"))
 
         phases_after = {0: (2, 3), 2: (4,), 3: (5, 6), 5: (7, 8), 7: (9, 10), 8: (11,)}
         quarters = [slice(HALF, HALF + P), slice(HALF + P, B)]
@@ -251,13 +267,16 @@ def tile_list_chord_phase_voicings_kernel(tc, tab_words, tab_scales, offs, pos1,
                 sin_terms[g] = keep.tile([P, PACK, B], F32, name="sin_terms", tag="sin_terms%d" % (g % 2))
                 cos_terms[g] = keep.tile([P, PACK, B], F32, name="cos_terms", tag="cos_terms%d" % (g % 2))
             make_colour(i)
-            if i == 1:
-                round_w1(2, 1, w1_halves[1], nc.scalar.copy)
             sines(i)
             sin_product(i, slice(0, B), sine[i][:])
-            if i in (0, 1):
-                make_w1_codes(i + 1, "size_of%d" % i)
-                quantise_w1(i + 1, 0, PACK)
+            if i == 0:
+                make_w1_codes(1, "size_of0")
+                quantise_w1(1, 0, PACK)
+            if i == 3:
+                make_w1_codes(2, "size_of3")
+                quantise_w1_last(0, 2, three[:, 0:2])
+                quantise_w1_last(2, 3, three[:, 2:3])
+                quantise_w1_last(3, 4, fourth[:])
             if i == 6:
                 quantise_z(0, 1, "size_of6", [rounded_z[0, 1]])
             if i == 8:
@@ -265,9 +284,12 @@ def tile_list_chord_phase_voicings_kernel(tc, tab_words, tab_scales, offs, pos1,
                 quantise_z(1, 0, "size_of8", [rounded_z[1, 0]])
             cos_product(i, slice(0, B), cosine[i][:])
             if i == 0:
-                w1_halves = [load_w1(2, 0, "first_tenant_tab_plane"), load_w1(2, 1, "first_tenant_w1_b")]
-                gpsimd_round_w1(2, "cosine_of0", w1_halves)
-            if i == 1:
+                w1_last = keep.tile([P, PACK, PASS], F32, name="w1_last", tag="first_tenant_w1_b", align_bytes=64)
+                nc.sync.dma_start(out=w1_last[:], in_=w1_rows[:, :, 2 * PASS : 3 * PASS])
+                three = round_w1_last(0, 3, "cosine_of0")
+            if i == 2:
+                fourth = round_w1_last(3, 4, "cosine_of2")
+            if i == 3:
                 w8_sb = keep.tile([P, PASSES, N], I32, name="w8_sb", tag="cosine_of0", align_bytes=64)
                 nc.sync.dma_start(out=w8_sb[:], in_=w8_words.rearrange("a p c i -> p a (c i)").bitcast(I32))
                 w8_planes = spot.tile([P, N], U8, name="w8_planes", align_bytes=64, offset=14336)
@@ -292,50 +314,57 @@ def tile_list_chord_phase_voicings_kernel(tc, tab_words, tab_scales, offs, pos1,
         make_colour(TILES - 2)
         make_colour(TILES - 1)
 
-        def score_pass(bank, members, c, g, h):
-            cols = slice(c * P, (c + 1) * P)
-            nc.tensor.matmul_mx(out=bank[:, halves[members.index(c)]], lhsT=w8_sb[:, g, cols].bitcast(FP8X4),
-                                lhsT_scale=w8_planes[4 * g :, cols], rhs=z_codes[g, h][:].bitcast(FP8X4),
-                                rhs_scale=z_plane[g, h][:], start=(g == 0 and c == members[0]),
-                                stop=(g == LAST_PASS and c == members[-1]))
+        groups = {0: [(0, 1), (2, 3), (4, 5)], 1: [(0, 1, 2), (3, 4, 5)], 2: [(0, 1, 2), (3, 4, 5)]}
+        score_banks = {n: [next_bank() for members in groups[n]] for n in range(len(pieces))}
 
-        def store_scores(score, c, h, on_scalar):
-            result = keep.tile([P, HALF], F32, name="result%d_%d" % (c, h))
-            if on_scalar:
-                nc.scalar.activation(result[:], score, ACT.Identity, bias=prior_sb[:, c : c + 1])
-            else:
-                nc.vector.tensor_scalar(result[:], score, prior_sb[:, c : c + 1], None, ALU.add)
-            nc.sync.dma_start(out=out[c * P : (c + 1) * P, halves[h]], in_=result[:])
+        def score_passes(g, n):
+            width = pieces[n].stop - pieces[n].start
+            for bank, members in zip(score_banks[n], groups[n]):
+                for place, c in enumerate(members):
+                    cols = slice(c * P, (c + 1) * P)
+                    nc.tensor.matmul_mx(out=bank[:, place * width : (place + 1) * width], lhsT=w8_sb[:, g, cols].bitcast(FP8X4),
+                                        lhsT_scale=w8_planes[4 * g :, cols], rhs=z_codes[g, n].bitcast(FP8X4),
+                                        rhs_scale=z_plane[g, n], start=(g == 0 and c == members[0]),
+                                        stop=(g == LAST_PASS and c == members[-1]))
 
-        groups = {0: [(0, 1), (2, 3), (4, 5)], 1: [(0, 1), (2,), (3,), (4,), (5,)]}
-        score_banks = {h: [next_bank() for members in groups[h]] for h in range(2)}
+        out_rows = out.rearrange("(c p) m -> p c m", p=P)
 
-        def score_passes(g, h):
-            for bank, members in zip(score_banks[h], groups[h]):
-                for c in members:
-                    score_pass(bank, members, c, g, h)
+        def store_scores(n):
+            width = pieces[n].stop - pieces[n].start
+            for bank, members in zip(score_banks[n], groups[n]):
+                count = len(members)
+                first = members[0]
+                result = keep.tile([P, count, width], F32, name="result%d_%d" % (n, first))
+                if n < 2 or first == 0:
+                    for place, c in enumerate(members):
+                        nc.scalar.activation(result[:, place, :], bank[:, place * width : (place + 1) * width], ACT.Identity,
+                                             bias=prior_sb[:, c : c + 1])
+                else:
+                    nc.vector.tensor_tensor(result[:], bank[:, 0 : count * width].rearrange("p (c m) -> p c m", c=count),
+                                            prior_sb[:, first : first + count].unsqueeze(2).to_broadcast([P, count, width]),
+                                            ALU.add)
+                nc.sync.dma_start(out=out_rows[:, first : first + count, pieces[n]], in_=result[:])
 
-        def close_scores(h):
-            for bank, members in zip(score_banks[h], groups[h]):
-                for c in members:
-                    score_pass(bank, members, c, LAST_PASS, h)
-                for c in members:
-                    store_scores(bank[:, halves[members.index(c)]], c, h, h == 0 or len(members) == 2)
+        def close_piece(n):
+            rounded = turn(nc.vector, LAST_PASS, pieces[n], "rounded_last%d" % n)
+            quantise_z(LAST_PASS, n, "last_z_codes%d" % n, [rounded])
+            score_passes(LAST_PASS, n)
+            store_scores(n)
 
         score_passes(0, 1)
-        for h in range(2):
-            both_sines, both_cosines = last_sines(h)
+        score_passes(0, 2)
+        for h, bars in enumerate(pieces):
+            both_sines, both_cosines = last_sines(h, bars)
             for n in range(2):
-                sin_product(TILES - 2 + n, halves[h], both_sines[:, n, :])
+                sin_product(TILES - 2 + n, bars, both_sines[:, n, :])
             if h == 0:
                 quantise_z(0, 0, "last_size0", [rounded_z[0, 0]])
                 score_passes(0, 0)
                 score_passes(1, 0)
-            else:
+            if h == 1:
                 quantise_z(1, 1, "last_size1", [gpsimd_quarter, vector_quarter])
                 score_passes(1, 1)
+                score_passes(1, 2)
             for n in range(2):
-                cos_product(TILES - 2 + n, halves[h], both_cosines[:, n, :])
-            rounded = turn(nc.vector, LAST_PASS, halves[h], "rounded_last%d" % h)
-            quantise_z(LAST_PASS, h, "last_z_codes%d" % h, [rounded])
-            close_scores(h)
+                cos_product(TILES - 2 + n, bars, both_cosines[:, n, :])
+            close_piece(h)

@@ -73,6 +73,11 @@ def tile_list_chord_phase_voicings_kernel(tc, tab_words, tab_scales, offs, pos1,
             nc.sync.dma_start(out=raw[:], in_=w1_rows[:, :, first : first + PASS // 2])
             return raw
 
+        def load_w1_part(g, tag):
+            raw = keep.tile([P, PACK, PASS], F32, name="w1_part", tag=tag, align_bytes=64)
+            nc.sync.dma_start(out=raw[:], in_=w1_rows[:, :, g * PASS : (g + 1) * PASS])
+            return raw
+
         offs_sb = load_list("offs_sb", offs, S)
         tab_sb = spot.tile([P, T], I32, name="tab_sb", align_bytes=64, offset=0)
         nc.sync.dma_start(out=tab_sb[:], in_=tab_words[0].rearrange("p t i -> p (t i)").bitcast(I32))
@@ -119,7 +124,7 @@ def tile_list_chord_phase_voicings_kernel(tc, tab_words, tab_scales, offs, pos1,
             picked_codes.append(codes)
         round_w1(0, 1, w1_halves[1], nc.scalar.copy, 0, P // 4)
         round_w1(0, 1, w1_halves[1], nc.vector.tensor_copy, P // 4, P // 2)
-        w1_halves = [load_w1(1, 0, "first_tenant_tab_plane"), load_w1(1, 1, None)]
+        w1_later = {1: load_w1_part(1, "first_tenant_tab_plane")}
         low_of = load_list("low_of", pos3, B)
         substitute_of = load_list("substitute_of", pos2, B)
         quantise_w1(0, 0, 1)
@@ -137,10 +142,8 @@ def tile_list_chord_phase_voicings_kernel(tc, tab_words, tab_scales, offs, pos1,
         for g in range(PASSES):
             w4_codes[g] = w4_ordered[:, g * PASS : (g + 1) * PASS]
         quantise_w1(0, 2, 4)
-        w1_rounded[1] = spot.tile([P, PACK, P, PACK], BF16, name="w1_rounded1", align_bytes=64, offset=14336)
-        for h in range(2):
-            nc.gpsimd.tensor_copy(w1_rounded[1][:, :, h * P // 2 : (h + 1) * P // 2, :],
-                                  w1_halves[h][:].rearrange("p j (m t) -> p t m j", t=PACK))
+        low = spot.tile([P, 2, P, PACK], BF16, name="w1_rounded1", align_bytes=64, offset=14336)
+        nc.gpsimd.tensor_copy(low[:], w1_later[1][:].rearrange("p j (m t) -> p t m j", t=PACK)[:, 0:2])
 
         banks_taken = []
 
@@ -157,6 +160,7 @@ def tile_list_chord_phase_voicings_kernel(tc, tab_words, tab_scales, offs, pos1,
                                     rhs_scale=picked_plane[:, chords], start=True, stop=True)
                 copies[h](rows[:, chords], bank[:])
 
+        stationary = {t: (w1_codes[0][:, t * P : (t + 1) * P], w1_plane[0][:, t * P : (t + 1) * P]) for t in range(PACK)}
         angle = {}
         last_angles = keep.tile([P, 2, B], F32, name="last_angles")
         colour = {}
@@ -165,7 +169,7 @@ def tile_list_chord_phase_voicings_kernel(tc, tab_words, tab_scales, offs, pos1,
             g, t = divmod(i, PACK)
             cols = slice(t * P, (t + 1) * P)
             phase = ring.tile([P, S], F32, name="phase")
-            first_stage(w1_codes[g][:, cols].bitcast(FP8X4), w1_plane[g][:, cols], phase,
+            first_stage(stationary[i][0].bitcast(FP8X4), stationary[i][1], phase,
                         [nc.scalar.copy, nc.scalar.copy])
             if i >= 10:
                 angle[i] = last_angles[:, i - 10, :]
@@ -219,11 +223,11 @@ def tile_list_chord_phase_voicings_kernel(tc, tab_words, tab_scales, offs, pos1,
             nc.vector.tensor_tensor(cos_terms[g][:, t, bars], colour[i][:].indirect(substitute_of[:, entries]),
                                     factor, ALU.mult)
 
-        def turn(engine, g, bars, tag):
+        def turn(engine, g, bars, tag, run):
             rounded = keep.tile([P, (bars.stop - bars.start) * PACK], BF16, name="rounded_z", tag=tag, align_bytes=64)
-            engine.tensor_tensor(rounded[:].rearrange("p (c i t) -> p c t i", i=4, t=PACK),
-                                 cos_terms[g][:, :, bars].rearrange("p t (c i) -> p c t i", i=4),
-                                 sin_terms[g][:, :, bars].rearrange("p t (c i) -> p c t i", i=4), ALU.subtract)
+            engine.tensor_tensor(rounded[:].rearrange("p (c i t) -> p c t i", i=run, t=PACK),
+                                 cos_terms[g][:, :, bars].rearrange("p t (c i) -> p c t i", i=run),
+                                 sin_terms[g][:, :, bars].rearrange("p t (c i) -> p c t i", i=run), ALU.subtract)
             return rounded
 
         pieces = [slice(0, HALF), slice(HALF, HALF + P), slice(HALF + P, B)]
@@ -247,14 +251,17 @@ def tile_list_chord_phase_voicings_kernel(tc, tab_words, tab_scales, offs, pos1,
                     z_plane[g, n] = plane[:, cols]
                 done = cols.stop
 
-        def round_w1_last(first, last, tag):
-            rounded = keep.tile([P, last - first, P, PACK], BF16, name="w1_rounded", tag=tag, align_bytes=64)
-            nc.gpsimd.tensor_copy(rounded[:], w1_last[:].rearrange("p j (m t) -> p t m j", t=PACK)[:, first:last])
+        def round_high(g, copy, tag):
+            rounded = keep.tile([P, 2, P, PACK], BF16, name="w1_high", tag=tag, align_bytes=64)
+            copy(rounded[:].rearrange("p t m j -> p m j t"), w1_later[g][:].rearrange("p j (m t) -> p m j t", t=PACK)[:, :, :, 2:4])
             return rounded
 
-        def quantise_w1_last(first, last, rounded):
-            nc.vector.quantize_mx(out=w1_codes[2][:, first * P : last * P].bitcast(FP8X4),
-                                  scales=w1_plane[2][:, first * P : last * P], in_=rounded.rearrange("p t m j -> p (t m j)"))
+        def quantise_pair(g, first, rounded, tag):
+            codes = keep.tile([P, 2 * P], U32, name="w1_pair_codes", tag=tag, align_bytes=64)
+            plane = keep.tile([P, 2 * P], U8, name="w1_pair_plane%d_%d" % (g, first), align_bytes=64)
+            nc.vector.quantize_mx(out=codes[:].bitcast(FP8X4), scales=plane[:], in_=rounded[:].rearrange("p t m j -> p (t m j)"))
+            for t in range(2):
+                stationary[PACK * g + first + t] = (codes[:, t * P : (t + 1) * P], plane[:, t * P : (t + 1) * P])
 
         phases_after = {0: (2, 3), 2: (4,), 3: (5, 6), 5: (7, 8), 7: (9, 10), 8: (11,)}
         quarters = [slice(HALF, HALF + P), slice(HALF + P, B)]
@@ -267,28 +274,30 @@ def tile_list_chord_phase_voicings_kernel(tc, tab_words, tab_scales, offs, pos1,
                 sin_terms[g] = keep.tile([P, PACK, B], F32, name="sin_terms", tag="sin_terms%d" % (g % 2))
                 cos_terms[g] = keep.tile([P, PACK, B], F32, name="cos_terms", tag="cos_terms%d" % (g % 2))
             make_colour(i)
+            if i == 4:
+                high = round_high(2, nc.scalar.copy, "w1_high_last")
             sines(i)
             sin_product(i, slice(0, B), sine[i][:])
             if i == 0:
-                make_w1_codes(1, "size_of0")
-                quantise_w1(1, 0, PACK)
+                quantise_pair(1, 0, low, "size_of0")
+            if i == 1:
+                high = round_high(1, nc.vector.tensor_copy, "size_of1")
+            if i == 2:
+                quantise_pair(1, 2, high, "size_of2")
             if i == 3:
-                make_w1_codes(2, "size_of3")
-                quantise_w1_last(0, 2, three[:, 0:2])
-                quantise_w1_last(2, 3, three[:, 2:3])
-                quantise_w1_last(3, 4, fourth[:])
+                quantise_pair(2, 0, low, "size_of3")
+            if i == 5:
+                quantise_pair(2, 2, high, "size_of5")
             if i == 6:
                 quantise_z(0, 1, "size_of6", [rounded_z[0, 1]])
             if i == 8:
-                vector_quarter = turn(nc.vector, 1, quarters[1], "angle_of8")
+                vector_quarter = turn(nc.vector, 1, quarters[1], "angle_of8", 2)
                 quantise_z(1, 0, "size_of8", [rounded_z[1, 0]])
             cos_product(i, slice(0, B), cosine[i][:])
             if i == 0:
-                w1_last = keep.tile([P, PACK, PASS], F32, name="w1_last", tag="first_tenant_w1_b", align_bytes=64)
-                nc.sync.dma_start(out=w1_last[:], in_=w1_rows[:, :, 2 * PASS : 3 * PASS])
-                three = round_w1_last(0, 3, "cosine_of0")
-            if i == 2:
-                fourth = round_w1_last(3, 4, "cosine_of2")
+                w1_later[2] = load_w1_part(2, "first_tenant_w1_b")
+                low = keep.tile([P, 2, P, PACK], BF16, name="w1_low", tag="cosine_of0", align_bytes=64)
+                nc.gpsimd.tensor_copy(low[:], w1_later[2][:].rearrange("p j (m t) -> p t m j", t=PACK)[:, 0:2])
             if i == 3:
                 w8_sb = keep.tile([P, PASSES, N], I32, name="w8_sb", tag="cosine_of0", align_bytes=64)
                 nc.sync.dma_start(out=w8_sb[:], in_=w8_words.rearrange("a p c i -> p a (c i)").bitcast(I32))
@@ -301,13 +310,13 @@ def tile_list_chord_phase_voicings_kernel(tc, tab_words, tab_scales, offs, pos1,
                 with nc.allow_non_contiguous_dma(reason="one prior value for each output row"):
                     nc.sync.dma_start(out=prior_sb[:], in_=prior.rearrange("(c p) -> p c", p=P))
             if i == 3:
-                rounded_z[0, 0] = turn(nc.gpsimd, 0, halves[0], "rounded_first")
+                rounded_z[0, 0] = turn(nc.gpsimd, 0, halves[0], "rounded_first", 4)
             if i == 5:
-                rounded_z[0, 1] = turn(nc.gpsimd, 0, halves[1], "cosine_of5")
+                rounded_z[0, 1] = turn(nc.gpsimd, 0, halves[1], "cosine_of5", 4)
             if i == 7:
-                rounded_z[1, 0] = turn(nc.gpsimd, 1, halves[0], "rounded_middle")
+                rounded_z[1, 0] = turn(nc.gpsimd, 1, halves[0], "rounded_middle", 4)
             if i == 8:
-                gpsimd_quarter = turn(nc.gpsimd, 1, quarters[0], "cosine_of8")
+                gpsimd_quarter = turn(nc.gpsimd, 1, quarters[0], "cosine_of8", 4)
             for later in phases_after.get(i, ()):
                 make_phase(later)
 
@@ -346,7 +355,7 @@ def tile_list_chord_phase_voicings_kernel(tc, tab_words, tab_scales, offs, pos1,
                 nc.sync.dma_start(out=out_rows[:, first : first + count, pieces[n]], in_=result[:])
 
         def close_piece(n):
-            rounded = turn(nc.vector, LAST_PASS, pieces[n], "rounded_last%d" % n)
+            rounded = turn(nc.vector, LAST_PASS, pieces[n], "rounded_last%d" % n, 2)
             quantise_z(LAST_PASS, n, "last_z_codes%d" % n, [rounded])
             score_passes(LAST_PASS, n)
             store_scores(n)

@@ -29,6 +29,10 @@ LAST_PASS = PASSES - 1
 OUT_TILES = N // P
 PER_COLUMN = 16
 HALF = B // 2
+SLOTS = 5
+SLOT_BYTES = 5120
+SECOND_HALF_AT = 19456
+SLOTS_AT = 29696
 
 
 def tile_list_chord_phase_voicings_kernel(tc, tab_words, tab_scales, offs, pos1, pos2, pos3, w1, w4_words,
@@ -68,7 +72,7 @@ def tile_list_chord_phase_voicings_kernel(tc, tab_words, tab_scales, offs, pos1,
             if tag is None:
                 raw = spot.tile([P, PACK, PASS // 2], F32, name="w1_raw%d" % g, align_bytes=64, offset=8192)
             else:
-                raw = keep.tile([P, PACK, PASS // 2], F32, name="w1_raw", tag=tag, align_bytes=64)
+                raw = spot.tile([P, PACK, PASS // 2], F32, name="w1_raw_b", align_bytes=64, offset=tag)
             first = g * PASS + h * PASS // 2
             nc.sync.dma_start(out=raw[:], in_=w1_rows[:, :, first : first + PASS // 2])
             return raw
@@ -81,7 +85,7 @@ def tile_list_chord_phase_voicings_kernel(tc, tab_words, tab_scales, offs, pos1,
         offs_sb = load_list("offs_sb", offs, S)
         tab_sb = spot.tile([P, T], I32, name="tab_sb", align_bytes=64, offset=0)
         nc.sync.dma_start(out=tab_sb[:], in_=tab_words[0].rearrange("p t i -> p (t i)").bitcast(I32))
-        w1_halves = [load_w1(0, 0, None), load_w1(0, 1, "first_tenant_w1_b")]
+        w1_halves = [load_w1(0, 0, None), load_w1(0, 1, SECOND_HALF_AT)]
         for q in range(4):
             nc.sync.dma_start(out=w4_plane_raw[:].bitcast(I32)[32 * q : 32 * q + 4 * PASSES, :],
                               in_=w4_scales[0][4 * q : 4 * q + 4, :].bitcast(I32).rearrange("j (g c) -> g j c", g=PASSES))
@@ -129,77 +133,83 @@ def tile_list_chord_phase_voicings_kernel(tc, tab_words, tab_scales, offs, pos1,
         substitute_of = load_list("substitute_of", pos2, B)
         quantise_w1(0, 0, 1)
         quantise_w1(0, 1, 2)
-        w4_plane_first = keep.tile([P, PASS], U8, name="w4_plane_first", align_bytes=64)
+        w4_plane_first = spot.tile([P, PASS], U8, name="w4_plane_first", align_bytes=64, offset=SECOND_HALF_AT + 1024)
         nc.vector.tensor_copy(w4_plane_first[:].rearrange("p (t m) -> p t m", t=PACK),
                               w4_plane_raw[:].rearrange("p (m t) -> p t m", t=PACK))
         w4_plane[0] = w4_plane_first[:]
         for g in range(1, PASSES):
             w4_plane[g] = w4_planes_later[:, (g - 1) * PASS : g * PASS]
             nc.sync.dma_start(out=w4_plane[g].bitcast(I32)[0 : P - 4 * g, :], in_=w4_plane_first[:].bitcast(I32)[4 * g : P, :])
-        w4_ordered = keep.tile([P, H], U16, name="w4_ordered", align_bytes=64)
-        nc.vector.tensor_copy(w4_ordered[:].rearrange("p (g t m) -> p g t m", t=PACK, m=P),
-                              w4_raw[:].bitcast(U16).rearrange("p (g m t) -> p g t m", t=PACK, m=P))
-        for g in range(PASSES):
-            w4_codes[g] = w4_ordered[:, g * PASS : (g + 1) * PASS]
+        w4_ordered = keep.tile([P, H - PASS], U16, name="w4_ordered", align_bytes=64)
+        w4_first = spot.tile([P, PASS], U16, name="w4_first", align_bytes=64, offset=SECOND_HALF_AT)
+        w4_unordered = w4_raw[:].bitcast(U16).rearrange("p (g m t) -> p g t m", t=PACK, m=P)
+        nc.vector.tensor_copy(w4_first[:].rearrange("p (t m) -> p t m", m=P), w4_unordered[:, 0])
+        w4_codes[0] = w4_first[:]
         quantise_w1(0, 2, 4)
-        low = spot.tile([P, 2, P, PACK], BF16, name="w1_rounded1", align_bytes=64, offset=14336)
-        nc.gpsimd.tensor_copy(low[:], w1_later[1][:].rearrange("p j (m t) -> p t m j", t=PACK)[:, 0:2])
+        nc.vector.tensor_copy(w4_ordered[:].rearrange("p (g t m) -> p g t m", t=PACK, m=P), w4_unordered[:, 1:])
+        for g in range(1, PASSES):
+            w4_codes[g] = w4_ordered[:, (g - 1) * PASS : g * PASS]
+        low = spot.tile([P, 2 * PASS], BF16, name="w1_rounded1", align_bytes=64, offset=13312)
+        nc.gpsimd.tensor_copy(low[:].rearrange("p (t m j) -> p t m j", t=2, j=PACK), w1_later[1][:].rearrange("p j (m t) -> p t m j", t=PACK)[:, 0:2])
 
-        banks_taken = []
-
-        def next_bank():
-            bank = psum.tile([P, BANK], F32, name="bank%d" % (len(banks_taken) % BANKS))
-            banks_taken.append(bank)
+        def bank_tile(number):
+            bank = psum.tile([P, BANK], F32, name="bank%d" % number)
             return bank
 
-        def first_stage(lhsT, lhsT_scale, rows, copies):
-            for h in range(S // BANK):
-                chords = slice(h * BANK, (h + 1) * BANK)
-                bank = next_bank()
-                nc.tensor.matmul_mx(out=bank[:], lhsT=lhsT, lhsT_scale=lhsT_scale, rhs=picked_codes[h][:].bitcast(FP8X4),
-                                    rhs_scale=picked_plane[:, chords], start=True, stop=True)
-                copies[h](rows[:, chords], bank[:])
+        def first_stage(lhsT, lhsT_scale, h, number):
+            bank = bank_tile(number)
+            nc.tensor.matmul_mx(out=bank[:], lhsT=lhsT, lhsT_scale=lhsT_scale, rhs=picked_codes[h][:].bitcast(FP8X4),
+                                rhs_scale=picked_plane[:, h * BANK : (h + 1) * BANK], start=True, stop=True)
+            return bank
 
         stationary = {t: (w1_codes[0][:, t * P : (t + 1) * P], w1_plane[0][:, t * P : (t + 1) * P]) for t in range(PACK)}
         angle = {}
         last_angles = keep.tile([P, 2, B], F32, name="last_angles")
         colour = {}
+        phase = {}
 
-        def make_phase(i):
-            g, t = divmod(i, PACK)
-            cols = slice(t * P, (t + 1) * P)
-            phase = ring.tile([P, S], F32, name="phase")
-            first_stage(stationary[i][0].bitcast(FP8X4), stationary[i][1], phase,
-                        [nc.scalar.copy, nc.scalar.copy])
-            if i >= 10:
-                angle[i] = last_angles[:, i - 10, :]
-            elif i == 8:
-                kept = keep.tile([P, B], F32, name="angle_kept", tag="angle_of8", align_bytes=64)
-                angle[i] = kept[:]
+        def slot(i):
+            return SLOTS_AT + (i % SLOTS) * SLOT_BYTES
+
+        def held(i, shape, dtype):
+            tile = spot.tile(shape, dtype, name="held%d" % i, align_bytes=64, offset=slot(i) + 4096)
+            return tile
+
+        phase_banks = {}
+
+        def phase_sums(i):
+            phase_banks[i] = [first_stage(stationary[i][0].bitcast(FP8X4), stationary[i][1], h, 2 * (i % 2) + h) for h in range(2)]
+
+        def phase_half(i, h):
+            if h == 0:
+                phase[i] = ring.tile([P, S], F32, name="phase")
+            nc.scalar.copy(phase[i][:, h * BANK : (h + 1) * BANK], phase_banks[i][h][:])
+
+        def pick_phase(i):
+            if i >= TILES - 2:
+                angle[i] = last_angles[:, i - (TILES - 2), :]
             else:
                 lone = deep.tile([P, B], F32, name="angle")
                 angle[i] = lone[:]
-            nc.vector.tensor_copy(angle[i], phase[:].indirect(current_of[:]))
+            nc.scalar.activation(angle[i], phase[i][:].indirect(current_of[:]), ACT.Copy)
 
         def make_colour(i):
-            colour[i] = deep.tile([P, S], F32, name="colour")
+            if i < 2:
+                colour[i] = keep.tile([P, S], F32, name="colour%d" % i)
+            else:
+                colour[i] = spot.tile([P, S], F32, name="colour%d" % i, align_bytes=64, offset=slot(i - 2))
             g, t = divmod(i, PACK)
             cols = slice(t * P, (t + 1) * P)
-            first_stage(w4_codes[g][:, cols].bitcast(FP4X4), w4_plane[g][:, cols], colour[i], [nc.scalar.copy, nc.scalar.copy])
+            for h in range(2):
+                bank = first_stage(w4_codes[g][:, cols].bitcast(FP4X4), w4_plane[g][:, cols], h, 4 + 2 * (i % 2) + h)
+                nc.vector.tensor_copy(colour[i][:, h * BANK : (h + 1) * BANK], bank[:])
 
         cos_terms = {}
         sin_terms = {}
         sine = {}
         cosine = {}
         halves = [slice(h * HALF, (h + 1) * HALF) for h in range(2)]
-
-        def sines(i):
-            sine[i] = ring.tile([P, B], F32, name="sine")
-            cosine[i] = keep.tile([P, B], F32, name="cosine", tag="cosine_of%d" % i, align_bytes=64)
-            size = keep.tile([P, B], F32, name="size", tag="size_of%d" % i, align_bytes=64)
-            nc.scalar.activation(sine[i][:], angle[i], ACT.Sin)
-            nc.scalar.activation(size[:], angle[i], ACT.Abs)
-            nc.scalar.activation(cosine[i][:], size[:], ACT.Sin, bias=half_pi[:], scale=-1.0)
+        quarters = [slice(q * P, (q + 1) * P) for q in range(4)]
 
         def last_sines(h, bars):
             width = bars.stop - bars.start
@@ -223,108 +233,132 @@ def tile_list_chord_phase_voicings_kernel(tc, tab_words, tab_scales, offs, pos1,
             nc.vector.tensor_tensor(cos_terms[g][:, t, bars], colour[i][:].indirect(substitute_of[:, entries]),
                                     factor, ALU.mult)
 
-        def turn(engine, g, bars, tag, run):
-            rounded = keep.tile([P, (bars.stop - bars.start) * PACK], BF16, name="rounded_z", tag=tag, align_bytes=64)
+        def turn(engine, g, bars, rounded, run):
             engine.tensor_tensor(rounded[:].rearrange("p (c i t) -> p c t i", i=run, t=PACK),
                                  cos_terms[g][:, :, bars].rearrange("p t (c i) -> p c t i", i=run),
                                  sin_terms[g][:, :, bars].rearrange("p t (c i) -> p c t i", i=run), ALU.subtract)
             return rounded
 
+        def after_sine(i):
+            tile = keep.tile([P, PASS], BF16, name="after_sine", tag="sine_of%d" % i, align_bytes=64)
+            return tile
+
         pieces = [slice(0, HALF), slice(HALF, HALF + P), slice(HALF + P, B)]
         z_codes = {}
         z_plane = {}
 
-        def quantise_z(g, first, tag, rounded_pieces):
-            width = sum(rounded.shape[1] for rounded in rounded_pieces) // PACK
-            codes = keep.tile([P, width], U32, name="z_codes", tag=tag, align_bytes=64)
-            plane = keep.tile([P, width], U8, name="z_plane%d_%d" % (g, first), align_bytes=64)
+        def quantise_into(codes, name, rounded_pieces):
+            plane = keep.tile([P, codes.shape[1]], U8, name=name, align_bytes=64)
             done = 0
             for rounded in rounded_pieces:
                 cols = slice(done, done + rounded.shape[1] // PACK)
                 nc.vector.quantize_mx(out=codes[:, cols].bitcast(FP8X4), scales=plane[:, cols], in_=rounded[:])
                 done = cols.stop
+            return plane
+
+        def quantise_z(g, first, codes, rounded_pieces):
+            plane = quantise_into(codes, "z_plane%d_%d" % (g, first), rounded_pieces)
             done = 0
             for n in range(first, len(pieces)):
                 cols = slice(done, done + pieces[n].stop - pieces[n].start)
-                if cols.stop <= width:
+                if cols.stop <= codes.shape[1]:
                     z_codes[g, n] = codes[:, cols]
                     z_plane[g, n] = plane[:, cols]
                 done = cols.stop
 
-        def round_high(g, copy, tag):
-            rounded = keep.tile([P, 2, P, PACK], BF16, name="w1_high", tag=tag, align_bytes=64)
-            copy(rounded[:].rearrange("p t m j -> p m j t"), w1_later[g][:].rearrange("p j (m t) -> p m j t", t=PACK)[:, :, :, 2:4])
+        def tagged_codes(width, tag):
+            codes = keep.tile([P, width], U32, name="z_codes", tag=tag, align_bytes=64)
+            return codes
+
+        def round_tile(g, t, copy, rounded):
+            copy(rounded[:].rearrange("p (m j) -> p m j", j=PACK), w1_later[g][:].rearrange("p j (m t) -> p t m j", t=PACK)[:, t])
             return rounded
 
-        def quantise_pair(g, first, rounded, tag):
-            codes = keep.tile([P, 2 * P], U32, name="w1_pair_codes", tag=tag, align_bytes=64)
-            plane = keep.tile([P, 2 * P], U8, name="w1_pair_plane%d_%d" % (g, first), align_bytes=64)
-            nc.vector.quantize_mx(out=codes[:].bitcast(FP8X4), scales=plane[:], in_=rounded[:].rearrange("p t m j -> p (t m j)"))
+        def round_high(g, copy):
+            rounded = keep.tile([P, 2 * PASS], BF16, name="w1_high", align_bytes=64)
+            copy(rounded[:].rearrange("p (t m j) -> p m j t", t=2, j=PACK),
+                 w1_later[g][:].rearrange("p j (m t) -> p m j t", t=PACK)[:, :, :, 2:4])
+            return rounded
+
+        def quantise_pair(g, first, codes, rounded_pieces):
+            plane = quantise_into(codes, "w1_pair_plane%d_%d" % (g, first), rounded_pieces)
             for t in range(2):
                 stationary[PACK * g + first + t] = (codes[:, t * P : (t + 1) * P], plane[:, t * P : (t + 1) * P])
 
-        phases_after = {0: (2, 3), 2: (4,), 3: (5, 6), 5: (7, 8), 7: (9, 10), 8: (11,)}
-        quarters = [slice(HALF, HALF + P), slice(HALF + P, B)]
-        rounded_z = {}
-        make_phase(0)
-        make_phase(1)
+        w1_later[2] = spot.tile([P, PACK, PASS], F32, name="w1_last", align_bytes=64, offset=SECOND_HALF_AT + 2048)
+        nc.sync.dma_start(out=w1_later[2][:], in_=w1_rows[:, :, 2 * PASS : 3 * PASS])
+        made = {}
+        phase_sums(0)
+        phase_sums(1)
+        phase_half(0, 0)
+        phase_half(0, 1)
+        make_colour(0)
+        make_colour(1)
         for i in range(TILES - 2):
             g, t = divmod(i, PACK)
             if t == 0:
                 sin_terms[g] = keep.tile([P, PACK, B], F32, name="sin_terms", tag="sin_terms%d" % (g % 2))
                 cos_terms[g] = keep.tile([P, PACK, B], F32, name="cos_terms", tag="cos_terms%d" % (g % 2))
-            make_colour(i)
+            sine[i] = keep.tile([P, B], F32, name="sine", tag="sine_of%d" % i, align_bytes=64)
+            cosine[i] = deep.tile([P, B], F32, name="cosine")
+            size = spot.tile([P, B], F32, name="size%d" % i, align_bytes=64, offset=slot(i) + 3072)
+            phase_sums(i + 2)
+            pick_phase(i)
+            phase_half(i + 1, 0)
+            nc.scalar.activation(sine[i][:], angle[i], ACT.Sin)
+            nc.scalar.activation(size[:], angle[i], ACT.Abs)
+            phase_half(i + 1, 1)
+            nc.scalar.activation(cosine[i][:], size[:], ACT.Sin, bias=half_pi[:], scale=-1.0)
             if i == 4:
-                high = round_high(2, nc.scalar.copy, "w1_high_last")
-            sines(i)
+                high = round_high(2, nc.vector.tensor_copy)
             sin_product(i, slice(0, B), sine[i][:])
+            if t == PACK - 1:
+                for bars in halves:
+                    cos_product(i, bars, cosine[i][:, bars])
+            else:
+                cos_product(i, slice(0, B), cosine[i][:])
+            if i < 2:
+                made[i] = round_tile(1, 2 + i, nc.gpsimd.tensor_copy, after_sine(i))
+            elif i == 2:
+                made[i] = round_tile(2, 0, nc.gpsimd.tensor_copy, after_sine(i))
+            else:
+                made[i] = turn(nc.gpsimd, (i - 3) // PACK, quarters[(i - 3) % PACK], after_sine(i), 4)
+            make_colour(i + 2)
             if i == 0:
-                quantise_pair(1, 0, low, "size_of0")
-            if i == 1:
-                high = round_high(1, nc.vector.tensor_copy, "size_of1")
+                quantise_pair(1, 0, held(i, [P, 2 * P], U32), [low])
             if i == 2:
-                quantise_pair(1, 2, high, "size_of2")
+                quantise_pair(1, 2, held(i, [P, 2 * P], U32), [made[0], made[1]])
             if i == 3:
-                quantise_pair(2, 0, low, "size_of3")
-            if i == 5:
-                quantise_pair(2, 2, high, "size_of5")
-            if i == 6:
-                quantise_z(0, 1, "size_of6", [rounded_z[0, 1]])
-            if i == 8:
-                vector_quarter = turn(nc.vector, 1, quarters[1], "angle_of8", 2)
-                quantise_z(1, 0, "size_of8", [rounded_z[1, 0]])
-            cos_product(i, slice(0, B), cosine[i][:])
-            if i == 0:
-                w1_later[2] = load_w1_part(2, "first_tenant_w1_b")
-                low = keep.tile([P, 2, P, PACK], BF16, name="w1_low", tag="cosine_of0", align_bytes=64)
-                nc.gpsimd.tensor_copy(low[:], w1_later[2][:].rearrange("p j (m t) -> p t m j", t=PACK)[:, 0:2])
-            if i == 3:
-                w8_sb = keep.tile([P, PASSES, N], I32, name="w8_sb", tag="cosine_of0", align_bytes=64)
+                second = round_tile(2, 1, nc.vector.tensor_copy, held(i, [P, PASS], BF16))
+                w8_sb = keep.tile([P, PASSES, N], I32, name="w8_sb", tag="first_tenant_tab_plane", align_bytes=64)
                 nc.sync.dma_start(out=w8_sb[:], in_=w8_words.rearrange("a p c i -> p a (c i)").bitcast(I32))
                 w8_planes = spot.tile([P, N], U8, name="w8_planes", align_bytes=64, offset=14336)
                 nc.gpsimd.memset(w8_planes[:].bitcast(I32), 0)
                 for q in range(4):
                     nc.sync.dma_start(out=w8_planes[:].bitcast(I32)[32 * q : 32 * q + 4 * PASSES, :],
                                       in_=w8_scales[:, 4 * q : 4 * q + 4, :].bitcast(I32))
-                prior_sb = keep.tile([P, OUT_TILES], F32, name="prior_sb", tag="first_tenant_w1_b", align_bytes=64)
+            if i == 4:
+                quantise_pair(2, 0, held(i, [P, 2 * P], U32), [made[2], second])
+                prior_sb = spot.tile([P, OUT_TILES], F32, name="prior_sb", align_bytes=64, offset=SECOND_HALF_AT + 2048)
                 with nc.allow_non_contiguous_dma(reason="one prior value for each output row"):
                     nc.sync.dma_start(out=prior_sb[:], in_=prior.rearrange("(c p) -> p c", p=P))
-            if i == 3:
-                rounded_z[0, 0] = turn(nc.gpsimd, 0, halves[0], "rounded_first", 4)
             if i == 5:
-                rounded_z[0, 1] = turn(nc.gpsimd, 0, halves[1], "cosine_of5", 4)
+                quantise_pair(2, 2, held(i, [P, 2 * P], U32), [high])
             if i == 7:
-                rounded_z[1, 0] = turn(nc.gpsimd, 1, halves[0], "rounded_middle", 4)
+                quantise_z(0, 1, held(i, [P, 2 * P], U32), [made[5], made[6]])
             if i == 8:
-                gpsimd_quarter = turn(nc.gpsimd, 1, quarters[0], "cosine_of8", 4)
-            for later in phases_after.get(i, ()):
-                make_phase(later)
+                vector_quarter = turn(nc.vector, 1, quarters[3], held(i, [P, PASS], BF16), 2)
+            if i == 9:
+                quantise_z(1, 0, held(i, [P, 2 * P], U32), [made[7], made[8]])
 
-        make_colour(TILES - 2)
-        make_colour(TILES - 1)
+        pick_phase(TILES - 2)
+        phase_half(TILES - 1, 0)
+        phase_half(TILES - 1, 1)
+        pick_phase(TILES - 1)
 
         groups = {0: [(0, 1), (2, 3), (4, 5)], 1: [(0, 1, 2), (3, 4, 5)], 2: [(0, 1, 2), (3, 4, 5)]}
-        score_banks = {n: [next_bank() for members in groups[n]] for n in range(len(pieces))}
+        bank_numbers = {0: (4, 5, 6), 1: (0, 1), 2: (2, 3)}
+        score_banks = {n: [bank_tile(number) for number in bank_numbers[n]] for n in range(len(pieces))}
 
         def score_passes(g, n):
             width = pieces[n].stop - pieces[n].start
@@ -355,8 +389,10 @@ def tile_list_chord_phase_voicings_kernel(tc, tab_words, tab_scales, offs, pos1,
                 nc.sync.dma_start(out=out_rows[:, first : first + count, pieces[n]], in_=result[:])
 
         def close_piece(n):
-            rounded = turn(nc.vector, LAST_PASS, pieces[n], "rounded_last%d" % n, 2)
-            quantise_z(LAST_PASS, n, "last_z_codes%d" % n, [rounded])
+            width = pieces[n].stop - pieces[n].start
+            rounded = keep.tile([P, width * PACK], BF16, name="rounded_last%d" % n, align_bytes=64)
+            turn(nc.vector, LAST_PASS, pieces[n], rounded, 2)
+            quantise_z(LAST_PASS, n, tagged_codes(width, "last_z_codes%d" % n), [rounded])
             score_passes(LAST_PASS, n)
             store_scores(n)
 
@@ -367,11 +403,11 @@ def tile_list_chord_phase_voicings_kernel(tc, tab_words, tab_scales, offs, pos1,
             for n in range(2):
                 sin_product(TILES - 2 + n, bars, both_sines[:, n, :])
             if h == 0:
-                quantise_z(0, 0, "last_size0", [rounded_z[0, 0]])
+                quantise_z(0, 0, tagged_codes(HALF, "last_size0"), [made[3], made[4]])
                 score_passes(0, 0)
                 score_passes(1, 0)
             if h == 1:
-                quantise_z(1, 1, "last_size1", [gpsimd_quarter, vector_quarter])
+                quantise_z(1, 1, tagged_codes(HALF, "last_size1"), [made[9], vector_quarter])
                 score_passes(1, 1)
                 score_passes(1, 2)
             for n in range(2):

@@ -30,7 +30,7 @@ OUT_TILES = N // P
 PER_COLUMN = 16
 HALF = B // 2
 SLOTS = 5
-SLOT_BYTES = 5120
+SLOT_BYTES = 9216
 SECOND_HALF_AT = 19456
 SLOTS_AT = 29696
 
@@ -40,7 +40,6 @@ def tile_list_chord_phase_voicings_kernel(tc, tab_words, tab_scales, offs, pos1,
     nc = tc.nc
     with ExitStack() as ctx:
         keep = ctx.enter_context(tc.tile_pool(name="keep", bufs=1))
-        ring = ctx.enter_context(tc.tile_pool(name="ring", bufs=3))
         deep = ctx.enter_context(tc.tile_pool(name="deep", bufs=4))
         spot = ctx.enter_context(tc.tile_pool(name="spot", bufs=1))
         psum = ctx.enter_context(tc.psum_pool(name="psum", bufs=1))
@@ -85,6 +84,8 @@ def tile_list_chord_phase_voicings_kernel(tc, tab_words, tab_scales, offs, pos1,
         offs_sb = load_list("offs_sb", offs, S)
         tab_sb = spot.tile([P, T], I32, name="tab_sb", align_bytes=64, offset=0)
         nc.sync.dma_start(out=tab_sb[:], in_=tab_words[0].rearrange("p t i -> p (t i)").bitcast(I32))
+        low_of = load_list("low_of", pos3, B)
+        substitute_of = load_list("substitute_of", pos2, B)
         w1_halves = [load_w1(0, 0, None), load_w1(0, 1, SECOND_HALF_AT)]
         for q in range(4):
             nc.sync.dma_start(out=w4_plane_raw[:].bitcast(I32)[32 * q : 32 * q + 4 * PASSES, :],
@@ -129,8 +130,6 @@ def tile_list_chord_phase_voicings_kernel(tc, tab_words, tab_scales, offs, pos1,
         round_w1(0, 1, w1_halves[1], nc.scalar.copy, 0, P // 4)
         round_w1(0, 1, w1_halves[1], nc.vector.tensor_copy, P // 4, P // 2)
         w1_later = {1: load_w1_part(1, "first_tenant_tab_plane")}
-        low_of = load_list("low_of", pos3, B)
-        substitute_of = load_list("substitute_of", pos2, B)
         quantise_w1(0, 0, 1)
         quantise_w1(0, 1, 2)
         w4_plane_first = spot.tile([P, PASS], U8, name="w4_plane_first", align_bytes=64, offset=SECOND_HALF_AT + 1024)
@@ -149,8 +148,6 @@ def tile_list_chord_phase_voicings_kernel(tc, tab_words, tab_scales, offs, pos1,
         nc.vector.tensor_copy(w4_ordered[:].rearrange("p (g t m) -> p g t m", t=PACK, m=P), w4_unordered[:, 1:])
         for g in range(1, PASSES):
             w4_codes[g] = w4_ordered[:, (g - 1) * PASS : g * PASS]
-        low = spot.tile([P, 2 * PASS], BF16, name="w1_rounded1", align_bytes=64, offset=13312)
-        nc.gpsimd.tensor_copy(low[:].rearrange("p (t m j) -> p t m j", t=2, j=PACK), w1_later[1][:].rearrange("p j (m t) -> p t m j", t=PACK)[:, 0:2])
 
         def bank_tile(number):
             bank = psum.tile([P, BANK], F32, name="bank%d" % number)
@@ -164,7 +161,7 @@ def tile_list_chord_phase_voicings_kernel(tc, tab_words, tab_scales, offs, pos1,
 
         stationary = {t: (w1_codes[0][:, t * P : (t + 1) * P], w1_plane[0][:, t * P : (t + 1) * P]) for t in range(PACK)}
         angle = {}
-        last_angles = keep.tile([P, 2, B], F32, name="last_angles")
+        last_angles = keep.tile([P, B], F32, name="last_angles")
         colour = {}
         phase = {}
 
@@ -178,16 +175,21 @@ def tile_list_chord_phase_voicings_kernel(tc, tab_words, tab_scales, offs, pos1,
         phase_banks = {}
 
         def phase_sums(i):
-            phase_banks[i] = [first_stage(stationary[i][0].bitcast(FP8X4), stationary[i][1], h, 2 * (i % 2) + h) for h in range(2)]
+            phase_banks[i] = [first_stage(stationary[i][0].bitcast(FP8X4), stationary[i][1], h, (2 if i == 1 else 0 if i % 2 or i == 0 else 4) + h) for h in range(2)]
 
         def phase_half(i, h):
             if h == 0:
-                phase[i] = ring.tile([P, S], F32, name="phase")
-            nc.scalar.copy(phase[i][:, h * BANK : (h + 1) * BANK], phase_banks[i][h][:])
+                place = {0: slot(SLOTS - 1) + 5120, 1: 9216}.get(i, slot(i - 2) + 5120)
+                phase[i] = spot.tile([P, S], F32, name="phase%d" % i, align_bytes=64, offset=place)
+            copy = nc.vector.tensor_copy if i == 1 else nc.scalar.copy
+            copy(phase[i][:, h * BANK : (h + 1) * BANK], phase_banks[i][h][:])
 
         def pick_phase(i):
-            if i >= TILES - 2:
-                angle[i] = last_angles[:, i - (TILES - 2), :]
+            if i == LAST_TILE:
+                angle[i] = last_angles[:]
+            elif i == 3:
+                kept = keep.tile([P, B], F32, name="angle_kept", tag="angle_of3", align_bytes=64)
+                angle[i] = kept[:]
             else:
                 lone = deep.tile([P, B], F32, name="angle")
                 angle[i] = lone[:]
@@ -195,13 +197,13 @@ def tile_list_chord_phase_voicings_kernel(tc, tab_words, tab_scales, offs, pos1,
 
         def make_colour(i):
             if i < 2:
-                colour[i] = keep.tile([P, S], F32, name="colour%d" % i)
+                colour[i] = keep.tile([P, S], F32, name="colour%d" % i, align_bytes=64)
             else:
                 colour[i] = spot.tile([P, S], F32, name="colour%d" % i, align_bytes=64, offset=slot(i - 2))
             g, t = divmod(i, PACK)
             cols = slice(t * P, (t + 1) * P)
             for h in range(2):
-                bank = first_stage(w4_codes[g][:, cols].bitcast(FP4X4), w4_plane[g][:, cols], h, 4 + 2 * (i % 2) + h)
+                bank = first_stage(w4_codes[g][:, cols].bitcast(FP4X4), w4_plane[g][:, cols], h, 2 + h)
                 nc.vector.tensor_copy(colour[i][:, h * BANK : (h + 1) * BANK], bank[:])
 
         cos_terms = {}
@@ -211,13 +213,13 @@ def tile_list_chord_phase_voicings_kernel(tc, tab_words, tab_scales, offs, pos1,
         halves = [slice(h * HALF, (h + 1) * HALF) for h in range(2)]
         quarters = [slice(q * P, (q + 1) * P) for q in range(4)]
 
-        def last_sines(h, bars):
+        def last_sines(i, h, bars):
             width = bars.stop - bars.start
-            both_sines = keep.tile([P, 2, width], F32, name="last_sines%d" % h)
-            both_cosines = keep.tile([P, 2, width], F32, name="last_cosines%d" % h)
-            size = keep.tile([P, 2, width], F32, name="size", tag="last_size%d" % h, align_bytes=64)
-            nc.scalar.activation(both_sines[:], last_angles[:, :, bars], ACT.Sin)
-            nc.scalar.activation(size[:], last_angles[:, :, bars], ACT.Abs)
+            both_sines = keep.tile([P, width], F32, name="last_sines%d_%d" % (i, h))
+            both_cosines = keep.tile([P, width], F32, name="last_cosines%d_%d" % (i, h))
+            size = keep.tile([P, width], F32, name="size", tag="last_size%d_%d" % (i, h), align_bytes=64)
+            nc.scalar.activation(both_sines[:], angle[i][:, bars], ACT.Sin)
+            nc.scalar.activation(size[:], angle[i][:, bars], ACT.Abs)
             nc.scalar.activation(both_cosines[:], size[:], ACT.Sin, bias=half_pi[:], scale=-1.0)
             return both_sines, both_cosines
 
@@ -275,7 +277,7 @@ def tile_list_chord_phase_voicings_kernel(tc, tab_words, tab_scales, offs, pos1,
             return rounded
 
         def round_high(g, copy):
-            rounded = keep.tile([P, 2 * PASS], BF16, name="w1_high", align_bytes=64)
+            rounded = keep.tile([P, 2 * PASS], BF16, name="w1_high", tag="angle_of3", align_bytes=64)
             copy(rounded[:].rearrange("p (t m j) -> p m j t", t=2, j=PACK),
                  w1_later[g][:].rearrange("p j (m t) -> p m j t", t=PACK)[:, :, :, 2:4])
             return rounded
@@ -292,8 +294,11 @@ def tile_list_chord_phase_voicings_kernel(tc, tab_words, tab_scales, offs, pos1,
         phase_sums(1)
         phase_half(0, 0)
         phase_half(0, 1)
+        low = spot.tile([P, 2 * PASS], BF16, name="w1_rounded1", align_bytes=64, offset=13312)
+        nc.gpsimd.tensor_copy(low[:].rearrange("p (t m j) -> p t m j", t=2, j=PACK), w1_later[1][:].rearrange("p j (m t) -> p t m j", t=PACK)[:, 0:2])
+        phase_half(1, 0)
+        phase_half(1, 1)
         make_colour(0)
-        make_colour(1)
         for i in range(TILES - 2):
             g, t = divmod(i, PACK)
             if t == 0:
@@ -301,15 +306,17 @@ def tile_list_chord_phase_voicings_kernel(tc, tab_words, tab_scales, offs, pos1,
                 cos_terms[g] = keep.tile([P, PACK, B], F32, name="cos_terms", tag="cos_terms%d" % (g % 2))
             sine[i] = keep.tile([P, B], F32, name="sine", tag="sine_of%d" % i, align_bytes=64)
             cosine[i] = deep.tile([P, B], F32, name="cosine")
-            size = spot.tile([P, B], F32, name="size%d" % i, align_bytes=64, offset=slot(i) + 3072)
+            size = spot.tile([P, B], F32, name="size%d" % i, align_bytes=64, offset=slot(i) + 3584)
             phase_sums(i + 2)
             pick_phase(i)
-            phase_half(i + 1, 0)
+            if i > 0:
+                phase_half(i + 1, 0)
             nc.scalar.activation(sine[i][:], angle[i], ACT.Sin)
             nc.scalar.activation(size[:], angle[i], ACT.Abs)
-            phase_half(i + 1, 1)
+            if i > 0:
+                phase_half(i + 1, 1)
             nc.scalar.activation(cosine[i][:], size[:], ACT.Sin, bias=half_pi[:], scale=-1.0)
-            if i == 4:
+            if i == 3:
                 high = round_high(2, nc.vector.tensor_copy)
             sin_product(i, slice(0, B), sine[i][:])
             if t == PACK - 1:
@@ -317,19 +324,22 @@ def tile_list_chord_phase_voicings_kernel(tc, tab_words, tab_scales, offs, pos1,
                     cos_product(i, bars, cosine[i][:, bars])
             else:
                 cos_product(i, slice(0, B), cosine[i][:])
-            if i < 2:
-                made[i] = round_tile(1, 2 + i, nc.gpsimd.tensor_copy, after_sine(i))
-            elif i == 2:
-                made[i] = round_tile(2, 0, nc.gpsimd.tensor_copy, after_sine(i))
+            if i == 0:
+                made[i] = keep.tile([P, 2 * PASS], BF16, name="upper", tag="sine_of0", align_bytes=64)
+                nc.gpsimd.tensor_copy(made[i][:].rearrange("p (t m j) -> p t m j", t=2, j=PACK),
+                                      w1_later[1][:].rearrange("p j (m t) -> p t m j", t=PACK)[:, 2:4])
+                make_colour(1)
+            elif i < 3:
+                made[i] = round_tile(2, i - 1, nc.gpsimd.tensor_copy, after_sine(i))
             else:
                 made[i] = turn(nc.gpsimd, (i - 3) // PACK, quarters[(i - 3) % PACK], after_sine(i), 4)
             make_colour(i + 2)
             if i == 0:
                 quantise_pair(1, 0, held(i, [P, 2 * P], U32), [low])
-            if i == 2:
-                quantise_pair(1, 2, held(i, [P, 2 * P], U32), [made[0], made[1]])
+            if i == 1:
+                quantise_pair(1, 2, held(i, [P, 2 * P], U32), [made[0]])
             if i == 3:
-                second = round_tile(2, 1, nc.vector.tensor_copy, held(i, [P, PASS], BF16))
+                quantise_pair(2, 0, held(i, [P, 2 * P], U32), [made[1], made[2]])
                 w8_sb = keep.tile([P, PASSES, N], I32, name="w8_sb", tag="first_tenant_tab_plane", align_bytes=64)
                 nc.sync.dma_start(out=w8_sb[:], in_=w8_words.rearrange("a p c i -> p a (c i)").bitcast(I32))
                 w8_planes = spot.tile([P, N], U8, name="w8_planes", align_bytes=64, offset=14336)
@@ -338,7 +348,6 @@ def tile_list_chord_phase_voicings_kernel(tc, tab_words, tab_scales, offs, pos1,
                     nc.sync.dma_start(out=w8_planes[:].bitcast(I32)[32 * q : 32 * q + 4 * PASSES, :],
                                       in_=w8_scales[:, 4 * q : 4 * q + 4, :].bitcast(I32))
             if i == 4:
-                quantise_pair(2, 0, held(i, [P, 2 * P], U32), [made[2], second])
                 prior_sb = spot.tile([P, OUT_TILES], F32, name="prior_sb", align_bytes=64, offset=SECOND_HALF_AT + 2048)
                 with nc.allow_non_contiguous_dma(reason="one prior value for each output row"):
                     nc.sync.dma_start(out=prior_sb[:], in_=prior.rearrange("(c p) -> p c", p=P))
@@ -351,13 +360,21 @@ def tile_list_chord_phase_voicings_kernel(tc, tab_words, tab_scales, offs, pos1,
             if i == 9:
                 quantise_z(1, 0, held(i, [P, 2 * P], U32), [made[7], made[8]])
 
-        pick_phase(TILES - 2)
-        phase_half(TILES - 1, 0)
-        phase_half(TILES - 1, 1)
-        pick_phase(TILES - 1)
+        pick_phase(LAST_TILE - 1)
+        phase_half(LAST_TILE, 0)
+        trig = {(LAST_TILE - 1, 0): last_sines(LAST_TILE - 1, 0, halves[0])}
+        phase_half(LAST_TILE, 1)
+        pick_phase(LAST_TILE)
+        trig[LAST_TILE, 0] = last_sines(LAST_TILE, 0, halves[0])
+        trig[LAST_TILE - 1, 1] = last_sines(LAST_TILE - 1, 1, halves[1])
+        trig[LAST_TILE, 1] = last_sines(LAST_TILE, 1, halves[1])
+        picked = keep.tile([P, 2, HALF], F32, name="picked_colours")
+        entries = slice(HALF // PER_COLUMN, B // PER_COLUMN)
+        nc.scalar.activation(picked[:, 0, :], colour[LAST_TILE][:].indirect(low_of[:, entries]), ACT.Copy)
+        nc.scalar.activation(picked[:, 1, :], colour[LAST_TILE][:].indirect(substitute_of[:, entries]), ACT.Copy)
 
         groups = {0: [(0, 1), (2, 3), (4, 5)], 1: [(0, 1, 2), (3, 4, 5)], 2: [(0, 1, 2), (3, 4, 5)]}
-        bank_numbers = {0: (4, 5, 6), 1: (0, 1), 2: (2, 3)}
+        bank_numbers = {0: (4, 5, 2), 1: (6, 7), 2: (0, 1)}
         score_banks = {n: [bank_tile(number) for number in bank_numbers[n]] for n in range(len(pieces))}
 
         def score_passes(g, n):
@@ -378,7 +395,7 @@ def tile_list_chord_phase_voicings_kernel(tc, tab_words, tab_scales, offs, pos1,
                 count = len(members)
                 first = members[0]
                 result = keep.tile([P, count, width], F32, name="result%d_%d" % (n, first))
-                if n < 2 or first == 0:
+                if n < 2:
                     for place, c in enumerate(members):
                         nc.scalar.activation(result[:, place, :], bank[:, place * width : (place + 1) * width], ACT.Identity,
                                              bias=prior_sb[:, c : c + 1])
@@ -398,18 +415,20 @@ def tile_list_chord_phase_voicings_kernel(tc, tab_words, tab_scales, offs, pos1,
 
         score_passes(0, 1)
         score_passes(0, 2)
-        for h, bars in enumerate(pieces):
-            both_sines, both_cosines = last_sines(h, bars)
-            for n in range(2):
-                sin_product(TILES - 2 + n, bars, both_sines[:, n, :])
-            if h == 0:
-                quantise_z(0, 0, tagged_codes(HALF, "last_size0"), [made[3], made[4]])
-                score_passes(0, 0)
-                score_passes(1, 0)
-            if h == 1:
-                quantise_z(1, 1, tagged_codes(HALF, "last_size1"), [made[9], vector_quarter])
-                score_passes(1, 1)
-                score_passes(1, 2)
-            for n in range(2):
-                cos_product(TILES - 2 + n, bars, both_cosines[:, n, :])
-            close_piece(h)
+        sin_product(LAST_TILE - 1, halves[0], trig[LAST_TILE - 1, 0][0][:])
+        cos_product(LAST_TILE - 1, halves[0], trig[LAST_TILE - 1, 0][1][:])
+        quantise_z(0, 0, tagged_codes(HALF, "last_size%d_0" % (LAST_TILE - 1)), [made[3], made[4]])
+        score_passes(0, 0)
+        score_passes(1, 0)
+        sin_product(LAST_TILE, halves[0], trig[LAST_TILE, 0][0][:])
+        cos_product(LAST_TILE, halves[0], trig[LAST_TILE, 0][1][:])
+        close_piece(0)
+        sin_product(LAST_TILE - 1, halves[1], trig[LAST_TILE - 1, 1][0][:])
+        cos_product(LAST_TILE - 1, halves[1], trig[LAST_TILE - 1, 1][1][:])
+        quantise_z(1, 1, tagged_codes(HALF, "last_size%d_1" % LAST_TILE), [made[9], vector_quarter])
+        score_passes(1, 1)
+        score_passes(1, 2)
+        nc.vector.tensor_tensor(sin_terms[LAST_PASS][:, PACK - 1, halves[1]], picked[:, 0, :], trig[LAST_TILE, 1][0][:], ALU.mult)
+        nc.vector.tensor_tensor(cos_terms[LAST_PASS][:, PACK - 1, halves[1]], picked[:, 1, :], trig[LAST_TILE, 1][1][:], ALU.mult)
+        close_piece(1)
+        close_piece(2)

@@ -29,10 +29,11 @@ LAST_PASS = PASSES - 1
 OUT_TILES = N // P
 PER_COLUMN = 16
 HALF = B // 2
-SLOTS = 5
 SLOT_BYTES = 9216
 SECOND_HALF_AT = 19456
-SLOTS_AT = 29696
+AREAS_AT = 29696
+SIZES_AT = AREAS_AT + 3 * 4096
+SLOTS_AT = SIZES_AT + 4 * 2048
 
 
 def tile_list_chord_phase_voicings_kernel(tc, tab_words, tab_scales, offs, pos1, pos2, pos3, w1, w4_words,
@@ -161,49 +162,47 @@ def tile_list_chord_phase_voicings_kernel(tc, tab_words, tab_scales, offs, pos1,
 
         stationary = {t: (w1_codes[0][:, t * P : (t + 1) * P], w1_plane[0][:, t * P : (t + 1) * P]) for t in range(PACK)}
         angle = {}
-        last_angles = keep.tile([P, B], F32, name="last_angles")
         colour = {}
         phase = {}
 
-        def slot(i):
-            return SLOTS_AT + (i % SLOTS) * SLOT_BYTES
+        def size_at(i):
+            if i == TILES - 3:
+                return SLOTS_AT + 3 * SLOT_BYTES + 3584
+            if i % 2:
+                return SIZES_AT + (i // 2) * 2048
+            return SLOTS_AT + (i // 2 % 3) * SLOT_BYTES + 3584
 
         def held(i, shape, dtype):
-            tile = spot.tile(shape, dtype, name="held%d" % i, align_bytes=64, offset=slot(i) + 4096)
+            tile = spot.tile(shape, dtype, name="held%d" % i, align_bytes=64, offset=size_at(i) + (0 if i == 3 else 512))
             return tile
 
         phase_banks = {}
 
         def phase_sums(i):
-            phase_banks[i] = [first_stage(stationary[i][0].bitcast(FP8X4), stationary[i][1], h, (2 if i == 1 else 0 if i % 2 or i == 0 else 4) + h) for h in range(2)]
+            phase_banks[i] = [first_stage(stationary[i][0].bitcast(FP8X4), stationary[i][1], h, (0, 2, 4, 0, 6, 2, 0, 4, 6, 2, 0, 4)[i] + h) for h in range(2)]
 
         def phase_half(i, h):
             if h == 0:
-                place = {0: slot(SLOTS - 1) + 5120, 1: 9216}.get(i, slot(i - 2) + 5120)
+                place = 9216 if i == 1 else AREAS_AT + (i % 3) * 4096
                 phase[i] = spot.tile([P, S], F32, name="phase%d" % i, align_bytes=64, offset=place)
             copy = nc.vector.tensor_copy if i == 1 else nc.scalar.copy
             copy(phase[i][:, h * BANK : (h + 1) * BANK], phase_banks[i][h][:])
 
         def pick_phase(i):
-            if i == LAST_TILE:
-                angle[i] = last_angles[:]
-            elif i == 3:
-                kept = keep.tile([P, B], F32, name="angle_kept", tag="angle_of3", align_bytes=64)
-                angle[i] = kept[:]
-            else:
-                lone = deep.tile([P, B], F32, name="angle")
-                angle[i] = lone[:]
+            picked_angles = spot.tile([P, B], F32, name="angle%d" % i, align_bytes=64, offset=AREAS_AT + ((i + 2) % 3) * 4096)
+            angle[i] = picked_angles[:]
             nc.scalar.activation(angle[i], phase[i][:].indirect(current_of[:]), ACT.Copy)
 
         def make_colour(i):
-            if i < 2:
+            if i == 0:
                 colour[i] = keep.tile([P, S], F32, name="colour%d" % i, align_bytes=64)
             else:
-                colour[i] = spot.tile([P, S], F32, name="colour%d" % i, align_bytes=64, offset=slot(i - 2))
+                place = size_at(i - 2) + 1536 if i % 2 == 0 else size_at(i - 1 if i < LAST_TILE else i - 2) - 3584
+                colour[i] = spot.tile([P, S], F32, name="colour%d" % i, align_bytes=64, offset=place)
             g, t = divmod(i, PACK)
             cols = slice(t * P, (t + 1) * P)
             for h in range(2):
-                bank = first_stage(w4_codes[g][:, cols].bitcast(FP4X4), w4_plane[g][:, cols], h, 2 + h)
+                bank = first_stage(w4_codes[g][:, cols].bitcast(FP4X4), w4_plane[g][:, cols], h, (2, 2, 4, 0, 4, 6, 2, 0, 4, 6, 2, 0)[i] + h)
                 nc.vector.tensor_copy(colour[i][:, h * BANK : (h + 1) * BANK], bank[:])
 
         cos_terms = {}
@@ -241,8 +240,8 @@ def tile_list_chord_phase_voicings_kernel(tc, tab_words, tab_scales, offs, pos1,
                                  sin_terms[g][:, :, bars].rearrange("p t (c i) -> p c t i", i=run), ALU.subtract)
             return rounded
 
-        def after_sine(i):
-            tile = keep.tile([P, PASS], BF16, name="after_sine", tag="sine_of%d" % i, align_bytes=64)
+        def after_sine(i, width):
+            tile = keep.tile([P, width * PACK], BF16, name="after_sine", tag="sine_of%d" % i, align_bytes=64)
             return tile
 
         pieces = [slice(0, HALF), slice(HALF, HALF + P), slice(HALF + P, B)]
@@ -272,12 +271,12 @@ def tile_list_chord_phase_voicings_kernel(tc, tab_words, tab_scales, offs, pos1,
             codes = keep.tile([P, width], U32, name="z_codes", tag=tag, align_bytes=64)
             return codes
 
-        def round_tile(g, t, copy, rounded):
-            copy(rounded[:].rearrange("p (m j) -> p m j", j=PACK), w1_later[g][:].rearrange("p j (m t) -> p t m j", t=PACK)[:, t])
+        def round_pair(g, first, rounded):
+            nc.gpsimd.tensor_copy(rounded[:].rearrange("p (t m j) -> p t m j", t=2, j=PACK),
+                                  w1_later[g][:].rearrange("p j (m t) -> p t m j", t=PACK)[:, first : first + 2])
             return rounded
 
-        def round_high(g, copy):
-            rounded = keep.tile([P, 2 * PASS], BF16, name="w1_high", tag="angle_of3", align_bytes=64)
+        def round_high(g, copy, rounded):
             copy(rounded[:].rearrange("p (t m j) -> p m j t", t=2, j=PACK),
                  w1_later[g][:].rearrange("p j (m t) -> p m j t", t=PACK)[:, :, :, 2:4])
             return rounded
@@ -295,7 +294,8 @@ def tile_list_chord_phase_voicings_kernel(tc, tab_words, tab_scales, offs, pos1,
         phase_half(0, 0)
         phase_half(0, 1)
         low = spot.tile([P, 2 * PASS], BF16, name="w1_rounded1", align_bytes=64, offset=13312)
-        nc.gpsimd.tensor_copy(low[:].rearrange("p (t m j) -> p t m j", t=2, j=PACK), w1_later[1][:].rearrange("p j (m t) -> p t m j", t=PACK)[:, 0:2])
+        round_pair(1, 0, low)
+        phase_sums(2)
         phase_half(1, 0)
         phase_half(1, 1)
         make_colour(0)
@@ -306,40 +306,35 @@ def tile_list_chord_phase_voicings_kernel(tc, tab_words, tab_scales, offs, pos1,
                 cos_terms[g] = keep.tile([P, PACK, B], F32, name="cos_terms", tag="cos_terms%d" % (g % 2))
             sine[i] = keep.tile([P, B], F32, name="sine", tag="sine_of%d" % i, align_bytes=64)
             cosine[i] = deep.tile([P, B], F32, name="cosine")
-            size = spot.tile([P, B], F32, name="size%d" % i, align_bytes=64, offset=slot(i) + 3584)
-            phase_sums(i + 2)
+            size = spot.tile([P, B], F32, name="size%d" % i, align_bytes=64, offset=size_at(i))
             pick_phase(i)
             if i > 0:
-                phase_half(i + 1, 0)
-            nc.scalar.activation(sine[i][:], angle[i], ACT.Sin)
-            nc.scalar.activation(size[:], angle[i], ACT.Abs)
-            if i > 0:
                 phase_half(i + 1, 1)
+                phase_sums(i + 2)
+            nc.scalar.activation(size[:], angle[i], ACT.Abs)
+            nc.scalar.activation(sine[i][:], angle[i], ACT.Sin)
             nc.scalar.activation(cosine[i][:], size[:], ACT.Sin, bias=half_pi[:], scale=-1.0)
-            if i == 3:
-                high = round_high(2, nc.vector.tensor_copy)
+            phase_half(i + 2, 0)
             sin_product(i, slice(0, B), sine[i][:])
-            if t == PACK - 1:
-                for bars in halves:
-                    cos_product(i, bars, cosine[i][:, bars])
-            else:
-                cos_product(i, slice(0, B), cosine[i][:])
+            cos_product(i, slice(0, B), cosine[i][:])
             if i == 0:
-                made[i] = keep.tile([P, 2 * PASS], BF16, name="upper", tag="sine_of0", align_bytes=64)
-                nc.gpsimd.tensor_copy(made[i][:].rearrange("p (t m j) -> p t m j", t=2, j=PACK),
-                                      w1_later[1][:].rearrange("p j (m t) -> p t m j", t=PACK)[:, 2:4])
-                make_colour(1)
-            elif i < 3:
-                made[i] = round_tile(2, i - 1, nc.gpsimd.tensor_copy, after_sine(i))
-            else:
-                made[i] = turn(nc.gpsimd, (i - 3) // PACK, quarters[(i - 3) % PACK], after_sine(i), 4)
-            make_colour(i + 2)
+                made[i] = round_pair(1, 2, after_sine(i, HALF))
+            if i == 2:
+                made[i] = round_pair(2, 0, after_sine(i, HALF))
+            if i in (4, 6, 8):
+                made[i] = turn(nc.gpsimd, (i - 4) // PACK, halves[i // 2 % 2], after_sine(i, HALF), 4)
+            if i == 9:
+                made[i] = turn(nc.gpsimd, 1, quarters[2], after_sine(i, P), 4)
+            if i % 2 == 0:
+                make_colour(i + 1)
+            if i % 2 == 0 or i == 9:
+                make_colour(i + 2)
             if i == 0:
                 quantise_pair(1, 0, held(i, [P, 2 * P], U32), [low])
             if i == 1:
                 quantise_pair(1, 2, held(i, [P, 2 * P], U32), [made[0]])
             if i == 3:
-                quantise_pair(2, 0, held(i, [P, 2 * P], U32), [made[1], made[2]])
+                high = round_high(2, nc.vector.tensor_copy, held(i, [P, 2 * PASS], BF16))
                 w8_sb = keep.tile([P, PASSES, N], I32, name="w8_sb", tag="first_tenant_tab_plane", align_bytes=64)
                 nc.sync.dma_start(out=w8_sb[:], in_=w8_words.rearrange("a p c i -> p a (c i)").bitcast(I32))
                 w8_planes = spot.tile([P, N], U8, name="w8_planes", align_bytes=64, offset=14336)
@@ -348,22 +343,22 @@ def tile_list_chord_phase_voicings_kernel(tc, tab_words, tab_scales, offs, pos1,
                     nc.sync.dma_start(out=w8_planes[:].bitcast(I32)[32 * q : 32 * q + 4 * PASSES, :],
                                       in_=w8_scales[:, 4 * q : 4 * q + 4, :].bitcast(I32))
             if i == 4:
+                quantise_pair(2, 0, held(i, [P, 2 * P], U32), [made[2]])
                 prior_sb = spot.tile([P, OUT_TILES], F32, name="prior_sb", align_bytes=64, offset=SECOND_HALF_AT + 2048)
                 with nc.allow_non_contiguous_dma(reason="one prior value for each output row"):
                     nc.sync.dma_start(out=prior_sb[:], in_=prior.rearrange("(c p) -> p c", p=P))
             if i == 5:
                 quantise_pair(2, 2, held(i, [P, 2 * P], U32), [high])
             if i == 7:
-                quantise_z(0, 1, held(i, [P, 2 * P], U32), [made[5], made[6]])
+                quantise_z(0, 1, held(i, [P, 2 * P], U32), [made[6]])
             if i == 8:
                 vector_quarter = turn(nc.vector, 1, quarters[3], held(i, [P, PASS], BF16), 2)
             if i == 9:
-                quantise_z(1, 0, held(i, [P, 2 * P], U32), [made[7], made[8]])
+                quantise_z(1, 0, held(i, [P, 2 * P], U32), [made[8]])
 
         pick_phase(LAST_TILE - 1)
-        phase_half(LAST_TILE, 0)
-        trig = {(LAST_TILE - 1, 0): last_sines(LAST_TILE - 1, 0, halves[0])}
         phase_half(LAST_TILE, 1)
+        trig = {(LAST_TILE - 1, 0): last_sines(LAST_TILE - 1, 0, halves[0])}
         pick_phase(LAST_TILE)
         trig[LAST_TILE, 0] = last_sines(LAST_TILE, 0, halves[0])
         trig[LAST_TILE - 1, 1] = last_sines(LAST_TILE - 1, 1, halves[1])
@@ -374,7 +369,7 @@ def tile_list_chord_phase_voicings_kernel(tc, tab_words, tab_scales, offs, pos1,
         nc.scalar.activation(picked[:, 1, :], colour[LAST_TILE][:].indirect(substitute_of[:, entries]), ACT.Copy)
 
         groups = {0: [(0, 1), (2, 3), (4, 5)], 1: [(0, 1, 2), (3, 4, 5)], 2: [(0, 1, 2), (3, 4, 5)]}
-        bank_numbers = {0: (4, 5, 2), 1: (6, 7), 2: (0, 1)}
+        bank_numbers = {0: (4, 5, 0), 1: (6, 7), 2: (2, 3)}
         score_banks = {n: [bank_tile(number) for number in bank_numbers[n]] for n in range(len(pieces))}
 
         def score_passes(g, n):
@@ -407,7 +402,8 @@ def tile_list_chord_phase_voicings_kernel(tc, tab_words, tab_scales, offs, pos1,
 
         def close_piece(n):
             width = pieces[n].stop - pieces[n].start
-            rounded = keep.tile([P, width * PACK], BF16, name="rounded_last%d" % n, align_bytes=64)
+            tag = "last_size%d_1" % (LAST_TILE - 1) if n == 0 else "rounded_last%d" % n
+            rounded = keep.tile([P, width * PACK], BF16, name="rounded_last", tag=tag, align_bytes=64)
             turn(nc.vector, LAST_PASS, pieces[n], rounded, 2)
             quantise_z(LAST_PASS, n, tagged_codes(width, "last_z_codes%d" % n), [rounded])
             score_passes(LAST_PASS, n)
@@ -417,18 +413,19 @@ def tile_list_chord_phase_voicings_kernel(tc, tab_words, tab_scales, offs, pos1,
         score_passes(0, 2)
         sin_product(LAST_TILE - 1, halves[0], trig[LAST_TILE - 1, 0][0][:])
         cos_product(LAST_TILE - 1, halves[0], trig[LAST_TILE - 1, 0][1][:])
-        quantise_z(0, 0, tagged_codes(HALF, "last_size%d_0" % (LAST_TILE - 1)), [made[3], made[4]])
+        quantise_z(0, 0, tagged_codes(HALF, "last_size%d_0" % (LAST_TILE - 1)), [made[4]])
         score_passes(0, 0)
         score_passes(1, 0)
         sin_product(LAST_TILE, halves[0], trig[LAST_TILE, 0][0][:])
         cos_product(LAST_TILE, halves[0], trig[LAST_TILE, 0][1][:])
-        close_piece(0)
         sin_product(LAST_TILE - 1, halves[1], trig[LAST_TILE - 1, 1][0][:])
+        close_piece(0)
         cos_product(LAST_TILE - 1, halves[1], trig[LAST_TILE - 1, 1][1][:])
-        quantise_z(1, 1, tagged_codes(HALF, "last_size%d_1" % LAST_TILE), [made[9], vector_quarter])
-        score_passes(1, 1)
-        score_passes(1, 2)
         nc.vector.tensor_tensor(sin_terms[LAST_PASS][:, PACK - 1, halves[1]], picked[:, 0, :], trig[LAST_TILE, 1][0][:], ALU.mult)
         nc.vector.tensor_tensor(cos_terms[LAST_PASS][:, PACK - 1, halves[1]], picked[:, 1, :], trig[LAST_TILE, 1][1][:], ALU.mult)
+        late_codes = spot.tile([P, HALF], U32, name="late_codes", align_bytes=64, offset=size_at(TILES - 3) - 3584)
+        quantise_z(1, 1, late_codes, [made[9], vector_quarter])
+        score_passes(1, 1)
+        score_passes(1, 2)
         close_piece(1)
         close_piece(2)

@@ -33,7 +33,7 @@ SLOT_BYTES = 9216
 SECOND_HALF_AT = 19456
 AREAS_AT = 29696
 SIZES_AT = AREAS_AT + 3 * 4096
-SLOTS_AT = SIZES_AT + 4 * 2048
+SLOTS_AT = SIZES_AT + 5 * 2048
 
 
 def tile_list_chord_phase_voicings_kernel(tc, tab_words, tab_scales, offs, pos1, pos2, pos3, w1, w4_words,
@@ -166,14 +166,12 @@ def tile_list_chord_phase_voicings_kernel(tc, tab_words, tab_scales, offs, pos1,
         phase = {}
 
         def size_at(i):
-            if i == TILES - 3:
-                return SLOTS_AT + 3 * SLOT_BYTES + 3584
             if i % 2:
                 return SIZES_AT + (i // 2) * 2048
             return SLOTS_AT + (i // 2 % 3) * SLOT_BYTES + 3584
 
         def held(i, shape, dtype):
-            tile = spot.tile(shape, dtype, name="held%d" % i, align_bytes=64, offset=size_at(i) + (0 if i == 3 else 512))
+            tile = spot.tile(shape, dtype, name="held%d" % i, align_bytes=64, offset=size_at(i) + (0 if i in (5, 9) else 512))
             return tile
 
         phase_banks = {}
@@ -194,16 +192,17 @@ def tile_list_chord_phase_voicings_kernel(tc, tab_words, tab_scales, offs, pos1,
             nc.scalar.activation(angle[i], phase[i][:].indirect(current_of[:]), ACT.Copy)
 
         def make_colour(i):
-            if i == 0:
-                colour[i] = keep.tile([P, S], F32, name="colour%d" % i, align_bytes=64)
+            if i in (0, LAST_TILE):
+                colour[i] = keep.tile([P, S], F32, name="colour", tag="colour%d" % i, align_bytes=64)
             else:
-                place = size_at(i - 2) + 1536 if i % 2 == 0 else size_at(i - 1 if i < LAST_TILE else i - 2) - 3584
+                place = size_at(i - 2) + 1536 if i % 2 == 0 else size_at(i - 1) - 3584
                 colour[i] = spot.tile([P, S], F32, name="colour%d" % i, align_bytes=64, offset=place)
             g, t = divmod(i, PACK)
             cols = slice(t * P, (t + 1) * P)
             for h in range(2):
                 bank = first_stage(w4_codes[g][:, cols].bitcast(FP4X4), w4_plane[g][:, cols], h, (2, 2, 4, 0, 4, 6, 2, 0, 4, 6, 2, 0)[i] + h)
-                nc.vector.tensor_copy(colour[i][:, h * BANK : (h + 1) * BANK], bank[:])
+                copy = nc.scalar.copy if i == LAST_TILE else nc.vector.tensor_copy
+                copy(colour[i][:, h * BANK : (h + 1) * BANK], bank[:])
 
         cos_terms = {}
         sin_terms = {}
@@ -315,6 +314,8 @@ def tile_list_chord_phase_voicings_kernel(tc, tab_words, tab_scales, offs, pos1,
             nc.scalar.activation(sine[i][:], angle[i], ACT.Sin)
             nc.scalar.activation(cosine[i][:], size[:], ACT.Sin, bias=half_pi[:], scale=-1.0)
             phase_half(i + 2, 0)
+            if i == 5:
+                high = round_high(2, nc.scalar.copy, held(i, [P, 2 * PASS], BF16))
             sin_product(i, slice(0, B), sine[i][:])
             cos_product(i, slice(0, B), cosine[i][:])
             if i == 0:
@@ -323,18 +324,15 @@ def tile_list_chord_phase_voicings_kernel(tc, tab_words, tab_scales, offs, pos1,
                 made[i] = round_pair(2, 0, after_sine(i, HALF))
             if i in (4, 6, 8):
                 made[i] = turn(nc.gpsimd, (i - 4) // PACK, halves[i // 2 % 2], after_sine(i, HALF), 4)
-            if i == 9:
-                made[i] = turn(nc.gpsimd, 1, quarters[2], after_sine(i, P), 4)
             if i % 2 == 0:
                 make_colour(i + 1)
-            if i % 2 == 0 or i == 9:
+            if i % 2 == 0:
                 make_colour(i + 2)
             if i == 0:
                 quantise_pair(1, 0, held(i, [P, 2 * P], U32), [low])
             if i == 1:
                 quantise_pair(1, 2, held(i, [P, 2 * P], U32), [made[0]])
             if i == 3:
-                high = round_high(2, nc.vector.tensor_copy, held(i, [P, 2 * PASS], BF16))
                 w8_sb = keep.tile([P, PASSES, N], I32, name="w8_sb", tag="first_tenant_tab_plane", align_bytes=64)
                 nc.sync.dma_start(out=w8_sb[:], in_=w8_words.rearrange("a p c i -> p a (c i)").bitcast(I32))
                 w8_planes = spot.tile([P, N], U8, name="w8_planes", align_bytes=64, offset=14336)
@@ -347,18 +345,17 @@ def tile_list_chord_phase_voicings_kernel(tc, tab_words, tab_scales, offs, pos1,
                 prior_sb = spot.tile([P, OUT_TILES], F32, name="prior_sb", align_bytes=64, offset=SECOND_HALF_AT + 2048)
                 with nc.allow_non_contiguous_dma(reason="one prior value for each output row"):
                     nc.sync.dma_start(out=prior_sb[:], in_=prior.rearrange("(c p) -> p c", p=P))
-            if i == 5:
+            if i == 6:
                 quantise_pair(2, 2, held(i, [P, 2 * P], U32), [high])
             if i == 7:
                 quantise_z(0, 1, held(i, [P, 2 * P], U32), [made[6]])
-            if i == 8:
-                vector_quarter = turn(nc.vector, 1, quarters[3], held(i, [P, PASS], BF16), 2)
             if i == 9:
-                quantise_z(1, 0, held(i, [P, 2 * P], U32), [made[8]])
+                made[i] = turn(nc.vector, 1, halves[1], held(i, [P, 2 * PASS], BF16), 2)
 
         pick_phase(LAST_TILE - 1)
         phase_half(LAST_TILE, 1)
         trig = {(LAST_TILE - 1, 0): last_sines(LAST_TILE - 1, 0, halves[0])}
+        make_colour(LAST_TILE)
         pick_phase(LAST_TILE)
         trig[LAST_TILE, 0] = last_sines(LAST_TILE, 0, halves[0])
         trig[LAST_TILE - 1, 1] = last_sines(LAST_TILE - 1, 1, halves[1])
@@ -415,16 +412,17 @@ def tile_list_chord_phase_voicings_kernel(tc, tab_words, tab_scales, offs, pos1,
         cos_product(LAST_TILE - 1, halves[0], trig[LAST_TILE - 1, 0][1][:])
         quantise_z(0, 0, tagged_codes(HALF, "last_size%d_0" % (LAST_TILE - 1)), [made[4]])
         score_passes(0, 0)
-        score_passes(1, 0)
         sin_product(LAST_TILE, halves[0], trig[LAST_TILE, 0][0][:])
         cos_product(LAST_TILE, halves[0], trig[LAST_TILE, 0][1][:])
+        quantise_z(1, 0, tagged_codes(HALF, "last_size%d_0" % LAST_TILE), [made[8]])
+        score_passes(1, 0)
         sin_product(LAST_TILE - 1, halves[1], trig[LAST_TILE - 1, 1][0][:])
         close_piece(0)
         cos_product(LAST_TILE - 1, halves[1], trig[LAST_TILE - 1, 1][1][:])
         nc.vector.tensor_tensor(sin_terms[LAST_PASS][:, PACK - 1, halves[1]], picked[:, 0, :], trig[LAST_TILE, 1][0][:], ALU.mult)
         nc.vector.tensor_tensor(cos_terms[LAST_PASS][:, PACK - 1, halves[1]], picked[:, 1, :], trig[LAST_TILE, 1][1][:], ALU.mult)
-        late_codes = spot.tile([P, HALF], U32, name="late_codes", align_bytes=64, offset=size_at(TILES - 3) - 3584)
-        quantise_z(1, 1, late_codes, [made[9], vector_quarter])
+        late_codes = tagged_codes(HALF, "colour%d" % LAST_TILE)
+        quantise_z(1, 1, late_codes, [made[9]])
         score_passes(1, 1)
         score_passes(1, 2)
         close_piece(1)

@@ -171,7 +171,7 @@ def tile_list_chord_phase_voicings_kernel(tc, tab_words, tab_scales, offs, pos1,
             return SLOTS_AT + (i // 2 % 3) * SLOT_BYTES + 3584
 
         def held(i, shape, dtype):
-            tile = spot.tile(shape, dtype, name="held%d" % i, align_bytes=64, offset=size_at(i) + (0 if i in (5, 9) else 512))
+            tile = spot.tile(shape, dtype, name="held%d" % i, align_bytes=64, offset=size_at(i) + (0 if i in (3, 9) else 512))
             return tile
 
         phase_banks = {}
@@ -314,8 +314,6 @@ def tile_list_chord_phase_voicings_kernel(tc, tab_words, tab_scales, offs, pos1,
             nc.scalar.activation(sine[i][:], angle[i], ACT.Sin)
             nc.scalar.activation(cosine[i][:], size[:], ACT.Sin, bias=half_pi[:], scale=-1.0)
             phase_half(i + 2, 0)
-            if i == 5:
-                high = round_high(2, nc.scalar.copy, held(i, [P, 2 * PASS], BF16))
             sin_product(i, slice(0, B), sine[i][:])
             cos_product(i, slice(0, B), cosine[i][:])
             if i == 0:
@@ -333,6 +331,7 @@ def tile_list_chord_phase_voicings_kernel(tc, tab_words, tab_scales, offs, pos1,
             if i == 1:
                 quantise_pair(1, 2, held(i, [P, 2 * P], U32), [made[0]])
             if i == 3:
+                high = round_high(2, nc.vector.tensor_copy, held(i, [P, 2 * PASS], BF16))
                 w8_sb = keep.tile([P, PASSES, N], I32, name="w8_sb", tag="first_tenant_tab_plane", align_bytes=64)
                 nc.sync.dma_start(out=w8_sb[:], in_=w8_words.rearrange("a p c i -> p a (c i)").bitcast(I32))
                 w8_planes = spot.tile([P, N], U8, name="w8_planes", align_bytes=64, offset=14336)
@@ -345,7 +344,7 @@ def tile_list_chord_phase_voicings_kernel(tc, tab_words, tab_scales, offs, pos1,
                 prior_sb = spot.tile([P, OUT_TILES], F32, name="prior_sb", align_bytes=64, offset=SECOND_HALF_AT + 2048)
                 with nc.allow_non_contiguous_dma(reason="one prior value for each output row"):
                     nc.sync.dma_start(out=prior_sb[:], in_=prior.rearrange("(c p) -> p c", p=P))
-            if i == 6:
+            if i == 5:
                 quantise_pair(2, 2, held(i, [P, 2 * P], U32), [high])
             if i == 7:
                 quantise_z(0, 1, held(i, [P, 2 * P], U32), [made[6]])

@@ -20,7 +20,7 @@ ALU = mybir.AluOpType
 P = 128
 PACK = 4
 BANK = 512
-BANKS = 8
+QUADRANT = 32
 PASS = P * PACK
 PASSES = H // PASS
 TILES = H // P
@@ -29,26 +29,50 @@ LAST_PASS = PASSES - 1
 OUT_TILES = N // P
 PER_COLUMN = 16
 HALF = B // 2
-SLOT_BYTES = 9216
-SECOND_HALF_AT = 19456
-AREAS_AT = 29696
-SIZES_AT = AREAS_AT + 3 * 4096
-SLOTS_AT = SIZES_AT + 5 * 2048
+COSINES_AHEAD = 4
+
+ROW_BYTES = 4 * S
+PICK_BYTES = 4 * B
+TABLE_AT = 0
+W1_FIRST_HALF_AT = TABLE_AT + 4 * T
+W4_WORDS_AT = W1_FIRST_HALF_AT + ROW_BYTES
+W1_ROUNDED_AT = W4_WORDS_AT + 2 * H
+W1_SECOND_HALF_AT = W1_ROUNDED_AT + 2 * PACK * PASS
+W1_LAST_PART_AT = W1_SECOND_HALF_AT + PICK_BYTES
+AREAS_AT = W1_LAST_PART_AT + 4 * PACK * PASS
+SIZES_AT = AREAS_AT + 3 * ROW_BYTES
+SLOTS_AT = SIZES_AT + (TILES - 2) * PICK_BYTES
+SLOT_GAP = 1024
+SLOT_BYTES = 2 * ROW_BYTES + SLOT_GAP
+
+WINDOWS = {0: (1, 2, 3, 4), 4: (5, 6, 7, 8), 8: (9, 10)}
+EARLY_PHASE = 1
+WINDOW_PHASE = 5
+PHASE_BANKS = (0, 2, 4, 0, 6, 2, 0, 4, 0, 4, 0, 4)
+COLOUR_BANKS = (2, 2, 4, 2, 4, 6, 2, 6, 2, 6, 2, 0)
 
 
 def tile_list_chord_phase_voicings_kernel(tc, tab_words, tab_scales, offs, pos1, pos2, pos3, w1, w4_words,
-                                                    w4_scales, w8_words, w8_scales, prior, out):
+                                                       w4_scales, w8_words, w8_scales, prior, out):
     nc = tc.nc
     with ExitStack() as ctx:
         keep = ctx.enter_context(tc.tile_pool(name="keep", bufs=1))
-        deep = ctx.enter_context(tc.tile_pool(name="deep", bufs=4))
+        deep = ctx.enter_context(tc.tile_pool(name="deep", bufs=COSINES_AHEAD))
         spot = ctx.enter_context(tc.tile_pool(name="spot", bufs=1))
         psum = ctx.enter_context(tc.psum_pool(name="psum", bufs=1))
 
-        tab_plane = keep.tile([P, T], U8, name="tab_plane", tag="first_tenant_tab_plane", align_bytes=64)
-        for q in range(4):
-            nc.sync.dma_start(out=tab_plane[:].bitcast(I32)[32 * q : 32 * q + 32, :],
-                              in_=tab_scales[0][4 * q : 4 * q + 4, :].bitcast(I32).partition_broadcast(8))
+        def placed(name, shape, dtype, offset):
+            tile = spot.tile(shape, dtype, name=name, align_bytes=64, offset=offset)
+            return tile
+
+        def tagged(tag, shape, dtype):
+            tile = keep.tile(shape, dtype, name="tagged", tag=tag, align_bytes=64)
+            return tile
+
+        tab_plane = tagged("table_plane_first", [P, T], U8)
+        for q in range(P // QUADRANT):
+            nc.sync.dma_start(out=tab_plane[:].bitcast(I32)[QUADRANT * q : QUADRANT * (q + 1), :],
+                              in_=tab_scales[0][4 * q : 4 * q + 4, :].bitcast(I32).partition_broadcast(QUADRANT // 4))
         w4_plane_raw = keep.tile([P, PASS], U8, name="w4_plane_raw", align_bytes=64)
         w4_planes_later = keep.tile([P, LAST_PASS * PASS], U8, name="w4_planes_later", align_bytes=64)
         zero = keep.tile([P, 1], F32, name="zero")
@@ -68,57 +92,38 @@ def tile_list_chord_phase_voicings_kernel(tc, tab_words, tab_scales, offs, pos1,
 
         w1_rows = w1.rearrange("(p j) r -> p j r", j=PACK)
 
-        def load_w1(g, h, tag):
-            if tag is None:
-                raw = spot.tile([P, PACK, PASS // 2], F32, name="w1_raw%d" % g, align_bytes=64, offset=8192)
-            else:
-                raw = spot.tile([P, PACK, PASS // 2], F32, name="w1_raw_b", align_bytes=64, offset=tag)
-            first = g * PASS + h * PASS // 2
-            nc.sync.dma_start(out=raw[:], in_=w1_rows[:, :, first : first + PASS // 2])
-            return raw
-
-        def load_w1_part(g, tag):
-            raw = keep.tile([P, PACK, PASS], F32, name="w1_part", tag=tag, align_bytes=64)
-            nc.sync.dma_start(out=raw[:], in_=w1_rows[:, :, g * PASS : (g + 1) * PASS])
+        def load_w1(raw, first):
+            nc.sync.dma_start(out=raw[:], in_=w1_rows[:, :, first : first + raw.shape[2]])
             return raw
 
         offs_sb = load_list("offs_sb", offs, S)
-        tab_sb = spot.tile([P, T], I32, name="tab_sb", align_bytes=64, offset=0)
+        tab_sb = placed("tab_sb", [P, T], I32, TABLE_AT)
         nc.sync.dma_start(out=tab_sb[:], in_=tab_words[0].rearrange("p t i -> p (t i)").bitcast(I32))
-        low_of = load_list("low_of", pos3, B)
+        bass_of = load_list("bass_of", pos3, B)
         substitute_of = load_list("substitute_of", pos2, B)
-        w1_halves = [load_w1(0, 0, None), load_w1(0, 1, SECOND_HALF_AT)]
-        for q in range(4):
-            nc.sync.dma_start(out=w4_plane_raw[:].bitcast(I32)[32 * q : 32 * q + 4 * PASSES, :],
+        w1_halves = [load_w1(placed("w1_half%d" % h, [P, PACK, PASS // 2], F32, place), h * PASS // 2)
+                     for h, place in enumerate((W1_FIRST_HALF_AT, W1_SECOND_HALF_AT))]
+        for q in range(P // QUADRANT):
+            nc.sync.dma_start(out=w4_plane_raw[:].bitcast(I32)[QUADRANT * q : QUADRANT * q + 4 * PASSES, :],
                               in_=w4_scales[0][4 * q : 4 * q + 4, :].bitcast(I32).rearrange("j (g c) -> g j c", g=PASSES))
-        w4_raw = spot.tile([P, H // 2], I32, name="w4_raw", align_bytes=64, offset=12288)
+        w4_raw = placed("w4_raw", [P, H // 2], I32, W4_WORDS_AT)
         nc.sync.dma_start(out=w4_raw[:], in_=w4_words[0].bitcast(I32))
         current_of = load_list("current_of", pos1, B)
 
-        w1_codes = {}
-        w1_plane = {}
-        w1_rounded = {}
+        first_codes = keep.tile([P, PASS], U32, name="first_codes", align_bytes=64)
+        first_plane = keep.tile([P, PASS], U8, name="first_plane", align_bytes=64)
+        first_rounded = placed("first_rounded", [P, PACK, P, PACK], BF16, W1_ROUNDED_AT)
 
-        def make_w1_codes(g, tag):
-            w1_codes[g] = keep.tile([P, PASS], U32, name="w1_codes", tag=tag, align_bytes=64)
-            w1_plane[g] = keep.tile([P, PASS], U8, name="w1_plane%d" % g, align_bytes=64)
+        def round_first(h, copy, first, last):
+            rounded = first_rounded[:, :, h * P // 2 + first : h * P // 2 + last, :].rearrange("p t m j -> p m j t")
+            copy(rounded, w1_halves[h][:, :, first * PACK : last * PACK].rearrange("p j (m t) -> p m j t", t=PACK))
 
-        make_w1_codes(0, "w1_codes_first")
+        def quantise_first(first, last):
+            nc.vector.quantize_mx(out=first_codes[:, first * P : last * P].bitcast(FP8X4),
+                                  scales=first_plane[:, first * P : last * P],
+                                  in_=first_rounded[:, first:last].rearrange("p t m j -> p (t m j)"))
 
-        def round_w1(g, h, raw, copy, first=0, last=P // 2):
-            rounded = w1_rounded[g][:, :, h * P // 2 + first : h * P // 2 + last, :].rearrange("p t m j -> p m j t")
-            copy(rounded, raw[:, :, first * PACK : last * PACK].rearrange("p j (m t) -> p m j t", t=PACK))
-
-        def quantise_w1(g, first, last):
-            nc.vector.quantize_mx(out=w1_codes[g][:, first * P : last * P].bitcast(FP8X4),
-                                  scales=w1_plane[g][:, first * P : last * P],
-                                  in_=w1_rounded[g][:, first:last].rearrange("p t m j -> p (t m j)"))
-
-        w4_codes = {}
-        w4_plane = {}
-
-        w1_rounded[0] = spot.tile([P, PACK, P, PACK], BF16, name="w1_rounded0", align_bytes=64, offset=15360)
-        round_w1(0, 0, w1_halves[0], nc.scalar.copy)
+        round_first(0, nc.scalar.copy, 0, P // 2)
 
         picked_plane = keep.tile([P, S], U8, name="picked_plane", align_bytes=64)
         nc.vector.tensor_copy(picked_plane[:], tab_plane[:].indirect(offs_sb[:]))
@@ -128,27 +133,28 @@ def tile_list_chord_phase_voicings_kernel(tc, tab_words, tab_scales, offs, pos1,
             entries = offs_sb[:, h * BANK // PER_COLUMN : (h + 1) * BANK // PER_COLUMN]
             nc.vector.tensor_copy(codes[:], tab_sb[:].bitcast(U32).indirect(entries))
             picked_codes.append(codes)
-        round_w1(0, 1, w1_halves[1], nc.scalar.copy, 0, P // 4)
-        round_w1(0, 1, w1_halves[1], nc.vector.tensor_copy, P // 4, P // 2)
-        w1_later = {1: load_w1_part(1, "first_tenant_tab_plane")}
-        quantise_w1(0, 0, 1)
-        quantise_w1(0, 1, 2)
-        w4_plane_first = spot.tile([P, PASS], U8, name="w4_plane_first", align_bytes=64, offset=SECOND_HALF_AT + 1024)
+        round_first(1, nc.scalar.copy, 0, P // 4)
+        round_first(1, nc.vector.tensor_copy, P // 4, P // 2)
+        w1_later = {1: load_w1(tagged("table_plane_first", [P, PACK, PASS], F32), PASS)}
+        quantise_first(0, 1)
+        quantise_first(1, 2)
+
+        w4_plane_first = placed("w4_plane_first", [P, PASS], U8, W1_SECOND_HALF_AT + 2 * PASS)
         nc.vector.tensor_copy(w4_plane_first[:].rearrange("p (t m) -> p t m", t=PACK),
                               w4_plane_raw[:].rearrange("p (m t) -> p t m", t=PACK))
-        w4_plane[0] = w4_plane_first[:]
+        w4_plane = {0: w4_plane_first[:]}
         for g in range(1, PASSES):
             w4_plane[g] = w4_planes_later[:, (g - 1) * PASS : g * PASS]
             nc.sync.dma_start(out=w4_plane[g].bitcast(I32)[0 : P - 4 * g, :], in_=w4_plane_first[:].bitcast(I32)[4 * g : P, :])
-        w4_ordered = keep.tile([P, H - PASS], U16, name="w4_ordered", align_bytes=64)
-        w4_first = spot.tile([P, PASS], U16, name="w4_first", align_bytes=64, offset=SECOND_HALF_AT)
+        w4_later = keep.tile([P, H - PASS], U16, name="w4_later", align_bytes=64)
+        w4_first = placed("w4_first", [P, PASS], U16, W1_SECOND_HALF_AT)
         w4_unordered = w4_raw[:].bitcast(U16).rearrange("p (g m t) -> p g t m", t=PACK, m=P)
         nc.vector.tensor_copy(w4_first[:].rearrange("p (t m) -> p t m", m=P), w4_unordered[:, 0])
-        w4_codes[0] = w4_first[:]
-        quantise_w1(0, 2, 4)
-        nc.vector.tensor_copy(w4_ordered[:].rearrange("p (g t m) -> p g t m", t=PACK, m=P), w4_unordered[:, 1:])
+        w4_codes = {0: w4_first[:]}
+        quantise_first(2, 4)
+        nc.vector.tensor_copy(w4_later[:].rearrange("p (g t m) -> p g t m", t=PACK, m=P), w4_unordered[:, 1:])
         for g in range(1, PASSES):
-            w4_codes[g] = w4_ordered[:, (g - 1) * PASS : g * PASS]
+            w4_codes[g] = w4_later[:, (g - 1) * PASS : g * PASS]
 
         def bank_tile(number):
             bank = psum.tile([P, BANK], F32, name="bank%d" % number)
@@ -160,78 +166,77 @@ def tile_list_chord_phase_voicings_kernel(tc, tab_words, tab_scales, offs, pos1,
                                 rhs_scale=picked_plane[:, h * BANK : (h + 1) * BANK], start=True, stop=True)
             return bank
 
-        stationary = {t: (w1_codes[0][:, t * P : (t + 1) * P], w1_plane[0][:, t * P : (t + 1) * P]) for t in range(PACK)}
+        stationary = {t: (first_codes[:, t * P : (t + 1) * P], first_plane[:, t * P : (t + 1) * P]) for t in range(PACK)}
         angle = {}
         colour = {}
         phase = {}
-
-        def size_at(i):
-            if i % 2:
-                return SIZES_AT + (i // 2) * 2048
-            return SLOTS_AT + (i // 2 % 3) * SLOT_BYTES + 3584
-
-        def held(i, shape, dtype):
-            tile = spot.tile(shape, dtype, name="held%d" % i, align_bytes=64, offset=size_at(i) + (0 if i in (3, 9) else 512))
-            return tile
-
         phase_banks = {}
 
+        def slot_at(i):
+            return SLOTS_AT + (i // 2 % 3) * SLOT_BYTES
+
+        def size_at(i):
+            if i in WINDOWS:
+                return slot_at(i) + ROW_BYTES - (PICK_BYTES - SLOT_GAP) // 2
+            return SIZES_AT + i * PICK_BYTES
+
+        def after_cosine(i, shape, dtype):
+            return placed("after_cosine%d" % i, shape, dtype, size_at(i))
+
         def phase_sums(i):
-            phase_banks[i] = [first_stage(stationary[i][0].bitcast(FP8X4), stationary[i][1], h, (0, 2, 4, 0, 6, 2, 0, 4, 6, 2, 0, 4)[i] + h) for h in range(2)]
+            codes, plane = stationary[i]
+            phase_banks[i] = [first_stage(codes.bitcast(FP8X4), plane, h, PHASE_BANKS[i] + h) for h in range(2)]
 
         def phase_half(i, h):
             if h == 0:
-                place = 9216 if i == 1 else AREAS_AT + (i % 3) * 4096
-                phase[i] = spot.tile([P, S], F32, name="phase%d" % i, align_bytes=64, offset=place)
-            copy = nc.vector.tensor_copy if i == 1 else nc.scalar.copy
+                own = {EARLY_PHASE: W4_WORDS_AT + 2 * PASS - ROW_BYTES, WINDOW_PHASE: TABLE_AT}
+                phase[i] = placed("phase%d" % i, [P, S], F32, own.get(i, AREAS_AT + (i % 3) * ROW_BYTES))
+            copy = nc.vector.tensor_copy if i == EARLY_PHASE or (i == WINDOW_PHASE and h == 0) else nc.scalar.copy
             copy(phase[i][:, h * BANK : (h + 1) * BANK], phase_banks[i][h][:])
 
         def pick_phase(i):
-            picked_angles = spot.tile([P, B], F32, name="angle%d" % i, align_bytes=64, offset=AREAS_AT + ((i + 2) % 3) * 4096)
-            angle[i] = picked_angles[:]
-            nc.scalar.activation(angle[i], phase[i][:].indirect(current_of[:]), ACT.Copy)
+            angle[i] = placed("angle%d" % i, [P, B], F32, AREAS_AT + ((i + 2) % 3) * ROW_BYTES)
+            nc.scalar.activation(angle[i][:], phase[i][:].indirect(current_of[:]), ACT.Copy)
 
         def make_colour(i):
             if i in (0, LAST_TILE):
-                colour[i] = keep.tile([P, S], F32, name="colour", tag="colour%d" % i, align_bytes=64)
+                colour[i] = tagged("colour%d" % i, [P, S], F32)
             else:
-                place = size_at(i - 2) + 1536 if i % 2 == 0 else size_at(i - 1) - 3584
-                colour[i] = spot.tile([P, S], F32, name="colour%d" % i, align_bytes=64, offset=place)
+                place = slot_at(i - 1) if i % 2 else slot_at(i - 2) + ROW_BYTES + SLOT_GAP
+                colour[i] = placed("colour%d" % i, [P, S], F32, place)
             g, t = divmod(i, PACK)
             cols = slice(t * P, (t + 1) * P)
+            copy = nc.scalar.copy if i == LAST_TILE else nc.vector.tensor_copy
             for h in range(2):
-                bank = first_stage(w4_codes[g][:, cols].bitcast(FP4X4), w4_plane[g][:, cols], h, (2, 2, 4, 0, 4, 6, 2, 0, 4, 6, 2, 0)[i] + h)
-                copy = nc.scalar.copy if i == LAST_TILE else nc.vector.tensor_copy
+                bank = first_stage(w4_codes[g][:, cols].bitcast(FP4X4), w4_plane[g][:, cols], h, COLOUR_BANKS[i] + h)
                 copy(colour[i][:, h * BANK : (h + 1) * BANK], bank[:])
 
         cos_terms = {}
         sin_terms = {}
-        sine = {}
-        cosine = {}
+        all_bars = slice(0, B)
         halves = [slice(h * HALF, (h + 1) * HALF) for h in range(2)]
-        quarters = [slice(q * P, (q + 1) * P) for q in range(4)]
 
-        def last_sines(i, h, bars):
-            width = bars.stop - bars.start
-            both_sines = keep.tile([P, width], F32, name="last_sines%d_%d" % (i, h))
-            both_cosines = keep.tile([P, width], F32, name="last_cosines%d_%d" % (i, h))
-            size = keep.tile([P, width], F32, name="size", tag="last_size%d_%d" % (i, h), align_bytes=64)
-            nc.scalar.activation(both_sines[:], angle[i][:, bars], ACT.Sin)
-            nc.scalar.activation(size[:], angle[i][:, bars], ACT.Abs)
-            nc.scalar.activation(both_cosines[:], size[:], ACT.Sin, bias=half_pi[:], scale=-1.0)
-            return both_sines, both_cosines
+        def half_sines(i, h):
+            sines = keep.tile([P, HALF], F32, name="half_sines%d_%d" % (i, h))
+            cosines = keep.tile([P, HALF], F32, name="half_cosines%d_%d" % (i, h))
+            size = tagged("half_size%d_%d" % (i, h), [P, HALF], F32)
+            nc.scalar.activation(sines[:], angle[i][:, halves[h]], ACT.Sin)
+            nc.scalar.activation(size[:], angle[i][:, halves[h]], ACT.Abs)
+            nc.scalar.activation(cosines[:], size[:], ACT.Sin, bias=half_pi[:], scale=-1.0)
+            return sines, cosines
+
+        def entries_of(chords, bars):
+            return chords[:, bars.start // PER_COLUMN : bars.stop // PER_COLUMN]
 
         def sin_product(i, bars, factor):
             g, t = divmod(i, PACK)
-            entries = slice(bars.start // PER_COLUMN, bars.stop // PER_COLUMN)
-            nc.vector.tensor_tensor(sin_terms[g][:, t, bars], colour[i][:].indirect(low_of[:, entries]),
-                                    factor, ALU.mult)
+            nc.vector.tensor_tensor(sin_terms[g][:, t, bars], colour[i][:].indirect(entries_of(bass_of, bars)),
+                                    factor[:], ALU.mult)
 
         def cos_product(i, bars, factor):
             g, t = divmod(i, PACK)
-            entries = slice(bars.start // PER_COLUMN, bars.stop // PER_COLUMN)
-            nc.vector.tensor_tensor(cos_terms[g][:, t, bars], colour[i][:].indirect(substitute_of[:, entries]),
-                                    factor, ALU.mult)
+            nc.vector.tensor_tensor(cos_terms[g][:, t, bars], colour[i][:].indirect(entries_of(substitute_of, bars)),
+                                    factor[:], ALU.mult)
 
         def turn(engine, g, bars, rounded, run):
             engine.tensor_tensor(rounded[:].rearrange("p (c i t) -> p c t i", i=run, t=PACK),
@@ -239,130 +244,121 @@ def tile_list_chord_phase_voicings_kernel(tc, tab_words, tab_scales, offs, pos1,
                                  sin_terms[g][:, :, bars].rearrange("p t (c i) -> p c t i", i=run), ALU.subtract)
             return rounded
 
-        def after_sine(i, width):
-            tile = keep.tile([P, width * PACK], BF16, name="after_sine", tag="sine_of%d" % i, align_bytes=64)
-            return tile
+        vector_run, gpsimd_run = 2, 4
 
         pieces = [slice(0, HALF), slice(HALF, HALF + P), slice(HALF + P, B)]
         z_codes = {}
         z_plane = {}
 
-        def quantise_into(codes, name, rounded_pieces):
+        def quantise(codes, name, rounded):
             plane = keep.tile([P, codes.shape[1]], U8, name=name, align_bytes=64)
-            done = 0
-            for rounded in rounded_pieces:
-                cols = slice(done, done + rounded.shape[1] // PACK)
-                nc.vector.quantize_mx(out=codes[:, cols].bitcast(FP8X4), scales=plane[:, cols], in_=rounded[:])
-                done = cols.stop
+            nc.vector.quantize_mx(out=codes[:].bitcast(FP8X4), scales=plane[:], in_=rounded[:])
             return plane
 
-        def quantise_z(g, first, codes, rounded_pieces):
-            plane = quantise_into(codes, "z_plane%d_%d" % (g, first), rounded_pieces)
-            done = 0
+        def quantise_z(g, first, codes, rounded):
+            plane = quantise(codes, "z_plane%d_%d" % (g, first), rounded)
             for n in range(first, len(pieces)):
-                cols = slice(done, done + pieces[n].stop - pieces[n].start)
+                cols = slice(pieces[n].start - pieces[first].start, pieces[n].stop - pieces[first].start)
                 if cols.stop <= codes.shape[1]:
                     z_codes[g, n] = codes[:, cols]
                     z_plane[g, n] = plane[:, cols]
-                done = cols.stop
 
-        def tagged_codes(width, tag):
-            codes = keep.tile([P, width], U32, name="z_codes", tag=tag, align_bytes=64)
-            return codes
+        def quantise_w1(first_tile, codes, rounded):
+            plane = quantise(codes, "w1_plane%d" % first_tile, rounded)
+            for t in range(codes.shape[1] // P):
+                stationary[first_tile + t] = (codes[:, t * P : (t + 1) * P], plane[:, t * P : (t + 1) * P])
 
-        def round_pair(g, first, rounded):
-            nc.gpsimd.tensor_copy(rounded[:].rearrange("p (t m j) -> p t m j", t=2, j=PACK),
-                                  w1_later[g][:].rearrange("p j (m t) -> p t m j", t=PACK)[:, first : first + 2])
+        def round_on_gpsimd(g, tiles, rounded):
+            nc.gpsimd.tensor_copy(rounded[:].rearrange("p (t m j) -> p t m j", t=tiles, j=PACK),
+                                  w1_later[g][:].rearrange("p j (m t) -> p t m j", t=PACK)[:, 0:tiles])
             return rounded
 
-        def round_high(g, copy, rounded):
-            copy(rounded[:].rearrange("p (t m j) -> p m j t", t=2, j=PACK),
-                 w1_later[g][:].rearrange("p j (m t) -> p m j t", t=PACK)[:, :, :, 2:4])
-            return rounded
-
-        def quantise_pair(g, first, codes, rounded_pieces):
-            plane = quantise_into(codes, "w1_pair_plane%d_%d" % (g, first), rounded_pieces)
-            for t in range(2):
-                stationary[PACK * g + first + t] = (codes[:, t * P : (t + 1) * P], plane[:, t * P : (t + 1) * P])
-
-        w1_later[2] = spot.tile([P, PACK, PASS], F32, name="w1_last", align_bytes=64, offset=SECOND_HALF_AT + 2048)
-        nc.sync.dma_start(out=w1_later[2][:], in_=w1_rows[:, :, 2 * PASS : 3 * PASS])
-        made = {}
+        w1_later[2] = load_w1(placed("w1_last_part", [P, PACK, PASS], F32, W1_LAST_PART_AT), 2 * PASS)
         phase_sums(0)
         phase_sums(1)
         phase_half(0, 0)
         phase_half(0, 1)
-        low = spot.tile([P, 2 * PASS], BF16, name="w1_rounded1", align_bytes=64, offset=13312)
-        round_pair(1, 0, low)
+        rounded_at = W1_ROUNDED_AT - PICK_BYTES
+        lower = round_on_gpsimd(1, 2, placed("w1_lower", [P, 2 * PASS], BF16, rounded_at))
         phase_sums(2)
-        phase_half(1, 0)
-        phase_half(1, 1)
+        phase_half(EARLY_PHASE, 0)
+        phase_half(EARLY_PHASE, 1)
         make_colour(0)
+        quantise_w1(PACK, tagged("w1_lower_codes", [P, 2 * P], U32), lower)
+        turned = {}
         for i in range(TILES - 2):
             g, t = divmod(i, PACK)
             if t == 0:
                 sin_terms[g] = keep.tile([P, PACK, B], F32, name="sin_terms", tag="sin_terms%d" % (g % 2))
                 cos_terms[g] = keep.tile([P, PACK, B], F32, name="cos_terms", tag="cos_terms%d" % (g % 2))
-            sine[i] = keep.tile([P, B], F32, name="sine", tag="sine_of%d" % i, align_bytes=64)
-            cosine[i] = deep.tile([P, B], F32, name="cosine")
-            size = spot.tile([P, B], F32, name="size%d" % i, align_bytes=64, offset=size_at(i))
+            if i == 0:
+                sine = placed("first_sine", [P, B], F32, W1_ROUNDED_AT)
+            else:
+                sine = tagged("sine_of%d" % i, [P, B], F32)
+            cosine = deep.tile([P, B], F32, name="cosine")
+            size = placed("size%d" % i, [P, B], F32, size_at(i))
+
             pick_phase(i)
-            if i > 0:
+            if i + 1 != EARLY_PHASE:
                 phase_half(i + 1, 1)
+            if i > 0 and i + 2 != WINDOW_PHASE:
                 phase_sums(i + 2)
-            nc.scalar.activation(size[:], angle[i], ACT.Abs)
-            nc.scalar.activation(sine[i][:], angle[i], ACT.Sin)
-            nc.scalar.activation(cosine[i][:], size[:], ACT.Sin, bias=half_pi[:], scale=-1.0)
-            phase_half(i + 2, 0)
-            sin_product(i, slice(0, B), sine[i][:])
-            cos_product(i, slice(0, B), cosine[i][:])
+            nc.scalar.activation(size[:], angle[i][:], ACT.Abs)
+            nc.scalar.activation(sine[:], angle[i][:], ACT.Sin)
+            nc.scalar.activation(cosine[:], size[:], ACT.Sin, bias=half_pi[:], scale=-1.0)
+            if i + 2 != WINDOW_PHASE:
+                phase_half(i + 2, 0)
+
+            sin_product(i, all_bars, sine)
+            cos_product(i, all_bars, cosine)
+
             if i == 0:
-                made[i] = round_pair(1, 2, after_sine(i, HALF))
-            if i == 2:
-                made[i] = round_pair(2, 0, after_sine(i, HALF))
-            if i in (4, 6, 8):
-                made[i] = turn(nc.gpsimd, (i - 4) // PACK, halves[i // 2 % 2], after_sine(i, HALF), 4)
-            if i % 2 == 0:
-                make_colour(i + 1)
-            if i % 2 == 0:
-                make_colour(i + 2)
+                third = round_on_gpsimd(2, PACK, placed("w1_third", [P, PACK * PASS], BF16, rounded_at))
+            elif i in WINDOWS:
+                bars = slice(0, P * len(WINDOWS[i]))
+                turned[g - 1] = turn(nc.gpsimd, g - 1, bars, tagged("sine_of%d" % i, [P, bars.stop * PACK], BF16), gpsimd_run)
+            for later in WINDOWS.get(i, ()):
+                make_colour(later)
             if i == 0:
-                quantise_pair(1, 0, held(i, [P, 2 * P], U32), [low])
+                phase_sums(WINDOW_PHASE)
+                phase_half(WINDOW_PHASE, 0)
+
             if i == 1:
-                quantise_pair(1, 2, held(i, [P, 2 * P], U32), [made[0]])
+                upper = after_cosine(i, [P, 2 * PASS], BF16)
+                nc.vector.tensor_copy(upper[:].rearrange("p (t m j) -> p m j t", t=2, j=PACK),
+                                      w1_later[1][:].rearrange("p j (m t) -> p m j t", t=PACK)[:, :, :, 2:4])
+            if i == 2:
+                quantise_w1(PACK + 2, after_cosine(i, [P, 2 * P], U32), upper)
             if i == 3:
-                high = round_high(2, nc.vector.tensor_copy, held(i, [P, 2 * PASS], BF16))
-                w8_sb = keep.tile([P, PASSES, N], I32, name="w8_sb", tag="first_tenant_tab_plane", align_bytes=64)
+                quantise_w1(2 * PACK, after_cosine(i, [P, PASS], U32), third)
+                w8_sb = tagged("table_plane_first", [P, PASSES, N], I32)
                 nc.sync.dma_start(out=w8_sb[:], in_=w8_words.rearrange("a p c i -> p a (c i)").bitcast(I32))
-                w8_planes = spot.tile([P, N], U8, name="w8_planes", align_bytes=64, offset=14336)
+                w8_planes = placed("w8_planes", [P, N], U8, rounded_at + 2 * PASS)
                 nc.gpsimd.memset(w8_planes[:].bitcast(I32), 0)
-                for q in range(4):
-                    nc.sync.dma_start(out=w8_planes[:].bitcast(I32)[32 * q : 32 * q + 4 * PASSES, :],
+                for q in range(P // QUADRANT):
+                    nc.sync.dma_start(out=w8_planes[:].bitcast(I32)[QUADRANT * q : QUADRANT * q + 4 * PASSES, :],
                                       in_=w8_scales[:, 4 * q : 4 * q + 4, :].bitcast(I32))
-            if i == 4:
-                quantise_pair(2, 0, held(i, [P, 2 * P], U32), [made[2]])
-                prior_sb = spot.tile([P, OUT_TILES], F32, name="prior_sb", align_bytes=64, offset=SECOND_HALF_AT + 2048)
+            if i == 5:
+                prior_sb = placed("prior_sb", [P, OUT_TILES], F32, W1_LAST_PART_AT)
                 with nc.allow_non_contiguous_dma(reason="one prior value for each output row"):
                     nc.sync.dma_start(out=prior_sb[:], in_=prior.rearrange("(c p) -> p c", p=P))
-            if i == 5:
-                quantise_pair(2, 2, held(i, [P, 2 * P], U32), [high])
             if i == 7:
-                quantise_z(0, 1, held(i, [P, 2 * P], U32), [made[6]])
+                quantise_z(0, 1, after_cosine(i, [P, HALF], U32), turned[0][:, HALF * PACK :])
             if i == 9:
-                made[i] = turn(nc.vector, 1, halves[1], held(i, [P, 2 * PASS], BF16), 2)
+                turned_late = turn(nc.vector, 1, halves[1], after_cosine(i, [P, HALF * PACK], BF16), vector_run)
 
-        pick_phase(LAST_TILE - 1)
+        before_last = LAST_TILE - 1
+        pick_phase(before_last)
         phase_half(LAST_TILE, 1)
-        trig = {(LAST_TILE - 1, 0): last_sines(LAST_TILE - 1, 0, halves[0])}
+        trig = {(before_last, 0): half_sines(before_last, 0)}
         make_colour(LAST_TILE)
         pick_phase(LAST_TILE)
-        trig[LAST_TILE, 0] = last_sines(LAST_TILE, 0, halves[0])
-        trig[LAST_TILE - 1, 1] = last_sines(LAST_TILE - 1, 1, halves[1])
-        trig[LAST_TILE, 1] = last_sines(LAST_TILE, 1, halves[1])
-        picked = keep.tile([P, 2, HALF], F32, name="picked_colours")
-        entries = slice(HALF // PER_COLUMN, B // PER_COLUMN)
-        nc.scalar.activation(picked[:, 0, :], colour[LAST_TILE][:].indirect(low_of[:, entries]), ACT.Copy)
-        nc.scalar.activation(picked[:, 1, :], colour[LAST_TILE][:].indirect(substitute_of[:, entries]), ACT.Copy)
+        trig[LAST_TILE, 0] = half_sines(LAST_TILE, 0)
+        trig[before_last, 1] = half_sines(before_last, 1)
+        trig[LAST_TILE, 1] = half_sines(LAST_TILE, 1)
+        last_colours = keep.tile([P, 2, HALF], F32, name="last_colours")
+        for side, chords in enumerate((bass_of, substitute_of)):
+            nc.scalar.activation(last_colours[:, side, :], colour[LAST_TILE][:].indirect(entries_of(chords, halves[1])), ACT.Copy)
 
         groups = {0: [(0, 1), (2, 3), (4, 5)], 1: [(0, 1, 2), (3, 4, 5)], 2: [(0, 1, 2), (3, 4, 5)]}
         bank_numbers = {0: (4, 5, 0), 1: (6, 7), 2: (2, 3)}
@@ -386,7 +382,7 @@ def tile_list_chord_phase_voicings_kernel(tc, tab_words, tab_scales, offs, pos1,
                 count = len(members)
                 first = members[0]
                 result = keep.tile([P, count, width], F32, name="result%d_%d" % (n, first))
-                if n < 2:
+                if n < len(pieces) - 1:
                     for place, c in enumerate(members):
                         nc.scalar.activation(result[:, place, :], bank[:, place * width : (place + 1) * width], ACT.Identity,
                                              bias=prior_sb[:, c : c + 1])
@@ -398,30 +394,26 @@ def tile_list_chord_phase_voicings_kernel(tc, tab_words, tab_scales, offs, pos1,
 
         def close_piece(n):
             width = pieces[n].stop - pieces[n].start
-            tag = "last_size%d_1" % (LAST_TILE - 1) if n == 0 else "rounded_last%d" % n
-            rounded = keep.tile([P, width * PACK], BF16, name="rounded_last", tag=tag, align_bytes=64)
-            turn(nc.vector, LAST_PASS, pieces[n], rounded, 2)
-            quantise_z(LAST_PASS, n, tagged_codes(width, "last_z_codes%d" % n), [rounded])
+            tag = "half_size%d_1" % before_last if n == 0 else "rounded_last%d" % n
+            rounded = turn(nc.vector, LAST_PASS, pieces[n], tagged(tag, [P, width * PACK], BF16), vector_run)
+            quantise_z(LAST_PASS, n, tagged("last_codes%d" % n, [P, width], U32), rounded)
             score_passes(LAST_PASS, n)
             store_scores(n)
 
         score_passes(0, 1)
         score_passes(0, 2)
-        sin_product(LAST_TILE - 1, halves[0], trig[LAST_TILE - 1, 0][0][:])
-        cos_product(LAST_TILE - 1, halves[0], trig[LAST_TILE - 1, 0][1][:])
-        quantise_z(0, 0, tagged_codes(HALF, "last_size%d_0" % (LAST_TILE - 1)), [made[4]])
-        score_passes(0, 0)
-        sin_product(LAST_TILE, halves[0], trig[LAST_TILE, 0][0][:])
-        cos_product(LAST_TILE, halves[0], trig[LAST_TILE, 0][1][:])
-        quantise_z(1, 0, tagged_codes(HALF, "last_size%d_0" % LAST_TILE), [made[8]])
-        score_passes(1, 0)
-        sin_product(LAST_TILE - 1, halves[1], trig[LAST_TILE - 1, 1][0][:])
+        for g, i in enumerate((before_last, LAST_TILE)):
+            sin_product(i, halves[0], trig[i, 0][0])
+            cos_product(i, halves[0], trig[i, 0][1])
+            quantise_z(g, 0, tagged("half_size%d_0" % i, [P, HALF], U32), turned[g][:, 0 : HALF * PACK])
+            score_passes(g, 0)
+        sin_product(before_last, halves[1], trig[before_last, 1][0])
         close_piece(0)
-        cos_product(LAST_TILE - 1, halves[1], trig[LAST_TILE - 1, 1][1][:])
-        nc.vector.tensor_tensor(sin_terms[LAST_PASS][:, PACK - 1, halves[1]], picked[:, 0, :], trig[LAST_TILE, 1][0][:], ALU.mult)
-        nc.vector.tensor_tensor(cos_terms[LAST_PASS][:, PACK - 1, halves[1]], picked[:, 1, :], trig[LAST_TILE, 1][1][:], ALU.mult)
-        late_codes = tagged_codes(HALF, "colour%d" % LAST_TILE)
-        quantise_z(1, 1, late_codes, [made[9]])
+        cos_product(before_last, halves[1], trig[before_last, 1][1])
+        for side, terms in enumerate((sin_terms, cos_terms)):
+            nc.vector.tensor_tensor(terms[LAST_PASS][:, PACK - 1, halves[1]], last_colours[:, side, :],
+                                    trig[LAST_TILE, 1][side][:], ALU.mult)
+        quantise_z(1, 1, tagged("colour%d" % LAST_TILE, [P, HALF], U32), turned_late)
         score_passes(1, 1)
         score_passes(1, 2)
         close_piece(1)

@@ -24,32 +24,28 @@ QUADRANT = 32
 PASS = P * PACK
 PASSES = H // PASS
 TILES = H // P
-LAST_TILE = TILES - 1
-LAST_PASS = PASSES - 1
 OUT_TILES = N // P
 PER_COLUMN = 16
-HALF = B // 2
-COSINES_AHEAD = 4
+AHEAD = 4
 
 ROW_BYTES = 4 * S
 PICK_BYTES = 4 * B
-TABLE_AT = 0
-W1_FIRST_HALF_AT = TABLE_AT + 4 * T
-W4_WORDS_AT = W1_FIRST_HALF_AT + ROW_BYTES
-W1_ROUNDED_AT = W4_WORDS_AT + 2 * H
-W1_SECOND_HALF_AT = W1_ROUNDED_AT + 2 * PACK * PASS
-W1_LAST_PART_AT = W1_SECOND_HALF_AT + PICK_BYTES
-AREAS_AT = W1_LAST_PART_AT + 4 * PACK * PASS
-SIZES_AT = AREAS_AT + 3 * ROW_BYTES
-SLOTS_AT = SIZES_AT + (TILES - 2) * PICK_BYTES
-SLOT_GAP = 1024
-SLOT_BYTES = 2 * ROW_BYTES + SLOT_GAP
+PART_BYTES = 4 * PACK * PASS
+ROUNDED_BYTES = 2 * PACK * PASS
 
-WINDOWS = {0: (1, 2, 3, 4), 4: (5, 6, 7, 8), 8: (9, 10)}
+RUNS = {1: ((3, 4, 5), ()), 4: ((6, 7, 8), (7, 8)), 8: ((9, 10, 11), ())}
+FIRST_RUN = (0, 1, 2)
 EARLY_PHASE = 1
-WINDOW_PHASE = 5
-PHASE_BANKS = (0, 2, 4, 0, 6, 2, 0, 4, 0, 4, 0, 4)
-COLOUR_BANKS = (2, 2, 4, 2, 4, 6, 2, 6, 2, 6, 2, 0)
+GPSIMD_BARS = {0: 512, 1: 384}
+RUN_PHASES = [k for i in RUNS for k in RUNS[i][1]]
+PIECES = (slice(0, 256), slice(256, 384), slice(384, 512))
+
+W1_AT = 0
+AREAS_AT = W1_AT + PASSES * PART_BYTES
+RUN_PHASE_AT = AREAS_AT + 3 * ROW_BYTES
+COLOURS_AT = RUN_PHASE_AT + ROW_BYTES
+ROUNDED_AT = COLOURS_AT + 6 * ROW_BYTES
+GATED_AT = ROUNDED_AT + 4 * ROUNDED_BYTES
 
 
 def tile_list_chord_phase_voicings_kernel(tc, tab_words, tab_scales, offs, pos1, pos2, pos3, w1, w4_words,
@@ -57,7 +53,7 @@ def tile_list_chord_phase_voicings_kernel(tc, tab_words, tab_scales, offs, pos1,
     nc = tc.nc
     with ExitStack() as ctx:
         keep = ctx.enter_context(tc.tile_pool(name="keep", bufs=1))
-        deep = ctx.enter_context(tc.tile_pool(name="deep", bufs=COSINES_AHEAD))
+        ring = ctx.enter_context(tc.tile_pool(name="ring", bufs=AHEAD))
         spot = ctx.enter_context(tc.tile_pool(name="spot", bufs=1))
         psum = ctx.enter_context(tc.psum_pool(name="psum", bufs=1))
 
@@ -65,96 +61,114 @@ def tile_list_chord_phase_voicings_kernel(tc, tab_words, tab_scales, offs, pos1,
             tile = spot.tile(shape, dtype, name=name, align_bytes=64, offset=offset)
             return tile
 
-        def tagged(tag, shape, dtype):
-            tile = keep.tile(shape, dtype, name="tagged", tag=tag, align_bytes=64)
+        def own(name, shape, dtype):
+            tile = keep.tile(shape, dtype, name=name, align_bytes=64)
             return tile
-
-        tab_plane = tagged("table_plane_first", [P, T], U8)
-        for q in range(P // QUADRANT):
-            nc.sync.dma_start(out=tab_plane[:].bitcast(I32)[QUADRANT * q : QUADRANT * (q + 1), :],
-                              in_=tab_scales[0][4 * q : 4 * q + 4, :].bitcast(I32).partition_broadcast(QUADRANT // 4))
-        w4_plane_raw = keep.tile([P, PASS], U8, name="w4_plane_raw", align_bytes=64)
-        w4_planes_later = keep.tile([P, LAST_PASS * PASS], U8, name="w4_planes_later", align_bytes=64)
-        zero = keep.tile([P, 1], F32, name="zero")
-        nc.gpsimd.memset(zero[:], 0.0)
-        nc.gpsimd.memset(w4_plane_raw[:].bitcast(I32), 0)
-        nc.gpsimd.memset(w4_planes_later[:].bitcast(I32), 0)
-
-        sin_zero = keep.tile([P, 1], F32, name="sin_zero")
-        nc.scalar.activation(sin_zero[:], zero[:], ACT.Sin)
-        half_pi = keep.tile([P, 1], F32, name="half_pi")
-        nc.gpsimd.tensor_scalar(half_pi[:], sin_zero[:], math.pi / 2, None, ALU.add)
 
         def load_list(name, entries, count):
             tile = keep.tile([P, count // PER_COLUMN], U16, name=name)
             nc.sync.dma_start(tile[:], entries)
             return tile
 
-        w1_rows = w1.rearrange("(p j) r -> p j r", j=PACK)
-
-        def load_w1(raw, first):
-            nc.sync.dma_start(out=raw[:], in_=w1_rows[:, :, first : first + raw.shape[2]])
-            return raw
+        w4_plane_raw = own("w4_plane_raw", [P, PASS], U8)
+        w4_planes_later = own("w4_planes_later", [P, (PASSES - 1) * PASS], U8)
+        w8_planes = own("w8_planes", [P, N], U8)
+        zero = keep.tile([P, 1], F32, name="zero")
+        nc.gpsimd.memset(zero[:], 0.0)
+        nc.gpsimd.memset(w4_plane_raw[:].bitcast(I32), 0)
+        nc.gpsimd.memset(w4_planes_later[:].bitcast(I32), 0)
+        nc.gpsimd.memset(w8_planes[:].bitcast(I32), 0)
+        sin_zero = keep.tile([P, 1], F32, name="sin_zero")
+        nc.scalar.activation(sin_zero[:], zero[:], ACT.Sin)
+        half_pi = keep.tile([P, 1], F32, name="half_pi")
+        nc.gpsimd.tensor_scalar(half_pi[:], sin_zero[:], math.pi / 2, None, ALU.add)
 
         offs_sb = load_list("offs_sb", offs, S)
-        tab_sb = placed("tab_sb", [P, T], I32, TABLE_AT)
+        tab_plane = own("tab_plane", [P, T], U8)
+        for q in range(P // QUADRANT):
+            nc.sync.dma_start(out=tab_plane[:].bitcast(I32)[QUADRANT * q : QUADRANT * (q + 1), :],
+                              in_=tab_scales[0][4 * q : 4 * q + 4, :].bitcast(I32).partition_broadcast(QUADRANT // 4))
+        tab_sb = own("tab_sb", [P, T], I32)
         nc.sync.dma_start(out=tab_sb[:], in_=tab_words[0].rearrange("p t i -> p (t i)").bitcast(I32))
-        bass_of = load_list("bass_of", pos3, B)
-        substitute_of = load_list("substitute_of", pos2, B)
-        w1_halves = [load_w1(placed("w1_half%d" % h, [P, PACK, PASS // 2], F32, place), h * PASS // 2)
-                     for h, place in enumerate((W1_FIRST_HALF_AT, W1_SECOND_HALF_AT))]
+        w1_rows = w1.rearrange("(p j) r -> p j r", j=PACK)
+
+        def load_w1(name, place, first, width):
+            raw = placed(name, [P, PACK, width], F32, place)
+            nc.sync.dma_start(out=raw[:], in_=w1_rows[:, :, first : first + width])
+            return raw
+
+        w1_halves = [load_w1("w1_half%d" % h, W1_AT + h * PART_BYTES // 2, h * PASS // 2, PASS // 2) for h in range(2)]
+        w4_raw = own("w4_raw", [P, H // 2], I32)
+        nc.sync.dma_start(out=w4_raw[:], in_=w4_words[0].bitcast(I32))
         for q in range(P // QUADRANT):
             nc.sync.dma_start(out=w4_plane_raw[:].bitcast(I32)[QUADRANT * q : QUADRANT * q + 4 * PASSES, :],
                               in_=w4_scales[0][4 * q : 4 * q + 4, :].bitcast(I32).rearrange("j (g c) -> g j c", g=PASSES))
-        w4_raw = placed("w4_raw", [P, H // 2], I32, W4_WORDS_AT)
-        nc.sync.dma_start(out=w4_raw[:], in_=w4_words[0].bitcast(I32))
         current_of = load_list("current_of", pos1, B)
+        w1_later = {1: load_w1("w1_part1", W1_AT + PART_BYTES, PASS, PASS)}
+        bass_of = load_list("bass_of", pos3, B)
+        substitute_of = load_list("substitute_of", pos2, B)
+        w1_later[2] = load_w1("w1_part2", W1_AT + 2 * PART_BYTES, 2 * PASS, PASS)
 
-        first_codes = keep.tile([P, PASS], U32, name="first_codes", align_bytes=64)
-        first_plane = keep.tile([P, PASS], U8, name="first_plane", align_bytes=64)
-        first_rounded = placed("first_rounded", [P, PACK, P, PACK], BF16, W1_ROUNDED_AT)
+        picked_plane = own("picked_plane", [P, S], U8)
+        nc.vector.tensor_copy(picked_plane[:], tab_plane[:].indirect(offs_sb[:]))
+        picked_codes = []
+        for h in range(S // BANK):
+            codes = own("picked_codes%d" % h, [P, BANK], U32)
+            entries = offs_sb[:, h * BANK // PER_COLUMN : (h + 1) * BANK // PER_COLUMN]
+            nc.vector.tensor_copy(codes[:], tab_sb[:].bitcast(U32).indirect(entries))
+            picked_codes.append(codes)
+
+        first_rounded = placed("first_rounded", [P, PACK, P, PACK], BF16, ROUNDED_AT)
 
         def round_first(h, copy, first, last):
             rounded = first_rounded[:, :, h * P // 2 + first : h * P // 2 + last, :].rearrange("p t m j -> p m j t")
             copy(rounded, w1_halves[h][:, :, first * PACK : last * PACK].rearrange("p j (m t) -> p m j t", t=PACK))
 
-        def quantise_first(first, last):
-            nc.vector.quantize_mx(out=first_codes[:, first * P : last * P].bitcast(FP8X4),
-                                  scales=first_plane[:, first * P : last * P],
-                                  in_=first_rounded[:, first:last].rearrange("p t m j -> p (t m j)"))
-
         round_first(0, nc.scalar.copy, 0, P // 2)
-
-        picked_plane = keep.tile([P, S], U8, name="picked_plane", align_bytes=64)
-        nc.vector.tensor_copy(picked_plane[:], tab_plane[:].indirect(offs_sb[:]))
-        picked_codes = []
-        for h in range(S // BANK):
-            codes = keep.tile([P, BANK], U32, name="picked_codes%d" % h, align_bytes=64)
-            entries = offs_sb[:, h * BANK // PER_COLUMN : (h + 1) * BANK // PER_COLUMN]
-            nc.vector.tensor_copy(codes[:], tab_sb[:].bitcast(U32).indirect(entries))
-            picked_codes.append(codes)
         round_first(1, nc.scalar.copy, 0, P // 4)
         round_first(1, nc.vector.tensor_copy, P // 4, P // 2)
-        w1_later = {1: load_w1(tagged("table_plane_first", [P, PACK, PASS], F32), PASS)}
+
+        stationary = {}
+
+        def quantise(codes, plane, rounded):
+            nc.vector.quantize_mx(out=codes.bitcast(FP8X4), scales=plane, in_=rounded)
+
+        first_codes = own("first_codes", [P, PASS], U32)
+        first_plane = own("first_plane", [P, PASS], U8)
+
+        def quantise_first(first, last):
+            cols = slice(first * P, last * P)
+            quantise(first_codes[:, cols], first_plane[:, cols], first_rounded[:, first:last].rearrange("p t m j -> p (t m j)"))
+            for t in range(first, last):
+                stationary[t] = (first_codes[:, t * P : (t + 1) * P], first_plane[:, t * P : (t + 1) * P])
+
         quantise_first(0, 1)
         quantise_first(1, 2)
-
-        w4_plane_first = placed("w4_plane_first", [P, PASS], U8, W1_SECOND_HALF_AT + 2 * PASS)
+        w4_plane_first = own("w4_plane_first", [P, PASS], U8)
         nc.vector.tensor_copy(w4_plane_first[:].rearrange("p (t m) -> p t m", t=PACK),
                               w4_plane_raw[:].rearrange("p (m t) -> p t m", t=PACK))
-        w4_plane = {0: w4_plane_first[:]}
-        for g in range(1, PASSES):
-            w4_plane[g] = w4_planes_later[:, (g - 1) * PASS : g * PASS]
-            nc.sync.dma_start(out=w4_plane[g].bitcast(I32)[0 : P - 4 * g, :], in_=w4_plane_first[:].bitcast(I32)[4 * g : P, :])
-        w4_later = keep.tile([P, H - PASS], U16, name="w4_later", align_bytes=64)
-        w4_first = placed("w4_first", [P, PASS], U16, W1_SECOND_HALF_AT)
         w4_unordered = w4_raw[:].bitcast(U16).rearrange("p (g m t) -> p g t m", t=PACK, m=P)
+        w4_first = own("w4_first", [P, PASS], U16)
         nc.vector.tensor_copy(w4_first[:].rearrange("p (t m) -> p t m", m=P), w4_unordered[:, 0])
         w4_codes = {0: w4_first[:]}
-        quantise_first(2, 4)
+        w4_plane = {0: w4_plane_first[:]}
+        w4_later = own("w4_later", [P, H - PASS], U16)
         nc.vector.tensor_copy(w4_later[:].rearrange("p (g t m) -> p g t m", t=PACK, m=P), w4_unordered[:, 1:])
         for g in range(1, PASSES):
             w4_codes[g] = w4_later[:, (g - 1) * PASS : g * PASS]
+        quantise_first(2, 4)
+
+        w8_sb = placed("w8_sb", [P, PASSES, N], I32, GATED_AT + 12 * PICK_BYTES)
+        nc.sync.dma_start(out=w8_sb[:], in_=w8_words.rearrange("a p c i -> p a (c i)").bitcast(I32))
+        for g in range(1, PASSES):
+            w4_plane[g] = w4_planes_later[:, (g - 1) * PASS : g * PASS]
+            nc.sync.dma_start(out=w4_plane[g].bitcast(I32)[0 : P - 4 * g, :], in_=w4_plane_first[:].bitcast(I32)[4 * g : P, :])
+        for q in range(P // QUADRANT):
+            nc.sync.dma_start(out=w8_planes[:].bitcast(I32)[QUADRANT * q : QUADRANT * q + 4 * PASSES, :],
+                              in_=w8_scales[:, 4 * q : 4 * q + 4, :].bitcast(I32))
+        prior_sb = own("prior_sb", [P, OUT_TILES], F32)
+        with nc.allow_non_contiguous_dma(reason="one prior value for each output row"):
+            nc.sync.dma_start(out=prior_sb[:], in_=prior.rearrange("(c p) -> p c", p=P))
 
         def bank_tile(number):
             bank = psum.tile([P, BANK], F32, name="bank%d" % number)
@@ -166,77 +180,62 @@ def tile_list_chord_phase_voicings_kernel(tc, tab_words, tab_scales, offs, pos1,
                                 rhs_scale=picked_plane[:, h * BANK : (h + 1) * BANK], start=True, stop=True)
             return bank
 
-        stationary = {t: (first_codes[:, t * P : (t + 1) * P], first_plane[:, t * P : (t + 1) * P]) for t in range(PACK)}
-        angle = {}
-        colour = {}
         phase = {}
         phase_banks = {}
+        colour = {}
+        angle = {}
 
-        def slot_at(i):
-            return SLOTS_AT + (i // 2 % 3) * SLOT_BYTES
+        def phase_sum(i, h):
+            if (i, h) not in phase_banks:
+                codes, plane = stationary[i]
+                phase_banks[i, h] = first_stage(codes.bitcast(FP8X4), plane, h, 2 * (i % 2) + h)
+
+        def phase_sums(i):
+            for h in range(2):
+                phase_sum(i, h)
+
+        def phase_half(i, h, copy):
+            if h == 0:
+                if i == EARLY_PHASE:
+                    phase[i] = own("early_phase", [P, S], F32)
+                elif i == RUN_PHASES[0]:
+                    phase[i] = placed("phase%d" % i, [P, S], F32, RUN_PHASE_AT)
+                elif i in RUN_PHASES:
+                    phase[i] = own("run_phase%d" % i, [P, S], F32)
+                else:
+                    phase[i] = placed("phase%d" % i, [P, S], F32, AREAS_AT + (i % 3) * ROW_BYTES)
+            copy(phase[i][:, h * BANK : (h + 1) * BANK], phase_banks[i, h][:])
+
+        def colour_at(i):
+            return COLOURS_AT + (i % 6) * ROW_BYTES
+
+        def make_colour(i):
+            colour[i] = placed("colour%d" % i, [P, S], F32, colour_at(i))
+            g, t = divmod(i, PACK)
+            cols = slice(t * P, (t + 1) * P)
+            for h in range(2):
+                bank = first_stage(w4_codes[g][:, cols].bitcast(FP4X4), w4_plane[g][:, cols], h, 4 + 2 * (i % 2) + h)
+                nc.vector.tensor_copy(colour[i][:, h * BANK : (h + 1) * BANK], bank[:])
 
         def size_at(i):
-            if i in WINDOWS:
-                return slot_at(i) + ROW_BYTES - (PICK_BYTES - SLOT_GAP) // 2
-            return SIZES_AT + i * PICK_BYTES
+            if i in RUNS and RUNS[i][1]:
+                return COLOURS_AT - PICK_BYTES // 2
+            if i in RUNS:
+                return colour_at(RUNS[i][0][1]) - PICK_BYTES // 2
+            return GATED_AT + (i + 1) * PICK_BYTES
 
         def after_cosine(i, shape, dtype):
             return placed("after_cosine%d" % i, shape, dtype, size_at(i))
 
-        def phase_sums(i):
-            codes, plane = stationary[i]
-            phase_banks[i] = [first_stage(codes.bitcast(FP8X4), plane, h, PHASE_BANKS[i] + h) for h in range(2)]
-
-        def phase_half(i, h):
-            if h == 0:
-                own = {EARLY_PHASE: W4_WORDS_AT + 2 * PASS - ROW_BYTES, WINDOW_PHASE: TABLE_AT}
-                phase[i] = placed("phase%d" % i, [P, S], F32, own.get(i, AREAS_AT + (i % 3) * ROW_BYTES))
-            copy = nc.vector.tensor_copy if i == EARLY_PHASE or (i == WINDOW_PHASE and h == 0) else nc.scalar.copy
-            copy(phase[i][:, h * BANK : (h + 1) * BANK], phase_banks[i][h][:])
-
-        def pick_phase(i):
-            angle[i] = placed("angle%d" % i, [P, B], F32, AREAS_AT + ((i + 2) % 3) * ROW_BYTES)
-            nc.scalar.activation(angle[i][:], phase[i][:].indirect(current_of[:]), ACT.Copy)
-
-        def make_colour(i):
-            if i in (0, LAST_TILE):
-                colour[i] = tagged("colour%d" % i, [P, S], F32)
-            else:
-                place = slot_at(i - 1) if i % 2 else slot_at(i - 2) + ROW_BYTES + SLOT_GAP
-                colour[i] = placed("colour%d" % i, [P, S], F32, place)
-            g, t = divmod(i, PACK)
-            cols = slice(t * P, (t + 1) * P)
-            copy = nc.scalar.copy if i == LAST_TILE else nc.vector.tensor_copy
-            for h in range(2):
-                bank = first_stage(w4_codes[g][:, cols].bitcast(FP4X4), w4_plane[g][:, cols], h, COLOUR_BANKS[i] + h)
-                copy(colour[i][:, h * BANK : (h + 1) * BANK], bank[:])
-
-        cos_terms = {}
-        sin_terms = {}
-        all_bars = slice(0, B)
-        halves = [slice(h * HALF, (h + 1) * HALF) for h in range(2)]
-
-        def half_sines(i, h):
-            sines = keep.tile([P, HALF], F32, name="half_sines%d_%d" % (i, h))
-            cosines = keep.tile([P, HALF], F32, name="half_cosines%d_%d" % (i, h))
-            size = tagged("half_size%d_%d" % (i, h), [P, HALF], F32)
-            nc.scalar.activation(sines[:], angle[i][:, halves[h]], ACT.Sin)
-            nc.scalar.activation(size[:], angle[i][:, halves[h]], ACT.Abs)
-            nc.scalar.activation(cosines[:], size[:], ACT.Sin, bias=half_pi[:], scale=-1.0)
-            return sines, cosines
-
         def entries_of(chords, bars):
             return chords[:, bars.start // PER_COLUMN : bars.stop // PER_COLUMN]
 
-        def sin_product(i, bars, factor):
-            g, t = divmod(i, PACK)
-            nc.vector.tensor_tensor(sin_terms[g][:, t, bars], colour[i][:].indirect(entries_of(bass_of, bars)),
-                                    factor[:], ALU.mult)
+        cos_terms = {}
+        sin_terms = {}
 
-        def cos_product(i, bars, factor):
+        def product(terms, chords, i, bars, factor):
             g, t = divmod(i, PACK)
-            nc.vector.tensor_tensor(cos_terms[g][:, t, bars], colour[i][:].indirect(entries_of(substitute_of, bars)),
-                                    factor[:], ALU.mult)
+            nc.vector.tensor_tensor(terms[g][:, t, bars], colour[i][:].indirect(entries_of(chords, bars)), factor, ALU.mult)
 
         def turn(engine, g, bars, rounded, run):
             engine.tensor_tensor(rounded[:].rearrange("p (c i t) -> p c t i", i=run, t=PACK),
@@ -246,175 +245,200 @@ def tile_list_chord_phase_voicings_kernel(tc, tab_words, tab_scales, offs, pos1,
 
         vector_run, gpsimd_run = 2, 4
 
-        pieces = [slice(0, HALF), slice(HALF, HALF + P), slice(HALF + P, B)]
+        def round_on_gpsimd(g, place):
+            rounded = placed("w1_rounded%d" % g, [P, PACK * PASS], BF16, place)
+            nc.gpsimd.tensor_copy(rounded[:].rearrange("p (t m j) -> p m t j", t=PACK, j=PACK),
+                                  w1_later[g][:].rearrange("p j (m t) -> p m t j", t=PACK))
+            return rounded
+
+        def quantise_w1(g, codes, rounded):
+            plane = own("w1_plane%d" % g, [P, PASS], U8)
+            quantise(codes[:], plane[:], rounded[:])
+            for t in range(PACK):
+                stationary[PACK * g + t] = (codes[:, t * P : (t + 1) * P], plane[:, t * P : (t + 1) * P])
+
         z_codes = {}
         z_plane = {}
 
-        def quantise(codes, name, rounded):
-            plane = keep.tile([P, codes.shape[1]], U8, name=name, align_bytes=64)
-            nc.vector.quantize_mx(out=codes[:].bitcast(FP8X4), scales=plane[:], in_=rounded[:])
-            return plane
-
         def quantise_z(g, first, codes, rounded):
-            plane = quantise(codes, "z_plane%d_%d" % (g, first), rounded)
-            for n in range(first, len(pieces)):
-                cols = slice(pieces[n].start - pieces[first].start, pieces[n].stop - pieces[first].start)
+            plane = own("z_plane%d_%d" % (g, first), [P, codes.shape[1]], U8)
+            quantise(codes[:], plane[:], rounded)
+            for n in range(first, len(PIECES)):
+                cols = slice(PIECES[n].start - PIECES[first].start, PIECES[n].stop - PIECES[first].start)
                 if cols.stop <= codes.shape[1]:
                     z_codes[g, n] = codes[:, cols]
                     z_plane[g, n] = plane[:, cols]
 
-        def quantise_w1(first_tile, codes, rounded):
-            plane = quantise(codes, "w1_plane%d" % first_tile, rounded)
-            for t in range(codes.shape[1] // P):
-                stationary[first_tile + t] = (codes[:, t * P : (t + 1) * P], plane[:, t * P : (t + 1) * P])
-
-        def round_on_gpsimd(g, tiles, rounded):
-            nc.gpsimd.tensor_copy(rounded[:].rearrange("p (t m j) -> p t m j", t=tiles, j=PACK),
-                                  w1_later[g][:].rearrange("p j (m t) -> p t m j", t=PACK)[:, 0:tiles])
-            return rounded
-
-        w1_later[2] = load_w1(placed("w1_last_part", [P, PACK, PASS], F32, W1_LAST_PART_AT), 2 * PASS)
         phase_sums(0)
         phase_sums(1)
-        phase_half(0, 0)
-        phase_half(0, 1)
-        rounded_at = W1_ROUNDED_AT - PICK_BYTES
-        lower = round_on_gpsimd(1, 2, placed("w1_lower", [P, 2 * PASS], BF16, rounded_at))
+        phase_half(0, 0, nc.scalar.copy)
+        phase_half(0, 1, nc.scalar.copy)
+        rounded_w1 = {1: round_on_gpsimd(1, ROUNDED_AT)}
         phase_sums(2)
-        phase_half(EARLY_PHASE, 0)
-        phase_half(EARLY_PHASE, 1)
-        make_colour(0)
-        quantise_w1(PACK, tagged("w1_lower_codes", [P, 2 * P], U32), lower)
+        phase_half(EARLY_PHASE, 0, nc.vector.tensor_copy)
+        phase_half(EARLY_PHASE, 1, nc.vector.tensor_copy)
+        for i in FIRST_RUN:
+            make_colour(i)
+
         turned = {}
+        rest = {}
+        all_bars = slice(0, B)
+        run_number = {i: n for n, i in enumerate(sorted(RUNS))}
         for i in range(TILES - 2):
             g, t = divmod(i, PACK)
             if t == 0:
                 sin_terms[g] = keep.tile([P, PACK, B], F32, name="sin_terms", tag="sin_terms%d" % (g % 2))
                 cos_terms[g] = keep.tile([P, PACK, B], F32, name="cos_terms", tag="cos_terms%d" % (g % 2))
-            if i == 0:
-                sine = placed("first_sine", [P, B], F32, W1_ROUNDED_AT)
+            if i in RUNS:
+                result_at = ROUNDED_AT + (1 + run_number[i]) * ROUNDED_BYTES
+                sine = placed("sine%d" % i, [P, B], F32, result_at)
             else:
-                sine = tagged("sine_of%d" % i, [P, B], F32)
-            cosine = deep.tile([P, B], F32, name="cosine")
-            size = placed("size%d" % i, [P, B], F32, size_at(i))
+                sine = ring.tile([P, B], F32, name="sine")
+            cosine = ring.tile([P, B], F32, name="cosine")
+            reach = S + B if i in RUNS and RUNS[i][1] else B
+            size = placed("size%d" % i, [P, reach], F32, size_at(i))[:, 0:B]
 
-            pick_phase(i)
+            angle[i] = placed("angle%d" % i, [P, B], F32, AREAS_AT + ((i + 2) % 3) * ROW_BYTES)
+            nc.scalar.activation(angle[i][:], phase[i][:].indirect(current_of[:]), ACT.Copy)
             if i + 1 != EARLY_PHASE:
-                phase_half(i + 1, 1)
-            if i > 0 and i + 2 != WINDOW_PHASE:
-                phase_sums(i + 2)
-            nc.scalar.activation(size[:], angle[i][:], ACT.Abs)
+                phase_half(i + 1, 1, nc.scalar.copy)
+            if i + 3 < TILES:
+                phase_sums(i + 3)
+            nc.scalar.activation(size, angle[i][:], ACT.Abs)
             nc.scalar.activation(sine[:], angle[i][:], ACT.Sin)
-            nc.scalar.activation(cosine[:], size[:], ACT.Sin, bias=half_pi[:], scale=-1.0)
-            if i + 2 != WINDOW_PHASE:
-                phase_half(i + 2, 0)
+            nc.scalar.activation(cosine[:], size, ACT.Sin, bias=half_pi[:], scale=-1.0)
+            if i + 2 not in RUN_PHASES:
+                phase_half(i + 2, 0, nc.scalar.copy)
 
-            sin_product(i, all_bars, sine)
-            cos_product(i, all_bars, cosine)
+            product(sin_terms, bass_of, i, all_bars, sine[:])
+            product(cos_terms, substitute_of, i, all_bars, cosine[:])
+
+            if i in RUNS:
+                if run_number[i] == 0:
+                    rounded_w1[2] = round_on_gpsimd(2, result_at)
+                else:
+                    done = run_number[i] - 1
+                    bars = slice(0, GPSIMD_BARS[done])
+                    turned[done] = turn(nc.gpsimd, done, bars, placed("turned%d" % done, [P, bars.stop * PACK], BF16, result_at),
+                                        gpsimd_run)
+                for later in RUNS[i][0]:
+                    make_colour(later)
+                for later in RUNS[i][1]:
+                    phase_sum(later, 0)
+                    phase_half(later, 0, nc.vector.tensor_copy)
 
             if i == 0:
-                third = round_on_gpsimd(2, PACK, placed("w1_third", [P, PACK * PASS], BF16, rounded_at))
-            elif i in WINDOWS:
-                bars = slice(0, P * len(WINDOWS[i]))
-                turned[g - 1] = turn(nc.gpsimd, g - 1, bars, tagged("sine_of%d" % i, [P, bars.stop * PACK], BF16), gpsimd_run)
-            for later in WINDOWS.get(i, ()):
-                make_colour(later)
-            if i == 0:
-                phase_sums(WINDOW_PHASE)
-                phase_half(WINDOW_PHASE, 0)
-
-            if i == 1:
-                upper = after_cosine(i, [P, 2 * PASS], BF16)
-                nc.vector.tensor_copy(upper[:].rearrange("p (t m j) -> p m j t", t=2, j=PACK),
-                                      w1_later[1][:].rearrange("p j (m t) -> p m j t", t=PACK)[:, :, :, 2:4])
+                quantise_w1(1, after_cosine(i, [P, PASS], U32), rounded_w1[1])
             if i == 2:
-                quantise_w1(PACK + 2, after_cosine(i, [P, 2 * P], U32), upper)
-            if i == 3:
-                quantise_w1(2 * PACK, after_cosine(i, [P, PASS], U32), third)
-                w8_sb = tagged("table_plane_first", [P, PASSES, N], I32)
-                nc.sync.dma_start(out=w8_sb[:], in_=w8_words.rearrange("a p c i -> p a (c i)").bitcast(I32))
-                w8_planes = placed("w8_planes", [P, N], U8, rounded_at + 2 * PASS)
-                nc.gpsimd.memset(w8_planes[:].bitcast(I32), 0)
-                for q in range(P // QUADRANT):
-                    nc.sync.dma_start(out=w8_planes[:].bitcast(I32)[QUADRANT * q : QUADRANT * q + 4 * PASSES, :],
-                                      in_=w8_scales[:, 4 * q : 4 * q + 4, :].bitcast(I32))
-            if i == 5:
-                prior_sb = placed("prior_sb", [P, OUT_TILES], F32, W1_LAST_PART_AT)
-                with nc.allow_non_contiguous_dma(reason="one prior value for each output row"):
-                    nc.sync.dma_start(out=prior_sb[:], in_=prior.rearrange("(c p) -> p c", p=P))
-            if i == 7:
-                quantise_z(0, 1, after_cosine(i, [P, HALF], U32), turned[0][:, HALF * PACK :])
+                quantise_w1(2, after_cosine(i, [P, PASS], U32), rounded_w1[2])
             if i == 9:
-                turned_late = turn(nc.vector, 1, halves[1], after_cosine(i, [P, HALF * PACK], BF16), vector_run)
+                done = i // PACK - 1
+                rest[done] = turn(nc.vector, done, PIECES[2], after_cosine(i, [P, P * PACK], BF16), vector_run)
+            if i == 6:
+                quantise_z(0, 1, after_cosine(i, [P, 2 * P], U32), turned[0][:, PIECES[1].start * PACK :])
 
-        before_last = LAST_TILE - 1
-        pick_phase(before_last)
-        phase_half(LAST_TILE, 1)
-        trig = {(before_last, 0): half_sines(before_last, 0)}
-        make_colour(LAST_TILE)
-        pick_phase(LAST_TILE)
-        trig[LAST_TILE, 0] = half_sines(LAST_TILE, 0)
-        trig[before_last, 1] = half_sines(before_last, 1)
-        trig[LAST_TILE, 1] = half_sines(LAST_TILE, 1)
-        last_colours = keep.tile([P, 2, HALF], F32, name="last_colours")
+        last_pass = PASSES - 1
+        early, late = TILES - 2, TILES - 1
+        halves = [slice(0, B // 2), slice(B // 2, B)]
+        trig = {}
+
+        def pick(i):
+            angle[i] = placed("angle%d" % i, [P, B], F32, AREAS_AT + ((i + 2) % 3) * ROW_BYTES)
+            nc.scalar.activation(angle[i][:], phase[i][:].indirect(current_of[:]), ACT.Copy)
+
+        def half_trig(i, h):
+            sines = own("half_sines%d_%d" % (i, h), [P, B // 2], F32)
+            cosines = own("half_cosines%d_%d" % (i, h), [P, B // 2], F32)
+            size = keep.tile([P, B // 2], F32, name="half_size", tag="half_size%d_%d" % (i, h), align_bytes=64)
+            nc.scalar.activation(size[:], angle[i][:, halves[h]], ACT.Abs)
+            nc.scalar.activation(sines[:], angle[i][:, halves[h]], ACT.Sin)
+            nc.scalar.activation(cosines[:], size[:], ACT.Sin, bias=half_pi[:], scale=-1.0)
+            trig[i, h] = (sines, cosines)
+
+        def after_half(i, h, shape, dtype):
+            tile = keep.tile(shape, dtype, name="after_half", tag="half_size%d_%d" % (i, h), align_bytes=64)
+            return tile
+
+        pick(early)
+        phase_half(late, 1, nc.scalar.copy)
+        half_trig(early, 0)
+        pick(late)
+        half_trig(late, 0)
+        half_trig(early, 1)
+        half_trig(late, 1)
+        last_colours = own("last_colours", [P, 2, B // 2], F32)
         for side, chords in enumerate((bass_of, substitute_of)):
-            nc.scalar.activation(last_colours[:, side, :], colour[LAST_TILE][:].indirect(entries_of(chords, halves[1])), ACT.Copy)
+            nc.scalar.activation(last_colours[:, side, :], colour[late][:].indirect(entries_of(chords, halves[1])), ACT.Copy)
 
         groups = {0: [(0, 1), (2, 3), (4, 5)], 1: [(0, 1, 2), (3, 4, 5)], 2: [(0, 1, 2), (3, 4, 5)]}
-        bank_numbers = {0: (4, 5, 0), 1: (6, 7), 2: (2, 3)}
-        score_banks = {n: [bank_tile(number) for number in bank_numbers[n]] for n in range(len(pieces))}
+        bank_numbers = {0: (0, 1, 2), 1: (4, 5), 2: (6, 7)}
+        score_banks = {n: [bank_tile(number) for number in bank_numbers[n]] for n in range(len(PIECES))}
 
         def score_passes(g, n):
-            width = pieces[n].stop - pieces[n].start
+            width = PIECES[n].stop - PIECES[n].start
             for bank, members in zip(score_banks[n], groups[n]):
                 for place, c in enumerate(members):
                     cols = slice(c * P, (c + 1) * P)
                     nc.tensor.matmul_mx(out=bank[:, place * width : (place + 1) * width], lhsT=w8_sb[:, g, cols].bitcast(FP8X4),
                                         lhsT_scale=w8_planes[4 * g :, cols], rhs=z_codes[g, n].bitcast(FP8X4),
                                         rhs_scale=z_plane[g, n], start=(g == 0 and c == members[0]),
-                                        stop=(g == LAST_PASS and c == members[-1]))
+                                        stop=(g == last_pass and c == members[-1]))
 
         out_rows = out.rearrange("(c p) m -> p c m", p=P)
 
-        def store_scores(n):
-            width = pieces[n].stop - pieces[n].start
-            for bank, members in zip(score_banks[n], groups[n]):
+        def store_scores(n, on_vector):
+            width = PIECES[n].stop - PIECES[n].start
+            for number, (bank, members) in enumerate(zip(score_banks[n], groups[n])):
                 count = len(members)
                 first = members[0]
-                result = keep.tile([P, count, width], F32, name="result%d_%d" % (n, first))
-                if n < len(pieces) - 1:
-                    for place, c in enumerate(members):
-                        nc.scalar.activation(result[:, place, :], bank[:, place * width : (place + 1) * width], ACT.Identity,
-                                             bias=prior_sb[:, c : c + 1])
-                else:
+                result = placed("result%d_%d" % (n, first), [P, count, width], F32,
+                                W1_AT + 4 * (OUT_TILES * PIECES[n].start + first * width))
+                if number in on_vector:
                     nc.vector.tensor_tensor(result[:], bank[:, 0 : count * width].rearrange("p (c m) -> p c m", c=count),
                                             prior_sb[:, first : first + count].unsqueeze(2).to_broadcast([P, count, width]),
                                             ALU.add)
-                nc.sync.dma_start(out=out_rows[:, first : first + count, pieces[n]], in_=result[:])
+                else:
+                    for place, c in enumerate(members):
+                        nc.scalar.activation(result[:, place, :], bank[:, place * width : (place + 1) * width], ACT.Identity,
+                                             bias=prior_sb[:, c : c + 1])
+                nc.sync.dma_start(out=out_rows[:, first : first + count, PIECES[n]], in_=result[:])
 
-        def close_piece(n):
-            width = pieces[n].stop - pieces[n].start
-            tag = "half_size%d_1" % before_last if n == 0 else "rounded_last%d" % n
-            rounded = turn(nc.vector, LAST_PASS, pieces[n], tagged(tag, [P, width * PACK], BF16), vector_run)
-            quantise_z(LAST_PASS, n, tagged("last_codes%d" % n, [P, width], U32), rounded)
-            score_passes(LAST_PASS, n)
-            store_scores(n)
+        def within_half(n):
+            return slice(PIECES[n].start - B // 2, PIECES[n].stop - B // 2)
+
+        def plain_products(n):
+            for side, terms in enumerate((sin_terms, cos_terms)):
+                nc.vector.tensor_tensor(terms[last_pass][:, PACK - 1, PIECES[n]], last_colours[:, side, within_half(n)],
+                                        trig[late, 1][side][:, within_half(n)], ALU.mult)
+
+        def turn_last(n, rounded):
+            return turn(nc.vector, last_pass, PIECES[n], rounded, vector_run)
+
+        def close(n, rounded, on_vector):
+            width = PIECES[n].stop - PIECES[n].start
+            quantise_z(last_pass, n, own("last_codes%d" % n, [P, width], U32), rounded[:])
+            score_passes(last_pass, n)
+            store_scores(n, on_vector)
 
         score_passes(0, 1)
         score_passes(0, 2)
-        for g, i in enumerate((before_last, LAST_TILE)):
-            sin_product(i, halves[0], trig[i, 0][0])
-            cos_product(i, halves[0], trig[i, 0][1])
-            quantise_z(g, 0, tagged("half_size%d_0" % i, [P, HALF], U32), turned[g][:, 0 : HALF * PACK])
+        for g, i in enumerate((early, late)):
+            product(sin_terms, bass_of, i, halves[0], trig[i, 0][0][:])
+            product(cos_terms, substitute_of, i, halves[0], trig[i, 0][1][:])
+            quantise_z(g, 0, after_half(i, 0, [P, B // 2], U32), turned[g][:, 0 : B // 2 * PACK])
             score_passes(g, 0)
-        sin_product(before_last, halves[1], trig[before_last, 1][0])
-        close_piece(0)
-        cos_product(before_last, halves[1], trig[before_last, 1][1])
-        for side, terms in enumerate((sin_terms, cos_terms)):
-            nc.vector.tensor_tensor(terms[LAST_PASS][:, PACK - 1, halves[1]], last_colours[:, side, :],
-                                    trig[LAST_TILE, 1][side][:], ALU.mult)
-        quantise_z(1, 1, tagged("colour%d" % LAST_TILE, [P, HALF], U32), turned_late)
+        product(sin_terms, bass_of, early, PIECES[1], trig[early, 1][0][:, within_half(1)])
+        first_turned = turn_last(0, after_half(early, 1, [P, B // 2 * PACK], BF16))
+        product(cos_terms, substitute_of, early, PIECES[1], trig[early, 1][1][:, within_half(1)])
+        close(0, first_turned, ())
+        plain_products(1)
+        quantise_z(1, 1, after_half(late, 1, [P, P], U32), turned[1][:, PIECES[1].start * PACK :])
         score_passes(1, 1)
+        second_turned = turn_last(1, own("second_turned", [P, P * PACK], BF16))
+        product(sin_terms, bass_of, early, PIECES[2], trig[early, 1][0][:, within_half(2)])
+        close(1, second_turned, ())
+        product(cos_terms, substitute_of, early, PIECES[2], trig[early, 1][1][:, within_half(2)])
+        plain_products(2)
+        quantise_z(1, 2, own("z_codes1_2", [P, P], U32), rest[1][:])
         score_passes(1, 2)
-        close_piece(1)
-        close_piece(2)
+        close(2, turn_last(2, own("third_turned", [P, P * PACK], BF16)), (1,))

@@ -33,19 +33,18 @@ PICK_BYTES = 4 * B
 PART_BYTES = 4 * PACK * PASS
 ROUNDED_BYTES = 2 * PACK * PASS
 
-RUNS = {1: ((3, 4, 5), ()), 4: ((6, 7, 8), (7, 8)), 8: ((9, 10, 11), ())}
-FIRST_RUN = (0, 1, 2)
+RUNS = {4: (5, 6, 7, 8), 8: (9, 10)}
+RUN_PHASE = 8
+WAIT_PHASE = 5
 EARLY_PHASE = 1
-GPSIMD_BARS = {0: 512, 1: 384}
-RUN_PHASES = [k for i in RUNS for k in RUNS[i][1]]
 PIECES = (slice(0, 256), slice(256, 384), slice(384, 512))
 
 W1_AT = 0
 AREAS_AT = W1_AT + PASSES * PART_BYTES
-RUN_PHASE_AT = AREAS_AT + 3 * ROW_BYTES
-COLOURS_AT = RUN_PHASE_AT + ROW_BYTES
-ROUNDED_AT = COLOURS_AT + 6 * ROW_BYTES
-GATED_AT = ROUNDED_AT + 4 * ROUNDED_BYTES
+COLOURS_AT = AREAS_AT + 3 * ROW_BYTES
+ROUNDED_AT = COLOURS_AT + 7 * ROW_BYTES
+PICKED_AT = ROUNDED_AT + 4 * ROUNDED_BYTES
+GATED_AT = PICKED_AT + PICK_BYTES
 
 
 def tile_list_chord_phase_voicings_kernel(tc, tab_words, tab_scales, offs, pos1, pos2, pos3, w1, w4_words,
@@ -70,13 +69,15 @@ def tile_list_chord_phase_voicings_kernel(tc, tab_words, tab_scales, offs, pos1,
             nc.sync.dma_start(tile[:], entries)
             return tile
 
-        w4_plane_raw = own("w4_plane_raw", [P, PASS], U8)
-        w4_planes_later = own("w4_planes_later", [P, (PASSES - 1) * PASS], U8)
+        w4_rows_first = placed("w4_rows_first", [P, PASS], U8, PICKED_AT)
+        w4_rows_later = own("w4_rows_later", [P, PASS], U8)
+        w4_plane_last = own("w4_plane_last", [P, PASS], U8)
         w8_planes = own("w8_planes", [P, N], U8)
         zero = keep.tile([P, 1], F32, name="zero")
         nc.gpsimd.memset(zero[:], 0.0)
-        nc.gpsimd.memset(w4_plane_raw[:].bitcast(I32), 0)
-        nc.gpsimd.memset(w4_planes_later[:].bitcast(I32), 0)
+        nc.gpsimd.memset(w4_rows_first[:].bitcast(I32), 0)
+        nc.gpsimd.memset(w4_rows_later[:].bitcast(I32), 0)
+        nc.gpsimd.memset(w4_plane_last[:].bitcast(I32), 0)
         nc.gpsimd.memset(w8_planes[:].bitcast(I32), 0)
         sin_zero = keep.tile([P, 1], F32, name="sin_zero")
         nc.scalar.activation(sin_zero[:], zero[:], ACT.Sin)
@@ -97,12 +98,17 @@ def tile_list_chord_phase_voicings_kernel(tc, tab_words, tab_scales, offs, pos1,
             nc.sync.dma_start(out=raw[:], in_=w1_rows[:, :, first : first + width])
             return raw
 
-        w1_halves = [load_w1("w1_half%d" % h, W1_AT + h * PART_BYTES // 2, h * PASS // 2, PASS // 2) for h in range(2)]
-        w4_raw = own("w4_raw", [P, H // 2], I32)
-        nc.sync.dma_start(out=w4_raw[:], in_=w4_words[0].bitcast(I32))
+        w4_raw_first = own("w4_raw_first", [P, PASS // 2], I32)
+        nc.sync.dma_start(out=w4_raw_first[:], in_=w4_words[0].bitcast(I32)[:, 0 : PASS // 2])
         for q in range(P // QUADRANT):
-            nc.sync.dma_start(out=w4_plane_raw[:].bitcast(I32)[QUADRANT * q : QUADRANT * q + 4 * PASSES, :],
-                              in_=w4_scales[0][4 * q : 4 * q + 4, :].bitcast(I32).rearrange("j (g c) -> g j c", g=PASSES))
+            nc.sync.dma_start(out=w4_rows_first[:].bitcast(I32)[QUADRANT * q : QUADRANT * q + 4, :],
+                              in_=w4_scales[0][4 * q : 4 * q + 4, 0:PASS].bitcast(I32))
+        w1_halves = [load_w1("w1_half%d" % h, place, h * PASS // 2, PASS // 2) for h, place in enumerate((W1_AT, COLOURS_AT))]
+        w4_raw_later = placed("w4_raw_later", [P, (H - PASS) // 2], I32, COLOURS_AT + 2 * ROW_BYTES - PICK_BYTES // 2)
+        nc.sync.dma_start(out=w4_raw_later[:], in_=w4_words[0].bitcast(I32)[:, PASS // 2 :])
+        for q in range(P // QUADRANT):
+            nc.sync.dma_start(out=w4_rows_later[:].bitcast(I32)[QUADRANT * q : QUADRANT * q + 4 * (PASSES - 1), :],
+                              in_=w4_scales[0][4 * q : 4 * q + 4, PASS:].bitcast(I32).rearrange("j (g c) -> g j c", g=PASSES - 1))
         current_of = load_list("current_of", pos1, B)
         w1_later = {1: load_w1("w1_part1", W1_AT + PART_BYTES, PASS, PASS)}
         bass_of = load_list("bass_of", pos3, B)
@@ -113,10 +119,17 @@ def tile_list_chord_phase_voicings_kernel(tc, tab_words, tab_scales, offs, pos1,
         nc.vector.tensor_copy(picked_plane[:], tab_plane[:].indirect(offs_sb[:]))
         picked_codes = []
         for h in range(S // BANK):
-            codes = own("picked_codes%d" % h, [P, BANK], U32)
+            codes = placed("picked_codes%d" % h, [P, BANK], U32, PICKED_AT) if h else own("picked_codes0", [P, BANK], U32)
             entries = offs_sb[:, h * BANK // PER_COLUMN : (h + 1) * BANK // PER_COLUMN]
             nc.vector.tensor_copy(codes[:], tab_sb[:].bitcast(U32).indirect(entries))
             picked_codes.append(codes)
+            if h == 0:
+                w4_plane_first = own("w4_plane_first", [P, PASS], U8)
+                nc.vector.tensor_copy(w4_plane_first[:].rearrange("p (t m) -> p t m", t=PACK),
+                                      w4_rows_first[:].rearrange("p (m t) -> p t m", t=PACK))
+        w4_first = own("w4_first", [P, PASS], U16)
+        nc.scalar.copy(w4_first[:].rearrange("p (t m) -> p m t", m=P),
+                       w4_raw_first[:].bitcast(U16).rearrange("p (m t) -> p m t", t=PACK))
 
         first_rounded = placed("first_rounded", [P, PACK, P, PACK], BF16, ROUNDED_AT)
 
@@ -144,25 +157,23 @@ def tile_list_chord_phase_voicings_kernel(tc, tab_words, tab_scales, offs, pos1,
 
         quantise_first(0, 1)
         quantise_first(1, 2)
-        w4_plane_first = own("w4_plane_first", [P, PASS], U8)
-        nc.vector.tensor_copy(w4_plane_first[:].rearrange("p (t m) -> p t m", t=PACK),
-                              w4_plane_raw[:].rearrange("p (m t) -> p t m", t=PACK))
-        w4_unordered = w4_raw[:].bitcast(U16).rearrange("p (g m t) -> p g t m", t=PACK, m=P)
-        w4_first = own("w4_first", [P, PASS], U16)
-        nc.vector.tensor_copy(w4_first[:].rearrange("p (t m) -> p t m", m=P), w4_unordered[:, 0])
         w4_codes = {0: w4_first[:]}
         w4_plane = {0: w4_plane_first[:]}
         w4_later = own("w4_later", [P, H - PASS], U16)
-        nc.vector.tensor_copy(w4_later[:].rearrange("p (g t m) -> p g t m", t=PACK, m=P), w4_unordered[:, 1:])
+        nc.vector.tensor_copy(w4_later[:].rearrange("p (g t m) -> p g t m", t=PACK, m=P),
+                              w4_raw_later[:].bitcast(U16).rearrange("p (g m t) -> p g t m", t=PACK, m=P))
+        w4_planes_later = own("w4_planes_later", [P, PASS], U8)
+        nc.vector.tensor_copy(w4_planes_later[:].rearrange("p (t m) -> p t m", t=PACK),
+                              w4_rows_later[:].rearrange("p (m t) -> p t m", t=PACK))
         for g in range(1, PASSES):
             w4_codes[g] = w4_later[:, (g - 1) * PASS : g * PASS]
+        w4_plane[1] = w4_planes_later[:]
+        w4_plane[2] = w4_plane_last[:]
         quantise_first(2, 4)
 
         w8_sb = placed("w8_sb", [P, PASSES, N], I32, GATED_AT + 12 * PICK_BYTES)
         nc.sync.dma_start(out=w8_sb[:], in_=w8_words.rearrange("a p c i -> p a (c i)").bitcast(I32))
-        for g in range(1, PASSES):
-            w4_plane[g] = w4_planes_later[:, (g - 1) * PASS : g * PASS]
-            nc.sync.dma_start(out=w4_plane[g].bitcast(I32)[0 : P - 4 * g, :], in_=w4_plane_first[:].bitcast(I32)[4 * g : P, :])
+        nc.sync.dma_start(out=w4_plane_last[:].bitcast(I32)[0 : P - 4, :], in_=w4_planes_later[:].bitcast(I32)[4:P, :])
         for q in range(P // QUADRANT):
             nc.sync.dma_start(out=w8_planes[:].bitcast(I32)[QUADRANT * q : QUADRANT * q + 4 * PASSES, :],
                               in_=w8_scales[:, 4 * q : 4 * q + 4, :].bitcast(I32))
@@ -198,30 +209,38 @@ def tile_list_chord_phase_voicings_kernel(tc, tab_words, tab_scales, offs, pos1,
             if h == 0:
                 if i == EARLY_PHASE:
                     phase[i] = own("early_phase", [P, S], F32)
-                elif i == RUN_PHASES[0]:
-                    phase[i] = placed("phase%d" % i, [P, S], F32, RUN_PHASE_AT)
-                elif i in RUN_PHASES:
+                elif i == WAIT_PHASE:
+                    phase[i] = placed("phase%d" % i, [P, S], F32, size_at(i - 2))
+                elif i == RUN_PHASE:
                     phase[i] = own("run_phase%d" % i, [P, S], F32)
                 else:
                     phase[i] = placed("phase%d" % i, [P, S], F32, AREAS_AT + (i % 3) * ROW_BYTES)
             copy(phase[i][:, h * BANK : (h + 1) * BANK], phase_banks[i, h][:])
 
         def colour_at(i):
-            return COLOURS_AT + (i % 6) * ROW_BYTES
+            return COLOURS_AT + (i % 7) * ROW_BYTES
 
-        def make_colour(i):
-            colour[i] = placed("colour%d" % i, [P, S], F32, colour_at(i))
-            g, t = divmod(i, PACK)
-            cols = slice(t * P, (t + 1) * P)
+        colour_banks = {}
+
+        def colour_sum(i, h):
+            if (i, h) not in colour_banks:
+                g, t = divmod(i, PACK)
+                cols = slice(t * P, (t + 1) * P)
+                colour_banks[i, h] = first_stage(w4_codes[g][:, cols].bitcast(FP4X4), w4_plane[g][:, cols], h, 4 + 2 * (i % 2) + h)
+
+        def colour_half(i, h, copy):
+            if h == 0:
+                colour[i] = placed("colour%d" % i, [P, S], F32, colour_at(i))
+            colour_sum(i, h)
+            copy(colour[i][:, h * BANK : (h + 1) * BANK], colour_banks[i, h][:])
+
+        def make_colour(i, copy):
             for h in range(2):
-                bank = first_stage(w4_codes[g][:, cols].bitcast(FP4X4), w4_plane[g][:, cols], h, 4 + 2 * (i % 2) + h)
-                nc.vector.tensor_copy(colour[i][:, h * BANK : (h + 1) * BANK], bank[:])
+                colour_half(i, h, copy)
 
         def size_at(i):
-            if i in RUNS and RUNS[i][1]:
-                return COLOURS_AT - PICK_BYTES // 2
             if i in RUNS:
-                return colour_at(RUNS[i][0][1]) - PICK_BYTES // 2
+                return colour_at(RUNS[i][1]) - PICK_BYTES // 2
             return GATED_AT + (i + 1) * PICK_BYTES
 
         def after_cosine(i, shape, dtype):
@@ -245,10 +264,9 @@ def tile_list_chord_phase_voicings_kernel(tc, tab_words, tab_scales, offs, pos1,
 
         vector_run, gpsimd_run = 2, 4
 
-        def round_on_gpsimd(g, place):
-            rounded = placed("w1_rounded%d" % g, [P, PACK * PASS], BF16, place)
-            nc.gpsimd.tensor_copy(rounded[:].rearrange("p (t m j) -> p m t j", t=PACK, j=PACK),
-                                  w1_later[g][:].rearrange("p j (m t) -> p m t j", t=PACK))
+        def round_w1(g, rounded):
+            nc.vector.tensor_copy(rounded[:].rearrange("p (t m j) -> p m j t", t=PACK, j=PACK),
+                                  w1_later[g][:].rearrange("p j (m t) -> p m j t", t=PACK))
             return rounded
 
         def quantise_w1(g, codes, rounded):
@@ -269,19 +287,25 @@ def tile_list_chord_phase_voicings_kernel(tc, tab_words, tab_scales, offs, pos1,
                     z_codes[g, n] = codes[:, cols]
                     z_plane[g, n] = plane[:, cols]
 
+        for h in range(2):
+            colour_sum(0, h)
+            colour_sum(1, h)
         phase_sums(0)
         phase_sums(1)
+        make_colour(0, nc.scalar.copy)
         phase_half(0, 0, nc.scalar.copy)
         phase_half(0, 1, nc.scalar.copy)
-        rounded_w1 = {1: round_on_gpsimd(1, ROUNDED_AT)}
         phase_sums(2)
+        make_colour(1, nc.vector.tensor_copy)
         phase_half(EARLY_PHASE, 0, nc.vector.tensor_copy)
         phase_half(EARLY_PHASE, 1, nc.vector.tensor_copy)
-        for i in FIRST_RUN:
-            make_colour(i)
+        make_colour(2, nc.vector.tensor_copy)
+        make_colour(3, nc.vector.tensor_copy)
+        second_rounded = round_w1(1, placed("second_rounded", [P, PACK * PASS], BF16, ROUNDED_AT))
+        make_colour(4, nc.vector.tensor_copy)
+        quantise_w1(1, own("w1_codes1", [P, PASS], U32), second_rounded)
 
         turned = {}
-        rest = {}
         all_bars = slice(0, B)
         run_number = {i: n for n, i in enumerate(sorted(RUNS))}
         for i in range(TILES - 2):
@@ -295,8 +319,7 @@ def tile_list_chord_phase_voicings_kernel(tc, tab_words, tab_scales, offs, pos1,
             else:
                 sine = ring.tile([P, B], F32, name="sine")
             cosine = ring.tile([P, B], F32, name="cosine")
-            reach = S + B if i in RUNS and RUNS[i][1] else B
-            size = placed("size%d" % i, [P, reach], F32, size_at(i))[:, 0:B]
+            size = placed("size%d" % i, [P, B], F32, size_at(i))[:]
 
             angle[i] = placed("angle%d" % i, [P, B], F32, AREAS_AT + ((i + 2) % 3) * ROW_BYTES)
             nc.scalar.activation(angle[i][:], phase[i][:].indirect(current_of[:]), ACT.Copy)
@@ -304,36 +327,37 @@ def tile_list_chord_phase_voicings_kernel(tc, tab_words, tab_scales, offs, pos1,
                 phase_half(i + 1, 1, nc.scalar.copy)
             if i + 3 < TILES:
                 phase_sums(i + 3)
+            if i == 0:
+                nc.scalar.activation(sine[:], angle[i][:], ACT.Sin)
             nc.scalar.activation(size, angle[i][:], ACT.Abs)
-            nc.scalar.activation(sine[:], angle[i][:], ACT.Sin)
+            if i > 0:
+                nc.scalar.activation(sine[:], angle[i][:], ACT.Sin)
             nc.scalar.activation(cosine[:], size, ACT.Sin, bias=half_pi[:], scale=-1.0)
-            if i + 2 not in RUN_PHASES:
+            if i + 2 not in (RUN_PHASE, WAIT_PHASE):
                 phase_half(i + 2, 0, nc.scalar.copy)
 
             product(sin_terms, bass_of, i, all_bars, sine[:])
             product(cos_terms, substitute_of, i, all_bars, cosine[:])
 
             if i in RUNS:
-                if run_number[i] == 0:
-                    rounded_w1[2] = round_on_gpsimd(2, result_at)
-                else:
-                    done = run_number[i] - 1
-                    bars = slice(0, GPSIMD_BARS[done])
-                    turned[done] = turn(nc.gpsimd, done, bars, placed("turned%d" % done, [P, bars.stop * PACK], BF16, result_at),
-                                        gpsimd_run)
-                for later in RUNS[i][0]:
-                    make_colour(later)
-                for later in RUNS[i][1]:
-                    phase_sum(later, 0)
-                    phase_half(later, 0, nc.vector.tensor_copy)
+                bars = slice(0, P * len(RUNS[i]))
+                turned[g - 1] = turn(nc.gpsimd, g - 1, bars, placed("turned%d" % g, [P, bars.stop * PACK], BF16, result_at), gpsimd_run)
+                for later in RUNS[i]:
+                    make_colour(later, nc.vector.tensor_copy)
+            if i == 4:
+                phase_sum(RUN_PHASE, 0)
+                phase_half(RUN_PHASE, 0, nc.vector.tensor_copy)
+            if i == 8:
+                colour_half(TILES - 1, 0, nc.vector.tensor_copy)
 
-            if i == 0:
-                quantise_w1(1, after_cosine(i, [P, PASS], U32), rounded_w1[1])
+            if i == 1:
+                third_rounded = round_w1(2, placed("third_rounded", [P, PACK * PASS], BF16, size_at(i) - PICK_BYTES))
             if i == 2:
-                quantise_w1(2, after_cosine(i, [P, PASS], U32), rounded_w1[2])
+                quantise_w1(2, after_cosine(i, [P, PASS], U32), third_rounded)
+            if i + 2 == WAIT_PHASE:
+                phase_half(WAIT_PHASE, 0, nc.vector.tensor_copy)
             if i == 9:
-                done = i // PACK - 1
-                rest[done] = turn(nc.vector, done, PIECES[2], after_cosine(i, [P, P * PACK], BF16), vector_run)
+                turned_late = turn(nc.vector, 1, slice(B // 2, B), after_cosine(i, [P, B // 2 * PACK], BF16), vector_run)
             if i == 6:
                 quantise_z(0, 1, after_cosine(i, [P, 2 * P], U32), turned[0][:, PIECES[1].start * PACK :])
 
@@ -362,6 +386,7 @@ def tile_list_chord_phase_voicings_kernel(tc, tab_words, tab_scales, offs, pos1,
         pick(early)
         phase_half(late, 1, nc.scalar.copy)
         half_trig(early, 0)
+        colour_half(late, 1, nc.scalar.copy)
         pick(late)
         half_trig(late, 0)
         half_trig(early, 1)
@@ -432,13 +457,13 @@ def tile_list_chord_phase_voicings_kernel(tc, tab_words, tab_scales, offs, pos1,
         product(cos_terms, substitute_of, early, PIECES[1], trig[early, 1][1][:, within_half(1)])
         close(0, first_turned, ())
         plain_products(1)
-        quantise_z(1, 1, after_half(late, 1, [P, P], U32), turned[1][:, PIECES[1].start * PACK :])
+        quantise_z(1, 1, after_half(late, 1, [P, P], U32), turned_late[:, 0 : P * PACK])
         score_passes(1, 1)
         second_turned = turn_last(1, own("second_turned", [P, P * PACK], BF16))
         product(sin_terms, bass_of, early, PIECES[2], trig[early, 1][0][:, within_half(2)])
         close(1, second_turned, ())
         product(cos_terms, substitute_of, early, PIECES[2], trig[early, 1][1][:, within_half(2)])
         plain_products(2)
-        quantise_z(1, 2, own("z_codes1_2", [P, P], U32), rest[1][:])
+        quantise_z(1, 2, own("z_codes1_2", [P, P], U32), turned_late[:, P * PACK :])
         score_passes(1, 2)
         close(2, turn_last(2, own("third_turned", [P, P * PACK], BF16)), (1,))

@@ -33,9 +33,10 @@ PICK_BYTES = 4 * B
 PART_BYTES = 4 * PACK * PASS
 ROUNDED_BYTES = 2 * PACK * PASS
 
-RUNS = {4: (5, 6, 7, 8), 8: (9, 10)}
+RUNS = {4: (5, 6, 7, 8), 8: (9, 10, 11)}
 RUN_PHASE = 8
 WAIT_PHASE = 5
+FIRST_RUN_PHASES = (2, 3)
 EARLY_PHASE = 1
 PIECES = (slice(0, 256), slice(256, 384), slice(384, 512))
 
@@ -43,7 +44,8 @@ W1_AT = 0
 AREAS_AT = W1_AT + PASSES * PART_BYTES
 COLOURS_AT = AREAS_AT + 3 * ROW_BYTES
 ROUNDED_AT = COLOURS_AT + 7 * ROW_BYTES
-PICKED_AT = ROUNDED_AT + 4 * ROUNDED_BYTES
+TABLE_AT = ROUNDED_AT + 3 * ROUNDED_BYTES
+PICKED_AT = TABLE_AT + 4 * PASSES * N
 GATED_AT = PICKED_AT + PICK_BYTES
 
 
@@ -89,7 +91,7 @@ def tile_list_chord_phase_voicings_kernel(tc, tab_words, tab_scales, offs, pos1,
         for q in range(P // QUADRANT):
             nc.sync.dma_start(out=tab_plane[:].bitcast(I32)[QUADRANT * q : QUADRANT * (q + 1), :],
                               in_=tab_scales[0][4 * q : 4 * q + 4, :].bitcast(I32).partition_broadcast(QUADRANT // 4))
-        tab_sb = own("tab_sb", [P, T], I32)
+        tab_sb = placed("tab_sb", [P, T], I32, TABLE_AT)
         nc.sync.dma_start(out=tab_sb[:], in_=tab_words[0].rearrange("p t i -> p (t i)").bitcast(I32))
         w1_rows = w1.rearrange("(p j) r -> p j r", j=PACK)
 
@@ -171,7 +173,7 @@ def tile_list_chord_phase_voicings_kernel(tc, tab_words, tab_scales, offs, pos1,
         w4_plane[2] = w4_plane_last[:]
         quantise_first(2, 4)
 
-        w8_sb = placed("w8_sb", [P, PASSES, N], I32, GATED_AT + 12 * PICK_BYTES)
+        w8_sb = placed("w8_sb", [P, PASSES, N], I32, TABLE_AT)
         nc.sync.dma_start(out=w8_sb[:], in_=w8_words.rearrange("a p c i -> p a (c i)").bitcast(I32))
         nc.sync.dma_start(out=w4_plane_last[:].bitcast(I32)[0 : P - 4, :], in_=w4_planes_later[:].bitcast(I32)[4:P, :])
         for q in range(P // QUADRANT):
@@ -211,7 +213,7 @@ def tile_list_chord_phase_voicings_kernel(tc, tab_words, tab_scales, offs, pos1,
                     phase[i] = own("early_phase", [P, S], F32)
                 elif i == WAIT_PHASE:
                     phase[i] = placed("phase%d" % i, [P, S], F32, size_at(i - 2))
-                elif i == RUN_PHASE:
+                elif i == RUN_PHASE or i in FIRST_RUN_PHASES:
                     phase[i] = own("run_phase%d" % i, [P, S], F32)
                 else:
                     phase[i] = placed("phase%d" % i, [P, S], F32, AREAS_AT + (i % 3) * ROW_BYTES)
@@ -241,7 +243,7 @@ def tile_list_chord_phase_voicings_kernel(tc, tab_words, tab_scales, offs, pos1,
         def size_at(i):
             if i in RUNS:
                 return colour_at(RUNS[i][1]) - PICK_BYTES // 2
-            return GATED_AT + (i + 1) * PICK_BYTES
+            return GATED_AT + (2 * i + 1) * PICK_BYTES
 
         def after_cosine(i, shape, dtype):
             return placed("after_cosine%d" % i, shape, dtype, size_at(i))
@@ -295,15 +297,19 @@ def tile_list_chord_phase_voicings_kernel(tc, tab_words, tab_scales, offs, pos1,
         make_colour(0, nc.scalar.copy)
         phase_half(0, 0, nc.scalar.copy)
         phase_half(0, 1, nc.scalar.copy)
+        second_rounded = placed("second_rounded", [P, PACK * PASS], BF16, ROUNDED_AT)
+        nc.gpsimd.tensor_copy(second_rounded[:].rearrange("p (t m j) -> p t m j", t=PACK, j=PACK),
+                              w1_later[1][:].rearrange("p j (m t) -> p t m j", t=PACK))
         phase_sums(2)
         make_colour(1, nc.vector.tensor_copy)
         phase_half(EARLY_PHASE, 0, nc.vector.tensor_copy)
         phase_half(EARLY_PHASE, 1, nc.vector.tensor_copy)
         make_colour(2, nc.vector.tensor_copy)
         make_colour(3, nc.vector.tensor_copy)
-        second_rounded = round_w1(1, placed("second_rounded", [P, PACK * PASS], BF16, ROUNDED_AT))
         make_colour(4, nc.vector.tensor_copy)
-        quantise_w1(1, own("w1_codes1", [P, PASS], U32), second_rounded)
+        for i in FIRST_RUN_PHASES:
+            phase_sum(i, 0)
+            phase_half(i, 0, nc.vector.tensor_copy)
 
         turned = {}
         all_bars = slice(0, B)
@@ -333,7 +339,7 @@ def tile_list_chord_phase_voicings_kernel(tc, tab_words, tab_scales, offs, pos1,
             if i > 0:
                 nc.scalar.activation(sine[:], angle[i][:], ACT.Sin)
             nc.scalar.activation(cosine[:], size, ACT.Sin, bias=half_pi[:], scale=-1.0)
-            if i + 2 not in (RUN_PHASE, WAIT_PHASE):
+            if i + 2 not in (RUN_PHASE, WAIT_PHASE) + FIRST_RUN_PHASES:
                 phase_half(i + 2, 0, nc.scalar.copy)
 
             product(sin_terms, bass_of, i, all_bars, sine[:])
@@ -347,17 +353,17 @@ def tile_list_chord_phase_voicings_kernel(tc, tab_words, tab_scales, offs, pos1,
             if i == 4:
                 phase_sum(RUN_PHASE, 0)
                 phase_half(RUN_PHASE, 0, nc.vector.tensor_copy)
-            if i == 8:
-                colour_half(TILES - 1, 0, nc.vector.tensor_copy)
 
+            if i == 0:
+                quantise_w1(1, placed("w1_codes1", [P, PASS], U32, size_at(i) - PICK_BYTES // 2), second_rounded)
             if i == 1:
-                third_rounded = round_w1(2, placed("third_rounded", [P, PACK * PASS], BF16, size_at(i) - PICK_BYTES))
+                third_rounded = round_w1(2, placed("third_rounded", [P, PACK * PASS], BF16, size_at(i) - PICK_BYTES // 2))
             if i == 2:
-                quantise_w1(2, after_cosine(i, [P, PASS], U32), third_rounded)
+                quantise_w1(2, placed("w1_codes2", [P, PASS], U32, size_at(i) + PICK_BYTES // 2), third_rounded)
             if i + 2 == WAIT_PHASE:
                 phase_half(WAIT_PHASE, 0, nc.vector.tensor_copy)
             if i == 9:
-                turned_late = turn(nc.vector, 1, slice(B // 2, B), after_cosine(i, [P, B // 2 * PACK], BF16), vector_run)
+                turned_late = turn(nc.vector, 1, PIECES[2], after_cosine(i, [P, P * PACK], BF16), vector_run)
             if i == 6:
                 quantise_z(0, 1, after_cosine(i, [P, 2 * P], U32), turned[0][:, PIECES[1].start * PACK :])
 
@@ -366,34 +372,43 @@ def tile_list_chord_phase_voicings_kernel(tc, tab_words, tab_scales, offs, pos1,
         halves = [slice(0, B // 2), slice(B // 2, B)]
         trig = {}
 
+        last_angles = placed("last_angles", [P, 2, B], F32, AREAS_AT + ((early + 2) % 3) * ROW_BYTES)
+
         def pick(i):
-            angle[i] = placed("angle%d" % i, [P, B], F32, AREAS_AT + ((i + 2) % 3) * ROW_BYTES)
-            nc.scalar.activation(angle[i][:], phase[i][:].indirect(current_of[:]), ACT.Copy)
+            nc.scalar.activation(last_angles[:, i - early, :], phase[i][:].indirect(current_of[:]), ACT.Copy)
 
-        def half_trig(i, h):
-            sines = own("half_sines%d_%d" % (i, h), [P, B // 2], F32)
-            cosines = own("half_cosines%d_%d" % (i, h), [P, B // 2], F32)
-            size = keep.tile([P, B // 2], F32, name="half_size", tag="half_size%d_%d" % (i, h), align_bytes=64)
-            nc.scalar.activation(size[:], angle[i][:, halves[h]], ACT.Abs)
-            nc.scalar.activation(sines[:], angle[i][:, halves[h]], ACT.Sin)
+        def first_half_trig(i):
+            sines = own("half_sines%d" % i, [P, B // 2], F32)
+            cosines = own("half_cosines%d" % i, [P, B // 2], F32)
+            size = keep.tile([P, B // 2], F32, name="half_size", tag="half_size%d" % i, align_bytes=64)
+            nc.scalar.activation(size[:], last_angles[:, i - early, halves[0]], ACT.Abs)
+            nc.scalar.activation(sines[:], last_angles[:, i - early, halves[0]], ACT.Sin)
             nc.scalar.activation(cosines[:], size[:], ACT.Sin, bias=half_pi[:], scale=-1.0)
-            trig[i, h] = (sines, cosines)
+            trig[i] = (sines, cosines)
 
-        def after_half(i, h, shape, dtype):
-            tile = keep.tile(shape, dtype, name="after_half", tag="half_size%d_%d" % (i, h), align_bytes=64)
+        def after_half(i, shape, dtype):
+            tile = keep.tile(shape, dtype, name="after_half", tag="half_size%d" % i, align_bytes=64)
             return tile
+
+        last_colours = own("last_colours", [P, 2, 2, B // 2], F32)
+
+        def fetch(side, i):
+            chords = (bass_of, substitute_of)[side]
+            nc.scalar.activation(last_colours[:, side, i - early, :], colour[i][:].indirect(entries_of(chords, halves[1])), ACT.Copy)
 
         pick(early)
         phase_half(late, 1, nc.scalar.copy)
-        half_trig(early, 0)
-        colour_half(late, 1, nc.scalar.copy)
+        first_half_trig(early)
         pick(late)
-        half_trig(late, 0)
-        half_trig(early, 1)
-        half_trig(late, 1)
-        last_colours = own("last_colours", [P, 2, B // 2], F32)
-        for side, chords in enumerate((bass_of, substitute_of)):
-            nc.scalar.activation(last_colours[:, side, :], colour[late][:].indirect(entries_of(chords, halves[1])), ACT.Copy)
+        first_half_trig(late)
+        last_trig = [own("last_trig%d" % side, [P, 2, B // 2], F32) for side in range(2)]
+        last_size = own("last_size", [P, 2, B // 2], F32)
+        nc.scalar.activation(last_size[:], last_angles[:, :, halves[1]], ACT.Abs)
+        nc.scalar.activation(last_trig[0][:], last_angles[:, :, halves[1]], ACT.Sin)
+        nc.scalar.activation(last_trig[1][:], last_size[:], ACT.Sin, bias=half_pi[:], scale=-1.0)
+        for side in range(2):
+            fetch(side, early)
+            fetch(side, late)
 
         groups = {0: [(0, 1), (2, 3), (4, 5)], 1: [(0, 1, 2), (3, 4, 5)], 2: [(0, 1, 2), (3, 4, 5)]}
         bank_numbers = {0: (0, 1, 2), 1: (4, 5), 2: (6, 7)}
@@ -431,10 +446,10 @@ def tile_list_chord_phase_voicings_kernel(tc, tab_words, tab_scales, offs, pos1,
         def within_half(n):
             return slice(PIECES[n].start - B // 2, PIECES[n].stop - B // 2)
 
-        def plain_products(n):
-            for side, terms in enumerate((sin_terms, cos_terms)):
-                nc.vector.tensor_tensor(terms[last_pass][:, PACK - 1, PIECES[n]], last_colours[:, side, within_half(n)],
-                                        trig[late, 1][side][:, within_half(n)], ALU.mult)
+        def plain_product(side, n):
+            terms = (sin_terms, cos_terms)[side]
+            nc.vector.tensor_tensor(terms[last_pass][:, PACK - 2 :, PIECES[n]], last_colours[:, side, :, within_half(n)],
+                                    last_trig[side][:, :, within_half(n)], ALU.mult)
 
         def turn_last(n, rounded):
             return turn(nc.vector, last_pass, PIECES[n], rounded, vector_run)
@@ -448,22 +463,20 @@ def tile_list_chord_phase_voicings_kernel(tc, tab_words, tab_scales, offs, pos1,
         score_passes(0, 1)
         score_passes(0, 2)
         for g, i in enumerate((early, late)):
-            product(sin_terms, bass_of, i, halves[0], trig[i, 0][0][:])
-            product(cos_terms, substitute_of, i, halves[0], trig[i, 0][1][:])
-            quantise_z(g, 0, after_half(i, 0, [P, B // 2], U32), turned[g][:, 0 : B // 2 * PACK])
+            product(sin_terms, bass_of, i, halves[0], trig[i][0][:])
+            product(cos_terms, substitute_of, i, halves[0], trig[i][1][:])
+            quantise_z(g, 0, after_half(i, [P, B // 2], U32), turned[g][:, 0 : B // 2 * PACK])
             score_passes(g, 0)
-        product(sin_terms, bass_of, early, PIECES[1], trig[early, 1][0][:, within_half(1)])
-        first_turned = turn_last(0, after_half(early, 1, [P, B // 2 * PACK], BF16))
-        product(cos_terms, substitute_of, early, PIECES[1], trig[early, 1][1][:, within_half(1)])
+        first_turned = turn_last(0, own("first_turned", [P, B // 2 * PACK], BF16))
+        plain_product(0, 1)
         close(0, first_turned, ())
-        plain_products(1)
-        quantise_z(1, 1, after_half(late, 1, [P, P], U32), turned_late[:, 0 : P * PACK])
+        plain_product(1, 1)
+        quantise_z(1, 1, own("z_codes1_1", [P, P], U32), turned[1][:, PIECES[1].start * PACK :])
         score_passes(1, 1)
         second_turned = turn_last(1, own("second_turned", [P, P * PACK], BF16))
-        product(sin_terms, bass_of, early, PIECES[2], trig[early, 1][0][:, within_half(2)])
+        plain_product(0, 2)
         close(1, second_turned, ())
-        product(cos_terms, substitute_of, early, PIECES[2], trig[early, 1][1][:, within_half(2)])
-        plain_products(2)
-        quantise_z(1, 2, own("z_codes1_2", [P, P], U32), turned_late[:, P * PACK :])
+        plain_product(1, 2)
+        quantise_z(1, 2, own("z_codes1_2", [P, P], U32), turned_late[:])
         score_passes(1, 2)
         close(2, turn_last(2, own("third_turned", [P, P * PACK], BF16)), (1,))

@@ -43,7 +43,7 @@ PIECES = (slice(0, 256), slice(256, 384), slice(384, 512))
 W1_AT = 0
 AREAS_AT = W1_AT + PASSES * PART_BYTES
 COLOURS_AT = AREAS_AT + 3 * ROW_BYTES
-ROUNDED_AT = COLOURS_AT + 7 * ROW_BYTES
+ROUNDED_AT = COLOURS_AT + 8 * ROW_BYTES
 TABLE_AT = ROUNDED_AT + 3 * ROUNDED_BYTES
 PICKED_AT = TABLE_AT + 4 * PASSES * N
 GATED_AT = PICKED_AT + PICK_BYTES
@@ -198,14 +198,20 @@ def tile_list_chord_phase_voicings_kernel(tc, tab_words, tab_scales, offs, pos1,
         colour = {}
         angle = {}
 
+        turn_taken = []
+
+        def next_bank():
+            turn_taken.append(0)
+            return 2 + (len(turn_taken) - 1) % 6
+
+        def on_vector(i, h):
+            return i == EARLY_PHASE or (h == 0 and i in (RUN_PHASE, WAIT_PHASE) + FIRST_RUN_PHASES)
+
         def phase_sum(i, h):
             if (i, h) not in phase_banks:
                 codes, plane = stationary[i]
-                phase_banks[i, h] = first_stage(codes.bitcast(FP8X4), plane, h, 2 * (i % 2) + h)
+                phase_banks[i, h] = first_stage(codes.bitcast(FP8X4), plane, h, next_bank() if on_vector(i, h) else h)
 
-        def phase_sums(i):
-            for h in range(2):
-                phase_sum(i, h)
 
         def phase_half(i, h, copy):
             if h == 0:
@@ -217,10 +223,11 @@ def tile_list_chord_phase_voicings_kernel(tc, tab_words, tab_scales, offs, pos1,
                     phase[i] = own("run_phase%d" % i, [P, S], F32)
                 else:
                     phase[i] = placed("phase%d" % i, [P, S], F32, AREAS_AT + (i % 3) * ROW_BYTES)
+            phase_sum(i, h)
             copy(phase[i][:, h * BANK : (h + 1) * BANK], phase_banks[i, h][:])
 
         def colour_at(i):
-            return COLOURS_AT + (i % 7) * ROW_BYTES
+            return COLOURS_AT + (i % 8) * ROW_BYTES
 
         colour_banks = {}
 
@@ -228,7 +235,7 @@ def tile_list_chord_phase_voicings_kernel(tc, tab_words, tab_scales, offs, pos1,
             if (i, h) not in colour_banks:
                 g, t = divmod(i, PACK)
                 cols = slice(t * P, (t + 1) * P)
-                colour_banks[i, h] = first_stage(w4_codes[g][:, cols].bitcast(FP4X4), w4_plane[g][:, cols], h, 4 + 2 * (i % 2) + h)
+                colour_banks[i, h] = first_stage(w4_codes[g][:, cols].bitcast(FP4X4), w4_plane[g][:, cols], h, next_bank())
 
         def colour_half(i, h, copy):
             if h == 0:
@@ -292,15 +299,15 @@ def tile_list_chord_phase_voicings_kernel(tc, tab_words, tab_scales, offs, pos1,
         for h in range(2):
             colour_sum(0, h)
             colour_sum(1, h)
-        phase_sums(0)
-        phase_sums(1)
+        for i in range(2):
+            for h in range(2):
+                phase_sum(i, h)
         make_colour(0, nc.scalar.copy)
         phase_half(0, 0, nc.scalar.copy)
         phase_half(0, 1, nc.scalar.copy)
         second_rounded = placed("second_rounded", [P, PACK * PASS], BF16, ROUNDED_AT)
         nc.gpsimd.tensor_copy(second_rounded[:].rearrange("p (t m j) -> p t m j", t=PACK, j=PACK),
                               w1_later[1][:].rearrange("p j (m t) -> p t m j", t=PACK))
-        phase_sums(2)
         make_colour(1, nc.vector.tensor_copy)
         phase_half(EARLY_PHASE, 0, nc.vector.tensor_copy)
         phase_half(EARLY_PHASE, 1, nc.vector.tensor_copy)
@@ -308,13 +315,12 @@ def tile_list_chord_phase_voicings_kernel(tc, tab_words, tab_scales, offs, pos1,
         make_colour(3, nc.vector.tensor_copy)
         make_colour(4, nc.vector.tensor_copy)
         for i in FIRST_RUN_PHASES:
-            phase_sum(i, 0)
             phase_half(i, 0, nc.vector.tensor_copy)
 
         turned = {}
         all_bars = slice(0, B)
         run_number = {i: n for n, i in enumerate(sorted(RUNS))}
-        for i in range(TILES - 2):
+        for i in range(TILES - 3):
             g, t = divmod(i, PACK)
             if t == 0:
                 sin_terms[g] = keep.tile([P, PACK, B], F32, name="sin_terms", tag="sin_terms%d" % (g % 2))
@@ -325,14 +331,12 @@ def tile_list_chord_phase_voicings_kernel(tc, tab_words, tab_scales, offs, pos1,
             else:
                 sine = ring.tile([P, B], F32, name="sine")
             cosine = ring.tile([P, B], F32, name="cosine")
-            size = placed("size%d" % i, [P, B], F32, size_at(i))[:]
+            size = placed("size%d" % i, [P, S + B if i in RUNS else B], F32, size_at(i))[:, 0:B]
 
             angle[i] = placed("angle%d" % i, [P, B], F32, AREAS_AT + ((i + 2) % 3) * ROW_BYTES)
             nc.scalar.activation(angle[i][:], phase[i][:].indirect(current_of[:]), ACT.Copy)
             if i + 1 != EARLY_PHASE:
                 phase_half(i + 1, 1, nc.scalar.copy)
-            if i + 3 < TILES:
-                phase_sums(i + 3)
             if i == 0:
                 nc.scalar.activation(sine[:], angle[i][:], ACT.Sin)
             nc.scalar.activation(size, angle[i][:], ACT.Abs)
@@ -351,7 +355,6 @@ def tile_list_chord_phase_voicings_kernel(tc, tab_words, tab_scales, offs, pos1,
                 for later in RUNS[i]:
                     make_colour(later, nc.vector.tensor_copy)
             if i == 4:
-                phase_sum(RUN_PHASE, 0)
                 phase_half(RUN_PHASE, 0, nc.vector.tensor_copy)
 
             if i == 0:
@@ -362,27 +365,25 @@ def tile_list_chord_phase_voicings_kernel(tc, tab_words, tab_scales, offs, pos1,
                 quantise_w1(2, placed("w1_codes2", [P, PASS], U32, size_at(i) + PICK_BYTES // 2), third_rounded)
             if i + 2 == WAIT_PHASE:
                 phase_half(WAIT_PHASE, 0, nc.vector.tensor_copy)
-            if i == 9:
-                turned_late = turn(nc.vector, 1, PIECES[2], after_cosine(i, [P, P * PACK], BF16), vector_run)
             if i == 6:
                 quantise_z(0, 1, after_cosine(i, [P, 2 * P], U32), turned[0][:, PIECES[1].start * PACK :])
 
         last_pass = PASSES - 1
-        early, late = TILES - 2, TILES - 1
+        third, early, late = TILES - 3, TILES - 2, TILES - 1
         halves = [slice(0, B // 2), slice(B // 2, B)]
         trig = {}
 
-        last_angles = placed("last_angles", [P, 2, B], F32, AREAS_AT + ((early + 2) % 3) * ROW_BYTES)
+        last_angles = placed("last_angles", [P, 3, B], F32, GATED_AT + 14 * PICK_BYTES)
 
         def pick(i):
-            nc.scalar.activation(last_angles[:, i - early, :], phase[i][:].indirect(current_of[:]), ACT.Copy)
+            nc.scalar.activation(last_angles[:, i - third, :], phase[i][:].indirect(current_of[:]), ACT.Copy)
 
         def first_half_trig(i):
             sines = own("half_sines%d" % i, [P, B // 2], F32)
             cosines = own("half_cosines%d" % i, [P, B // 2], F32)
             size = keep.tile([P, B // 2], F32, name="half_size", tag="half_size%d" % i, align_bytes=64)
-            nc.scalar.activation(size[:], last_angles[:, i - early, halves[0]], ACT.Abs)
-            nc.scalar.activation(sines[:], last_angles[:, i - early, halves[0]], ACT.Sin)
+            nc.scalar.activation(size[:], last_angles[:, i - third, halves[0]], ACT.Abs)
+            nc.scalar.activation(sines[:], last_angles[:, i - third, halves[0]], ACT.Sin)
             nc.scalar.activation(cosines[:], size[:], ACT.Sin, bias=half_pi[:], scale=-1.0)
             trig[i] = (sines, cosines)
 
@@ -390,28 +391,33 @@ def tile_list_chord_phase_voicings_kernel(tc, tab_words, tab_scales, offs, pos1,
             tile = keep.tile(shape, dtype, name="after_half", tag="half_size%d" % i, align_bytes=64)
             return tile
 
-        last_colours = own("last_colours", [P, 2, 2, B // 2], F32)
+        last_colours = own("last_colours", [P, 2, 2, 2, P], F32)
 
-        def fetch(side, i):
+        def fetch(side, i, n):
             chords = (bass_of, substitute_of)[side]
-            nc.scalar.activation(last_colours[:, side, i - early, :], colour[i][:].indirect(entries_of(chords, halves[1])), ACT.Copy)
+            nc.scalar.activation(last_colours[:, n - 1, side, i - early, :], colour[i][:].indirect(entries_of(chords, PIECES[n])), ACT.Copy)
 
+        pick(third)
+        phase_half(early, 1, nc.scalar.copy)
+        first_half_trig(third)
+        phase_half(late, 0, nc.scalar.copy)
         pick(early)
         phase_half(late, 1, nc.scalar.copy)
         first_half_trig(early)
         pick(late)
         first_half_trig(late)
-        last_trig = [own("last_trig%d" % side, [P, 2, B // 2], F32) for side in range(2)]
-        last_size = own("last_size", [P, 2, B // 2], F32)
+        last_trig = [own("last_trig%d" % side, [P, 3, B // 2], F32) for side in range(2)]
+        last_size = own("last_size", [P, 3, B // 2], F32)
         nc.scalar.activation(last_size[:], last_angles[:, :, halves[1]], ACT.Abs)
         nc.scalar.activation(last_trig[0][:], last_angles[:, :, halves[1]], ACT.Sin)
         nc.scalar.activation(last_trig[1][:], last_size[:], ACT.Sin, bias=half_pi[:], scale=-1.0)
-        for side in range(2):
-            fetch(side, early)
-            fetch(side, late)
+        for n in (1, 2):
+            for side in range(2):
+                fetch(side, early, n)
+                fetch(side, late, n)
 
-        groups = {0: [(0, 1), (2, 3), (4, 5)], 1: [(0, 1, 2), (3, 4, 5)], 2: [(0, 1, 2), (3, 4, 5)]}
-        bank_numbers = {0: (0, 1, 2), 1: (4, 5), 2: (6, 7)}
+        groups = {0: [(0, 1), (2, 3), (4, 5)], 1: [(0, 1, 2), (3, 4, 5)], 2: [(0, 1), (2, 3), (4, 5)]}
+        bank_numbers = {0: (0, 1, 2), 1: (4, 5), 2: (3, 6, 7)}
         score_banks = {n: [bank_tile(number) for number in bank_numbers[n]] for n in range(len(PIECES))}
 
         def score_passes(g, n):
@@ -448,8 +454,8 @@ def tile_list_chord_phase_voicings_kernel(tc, tab_words, tab_scales, offs, pos1,
 
         def plain_product(side, n):
             terms = (sin_terms, cos_terms)[side]
-            nc.vector.tensor_tensor(terms[last_pass][:, PACK - 2 :, PIECES[n]], last_colours[:, side, :, within_half(n)],
-                                    last_trig[side][:, :, within_half(n)], ALU.mult)
+            nc.vector.tensor_tensor(terms[last_pass][:, PACK - 2 :, PIECES[n]], last_colours[:, n - 1, side],
+                                    last_trig[side][:, 1:, within_half(n)], ALU.mult)
 
         def turn_last(n, rounded):
             return turn(nc.vector, last_pass, PIECES[n], rounded, vector_run)
@@ -462,21 +468,31 @@ def tile_list_chord_phase_voicings_kernel(tc, tab_words, tab_scales, offs, pos1,
 
         score_passes(0, 1)
         score_passes(0, 2)
+        def fused(side, n):
+            product((sin_terms, cos_terms)[side], (bass_of, substitute_of)[side], third, PIECES[n], last_trig[side][:, 0, within_half(n)])
+
+        product(sin_terms, bass_of, third, halves[0], trig[third][0][:])
+        product(cos_terms, substitute_of, third, halves[0], trig[third][1][:])
+        turned_late = turn(nc.vector, 1, PIECES[2], after_half(third, [P, P * PACK], BF16), vector_run)
         for g, i in enumerate((early, late)):
             product(sin_terms, bass_of, i, halves[0], trig[i][0][:])
             product(cos_terms, substitute_of, i, halves[0], trig[i][1][:])
             quantise_z(g, 0, after_half(i, [P, B // 2], U32), turned[g][:, 0 : B // 2 * PACK])
             score_passes(g, 0)
         first_turned = turn_last(0, own("first_turned", [P, B // 2 * PACK], BF16))
-        plain_product(0, 1)
-        close(0, first_turned, ())
-        plain_product(1, 1)
         quantise_z(1, 1, own("z_codes1_1", [P, P], U32), turned[1][:, PIECES[1].start * PACK :])
         score_passes(1, 1)
+        close(0, first_turned, ())
+        fused(0, 1)
+        fused(1, 1)
+        plain_product(0, 1)
+        plain_product(1, 1)
+        fused(0, 2)
         second_turned = turn_last(1, own("second_turned", [P, P * PACK], BF16))
-        plain_product(0, 2)
+        fused(1, 2)
         close(1, second_turned, ())
+        plain_product(0, 2)
         plain_product(1, 2)
         quantise_z(1, 2, own("z_codes1_2", [P, P], U32), turned_late[:])
         score_passes(1, 2)
-        close(2, turn_last(2, own("third_turned", [P, P * PACK], BF16)), (1,))
+        close(2, turn_last(2, own("third_turned", [P, P * PACK], BF16)), (1, 2))

@@ -273,16 +273,11 @@ def tile_list_chord_phase_voicings_kernel(tc, tab_words, tab_scales, offs, pos1,
 
         vector_run, gpsimd_run = 2, 4
 
-        def round_w1(g, rounded):
-            nc.vector.tensor_copy(rounded[:].rearrange("p (t m j) -> p m j t", t=PACK, j=PACK),
-                                  w1_later[g][:].rearrange("p j (m t) -> p m j t", t=PACK))
-            return rounded
-
-        def quantise_w1(g, codes, rounded):
-            plane = own("w1_plane%d" % g, [P, PASS], U8)
+        def quantise_w1(first, codes, rounded):
+            plane = own("w1_plane%d" % first, [P, codes.shape[1]], U8)
             quantise(codes[:], plane[:], rounded[:])
-            for t in range(PACK):
-                stationary[PACK * g + t] = (codes[:, t * P : (t + 1) * P], plane[:, t * P : (t + 1) * P])
+            for t in range(codes.shape[1] // P):
+                stationary[first + t] = (codes[:, t * P : (t + 1) * P], plane[:, t * P : (t + 1) * P])
 
         z_codes = {}
         z_plane = {}
@@ -308,6 +303,9 @@ def tile_list_chord_phase_voicings_kernel(tc, tab_words, tab_scales, offs, pos1,
         second_rounded = placed("second_rounded", [P, PACK * PASS], BF16, ROUNDED_AT)
         nc.gpsimd.tensor_copy(second_rounded[:].rearrange("p (t m j) -> p t m j", t=PACK, j=PACK),
                               w1_later[1][:].rearrange("p j (m t) -> p t m j", t=PACK))
+        last_rounded = own("last_rounded", [P, PASS], BF16)
+        nc.gpsimd.tensor_copy(last_rounded[:].rearrange("p (m j) -> p m j", j=PACK),
+                              w1_later[2][:].rearrange("p j (m t) -> p t m j", t=PACK)[:, PACK - 1])
         make_colour(1, nc.vector.tensor_copy)
         phase_half(EARLY_PHASE, 0, nc.vector.tensor_copy)
         phase_half(EARLY_PHASE, 1, nc.vector.tensor_copy)
@@ -358,15 +356,19 @@ def tile_list_chord_phase_voicings_kernel(tc, tab_words, tab_scales, offs, pos1,
                 phase_half(RUN_PHASE, 0, nc.vector.tensor_copy)
 
             if i == 0:
-                quantise_w1(1, placed("w1_codes1", [P, PASS], U32, size_at(i) - PICK_BYTES // 2), second_rounded)
+                quantise_w1(PACK, placed("w1_codes1", [P, PASS], U32, size_at(i) - PICK_BYTES // 2), second_rounded)
             if i == 1:
-                third_rounded = round_w1(2, placed("third_rounded", [P, PACK * PASS], BF16, size_at(i) - PICK_BYTES // 2))
+                third_rounded = placed("third_rounded", [P, (PACK - 1) * PASS], BF16, size_at(i) - PICK_BYTES // 2)
+                nc.vector.tensor_copy(third_rounded[:].rearrange("p (t m j) -> p m j t", t=PACK - 1, j=PACK),
+                                      w1_later[2][:].rearrange("p j (m t) -> p m j t", t=PACK)[:, :, :, 0 : PACK - 1])
             if i == 2:
-                quantise_w1(2, placed("w1_codes2", [P, PASS], U32, size_at(i) + PICK_BYTES // 2), third_rounded)
+                quantise_w1(2 * PACK, placed("w1_codes2", [P, PASS - P], U32, size_at(i) + PICK_BYTES // 2), third_rounded)
+            if i == 5:
+                quantise_w1(TILES - 1, after_cosine(i, [P, P], U32), last_rounded)
             if i + 2 == WAIT_PHASE:
                 phase_half(WAIT_PHASE, 0, nc.vector.tensor_copy)
             if i == 6:
-                quantise_z(0, 1, after_cosine(i, [P, 2 * P], U32), turned[0][:, PIECES[1].start * PACK :])
+                quantise_z(0, 1, after_cosine(i, [P, P], U32), turned[0][:, PIECES[1].start * PACK : PIECES[1].stop * PACK])
 
         last_pass = PASSES - 1
         third, early, late = TILES - 3, TILES - 2, TILES - 1
@@ -407,7 +409,7 @@ def tile_list_chord_phase_voicings_kernel(tc, tab_words, tab_scales, offs, pos1,
         pick(late)
         first_half_trig(late)
         last_trig = [own("last_trig%d" % side, [P, 3, B // 2], F32) for side in range(2)]
-        last_size = own("last_size", [P, 3, B // 2], F32)
+        last_size = keep.tile([P, 3, B // 2], F32, name="last_size", tag="last_size", align_bytes=64)
         nc.scalar.activation(last_size[:], last_angles[:, :, halves[1]], ACT.Abs)
         nc.scalar.activation(last_trig[0][:], last_angles[:, :, halves[1]], ACT.Sin)
         nc.scalar.activation(last_trig[1][:], last_size[:], ACT.Sin, bias=half_pi[:], scale=-1.0)
@@ -467,7 +469,6 @@ def tile_list_chord_phase_voicings_kernel(tc, tab_words, tab_scales, offs, pos1,
             store_scores(n, on_vector)
 
         score_passes(0, 1)
-        score_passes(0, 2)
         def fused(side, n):
             product((sin_terms, cos_terms)[side], (bass_of, substitute_of)[side], third, PIECES[n], last_trig[side][:, 0, within_half(n)])
 
@@ -488,11 +489,13 @@ def tile_list_chord_phase_voicings_kernel(tc, tab_words, tab_scales, offs, pos1,
         plain_product(0, 1)
         plain_product(1, 1)
         fused(0, 2)
-        second_turned = turn_last(1, own("second_turned", [P, P * PACK], BF16))
+        second_turned = turn_last(1, keep.tile([P, P * PACK], BF16, name="second_turned", tag="second", align_bytes=64))
         fused(1, 2)
         close(1, second_turned, ())
         plain_product(0, 2)
+        quantise_z(0, 2, keep.tile([P, P], U32, name="z_codes0_2", tag="second", align_bytes=64), turned[0][:, PIECES[2].start * PACK :])
+        score_passes(0, 2)
         plain_product(1, 2)
-        quantise_z(1, 2, own("z_codes1_2", [P, P], U32), turned_late[:])
+        quantise_z(1, 2, keep.tile([P, P], U32, name="z_codes1_2", tag="last_size", align_bytes=64), turned_late[:])
         score_passes(1, 2)
         close(2, turn_last(2, own("third_turned", [P, P * PACK], BF16)), (1, 2))

@@ -71,7 +71,7 @@ def tile_list_chord_phase_voicings_kernel(tc, tab_words, tab_scales, offs, pos1,
             nc.sync.dma_start(tile[:], entries)
             return tile
 
-        w4_rows_first = placed("w4_rows_first", [P, PASS], U8, PICKED_AT)
+        w4_rows_first = own("w4_rows_first", [P, PASS], U8)
         w4_rows_later = own("w4_rows_later", [P, PASS], U8)
         w4_plane_last = own("w4_plane_last", [P, PASS], U8)
         w8_planes = own("w8_planes", [P, N], U8)
@@ -100,11 +100,11 @@ def tile_list_chord_phase_voicings_kernel(tc, tab_words, tab_scales, offs, pos1,
             nc.sync.dma_start(out=raw[:], in_=w1_rows[:, :, first : first + width])
             return raw
 
-        w4_raw_first = own("w4_raw_first", [P, PASS // 2], I32)
-        nc.sync.dma_start(out=w4_raw_first[:], in_=w4_words[0].bitcast(I32)[:, 0 : PASS // 2])
         for q in range(P // QUADRANT):
             nc.sync.dma_start(out=w4_rows_first[:].bitcast(I32)[QUADRANT * q : QUADRANT * q + 4, :],
                               in_=w4_scales[0][4 * q : 4 * q + 4, 0:PASS].bitcast(I32))
+        w4_raw_first = placed("w4_raw_first", [P, PASS // 2], I32, PICKED_AT)
+        nc.sync.dma_start(out=w4_raw_first[:], in_=w4_words[0].bitcast(I32)[:, 0 : PASS // 2])
         w1_halves = [load_w1("w1_half%d" % h, place, h * PASS // 2, PASS // 2) for h, place in enumerate((W1_AT, COLOURS_AT))]
         w4_raw_later = placed("w4_raw_later", [P, (H - PASS) // 2], I32, COLOURS_AT + 2 * ROW_BYTES - PICK_BYTES // 2)
         nc.sync.dma_start(out=w4_raw_later[:], in_=w4_words[0].bitcast(I32)[:, PASS // 2 :])
@@ -120,6 +120,9 @@ def tile_list_chord_phase_voicings_kernel(tc, tab_words, tab_scales, offs, pos1,
         picked_plane = own("picked_plane", [P, S], U8)
         nc.vector.tensor_copy(picked_plane[:], tab_plane[:].indirect(offs_sb[:]))
         picked_codes = []
+        w4_first = own("w4_first", [P, PASS], U16)
+        nc.scalar.copy(w4_first[:].rearrange("p (t m) -> p m t", m=P),
+                       w4_raw_first[:].bitcast(U16).rearrange("p (m t) -> p m t", t=PACK))
         for h in range(S // BANK):
             codes = placed("picked_codes%d" % h, [P, BANK], U32, PICKED_AT) if h else own("picked_codes0", [P, BANK], U32)
             entries = offs_sb[:, h * BANK // PER_COLUMN : (h + 1) * BANK // PER_COLUMN]
@@ -129,9 +132,6 @@ def tile_list_chord_phase_voicings_kernel(tc, tab_words, tab_scales, offs, pos1,
                 w4_plane_first = own("w4_plane_first", [P, PASS], U8)
                 nc.vector.tensor_copy(w4_plane_first[:].rearrange("p (t m) -> p t m", t=PACK),
                                       w4_rows_first[:].rearrange("p (m t) -> p t m", t=PACK))
-        w4_first = own("w4_first", [P, PASS], U16)
-        nc.scalar.copy(w4_first[:].rearrange("p (t m) -> p m t", m=P),
-                       w4_raw_first[:].bitcast(U16).rearrange("p (m t) -> p m t", t=PACK))
 
         first_rounded = placed("first_rounded", [P, PACK, P, PACK], BF16, ROUNDED_AT)
 
@@ -480,7 +480,7 @@ def tile_list_chord_phase_voicings_kernel(tc, tab_words, tab_scales, offs, pos1,
             product(cos_terms, substitute_of, i, halves[0], trig[i][1][:])
             quantise_z(g, 0, after_half(i, [P, B // 2], U32), turned[g][:, 0 : B // 2 * PACK])
             score_passes(g, 0)
-        first_turned = turn_last(0, own("first_turned", [P, B // 2 * PACK], BF16))
+        first_turned = turn_last(0, keep.tile([P, B // 2 * PACK], BF16, name="first_turned", tag="first", align_bytes=64))
         quantise_z(1, 1, own("z_codes1_1", [P, P], U32), turned[1][:, PIECES[1].start * PACK :])
         score_passes(1, 1)
         close(0, first_turned, ())
@@ -488,14 +488,14 @@ def tile_list_chord_phase_voicings_kernel(tc, tab_words, tab_scales, offs, pos1,
         fused(1, 1)
         plain_product(0, 1)
         plain_product(1, 1)
+        quantise_z(0, 2, keep.tile([P, P], U32, name="z_codes0_2", tag="first", align_bytes=64), turned[0][:, PIECES[2].start * PACK :])
+        score_passes(0, 2)
         fused(0, 2)
         second_turned = turn_last(1, keep.tile([P, P * PACK], BF16, name="second_turned", tag="second", align_bytes=64))
         fused(1, 2)
         close(1, second_turned, ())
         plain_product(0, 2)
-        quantise_z(0, 2, keep.tile([P, P], U32, name="z_codes0_2", tag="second", align_bytes=64), turned[0][:, PIECES[2].start * PACK :])
-        score_passes(0, 2)
-        plain_product(1, 2)
-        quantise_z(1, 2, keep.tile([P, P], U32, name="z_codes1_2", tag="last_size", align_bytes=64), turned_late[:])
+        quantise_z(1, 2, keep.tile([P, P], U32, name="z_codes1_2", tag="second", align_bytes=64), turned_late[:])
         score_passes(1, 2)
+        plain_product(1, 2)
         close(2, turn_last(2, own("third_turned", [P, P * PACK], BF16)), (1, 2))

@@ -34,10 +34,10 @@ PART_BYTES = 4 * PACK * PASS
 ROUNDED_BYTES = 2 * PACK * PASS
 
 RUNS = {4: (5, 6, 7, 8), 8: (9, 10, 11)}
-RUN_PHASE = 8
-WAIT_PHASE = 5
-FIRST_RUN_PHASES = (2, 3)
 EARLY_PHASE = 1
+FIRST_RUN_PHASES = (2, 3)
+WAIT_PHASE = 5
+RUN_PHASE = 8
 PIECES = (slice(0, 256), slice(256, 384), slice(384, 512))
 
 W1_AT = 0
@@ -45,8 +45,7 @@ AREAS_AT = W1_AT + PASSES * PART_BYTES
 COLOURS_AT = AREAS_AT + 3 * ROW_BYTES
 ROUNDED_AT = COLOURS_AT + 8 * ROW_BYTES
 TABLE_AT = ROUNDED_AT + 3 * ROUNDED_BYTES
-PICKED_AT = TABLE_AT + 4 * PASSES * N
-GATED_AT = PICKED_AT + PICK_BYTES
+GATED_AT = TABLE_AT + 4 * PASSES * N
 
 
 def tile_list_chord_phase_voicings_kernel(tc, tab_words, tab_scales, offs, pos1, pos2, pos3, w1, w4_words,
@@ -103,7 +102,7 @@ def tile_list_chord_phase_voicings_kernel(tc, tab_words, tab_scales, offs, pos1,
         for q in range(P // QUADRANT):
             nc.sync.dma_start(out=w4_rows_first[:].bitcast(I32)[QUADRANT * q : QUADRANT * q + 4, :],
                               in_=w4_scales[0][4 * q : 4 * q + 4, 0:PASS].bitcast(I32))
-        w4_raw_first = placed("w4_raw_first", [P, PASS // 2], I32, PICKED_AT)
+        w4_raw_first = own("w4_raw_first", [P, PASS // 2], I32)
         nc.sync.dma_start(out=w4_raw_first[:], in_=w4_words[0].bitcast(I32)[:, 0 : PASS // 2])
         w1_halves = [load_w1("w1_half%d" % h, place, h * PASS // 2, PASS // 2) for h, place in enumerate((W1_AT, COLOURS_AT))]
         w4_raw_later = placed("w4_raw_later", [P, (H - PASS) // 2], I32, COLOURS_AT + 2 * ROW_BYTES - PICK_BYTES // 2)
@@ -124,13 +123,13 @@ def tile_list_chord_phase_voicings_kernel(tc, tab_words, tab_scales, offs, pos1,
         nc.scalar.copy(w4_first[:].rearrange("p (t m) -> p m t", m=P),
                        w4_raw_first[:].bitcast(U16).rearrange("p (m t) -> p m t", t=PACK))
         for h in range(S // BANK):
-            codes = placed("picked_codes%d" % h, [P, BANK], U32, PICKED_AT) if h else own("picked_codes0", [P, BANK], U32)
+            codes = own("picked_codes%d" % h, [P, BANK], U32)
             entries = offs_sb[:, h * BANK // PER_COLUMN : (h + 1) * BANK // PER_COLUMN]
             nc.vector.tensor_copy(codes[:], tab_sb[:].bitcast(U32).indirect(entries))
             picked_codes.append(codes)
             if h == 0:
                 w4_plane_first = own("w4_plane_first", [P, PASS], U8)
-                nc.vector.tensor_copy(w4_plane_first[:].rearrange("p (t m) -> p t m", t=PACK),
+                nc.gpsimd.tensor_copy(w4_plane_first[:].rearrange("p (t m) -> p t m", t=PACK),
                                       w4_rows_first[:].rearrange("p (m t) -> p t m", t=PACK))
 
         first_rounded = placed("first_rounded", [P, PACK, P, PACK], BF16, ROUNDED_AT)
@@ -164,14 +163,14 @@ def tile_list_chord_phase_voicings_kernel(tc, tab_words, tab_scales, offs, pos1,
         w4_later = own("w4_later", [P, H - PASS], U16)
         nc.vector.tensor_copy(w4_later[:].rearrange("p (g t m) -> p g t m", t=PACK, m=P),
                               w4_raw_later[:].bitcast(U16).rearrange("p (g m t) -> p g t m", t=PACK, m=P))
-        w4_planes_later = own("w4_planes_later", [P, PASS], U8)
-        nc.vector.tensor_copy(w4_planes_later[:].rearrange("p (t m) -> p t m", t=PACK),
-                              w4_rows_later[:].rearrange("p (m t) -> p t m", t=PACK))
         for g in range(1, PASSES):
             w4_codes[g] = w4_later[:, (g - 1) * PASS : g * PASS]
+        quantise_first(2, 4)
+        w4_planes_later = placed("w4_planes_later", [P, PASS], U8, ROUNDED_AT + ROUNDED_BYTES - PASS)
+        nc.gpsimd.tensor_copy(w4_planes_later[:].rearrange("p (t m) -> p t m", t=PACK),
+                              w4_rows_later[:].rearrange("p (m t) -> p t m", t=PACK))
         w4_plane[1] = w4_planes_later[:]
         w4_plane[2] = w4_plane_last[:]
-        quantise_first(2, 4)
 
         w8_sb = placed("w8_sb", [P, PASSES, N], I32, TABLE_AT)
         nc.sync.dma_start(out=w8_sb[:], in_=w8_words.rearrange("a p c i -> p a (c i)").bitcast(I32))
@@ -211,7 +210,6 @@ def tile_list_chord_phase_voicings_kernel(tc, tab_words, tab_scales, offs, pos1,
             if (i, h) not in phase_banks:
                 codes, plane = stationary[i]
                 phase_banks[i, h] = first_stage(codes.bitcast(FP8X4), plane, h, next_bank() if on_vector(i, h) else h)
-
 
         def phase_half(i, h, copy):
             if h == 0:
@@ -300,12 +298,9 @@ def tile_list_chord_phase_voicings_kernel(tc, tab_words, tab_scales, offs, pos1,
         make_colour(0, nc.scalar.copy)
         phase_half(0, 0, nc.scalar.copy)
         phase_half(0, 1, nc.scalar.copy)
-        second_rounded = placed("second_rounded", [P, PACK * PASS], BF16, ROUNDED_AT)
+        second_rounded = placed("second_rounded", [P, PACK * PASS], BF16, ROUNDED_AT - PASS)
         nc.gpsimd.tensor_copy(second_rounded[:].rearrange("p (t m j) -> p t m j", t=PACK, j=PACK),
                               w1_later[1][:].rearrange("p j (m t) -> p t m j", t=PACK))
-        last_rounded = own("last_rounded", [P, PASS], BF16)
-        nc.gpsimd.tensor_copy(last_rounded[:].rearrange("p (m j) -> p m j", j=PACK),
-                              w1_later[2][:].rearrange("p j (m t) -> p t m j", t=PACK)[:, PACK - 1])
         make_colour(1, nc.vector.tensor_copy)
         phase_half(EARLY_PHASE, 0, nc.vector.tensor_copy)
         phase_half(EARLY_PHASE, 1, nc.vector.tensor_copy)
@@ -358,13 +353,11 @@ def tile_list_chord_phase_voicings_kernel(tc, tab_words, tab_scales, offs, pos1,
             if i == 0:
                 quantise_w1(PACK, placed("w1_codes1", [P, PASS], U32, size_at(i) - PICK_BYTES // 2), second_rounded)
             if i == 1:
-                third_rounded = placed("third_rounded", [P, (PACK - 1) * PASS], BF16, size_at(i) - PICK_BYTES // 2)
-                nc.vector.tensor_copy(third_rounded[:].rearrange("p (t m j) -> p m j t", t=PACK - 1, j=PACK),
-                                      w1_later[2][:].rearrange("p j (m t) -> p m j t", t=PACK)[:, :, :, 0 : PACK - 1])
+                third_rounded = placed("third_rounded", [P, PACK * PASS], BF16, size_at(i) - PICK_BYTES // 2)
+                nc.vector.tensor_copy(third_rounded[:].rearrange("p (t m j) -> p m j t", t=PACK, j=PACK),
+                                      w1_later[2][:].rearrange("p j (m t) -> p m j t", t=PACK))
             if i == 2:
-                quantise_w1(2 * PACK, placed("w1_codes2", [P, PASS - P], U32, size_at(i) + PICK_BYTES // 2), third_rounded)
-            if i == 5:
-                quantise_w1(TILES - 1, after_cosine(i, [P, P], U32), last_rounded)
+                quantise_w1(2 * PACK, placed("w1_codes2", [P, PASS], U32, size_at(i) + PICK_BYTES // 2), third_rounded)
             if i + 2 == WAIT_PHASE:
                 phase_half(WAIT_PHASE, 0, nc.vector.tensor_copy)
             if i == 6:
@@ -468,10 +461,11 @@ def tile_list_chord_phase_voicings_kernel(tc, tab_words, tab_scales, offs, pos1,
             score_passes(last_pass, n)
             store_scores(n, on_vector)
 
-        score_passes(0, 1)
         def fused(side, n):
-            product((sin_terms, cos_terms)[side], (bass_of, substitute_of)[side], third, PIECES[n], last_trig[side][:, 0, within_half(n)])
+            product((sin_terms, cos_terms)[side], (bass_of, substitute_of)[side], third, PIECES[n],
+                    last_trig[side][:, 0, within_half(n)])
 
+        score_passes(0, 1)
         product(sin_terms, bass_of, third, halves[0], trig[third][0][:])
         product(cos_terms, substitute_of, third, halves[0], trig[third][1][:])
         turned_late = turn(nc.vector, 1, PIECES[2], after_half(third, [P, P * PACK], BF16), vector_run)

@@ -74,6 +74,8 @@ def tile_list_chord_phase_voicings_kernel(tc, tab_words, tab_scales, offs, pos1,
         w4_rows_later = own("w4_rows_later", [P, PASS], U8)
         w4_plane_last = own("w4_plane_last", [P, PASS], U8)
         w8_planes = own("w8_planes", [P, N], U8)
+        tab_plane = own("tab_plane", [P, T], U8)
+        nc.gpsimd.memset(tab_plane[:].bitcast(I32)[P // 2 :, :], 0)
         zero = keep.tile([P, 1], F32, name="zero")
         nc.gpsimd.memset(zero[:], 0.0)
         nc.gpsimd.memset(w4_rows_first[:].bitcast(I32), 0)
@@ -86,10 +88,13 @@ def tile_list_chord_phase_voicings_kernel(tc, tab_words, tab_scales, offs, pos1,
         nc.gpsimd.tensor_scalar(half_pi[:], sin_zero[:], math.pi / 2, None, ALU.add)
 
         offs_sb = load_list("offs_sb", offs, S)
-        tab_plane = own("tab_plane", [P, T], U8)
         for q in range(P // QUADRANT):
-            nc.sync.dma_start(out=tab_plane[:].bitcast(I32)[QUADRANT * q : QUADRANT * (q + 1), :],
-                              in_=tab_scales[0][4 * q : 4 * q + 4, :].bitcast(I32).partition_broadcast(QUADRANT // 4))
+            rows = tab_scales[0][4 * q : 4 * q + 4, :].bitcast(I32)
+            if q < 2:
+                nc.sync.dma_start(out=tab_plane[:].bitcast(I32)[QUADRANT * q : QUADRANT * (q + 1), :],
+                                  in_=rows.partition_broadcast(QUADRANT // 4))
+            else:
+                nc.sync.dma_start(out=tab_plane[:].bitcast(I32)[QUADRANT * q : QUADRANT * q + 4, :], in_=rows)
         tab_sb = placed("tab_sb", [P, T], I32, TABLE_AT)
         nc.sync.dma_start(out=tab_sb[:], in_=tab_words[0].rearrange("p t i -> p (t i)").bitcast(I32))
         w1_rows = w1.rearrange("(p j) r -> p j r", j=PACK)

import math
from contextlib import ExitStack

import concourse.mybir as mybir

K, T, S, H, B, N = 512, 2048, 1024, 1536, 512, 768
FLOPS = 2 * K * H * S * 2 + 2 * H * N * B

F32 = mybir.dt.float32
BF16 = mybir.dt.bfloat16
I32 = mybir.dt.int32
U32 = mybir.dt.uint32
U16 = mybir.dt.uint16
U8 = mybir.dt.uint8
FP8X4 = mybir.dt.float8_e4m3fn_x4
FP4X4 = mybir.dt.float4_e2m1fn_x4
ACT = mybir.ActivationFunctionType
ALU = mybir.AluOpType

P = 128
PACK = 4
BANK = 512
QUADRANT = 32
PASS = P * PACK
PASSES = H // PASS
TILES = H // P
OUT_TILES = N // P
PER_COLUMN = 16
AHEAD = 4

ROW_BYTES = 4 * S
PICK_BYTES = 4 * B
PART_BYTES = 4 * PACK * PASS
ROUNDED_BYTES = 2 * PACK * PASS

RUNS = {4: (5, 6, 7, 8), 8: (9, 10, 11)}
EARLY_PHASE = 1
FIRST_RUN_PHASES = (2, 3)
WAIT_PHASE = 5
RUN_PHASE = 8
PIECES = (slice(0, 256), slice(256, 384), slice(384, 512))

W1_AT = 0
AREAS_AT = W1_AT + PASSES * PART_BYTES
COLOURS_AT = AREAS_AT + 3 * ROW_BYTES
ROUNDED_AT = COLOURS_AT + 8 * ROW_BYTES
TABLE_AT = ROUNDED_AT + 3 * ROUNDED_BYTES
GATED_AT = TABLE_AT + 4 * PASSES * N


def tile_list_chord_phase_voicings_kernel(tc, tab_words, tab_scales, offs, pos1, pos2, pos3, w1, w4_words,
                                                       w4_scales, w8_words, w8_scales, prior, out):
    nc = tc.nc
    with ExitStack() as ctx:
        keep = ctx.enter_context(tc.tile_pool(name="keep", bufs=1))
        ring = ctx.enter_context(tc.tile_pool(name="ring", bufs=AHEAD))
        spot = ctx.enter_context(tc.tile_pool(name="spot", bufs=1))
        psum = ctx.enter_context(tc.psum_pool(name="psum", bufs=1))

        def placed(name, shape, dtype, offset):
            tile = spot.tile(shape, dtype, name=name, align_bytes=64, offset=offset)
            return tile

        def own(name, shape, dtype):
            tile = keep.tile(shape, dtype, name=name, align_bytes=64)
            return tile

        def load_list(name, entries, count):
            tile = keep.tile([P, count // PER_COLUMN], U16, name=name)
            nc.sync.dma_start(tile[:], entries)
            return tile

        w4_rows_first = own("w4_rows_first", [P, PASS], U8)
        w4_rows_later = own("w4_rows_later", [P, PASS], U8)
        w4_plane_last = own("w4_plane_last", [P, PASS], U8)
        w8_planes = own("w8_planes", [P, N], U8)
        tab_plane = own("tab_plane", [P, T], U8)
        nc.gpsimd.memset(tab_plane[:].bitcast(I32)[P // 2 :, :], 0)
        zero = keep.tile([P, 1], F32, name="zero")
        nc.gpsimd.memset(zero[:], 0.0)
        nc.gpsimd.memset(w4_rows_first[:].bitcast(I32), 0)
        nc.gpsimd.memset(w4_rows_later[:].bitcast(I32), 0)
        nc.gpsimd.memset(w4_plane_last[:].bitcast(I32), 0)
        nc.gpsimd.memset(w8_planes[:].bitcast(I32), 0)
        sin_zero = keep.tile([P, 1], F32, name="sin_zero")
        nc.scalar.activation(sin_zero[:], zero[:], ACT.Sin)
        half_pi = keep.tile([P, 1], F32, name="half_pi")
        nc.gpsimd.tensor_scalar(half_pi[:], sin_zero[:], math.pi / 2, None, ALU.add)

        offs_sb = load_list("offs_sb", offs, S)
        for q in range(P // QUADRANT):
            rows = tab_scales[0][4 * q : 4 * q + 4, :].bitcast(I32)
            if q < 2:
                nc.sync.dma_start(out=tab_plane[:].bitcast(I32)[QUADRANT * q : QUADRANT * (q + 1), :],
                                  in_=rows.partition_broadcast(QUADRANT // 4))
            else:
                nc.sync.dma_start(out=tab_plane[:].bitcast(I32)[QUADRANT * q : QUADRANT * q + 4, :], in_=rows)
        tab_sb = placed("tab_sb", [P, T], I32, TABLE_AT)
        nc.sync.dma_start(out=tab_sb[:], in_=tab_words[0].rearrange("p t i -> p (t i)").bitcast(I32))
        w1_rows = w1.rearrange("(p j) r -> p j r", j=PACK)

        def load_w1(name, place, first, width):
            raw = placed(name, [P, PACK, width], F32, place)
            nc.sync.dma_start(out=raw[:], in_=w1_rows[:, :, first : first + width])
            return raw

        for q in range(P // QUADRANT):
            nc.sync.dma_start(out=w4_rows_first[:].bitcast(I32)[QUADRANT * q : QUADRANT * q + 4, :],
                              in_=w4_scales[0][4 * q : 4 * q + 4, 0:PASS].bitcast(I32))
        w4_raw_first = own("w4_raw_first", [P, PASS // 2], I32)
        nc.sync.dma_start(out=w4_raw_first[:], in_=w4_words[0].bitcast(I32)[:, 0 : PASS // 2])
        w1_halves = [load_w1("w1_half%d" % h, place, h * PASS // 2, PASS // 2) for h, place in enumerate((W1_AT, COLOURS_AT))]
        w4_raw_later = placed("w4_raw_later", [P, (H - PASS) // 2], I32, COLOURS_AT + 2 * ROW_BYTES - PICK_BYTES // 2)
        nc.sync.dma_start(out=w4_raw_later[:], in_=w4_words[0].bitcast(I32)[:, PASS // 2 :])
        for q in range(P // QUADRANT):
            nc.sync.dma_start(out=w4_rows_later[:].bitcast(I32)[QUADRANT * q : QUADRANT * q + 4 * (PASSES - 1), :],
                              in_=w4_scales[0][4 * q : 4 * q + 4, PASS:].bitcast(I32).rearrange("j (g c) -> g j c", g=PASSES - 1))
        current_of = load_list("current_of", pos1, B)
        w1_later = {1: load_w1("w1_part1", W1_AT + PART_BYTES, PASS, PASS)}
        bass_of = load_list("bass_of", pos3, B)
        substitute_of = load_list("substitute_of", pos2, B)
        w1_later[2] = load_w1("w1_part2", W1_AT + 2 * PART_BYTES, 2 * PASS, PASS)

        picked_plane = own("picked_plane", [P, S], U8)
        nc.vector.tensor_copy(picked_plane[:], tab_plane[:].indirect(offs_sb[:]))
        picked_codes = []
        w4_first = own("w4_first", [P, PASS], U16)
        nc.scalar.copy(w4_first[:].rearrange("p (t m) -> p m t", m=P),
                       w4_raw_first[:].bitcast(U16).rearrange("p (m t) -> p m t", t=PACK))
        for h in range(S // BANK):
            codes = own("picked_codes%d" % h, [P, BANK], U32)
            entries = offs_sb[:, h * BANK // PER_COLUMN : (h + 1) * BANK // PER_COLUMN]
            nc.vector.tensor_copy(codes[:], tab_sb[:].bitcast(U32).indirect(entries))
            picked_codes.append(codes)
            if h == 0:
                w4_plane_first = own("w4_plane_first", [P, PASS], U8)
                nc.gpsimd.tensor_copy(w4_plane_first[:].rearrange("p (t m) -> p t m", t=PACK),
                                      w4_rows_first[:].rearrange("p (m t) -> p t m", t=PACK))

        first_rounded = placed("first_rounded", [P, PACK, P, PACK], BF16, ROUNDED_AT)

        def round_first(h, copy, first, last):
            rounded = first_rounded[:, :, h * P // 2 + first : h * P // 2 + last, :].rearrange("p t m j -> p m j t")
            copy(rounded, w1_halves[h][:, :, first * PACK : last * PACK].rearrange("p j (m t) -> p m j t", t=PACK))

        round_first(0, nc.scalar.copy, 0, P // 2)
        round_first(1, nc.scalar.copy, 0, P // 4)
        round_first(1, nc.vector.tensor_copy, P // 4, P // 2)

        stationary = {}

        def quantise(codes, plane, rounded):
            nc.vector.quantize_mx(out=codes.bitcast(FP8X4), scales=plane, in_=rounded)

        first_codes = own("first_codes", [P, PASS], U32)
        first_plane = own("first_plane", [P, PASS], U8)

        def quantise_first(first, last):
            cols = slice(first * P, last * P)
            quantise(first_codes[:, cols], first_plane[:, cols], first_rounded[:, first:last].rearrange("p t m j -> p (t m j)"))
            for t in range(first, last):
                stationary[t] = (first_codes[:, t * P : (t + 1) * P], first_plane[:, t * P : (t + 1) * P])

        quantise_first(0, 1)
        quantise_first(1, 2)
        w4_codes = {0: w4_first[:]}
        w4_plane = {0: w4_plane_first[:]}
        w4_later = own("w4_later", [P, H - PASS], U16)
        nc.vector.tensor_copy(w4_later[:].rearrange("p (g t m) -> p g t m", t=PACK, m=P),
                              w4_raw_later[:].bitcast(U16).rearrange("p (g m t) -> p g t m", t=PACK, m=P))
        for g in range(1, PASSES):
            w4_codes[g] = w4_later[:, (g - 1) * PASS : g * PASS]
        quantise_first(2, 4)
        w4_planes_later = placed("w4_planes_later", [P, PASS], U8, ROUNDED_AT + ROUNDED_BYTES - PASS)
        nc.gpsimd.tensor_copy(w4_planes_later[:].rearrange("p (t m) -> p t m", t=PACK),
                              w4_rows_later[:].rearrange("p (m t) -> p t m", t=PACK))
        w4_plane[1] = w4_planes_later[:]
        w4_plane[2] = w4_plane_last[:]

        w8_sb = placed("w8_sb", [P, PASSES, N], I32, TABLE_AT)
        nc.sync.dma_start(out=w8_sb[:], in_=w8_words.rearrange("a p c i -> p a (c i)").bitcast(I32))
        nc.sync.dma_start(out=w4_plane_last[:].bitcast(I32)[0 : P - 4, :], in_=w4_planes_later[:].bitcast(I32)[4:P, :])
        for q in range(P // QUADRANT):
            nc.sync.dma_start(out=w8_planes[:].bitcast(I32)[QUADRANT * q : QUADRANT * q + 4 * PASSES, :],
                              in_=w8_scales[:, 4 * q : 4 * q + 4, :].bitcast(I32))
        prior_sb = own("prior_sb", [P, OUT_TILES], F32)
        with nc.allow_non_contiguous_dma(reason="one prior value for each output row"):
            nc.sync.dma_start(out=prior_sb[:], in_=prior.rearrange("(c p) -> p c", p=P))

        def bank_tile(number):
            bank = psum.tile([P, BANK], F32, name="bank%d" % number)
            return bank

        def first_stage(lhsT, lhsT_scale, h, number):
            bank = bank_tile(number)
            nc.tensor.matmul_mx(out=bank[:], lhsT=lhsT, lhsT_scale=lhsT_scale, rhs=picked_codes[h][:].bitcast(FP8X4),
                                rhs_scale=picked_plane[:, h * BANK : (h + 1) * BANK], start=True, stop=True)
            return bank

        phase = {}
        phase_banks = {}
        colour = {}
        angle = {}

        turn_taken = []

        def next_bank():
            turn_taken.append(0)
            return 2 + (len(turn_taken) - 1) % 6

        def on_vector(i, h):
            return i == EARLY_PHASE or (h == 0 and i in (RUN_PHASE, WAIT_PHASE) + FIRST_RUN_PHASES)

        def phase_sum(i, h):
            if (i, h) not in phase_banks:
                codes, plane = stationary[i]
                phase_banks[i, h] = first_stage(codes.bitcast(FP8X4), plane, h, next_bank() if on_vector(i, h) else h)

        def phase_half(i, h, copy):
            if h == 0:
                if i == EARLY_PHASE:
                    phase[i] = own("early_phase", [P, S], F32)
                elif i == WAIT_PHASE:
                    phase[i] = placed("phase%d" % i, [P, S], F32, size_at(i - 2))
                elif i == RUN_PHASE or i in FIRST_RUN_PHASES:
                    phase[i] = own("run_phase%d" % i, [P, S], F32)
                else:
                    phase[i] = placed("phase%d" % i, [P, S], F32, AREAS_AT + (i % 3) * ROW_BYTES)
            phase_sum(i, h)
            copy(phase[i][:, h * BANK : (h + 1) * BANK], phase_banks[i, h][:])

        def colour_at(i):
            return COLOURS_AT + (i % 8) * ROW_BYTES

        colour_banks = {}

        def colour_sum(i, h):
            if (i, h) not in colour_banks:
                g, t = divmod(i, PACK)
                cols = slice(t * P, (t + 1) * P)
                colour_banks[i, h] = first_stage(w4_codes[g][:, cols].bitcast(FP4X4), w4_plane[g][:, cols], h, next_bank())

        def colour_half(i, h, copy):
            if h == 0:
                colour[i] = placed("colour%d" % i, [P, S], F32, colour_at(i))
            colour_sum(i, h)
            copy(colour[i][:, h * BANK : (h + 1) * BANK], colour_banks[i, h][:])

        def make_colour(i, copy):
            for h in range(2):
                colour_half(i, h, copy)

        def size_at(i):
            if i in RUNS:
                return colour_at(RUNS[i][1]) - PICK_BYTES // 2
            return GATED_AT + (2 * i + 1) * PICK_BYTES

        def after_cosine(i, shape, dtype):
            return placed("after_cosine%d" % i, shape, dtype, size_at(i))

        def entries_of(chords, bars):
            return chords[:, bars.start // PER_COLUMN : bars.stop // PER_COLUMN]

        cos_terms = {}
        sin_terms = {}

        def product(terms, chords, i, bars, factor):
            g, t = divmod(i, PACK)
            nc.vector.tensor_tensor(terms[g][:, t, bars], colour[i][:].indirect(entries_of(chords, bars)), factor, ALU.mult)

        def turn(engine, g, bars, rounded, run):
            engine.tensor_tensor(rounded[:].rearrange("p (c i t) -> p c t i", i=run, t=PACK),
                                 cos_terms[g][:, :, bars].rearrange("p t (c i) -> p c t i", i=run),
                                 sin_terms[g][:, :, bars].rearrange("p t (c i) -> p c t i", i=run), ALU.subtract)
            return rounded

        vector_run, gpsimd_run = 2, 4

        def quantise_w1(first, codes, rounded):
            plane = own("w1_plane%d" % first, [P, codes.shape[1]], U8)
            quantise(codes[:], plane[:], rounded[:])
            for t in range(codes.shape[1] // P):
                stationary[first + t] = (codes[:, t * P : (t + 1) * P], plane[:, t * P : (t + 1) * P])

        z_codes = {}
        z_plane = {}

        def quantise_z(g, first, codes, rounded):
            plane = own("z_plane%d_%d" % (g, first), [P, codes.shape[1]], U8)
            quantise(codes[:], plane[:], rounded)
            for n in range(first, len(PIECES)):
                cols = slice(PIECES[n].start - PIECES[first].start, PIECES[n].stop - PIECES[first].start)
                if cols.stop <= codes.shape[1]:
                    z_codes[g, n] = codes[:, cols]
                    z_plane[g, n] = plane[:, cols]

        for h in range(2):
            colour_sum(0, h)
            colour_sum(1, h)
        for i in range(2):
            for h in range(2):
                phase_sum(i, h)
        make_colour(0, nc.scalar.copy)
        phase_half(0, 0, nc.scalar.copy)
        phase_half(0, 1, nc.scalar.copy)
        second_rounded = placed("second_rounded", [P, PACK * PASS], BF16, ROUNDED_AT - PASS)
        nc.gpsimd.tensor_copy(second_rounded[:].rearrange("p (t m j) -> p t m j", t=PACK, j=PACK),
                              w1_later[1][:].rearrange("p j (m t) -> p t m j", t=PACK))
        make_colour(1, nc.vector.tensor_copy)
        phase_half(EARLY_PHASE, 0, nc.vector.tensor_copy)
        phase_half(EARLY_PHASE, 1, nc.vector.tensor_copy)
        make_colour(2, nc.vector.tensor_copy)
        make_colour(3, nc.vector.tensor_copy)
        make_colour(4, nc.vector.tensor_copy)
        for i in FIRST_RUN_PHASES:
            phase_half(i, 0, nc.vector.tensor_copy)

        turned = {}
        all_bars = slice(0, B)
        run_number = {i: n for n, i in enumerate(sorted(RUNS))}
        for i in range(TILES - 3):
            g, t = divmod(i, PACK)
            if t == 0:
                sin_terms[g] = keep.tile([P, PACK, B], F32, name="sin_terms", tag="sin_terms%d" % (g % 2))
                cos_terms[g] = keep.tile([P, PACK, B], F32, name="cos_terms", tag="cos_terms%d" % (g % 2))
            if i in RUNS:
                result_at = ROUNDED_AT + (1 + run_number[i]) * ROUNDED_BYTES
                sine = placed("sine%d" % i, [P, B], F32, result_at)
            else:
                sine = ring.tile([P, B], F32, name="sine")
            cosine = ring.tile([P, B], F32, name="cosine")
            size = placed("size%d" % i, [P, S + B if i in RUNS else B], F32, size_at(i))[:, 0:B]

            angle[i] = placed("angle%d" % i, [P, B], F32, AREAS_AT + ((i + 2) % 3) * ROW_BYTES)
            nc.scalar.activation(angle[i][:], phase[i][:].indirect(current_of[:]), ACT.Copy)
            if i + 1 != EARLY_PHASE:
                phase_half(i + 1, 1, nc.scalar.copy)
            if i == 0:
                nc.scalar.activation(sine[:], angle[i][:], ACT.Sin)
            nc.scalar.activation(size, angle[i][:], ACT.Abs)
            if i > 0:
                nc.scalar.activation(sine[:], angle[i][:], ACT.Sin)
            nc.scalar.activation(cosine[:], size, ACT.Sin, bias=half_pi[:], scale=-1.0)
            if i + 2 not in (RUN_PHASE, WAIT_PHASE) + FIRST_RUN_PHASES:
                phase_half(i + 2, 0, nc.scalar.copy)

            product(sin_terms, bass_of, i, all_bars, sine[:])
            product(cos_terms, substitute_of, i, all_bars, cosine[:])

            if i in RUNS:
                bars = slice(0, P * len(RUNS[i]))
                turned[g - 1] = turn(nc.gpsimd, g - 1, bars, placed("turned%d" % g, [P, bars.stop * PACK], BF16, result_at), gpsimd_run)
                for later in RUNS[i]:
                    make_colour(later, nc.vector.tensor_copy)
            if i == 4:
                phase_half(RUN_PHASE, 0, nc.vector.tensor_copy)

            if i == 0:
                quantise_w1(PACK, placed("w1_codes1", [P, PASS], U32, size_at(i) - PICK_BYTES // 2), second_rounded)
            if i == 1:
                third_rounded = placed("third_rounded", [P, PACK * PASS], BF16, size_at(i) - PICK_BYTES // 2)
                nc.vector.tensor_copy(third_rounded[:].rearrange("p (t m j) -> p m j t", t=PACK, j=PACK),
                                      w1_later[2][:].rearrange("p j (m t) -> p m j t", t=PACK))
            if i == 2:
                quantise_w1(2 * PACK, placed("w1_codes2", [P, PASS], U32, size_at(i) + PICK_BYTES // 2), third_rounded)
            if i + 2 == WAIT_PHASE:
                phase_half(WAIT_PHASE, 0, nc.vector.tensor_copy)
            if i == 6:
                quantise_z(0, 1, after_cosine(i, [P, P], U32), turned[0][:, PIECES[1].start * PACK : PIECES[1].stop * PACK])

        last_pass = PASSES - 1
        third, early, late = TILES - 3, TILES - 2, TILES - 1
        halves = [slice(0, B // 2), slice(B // 2, B)]
        trig = {}

        last_angles = placed("last_angles", [P, 3, B], F32, GATED_AT + 14 * PICK_BYTES)

        def pick(i):
            nc.scalar.activation(last_angles[:, i - third, :], phase[i][:].indirect(current_of[:]), ACT.Copy)

        def first_half_trig(i):
            sines = own("half_sines%d" % i, [P, B // 2], F32)
            cosines = own("half_cosines%d" % i, [P, B // 2], F32)
            size = keep.tile([P, B // 2], F32, name="half_size", tag="half_size%d" % i, align_bytes=64)
            nc.scalar.activation(size[:], last_angles[:, i - third, halves[0]], ACT.Abs)
            nc.scalar.activation(sines[:], last_angles[:, i - third, halves[0]], ACT.Sin)
            nc.scalar.activation(cosines[:], size[:], ACT.Sin, bias=half_pi[:], scale=-1.0)
            trig[i] = (sines, cosines)

        def after_half(i, shape, dtype):
            tile = keep.tile(shape, dtype, name="after_half", tag="half_size%d" % i, align_bytes=64)
            return tile

        last_colours = own("last_colours", [P, 2, 2, 2, P], F32)

        def fetch(side, i, n):
            chords = (bass_of, substitute_of)[side]
            nc.scalar.activation(last_colours[:, n - 1, side, i - early, :], colour[i][:].indirect(entries_of(chords, PIECES[n])), ACT.Copy)

        pick(third)
        phase_half(early, 1, nc.scalar.copy)
        first_half_trig(third)
        phase_half(late, 0, nc.scalar.copy)
        pick(early)
        phase_half(late, 1, nc.scalar.copy)
        first_half_trig(early)
        pick(late)
        first_half_trig(late)
        last_trig = [own("last_trig%d" % side, [P, 3, B // 2], F32) for side in range(2)]
        last_size = keep.tile([P, 3, B // 2], F32, name="last_size", tag="last_size", align_bytes=64)
        nc.scalar.activation(last_size[:], last_angles[:, :, halves[1]], ACT.Abs)
        nc.scalar.activation(last_trig[0][:], last_angles[:, :, halves[1]], ACT.Sin)
        nc.scalar.activation(last_trig[1][:], last_size[:], ACT.Sin, bias=half_pi[:], scale=-1.0)
        for n in (1, 2):
            for side in range(2):
                fetch(side, early, n)
                fetch(side, late, n)

        groups = {0: [(0, 1), (2, 3), (4, 5)], 1: [(0, 1, 2), (3, 4, 5)], 2: [(0, 1), (2, 3), (4, 5)]}
        bank_numbers = {0: (0, 1, 2), 1: (4, 5), 2: (3, 6, 7)}
        score_banks = {n: [bank_tile(number) for number in bank_numbers[n]] for n in range(len(PIECES))}

        def score_passes(g, n):
            width = PIECES[n].stop - PIECES[n].start
            for bank, members in zip(score_banks[n], groups[n]):
                for place, c in enumerate(members):
                    cols = slice(c * P, (c + 1) * P)
                    nc.tensor.matmul_mx(out=bank[:, place * width : (place + 1) * width], lhsT=w8_sb[:, g, cols].bitcast(FP8X4),
                                        lhsT_scale=w8_planes[4 * g :, cols], rhs=z_codes[g, n].bitcast(FP8X4),
                                        rhs_scale=z_plane[g, n], start=(g == 0 and c == members[0]),
                                        stop=(g == last_pass and c == members[-1]))

        out_rows = out.rearrange("(c p) m -> p c m", p=P)

        def store_scores(n, on_vector):
            width = PIECES[n].stop - PIECES[n].start
            for number, (bank, members) in enumerate(zip(score_banks[n], groups[n])):
                count = len(members)
                first = members[0]
                result = placed("result%d_%d" % (n, first), [P, count, width], F32,
                                W1_AT + 4 * (OUT_TILES * PIECES[n].start + first * width))
                if number in on_vector:
                    nc.vector.tensor_tensor(result[:], bank[:, 0 : count * width].rearrange("p (c m) -> p c m", c=count),
                                            prior_sb[:, first : first + count].unsqueeze(2).to_broadcast([P, count, width]),
                                            ALU.add)
                else:
                    for place, c in enumerate(members):
                        nc.scalar.activation(result[:, place, :], bank[:, place * width : (place + 1) * width], ACT.Identity,
                                             bias=prior_sb[:, c : c + 1])
                nc.sync.dma_start(out=out_rows[:, first : first + count, PIECES[n]], in_=result[:])

        def within_half(n):
            return slice(PIECES[n].start - B // 2, PIECES[n].stop - B // 2)

        def plain_product(side, n):
            terms = (sin_terms, cos_terms)[side]
            nc.vector.tensor_tensor(terms[last_pass][:, PACK - 2 :, PIECES[n]], last_colours[:, n - 1, side],
                                    last_trig[side][:, 1:, within_half(n)], ALU.mult)

        def turn_last(n, rounded):
            return turn(nc.vector, last_pass, PIECES[n], rounded, vector_run)

        def close(n, rounded, on_vector):
            width = PIECES[n].stop - PIECES[n].start
            quantise_z(last_pass, n, own("last_codes%d" % n, [P, width], U32), rounded[:])
            score_passes(last_pass, n)
            store_scores(n, on_vector)

        def fused(side, n):
            product((sin_terms, cos_terms)[side], (bass_of, substitute_of)[side], third, PIECES[n],
                    last_trig[side][:, 0, within_half(n)])

        score_passes(0, 1)
        product(sin_terms, bass_of, third, halves[0], trig[third][0][:])
        product(cos_terms, substitute_of, third, halves[0], trig[third][1][:])
        turned_late = turn(nc.vector, 1, PIECES[2], after_half(third, [P, P * PACK], BF16), vector_run)
        for g, i in enumerate((early, late)):
            product(sin_terms, bass_of, i, halves[0], trig[i][0][:])
            product(cos_terms, substitute_of, i, halves[0], trig[i][1][:])
            quantise_z(g, 0, after_half(i, [P, B // 2], U32), turned[g][:, 0 : B // 2 * PACK])
            score_passes(g, 0)
        first_turned = turn_last(0, keep.tile([P, B // 2 * PACK], BF16, name="first_turned", tag="first", align_bytes=64))
        quantise_z(1, 1, own("z_codes1_1", [P, P], U32), turned[1][:, PIECES[1].start * PACK :])
        score_passes(1, 1)
        close(0, first_turned, ())
        fused(0, 1)
        fused(1, 1)
        plain_product(0, 1)
        plain_product(1, 1)
        quantise_z(0, 2, keep.tile([P, P], U32, name="z_codes0_2", tag="first", align_bytes=64), turned[0][:, PIECES[2].start * PACK :])
        score_passes(0, 2)
        fused(0, 2)
        second_turned = turn_last(1, keep.tile([P, P * PACK], BF16, name="second_turned", tag="second", align_bytes=64))
        fused(1, 2)
        close(1, second_turned, ())
        plain_product(0, 2)
        quantise_z(1, 2, keep.tile([P, P], U32, name="z_codes1_2", tag="second", align_bytes=64), turned_late[:])
        score_passes(1, 2)
        plain_product(1, 2)
        close(2, turn_last(2, own("third_turned", [P, P * PACK], BF16)), (1, 2))
